import numpy as np
import ml_dtypes


def mxq(x, axis, fmt="e4m3"):
    dtype, down = {"e4m3": (ml_dtypes.float8_e4m3fn, 7), "e5m2": (ml_dtypes.float8_e5m2, 14)}[fmt]
    v = np.moveaxis(np.asarray(x, np.float32).astype(ml_dtypes.bfloat16).astype(np.float64), axis, -1)
    blocks = v.reshape(v.shape[:-1] + (-1, 32))
    amax = np.abs(blocks).max(-1, keepdims=True)
    byte = np.maximum(np.where(amax > 0, np.frexp(amax)[1] - 1 + 127, 0) - down, 1)
    scale = np.exp2(byte - 127.0)
    codes = (blocks / scale).astype(np.float32).astype(dtype).astype(np.float64)
    return np.moveaxis((codes * scale).reshape(v.shape), -1, axis)


WIDE = False


def mx_kscale(k):
    if not WIDE:
        return np.ones(k)
    levels = np.array([10, -10, 5, -5, 0])
    if k % 512:
        return np.exp2(np.random.permutation(np.resize(levels, k // 32))).repeat(32)
    a = np.empty((k // 512, 16))
    for p in range(k // 512):
        a[p, :8] = np.random.permutation(np.resize(levels, 8))
        for g in range(8):
            far = levels[np.abs(levels - a[p, g]) >= 10]
            a[p, g + 8] = far[np.random.randint(len(far))]
    return np.exp2(a.ravel()).repeat(32)


BF16 = ml_dtypes.bfloat16


def bf(x):
    return np.asarray(x, np.float32).astype(BF16)


def f64(x):
    return np.asarray(x).astype(np.float64)


E2M1 = np.array([0.0, 0.5, 1.0, 1.5, 2.0, 3.0, 4.0, 6.0, -0.0, -0.5, -1.0, -1.5, -2.0, -3.0, -4.0, -6.0])


def pack_weight(w, fmt):
    k, n = w.shape
    w = f64(bf(w)).reshape(k // 32, 32, n)
    amax = np.abs(w).max(1)
    if fmt == "e4m3":
        byte = np.frexp(amax)[1] - 1 + 127 - 7
    else:
        mant, ex = np.frexp(amax / 6.0)
        byte = np.where(mant > 0.5, ex, ex - 1) + 127
    byte = np.clip(np.where(amax > 0, byte, 1), 1, 254)
    scaled = (w * np.exp2(127.0 - byte)[:, None, :]).reshape(k, n).astype(np.float32)
    by_word = np.ascontiguousarray(scaled.reshape(k // 512, 128, 4, n).transpose(0, 1, 3, 2))
    if fmt == "e4m3":
        words = by_word.astype(ml_dtypes.float8_e4m3fn).view(np.uint8)
    else:
        c = by_word.astype(ml_dtypes.float4_e2m1fn).view(np.uint8) & 0xF
        words = c[..., 0::2] | (c[..., 1::2] << 4)
    return np.ascontiguousarray(words), np.ascontiguousarray(byte.astype(np.uint8).reshape(k // 512, 16, n))


def unpack_weight(words, scales, fmt):
    g, p, n, _ = words.shape
    if fmt == "e4m3":
        vals = np.ascontiguousarray(words).view(ml_dtypes.float8_e4m3fn).astype(np.float64)
    else:
        nib = np.empty((g, p, n, 4), np.uint8)
        nib[..., 0::2] = words & 0xF
        nib[..., 1::2] = words >> 4
        vals = E2M1[nib]
    vals = vals * np.repeat(np.exp2(scales.astype(np.float64) - 127.0), 8, axis=1)[..., None]
    return vals.transpose(0, 1, 3, 2).reshape(g * 512, n)
def pack4(w):
    words, scales = pack_weight(w, "e2m1")
    return words.reshape(words.shape[0], 128, -1), scales


def unpack4(words, scales):
    return unpack_weight(words.reshape(words.shape[0], 128, -1, 2), scales, "e2m1")


E4M3FN = np.array([(-1.0 if i & 128 else 1.0) * ((1.0 + (i & 7) / 8.0) * 2.0 ** (((i >> 3) & 15) - 7) if i & 120 else (i & 7) * 2.0 ** -9) for i in range(256)])


def e4m3fn_bytes(y):
    return np.clip(np.asarray(y, np.float64), -448.0, 448.0).astype(np.float32).astype(ml_dtypes.float8_e4m3fn).view(np.uint8)


def e4m3fn_values(b):
    return E4M3FN[b]

def planes(Y):
    n, m = Y.shape
    b = f64(bf(Y)).reshape(n // 32, 32, m)
    amax = np.abs(b).max(1)
    byte = np.clip(np.where(amax > 0, np.frexp(amax)[1] - 1 + 127 - 7, 1), 1, 254)
    codes = (b * np.exp2(127.0 - byte)[:, None, :]).reshape(n, m).astype(np.float32).astype(ml_dtypes.float8_e4m3fn).view(np.uint8)
    words = codes.reshape(n // 512, 128, 4, m).transpose(0, 1, 3, 2)
    return np.ascontiguousarray(words), np.ascontiguousarray(byte.astype(np.uint8).reshape(n // 512, 16, m))


T, K, F, N, B = 768, 1536, 1024, 2048, 128

def setup_inputs():
    s = mx_kscale(K)
    t = mx_kscale(F)
    X = np.random.randn(T, K) * np.exp(0.3 * np.random.randn(T, 1)) * s
    X_scale = (np.abs(X).reshape(T, K // B, B).max(axis=2) / 448.0).astype(np.float32)
    X_bytes = e4m3fn_bytes(X / np.repeat(f64(X_scale), B, axis=1))
    W = np.random.randn(K, F) / np.sqrt(K) / s[:, None]
    W_scale = (np.abs(W).reshape(K // B, B, F // B, B).max(axis=(1, 3)) / 448.0).astype(np.float32)
    W_bytes = e4m3fn_bytes(W / np.repeat(np.repeat(f64(W_scale), B, axis=0), B, axis=1))
    gain = bf(np.exp(0.3 * np.random.randn(F)) * t)
    V_words, V_scales = pack4(1.2 * np.random.randn(F, N) / np.sqrt(F) / t[:, None])
    item_bias = bf(0.5 * np.random.randn(N))
    bid = bf(np.exp(0.8 * np.random.randn(N)))
    return {"X_bytes": X_bytes, "X_scale": X_scale, "W_bytes": W_bytes, "W_scale": W_scale,
            "gain": gain, "V_words": V_words, "V_scales": V_scales,
            "item_bias": item_bias, "bid": bid}

def reference(X_bytes, X_scale, W_bytes, W_scale, gain, V_words, V_scales, item_bias, bid):
    X = e4m3fn_values(X_bytes) * np.repeat(f64(X_scale), B, axis=1)
    W = e4m3fn_values(W_bytes) * np.repeat(np.repeat(f64(W_scale), B, axis=0), B, axis=1)
    V = unpack4(V_words, V_scales)
    a = mxq(X, 1) @ mxq(W, 0)
    h = np.maximum(a, 0.0) * f64(gain)
    z = (mxq(h, 1) @ V) + f64(item_bias)
    prob = 1.0 / (1.0 + np.exp(-z))
    y = prob * f64(bid)
    words, scales = planes(y.T)
    return y, words, scales

@@ -1,0 +1,474 @@
+from contextlib import ExitStack
+
+import concourse.mybir as mybir
+from concourse.masks import make_identity
+
+T, K, F, N = 768, 1536, 1024, 2048
+FLOPS = 2 * T * K * F + 2 * T * F * N
+
+F32 = mybir.dt.float32
+BF16 = mybir.dt.bfloat16
+I32 = mybir.dt.int32
+U32 = mybir.dt.uint32
+U8 = mybir.dt.uint8
+FP8 = mybir.dt.float8_e4m3fn
+FP8X4 = mybir.dt.float8_e4m3fn_x4
+FP4X4 = mybir.dt.float4_e2m1fn_x4
+ALU = mybir.AluOpType
+ACT = mybir.ActivationFunctionType
+
+P = 128
+PASS = 512
+KG = K // PASS
+FH = F // PASS
+NG = N // PASS
+NARROW, WIDE = 0, 1
+USERS = {NARROW: (0, 256), WIDE: (256, 512)}
+
+
+def tile_click_value_planes_b4_kernel(
+    tc, X_bytes, X_scale, W_bytes, W_scale, gain, V_words, V_scales, item_bias, bid, out_0, out_1, out_2
+):
+    nc = tc.nc
+    with ExitStack() as ctx:
+        keep = ctx.enter_context(tc.tile_pool(name="keep", bufs=1))
+        work = ctx.enter_context(tc.tile_pool(name="work", bufs=3))
+        psum = ctx.enter_context(tc.psum_pool(name="psum", bufs=8))
+        ctx.enter_context(tc.manual_schedule())
+
+        def bank():
+            return psum.tile([P, PASS], F32, name="bank", tag="bank")
+
+        def mx_pair(pool, name, width):
+            codes = pool.tile([P, width], U32, name=name + "_codes", align_bytes=64)
+            scales = pool.tile([P, width], U8, name=name + "_scales", align_bytes=64)
+            return codes, scales
+
+        x_scale = keep.tile([P, T // P, K // P], F32, name="x_scale")
+        x_raw = [keep.tile([P, K], U8, name="x_raw%d" % i) for i in range(T // P)]
+        w_raw = [keep.tile([P, 4 * F], U8, name="w_raw%d" % g) for g in range(KG)]
+        w_scale_all = keep.tile([P, 96], F32, name="w_scale_all")
+        w_scale = keep.tile([P, KG, 8], F32, name="w_scale")
+        gain_bf = keep.tile([P, FH, 4], BF16, name="gain_bf")
+        gain_col = keep.tile([P, FH * 4], F32, name="gain_col")
+        v_words = [keep.tile([P, 2 * N], U8, name="v_words%d" % h, align_bytes=64) for h in range(FH)]
+        v_scales = keep.tile([P, FH, N], U8, name="v_scales", align_bytes=64)
+        bias_rows = keep.tile([P, P], BF16, name="bias_rows")
+        bias_rows32 = keep.tile([P, P], F32, name="bias_rows32")
+        bias_col = keep.tile([P, N // P], F32, name="bias_col")
+        bias_wide = keep.tile([P, N], BF16, name="bias_wide")
+        bid_wide = keep.tile([P, N], BF16, name="bid_wide")
+        ident = keep.tile([P, P], F32, name="ident")
+        warm = keep.tile([P, 1], F32, name="warm")
+        y_scales = keep.tile([P, T], U8, name="y_scales", align_bytes=64)
+
+        def load_x(i):
+            nc.sync.dma_start(out=x_raw[i][:], in_=X_bytes[P * i : P * (i + 1), :])
+
+        def load_w(g):
+            nc.sync.dma_start(out=w_raw[g][:], in_=W_bytes[PASS * g : PASS * (g + 1), :].rearrange("(p j) f -> p (j f)", j=4))
+
+        nc.vector.memset(warm[:], 0.0)
+        nc.vector.memset(bias_rows[:], 0.0)
+        nc.vector.memset(v_scales[:].rearrange("p h n -> p (h n)").bitcast(I32), 0)
+        nc.scalar.activation(out=warm[:], in_=warm[:], func=ACT.Sigmoid)
+        make_identity(nc, ident[:])
+
+        nc.sync.dma_start(out=x_scale[:], in_=X_scale.rearrange("(i p) c -> p i c", p=P))
+        load_x(0)
+        load_x(1)
+        load_w(0)
+        load_x(2)
+        load_x(3)
+        nc.sync.dma_start(out=w_scale_all[:], in_=W_scale.rearrange("a b -> (a b)").partition_broadcast(P))
+        load_w(1)
+        load_x(4)
+        load_x(5)
+        load_w(2)
+        nc.sync.dma_start(out=gain_bf[:], in_=gain.rearrange("(h p t) -> p h t", h=FH, t=4))
+        nc.sync.dma_start(out=bias_rows[0:16, :], in_=item_bias.rearrange("(c p) -> c p", p=P))
+        for q in range(4):
+            nc.sync.dma_start(
+                out=v_scales[32 * q : 32 * q + 4, :, :].bitcast(I32),
+                in_=V_scales[:, 4 * q : 4 * q + 4, :].rearrange("h r n -> r h n").bitcast(I32),
+            )
+        for h in range(FH):
+            nc.sync.dma_start(out=v_words[h][:].bitcast(I32), in_=V_words[h].bitcast(I32))
+        nc.sync.dma_start(out=bias_wide[:], in_=item_bias.partition_broadcast(P))
+        nc.sync.dma_start(out=bid_wide[:], in_=bid.partition_broadcast(P))
+
+        x_wide, x_banks, x_grouped, x_mx = {}, {}, {}, {}
+        w_cast, w_grouped, w_mx = {}, {}, {}
+        a_banks, h_planes, h_grouped, h_mx = {}, {}, {}, {}
+        z_banks, probs, turned, y32, y16, y_banks, y_grouped, logits = {}, {}, {}, {}, {}, {}, {}, {}
+
+        def pick_w_scales():
+            rows = w_scale_all[:].rearrange("p (g q f) -> p g q f", q=4, f=8)
+            for q in range(4):
+                part = slice(32 * q, 32 * q + 32)
+                nc.vector.tensor_copy(out=w_scale[part, :, :], in_=rows[part, :, q, :])
+
+        def small_vectors():
+            nc.vector.tensor_copy(out=gain_col[:], in_=gain_bf[:].rearrange("p h t -> p (h t)"))
+            nc.vector.tensor_copy(out=bias_rows32[:], in_=bias_rows[:])
+
+        def turn_bias():
+            b = bank()
+            nc.tensor.transpose(b[:, 0:P], bias_rows32[:], ident[:])
+            nc.scalar.copy(out=bias_col[:], in_=b[:, 0 : N // P])
+
+        def x_widen(i):
+            x_wide[i] = work.tile([P, KG, 2, P, 2], BF16, name="x_wide", bufs=4)
+            for g in range(KG):
+                for q in range(4):
+                    k0 = PASS * g + P * q
+                    nc.vector.tensor_scalar(
+                        out=x_wide[i][:, g, :, 32 * q : 32 * q + 32, :].rearrange("p u r e -> p r u e"),
+                        in0=x_raw[i][:, k0 : k0 + P].bitcast(FP8).rearrange("p (r u e) -> p r u e", u=2, e=2),
+                        scalar1=x_scale[:, i, 4 * g + q : 4 * g + q + 1],
+                        scalar2=None,
+                        op0=ALU.mult,
+                    )
+
+        def x_turn(pair, g):
+            x_banks[pair, g] = bank()
+            for ii in range(2):
+                words = x_wide[2 * pair + ii][:].rearrange("p g u r e -> p (g u r e)").bitcast(F32)
+                for u in range(2):
+                    nc.tensor.transpose(
+                        x_banks[pair, g][:, 256 * u + P * ii : 256 * u + P * (ii + 1)],
+                        words[:, 256 * g + P * u : 256 * g + P * (u + 1)],
+                        ident[:],
+                    )
+
+        def x_out(pair, g):
+            chunk = NARROW if pair == 0 else WIDE
+            if (chunk, g) not in x_grouped:
+                x_grouped[chunk, g] = keep.tile([P, 4 * USERS[chunk][1]], BF16, name="x_grouped%d_%d" % (chunk, g), align_bytes=64)
+            first = 256 * pair - USERS[chunk][0]
+            nc.scalar.copy(
+                out=x_grouped[chunk, g][:].bitcast(F32)[:, 2 * first : 2 * first + 512].rearrange("p (r u) -> p r u", u=2),
+                in_=x_banks[pair, g][:].rearrange("p (u r) -> p r u", u=2),
+            )
+
+        def x_quant(chunk, g):
+            x_mx[chunk, g] = mx_pair(keep, "x%d_%d" % (chunk, g), USERS[chunk][1])
+            codes, scales = x_mx[chunk, g]
+            nc.vector.quantize_mx(out=codes[:].bitcast(FP8X4), scales=scales[:], in_=x_grouped[chunk, g][:])
+
+        def w_widen(g, h, copy, rows=range(4)):
+            if (g, h) not in w_cast:
+                w_cast[g, h] = work.tile([P, 4, PASS], BF16, name="w_cast", tag="planes", bufs=5)
+            for j in rows:
+                f0 = F * j + PASS * h
+                copy(out=w_cast[g, h][:, j, :], in_=w_raw[g][:, f0 : f0 + PASS].bitcast(FP8))
+
+        def w_group(g, h):
+            w_grouped[g, h] = work.tile([P, 4 * PASS], BF16, name="w_grouped", tag="grouped", align_bytes=64)
+            dst = w_grouped[g, h][:].rearrange("p (t m j) -> p t m j", t=4, j=4)
+            src = w_cast[g, h][:].rearrange("p j (m t) -> p t m j", t=4)
+            for b in range(4):
+                nc.vector.tensor_scalar(
+                    out=dst[:, :, 32 * b : 32 * b + 32, :],
+                    in0=src[:, :, 32 * b : 32 * b + 32, :],
+                    scalar1=w_scale[:, g, 4 * h + b : 4 * h + b + 1],
+                    scalar2=None,
+                    op0=ALU.mult,
+                )
+
+        def w_quant(g, h):
+            w_mx[g, h] = mx_pair(keep, "w%d_%d" % (g, h), PASS)
+            codes, scales = w_mx[g, h]
+            nc.vector.quantize_mx(out=codes[:].bitcast(FP8X4), scales=scales[:], in_=w_grouped[g, h][:])
+
+        def hidden_pass(chunk, h, t, g):
+            users = USERS[chunk][1]
+            per_bank = PASS // users
+            if g == 0 and t % per_bank == 0:
+                a_banks[chunk, h, t // per_bank] = bank()
+            first = users * (t % per_bank)
+            w_codes, w_scales = w_mx[g, h]
+            x_codes, x_scales = x_mx[chunk, g]
+            nc.tensor.matmul_mx(
+                out=a_banks[chunk, h, t // per_bank][:, first : first + users],
+                lhsT=w_codes[:, P * t : P * (t + 1)].bitcast(FP8X4),
+                lhsT_scale=w_scales[:, P * t : P * (t + 1)],
+                rhs=x_codes[:].bitcast(FP8X4),
+                rhs_scale=x_scales[:],
+                start=(g == 0),
+                stop=(g == KG - 1),
+            )
+
+        def hidden(chunk, h, t):
+            for g in range(KG):
+                hidden_pass(chunk, h, t, g)
+
+        def h_relu(chunk, h, t):
+            users = USERS[chunk][1]
+            per_bank = PASS // users
+            if t == 0:
+                h_planes[chunk, h] = work.tile([P, 4, users], BF16, name="h_planes", tag="planes", bufs=5)
+            first = users * (t % per_bank)
+            nc.scalar.activation(
+                out=h_planes[chunk, h][:, t, :],
+                in_=a_banks[chunk, h, t // per_bank][:, first : first + users],
+                func=ACT.Relu,
+                scale=gain_col[:, 4 * h + t : 4 * h + t + 1],
+            )
+
+        def h_group(chunk, h):
+            h_grouped[chunk, h] = work.tile([P, 4 * USERS[chunk][1]], BF16, name="h_grouped", tag="grouped", align_bytes=64)
+            nc.vector.tensor_copy(
+                out=h_grouped[chunk, h][:].rearrange("p (c i t) -> p c t i", i=4, t=4),
+                in_=h_planes[chunk, h][:].rearrange("p t (c i) -> p c t i", i=4),
+            )
+
+        def h_quant(chunk, h):
+            h_mx[chunk, h] = mx_pair(keep, "h%d_%d" % (chunk, h), USERS[chunk][1])
+            codes, scales = h_mx[chunk, h]
+            nc.vector.quantize_mx(out=codes[:].bitcast(FP8X4), scales=scales[:], in_=h_grouped[chunk, h][:])
+
+        def wide_logits(c):
+            z_banks[WIDE, c] = bank()
+            for h in range(FH):
+                codes, scales = h_mx[WIDE, h]
+                nc.tensor.matmul_mx(
+                    out=z_banks[WIDE, c][:],
+                    lhsT=v_words[h][:, 2 * P * c : 2 * P * (c + 1)].bitcast(FP4X4),
+                    lhsT_scale=v_scales[:, h, P * c : P * (c + 1)],
+                    rhs=codes[:].bitcast(FP8X4),
+                    rhs_scale=scales[:],
+                    start=(h == 0),
+                    stop=(h == FH - 1),
+                )
+
+        def wide_sigmoid(c):
+            probs[WIDE, c] = work.tile([P, PASS], F32, name="wide_prob", bufs=4)
+            nc.scalar.activation(out=probs[WIDE, c][:], in_=z_banks[WIDE, c][:], func=ACT.Sigmoid, bias=bias_col[:, c : c + 1])
+
+        def wide_turn(c):
+            turned[c] = bank()
+            for i in range(4):
+                nc.tensor.transpose(turned[c][:, P * i : P * (i + 1)], probs[WIDE, c][:, P * i : P * (i + 1)], ident[:])
+
+        def wide_value(c):
+            n = c // 4
+            if c % 4 == 0:
+                y32[WIDE, n] = work.tile([P, 4, PASS], F32, name="y_wide", bufs=2)
+            nc.vector.tensor_tensor(
+                out=y32[WIDE, n][:, :, P * (c % 4) : P * (c % 4 + 1)],
+                in0=turned[c][:].rearrange("p (i m) -> p i m", i=4),
+                in1=bid_wide[:, P * c : P * (c + 1)].unsqueeze(1).to_broadcast([P, 4, P]),
+                op=ALU.mult,
+            )
+
+        def narrow_logits(n, i):
+            z_banks[NARROW, n, i] = bank()
+            for h in range(FH):
+                codes, scales = h_mx[NARROW, h]
+                nc.tensor.matmul_mx(
+                    out=z_banks[NARROW, n, i][:],
+                    lhsT=codes[:, P * i : P * (i + 1)].bitcast(FP8X4),
+                    lhsT_scale=scales[:, P * i : P * (i + 1)],
+                    rhs=v_words[h][:, 2 * PASS * n : 2 * PASS * (n + 1)].bitcast(FP4X4),
+                    rhs_scale=v_scales[:, h, PASS * n : PASS * (n + 1)],
+                    start=(h == 0),
+                    stop=(h == FH - 1),
+                )
+
+        def narrow_bias(n, i):
+            logits[n, i] = work.tile([P, PASS], F32, name="narrow_logit", bufs=4)
+            nc.vector.tensor_tensor(
+                out=logits[n, i][:], in0=z_banks[NARROW, n, i][:], in1=bias_wide[:, PASS * n : PASS * (n + 1)], op=ALU.add
+            )
+
+        def narrow_sigmoid(n, i):
+            probs[NARROW, n, i] = work.tile([P, PASS], F32, name="narrow_prob", bufs=4)
+            nc.scalar.activation(out=probs[NARROW, n, i][:], in_=logits[n, i][:], func=ACT.Sigmoid)
+
+        def narrow_value(n, i):
+            if i == 0:
+                y32[NARROW, n] = work.tile([P, 2, PASS], F32, name="y_narrow", bufs=2)
+            nc.vector.tensor_tensor(
+                out=y32[NARROW, n][:, i, :], in0=probs[NARROW, n, i][:], in1=bid_wide[:, PASS * n : PASS * (n + 1)], op=ALU.mult
+            )
+
+        def wide_store(n, half):
+            items = slice(256 * half, 256 * (half + 1))
+            nc.sync.dma_start(
+                out=out_0[256:T, PASS * n : PASS * (n + 1)][:, items].rearrange("(i p) n -> p i n", p=P),
+                in_=y32[WIDE, n][:, :, items],
+            )
+
+        def pair_rows(n, pair):
+            if pair == 0:
+                return y32[NARROW, n][:]
+            return y32[WIDE, n][:, 2 * (pair - 1) : 2 * pair, :]
+
+        def y_store(n, pair):
+            nc.sync.dma_start(
+                out=out_0[256 * pair : 256 * (pair + 1), PASS * n : PASS * (n + 1)].rearrange("(i p) n -> p i n", p=P),
+                in_=pair_rows(n, pair),
+            )
+
+        def y_round(n, pair, copy):
+            y16[n, pair] = work.tile([P, 2, 2, P, 2], BF16, name="y16", bufs=4)
+            copy(out=y16[n, pair][:], in_=pair_rows(n, pair).rearrange("p i (r u e) -> p i u r e", u=2, e=2))
+
+        def y_turn(n, pair):
+            y_banks[n, pair] = bank()
+            words = y16[n, pair][:].rearrange("p i u r e -> p (i u r e)").bitcast(F32)
+            for ii in range(2):
+                for u in range(2):
+                    nc.tensor.transpose(
+                        y_banks[n, pair][:, 256 * u + P * ii : 256 * u + P * (ii + 1)],
+                        words[:, 256 * ii + P * u : 256 * ii + P * (u + 1)],
+                        ident[:],
+                    )
+
+        def y_out(n, pair, copy):
+            y_grouped[n, pair] = work.tile([P, 1024], BF16, name="y_grouped", bufs=4, align_bytes=64)
+            copy(
+                out=y_grouped[n, pair][:].bitcast(F32).rearrange("p (r u) -> p r u", u=2),
+                in_=y_banks[n, pair][:].rearrange("p (u r) -> p r u", u=2),
+            )
+
+        def y_quant(n, pair):
+            codes = work.tile([P, 256], U32, name="y_codes", bufs=4, align_bytes=64)
+            users = slice(256 * pair, 256 * (pair + 1))
+            scales = y_scales[4 * n : P, users]
+            nc.vector.quantize_mx(out=codes[:].bitcast(FP8X4), scales=scales, in_=y_grouped[n, pair][:])
+            nc.sync.dma_start(
+                out=out_1[n][:, users, :].rearrange("p m t -> p (m t)").bitcast(I32), in_=codes[:].bitcast(I32)
+            )
+
+        def store_scales():
+            for q in range(4):
+                nc.sync.dma_start(
+                    out=out_2[:, 4 * q : 4 * q + 4, :].bitcast(I32),
+                    in_=y_scales[32 * q : 32 * q + 16, :].bitcast(I32),
+                )
+
+        on_s, on_v = nc.scalar.copy, nc.vector.tensor_copy
+
+        def each_pass(step, what):
+            for g in range(KG):
+                step(what, g)
+
+        def each_slot(step, chunk, h):
+            for t in range(4):
+                step(chunk, h, t)
+
+        x_widen(0)
+        x_widen(1)
+        w_widen(0, 0, on_s)
+        each_pass(x_turn, 0)
+        x_widen(2)
+        x_widen(3)
+        pick_w_scales()
+        w_widen(1, 0, on_s)
+        each_pass(x_out, 0)
+        each_pass(x_turn, 1)
+        w_group(0, 0)
+        x_widen(4)
+        w_quant(0, 0)
+        w_widen(2, 0, on_s)
+        each_pass(x_out, 1)
+        w_group(1, 0)
+        x_widen(5)
+        w_quant(1, 0)
+        each_pass(x_turn, 2)
+        each_pass(x_out, 2)
+        each_pass(x_quant, NARROW)
+        w_group(2, 0)
+        small_vectors()
+        w_widen(2, 1, on_v, (0, 1))
+        w_quant(2, 0)
+        w_widen(0, 1, on_s)
+        each_slot(hidden, NARROW, 0)
+        each_pass(x_quant, WIDE)
+        w_widen(1, 1, on_s)
+        w_group(0, 1)
+        w_widen(2, 1, on_s, (2, 3))
+        each_slot(h_relu, NARROW, 0)
+        for t in range(4):
+            hidden(WIDE, 0, t)
+            h_relu(WIDE, 0, t)
+        w_quant(0, 1)
+        w_group(1, 1)
+        turn_bias()
+        w_quant(1, 1)
+        w_group(2, 1)
+        for g in range(KG - 1):
+            for t in (0, 2):
+                hidden_pass(NARROW, 1, t, g)
+        for t in range(4):
+            for g in range(KG - 1):
+                hidden_pass(WIDE, 1, t, g)
+        h_group(NARROW, 0)
+        w_quant(2, 1)
+        h_quant(NARROW, 0)
+        for t in (0, 2):
+            hidden_pass(NARROW, 1, t, KG - 1)
+            hidden(NARROW, 1, t + 1)
+        each_slot(h_relu, NARROW, 1)
+        for t in range(4):
+            hidden_pass(WIDE, 1, t, KG - 1)
+        each_slot(h_relu, WIDE, 1)
+        h_group(WIDE, 0)
+        h_group(NARROW, 1)
+        h_quant(WIDE, 0)
+        h_quant(NARROW, 1)
+
+        for n in range(2):
+            for i in range(2):
+                narrow_logits(n, i)
+        narrow_bias(0, 0)
+        narrow_sigmoid(0, 0)
+        h_group(WIDE, 1)
+        narrow_bias(0, 1)
+        h_quant(WIDE, 1)
+        narrow_sigmoid(0, 1)
+        for i in range(2):
+            narrow_bias(1, i)
+            narrow_sigmoid(1, i)
+        for n in range(2):
+            for i in range(2):
+                narrow_value(n, i)
+            y_store(n, 0)
+
+        ON_S = [(0, 0), (1, 0), (2, 0), (3, 0), (0, 2), (3, 2)]
+        late_narrow = {1: (2, 0), 2: (2, 1), 4: (3, 0), 5: (3, 1)}
+        to_round = {0: [(0, 0)], 1: [(1, 0)], 2: [(0, 1)], 3: [(0, 2), (2, 0)], 4: [(1, 1)], 5: [(1, 2)], 6: [(2, 1), (3, 0)],
+                    7: [(2, 2)], 8: [(3, 1), (3, 2)]}
+        for s in range(11):
+            logits_now = [c for c in (2 * s, 2 * s + 1) if c < 16]
+            values_now = [c for c in (2 * s - 2, 2 * s - 1) if 0 <= c < 16]
+            for c in logits_now:
+                wide_logits(c)
+            if s in late_narrow:
+                narrow_logits(*late_narrow[s])
+            for c in values_now:
+                wide_turn(c)
+            for unit in to_round.get(s - 1, []):
+                y_turn(*unit)
+            for c in logits_now:
+                wide_sigmoid(c)
+            for unit in to_round.get(s - 2, []):
+                y_quant(*unit)
+            if s in late_narrow:
+                narrow_bias(*late_narrow[s])
+                narrow_sigmoid(*late_narrow[s])
+            for c in values_now:
+                wide_value(c)
+            for unit in to_round.get(s - 1, []):
+                y_out(*unit, on_s)
+            if s - 1 in late_narrow:
+                narrow_value(*late_narrow[s - 1])
+            if 1 <= s <= 8:
+                wide_store((s - 1) // 2, (s - 1) % 2)
+            if s in (3, 6):
+                y_store(s // 3 + 1, 0)
+            for unit in to_round.get(s, []):
+                y_round(*unit, on_s if unit in ON_S else on_v)
+        store_scales()

@@ -18,12 +18,20 @@ ALU = mybir.AluOpType
 ACT = mybir.ActivationFunctionType
 
 P = 128
-PASS = 512
-KG = K // PASS
-FH = F // PASS
-NG = N // PASS
+SLOTS = 4
+PASS = P * SLOTS
+QUAD = 32
+K_PASSES = K // PASS
+HALVES = F // PASS
+GROUPS = N // PASS
+ITEM_TILES = N // P
+USER_TILES = T // P
+PAIR = 2 * P
 NARROW, WIDE = 0, 1
-USERS = {NARROW: (0, 256), WIDE: (256, 512)}
+FIRST_USER = {NARROW: 0, WIDE: PAIR}
+USERS = {NARROW: PAIR, WIDE: 2 * PAIR}
+STEPS = ITEM_TILES // 2
+TURN_LAG = 2
 
 
 def tile_click_value_planes_b4_kernel(
@@ -35,38 +43,37 @@ def tile_click_value_planes_b4_kernel(
         work = ctx.enter_context(tc.tile_pool(name="work", bufs=3))
         psum = ctx.enter_context(tc.psum_pool(name="psum", bufs=8))
         ctx.enter_context(tc.manual_schedule())
+        on_scalar, on_vector = nc.scalar.copy, nc.vector.tensor_copy
 
         def bank():
             return psum.tile([P, PASS], F32, name="bank", tag="bank")
 
-        def mx_pair(pool, name, width):
-            codes = pool.tile([P, width], U32, name=name + "_codes", align_bytes=64)
-            scales = pool.tile([P, width], U8, name=name + "_scales", align_bytes=64)
+        def quantised(name, grouped):
+            width = grouped.shape[1] // SLOTS
+            codes = keep.tile([P, width], U32, name=name + "_codes", align_bytes=64)
+            scales = keep.tile([P, width], U8, name=name + "_scales", align_bytes=64)
+            nc.vector.quantize_mx(out=codes[:].bitcast(FP8X4), scales=scales[:], in_=grouped[:])
             return codes, scales
 
-        x_scale = keep.tile([P, T // P, K // P], F32, name="x_scale")
-        x_raw = [keep.tile([P, K], U8, name="x_raw%d" % i) for i in range(T // P)]
-        w_raw = [keep.tile([P, 4 * F], U8, name="w_raw%d" % g) for g in range(KG)]
-        w_scale_all = keep.tile([P, 96], F32, name="w_scale_all")
-        w_scale = keep.tile([P, KG, 8], F32, name="w_scale")
-        gain_bf = keep.tile([P, FH, 4], BF16, name="gain_bf")
-        gain_col = keep.tile([P, FH * 4], F32, name="gain_col")
-        v_words = [keep.tile([P, 2 * N], U8, name="v_words%d" % h, align_bytes=64) for h in range(FH)]
-        v_scales = keep.tile([P, FH, N], U8, name="v_scales", align_bytes=64)
+        x_scale = [keep.tile([P, USERS[c] // P, 16], F32, name="x_scale%d" % c) for c in (NARROW, WIDE)]
+        x_raw = [keep.tile([P, K], U8, name="x_raw%d" % i) for i in range(USER_TILES)]
+        w_raw = {
+            (g, h): keep.tile([P, SLOTS * PASS], U8, name="w_raw%d_%d" % (g, h)) for g in range(K_PASSES) for h in range(HALVES)
+        }
+        w_scale_all = keep.tile([P, (K // P) * (F // P)], F32, name="w_scale_all")
+        w_scale = keep.tile([P, K_PASSES, F // P], F32, name="w_scale")
+        gain_bf = keep.tile([P, HALVES, SLOTS], BF16, name="gain_bf")
+        gain_col = keep.tile([P, HALVES * SLOTS], F32, name="gain_col")
+        v_words = [keep.tile([P, 2 * N], U8, name="v_words%d" % h, align_bytes=64) for h in range(HALVES)]
+        v_scales = keep.tile([P, HALVES, N], U8, name="v_scales", align_bytes=64)
         bias_rows = keep.tile([P, P], BF16, name="bias_rows")
         bias_rows32 = keep.tile([P, P], F32, name="bias_rows32")
-        bias_col = keep.tile([P, N // P], F32, name="bias_col")
-        bias_wide = keep.tile([P, N], BF16, name="bias_wide")
-        bid_wide = keep.tile([P, N], BF16, name="bid_wide")
+        bias_col = keep.tile([P, ITEM_TILES], F32, name="bias_col")
+        bias_spread = keep.tile([P, N], BF16, name="bias_spread")
+        bid_spread = keep.tile([P, N], BF16, name="bid_spread")
         ident = keep.tile([P, P], F32, name="ident")
         warm = keep.tile([P, 1], F32, name="warm")
         y_scales = keep.tile([P, T], U8, name="y_scales", align_bytes=64)
-
-        def load_x(i):
-            nc.sync.dma_start(out=x_raw[i][:], in_=X_bytes[P * i : P * (i + 1), :])
-
-        def load_w(g):
-            nc.sync.dma_start(out=w_raw[g][:], in_=W_bytes[PASS * g : PASS * (g + 1), :].rearrange("(p j) f -> p (j f)", j=4))
 
         nc.vector.memset(warm[:], 0.0)
         nc.vector.memset(bias_rows[:], 0.0)
@@ -74,163 +81,192 @@ def tile_click_value_planes_b4_kernel(
         nc.scalar.activation(out=warm[:], in_=warm[:], func=ACT.Sigmoid)
         make_identity(nc, ident[:])
 
-        nc.sync.dma_start(out=x_scale[:], in_=X_scale.rearrange("(i p) c -> p i c", p=P))
+        def load_x_scale(chunk):
+            users = slice(FIRST_USER[chunk], FIRST_USER[chunk] + USERS[chunk])
+            nc.sync.dma_start(out=x_scale[chunk][:, :, 0 : K // P], in_=X_scale[users, :].rearrange("(i p) c -> p i c", p=P))
+
+        def load_x(i):
+            nc.sync.dma_start(out=x_raw[i][:], in_=X_bytes[P * i : P * (i + 1), :])
+
+        def load_w(g, h):
+            nc.sync.dma_start(
+                out=w_raw[g, h][:].rearrange("p (j f) -> p j f", j=SLOTS),
+                in_=W_bytes[PASS * g : PASS * (g + 1), PASS * h : PASS * (h + 1)].rearrange("(p j) f -> p j f", j=SLOTS),
+            )
+
         load_x(0)
-        load_x(1)
-        load_w(0)
-        load_x(2)
-        load_x(3)
+        load_x_scale(NARROW)
+        load_w(0, 0)
         nc.sync.dma_start(out=w_scale_all[:], in_=W_scale.rearrange("a b -> (a b)").partition_broadcast(P))
-        load_w(1)
+        load_x(1)
+        load_x(2)
+        load_x_scale(WIDE)
+        load_w(1, 0)
+        load_x(3)
+        load_w(2, 0)
         load_x(4)
         load_x(5)
-        load_w(2)
-        nc.sync.dma_start(out=gain_bf[:], in_=gain.rearrange("(h p t) -> p h t", h=FH, t=4))
-        nc.sync.dma_start(out=bias_rows[0:16, :], in_=item_bias.rearrange("(c p) -> c p", p=P))
-        for q in range(4):
+        for g in range(K_PASSES):
+            load_w(g, 1)
+        nc.sync.dma_start(out=gain_bf[:], in_=gain.rearrange("(h p t) -> p h t", h=HALVES, t=SLOTS))
+        nc.sync.dma_start(out=bias_rows[0:ITEM_TILES, :], in_=item_bias.rearrange("(c p) -> c p", p=P))
+        for q in range(P // QUAD):
             nc.sync.dma_start(
-                out=v_scales[32 * q : 32 * q + 4, :, :].bitcast(I32),
+                out=v_scales[QUAD * q : QUAD * q + 4, :, :].bitcast(I32),
                 in_=V_scales[:, 4 * q : 4 * q + 4, :].rearrange("h r n -> r h n").bitcast(I32),
             )
-        for h in range(FH):
+        for h in range(HALVES):
             nc.sync.dma_start(out=v_words[h][:].bitcast(I32), in_=V_words[h].bitcast(I32))
-        nc.sync.dma_start(out=bias_wide[:], in_=item_bias.partition_broadcast(P))
-        nc.sync.dma_start(out=bid_wide[:], in_=bid.partition_broadcast(P))
+        nc.sync.dma_start(out=bias_spread[:], in_=item_bias.partition_broadcast(P))
+        nc.sync.dma_start(out=bid_spread[:], in_=bid.partition_broadcast(P))
 
         x_wide, x_banks, x_grouped, x_mx = {}, {}, {}, {}
-        w_cast, w_grouped, w_mx = {}, {}, {}
+        w_wide, w_grouped, w_mx = {}, {}, {}
         a_banks, h_planes, h_grouped, h_mx = {}, {}, {}, {}
-        z_banks, probs, turned, y32, y16, y_banks, y_grouped, logits = {}, {}, {}, {}, {}, {}, {}, {}
+        z_banks, logits, probs, prob_banks = {}, {}, {}, {}
+        y32, y16, y_banks, y_grouped = {}, {}, {}, {}
 
         def pick_w_scales():
-            rows = w_scale_all[:].rearrange("p (g q f) -> p g q f", q=4, f=8)
-            for q in range(4):
-                part = slice(32 * q, 32 * q + 32)
-                nc.vector.tensor_copy(out=w_scale[part, :, :], in_=rows[part, :, q, :])
+            rows = w_scale_all[:].rearrange("p (g q b) -> p g q b", q=P // QUAD, b=F // P)
+            for q in range(P // QUAD):
+                part = slice(QUAD * q, QUAD * (q + 1))
+                nc.scalar.copy(out=w_scale[part, :, :], in_=rows[part, :, q, :])
 
-        def small_vectors():
-            nc.vector.tensor_copy(out=gain_col[:], in_=gain_bf[:].rearrange("p h t -> p (h t)"))
-            nc.vector.tensor_copy(out=bias_rows32[:], in_=bias_rows[:])
+        def widen_vectors():
+            nc.scalar.copy(out=gain_col[:], in_=gain_bf[:].rearrange("p h t -> p (h t)"))
+            nc.scalar.copy(out=bias_rows32[:], in_=bias_rows[:])
 
         def turn_bias():
-            b = bank()
-            nc.tensor.transpose(b[:, 0:P], bias_rows32[:], ident[:])
-            nc.scalar.copy(out=bias_col[:], in_=b[:, 0 : N // P])
+            turned = bank()
+            nc.tensor.transpose(turned[:, 0:P], bias_rows32[:], ident[:])
+            nc.scalar.copy(out=bias_col[:], in_=turned[:, 0:ITEM_TILES])
+
+        def chunk_of(pair):
+            return NARROW if pair == 0 else WIDE
 
         def x_widen(i):
-            x_wide[i] = work.tile([P, KG, 2, P, 2], BF16, name="x_wide", bufs=4)
-            for g in range(KG):
-                for q in range(4):
-                    k0 = PASS * g + P * q
-                    nc.vector.tensor_scalar(
-                        out=x_wide[i][:, g, :, 32 * q : 32 * q + 32, :].rearrange("p u r e -> p r u e"),
-                        in0=x_raw[i][:, k0 : k0 + P].bitcast(FP8).rearrange("p (r u e) -> p r u e", u=2, e=2),
-                        scalar1=x_scale[:, i, 4 * g + q : 4 * g + q + 1],
-                        scalar2=None,
-                        op0=ALU.mult,
-                    )
-
-        def x_turn(pair, g):
-            x_banks[pair, g] = bank()
-            for ii in range(2):
-                words = x_wide[2 * pair + ii][:].rearrange("p g u r e -> p (g u r e)").bitcast(F32)
-                for u in range(2):
-                    nc.tensor.transpose(
-                        x_banks[pair, g][:, 256 * u + P * ii : 256 * u + P * (ii + 1)],
-                        words[:, 256 * g + P * u : 256 * g + P * (u + 1)],
-                        ident[:],
-                    )
-
-        def x_out(pair, g):
-            chunk = NARROW if pair == 0 else WIDE
-            if (chunk, g) not in x_grouped:
-                x_grouped[chunk, g] = keep.tile([P, 4 * USERS[chunk][1]], BF16, name="x_grouped%d_%d" % (chunk, g), align_bytes=64)
-            first = 256 * pair - USERS[chunk][0]
-            nc.scalar.copy(
-                out=x_grouped[chunk, g][:].bitcast(F32)[:, 2 * first : 2 * first + 512].rearrange("p (r u) -> p r u", u=2),
-                in_=x_banks[pair, g][:].rearrange("p (u r) -> p r u", u=2),
-            )
-
-        def x_quant(chunk, g):
-            x_mx[chunk, g] = mx_pair(keep, "x%d_%d" % (chunk, g), USERS[chunk][1])
-            codes, scales = x_mx[chunk, g]
-            nc.vector.quantize_mx(out=codes[:].bitcast(FP8X4), scales=scales[:], in_=x_grouped[chunk, g][:])
-
-        def w_widen(g, h, copy, rows=range(4)):
-            if (g, h) not in w_cast:
-                w_cast[g, h] = work.tile([P, 4, PASS], BF16, name="w_cast", tag="planes", bufs=5)
-            for j in rows:
-                f0 = F * j + PASS * h
-                copy(out=w_cast[g, h][:, j, :], in_=w_raw[g][:, f0 : f0 + PASS].bitcast(FP8))
-
-        def w_group(g, h):
-            w_grouped[g, h] = work.tile([P, 4 * PASS], BF16, name="w_grouped", tag="grouped", align_bytes=64)
-            dst = w_grouped[g, h][:].rearrange("p (t m j) -> p t m j", t=4, j=4)
-            src = w_cast[g, h][:].rearrange("p j (m t) -> p t m j", t=4)
-            for b in range(4):
+            chunk = chunk_of(i // 2)
+            row = i - FIRST_USER[chunk] // P
+            x_wide[i] = work.tile([P, K], BF16, name="x_wide", bufs=4)
+            for b in range(K // P):
+                block = slice(P * b, P * (b + 1))
                 nc.vector.tensor_scalar(
-                    out=dst[:, :, 32 * b : 32 * b + 32, :],
-                    in0=src[:, :, 32 * b : 32 * b + 32, :],
-                    scalar1=w_scale[:, g, 4 * h + b : 4 * h + b + 1],
+                    out=x_wide[i][:, block],
+                    in0=x_raw[i][:, block].bitcast(FP8),
+                    scalar1=x_scale[chunk][:, row, b : b + 1],
                     scalar2=None,
                     op0=ALU.mult,
                 )
 
+        def x_turn(pair):
+            for g in range(K_PASSES):
+                x_banks[pair, g] = bank()
+                for ii in range(2):
+                    words = x_wide[2 * pair + ii][:].bitcast(F32)
+                    for u in range(2):
+                        nc.tensor.transpose(
+                            x_banks[pair, g][:, PAIR * u + P * ii : PAIR * u + P * (ii + 1)],
+                            words[:, 2 * P * g + u : 2 * P * (g + 1) : 2],
+                            ident[:],
+                        )
+
+        def x_out(pair):
+            chunk = chunk_of(pair)
+            first_word = 2 * (PAIR * pair - FIRST_USER[chunk])
+            for g in range(K_PASSES):
+                if first_word == 0:
+                    x_grouped[chunk, g] = keep.tile(
+                        [P, SLOTS * USERS[chunk]], BF16, name="x_grouped%d_%d" % (chunk, g), align_bytes=64
+                    )
+                words = x_grouped[chunk, g][:].bitcast(F32)[:, first_word : first_word + 2 * PAIR]
+                nc.scalar.copy(
+                    out=words.rearrange("p (m u) -> p m u", u=2), in_=x_banks[pair, g][:].rearrange("p (u m) -> p m u", u=2)
+                )
+
+        def x_quant(chunk, g):
+            x_mx[chunk, g] = quantised("x%d_%d" % (chunk, g), x_grouped[chunk, g])
+
+        def slot_planes(name, width):
+            return work.tile([P, SLOTS, width], BF16, name=name, tag="planes", bufs=5)
+
+        def grouped_tile(name, width):
+            return work.tile([P, SLOTS * width], BF16, name=name, tag="grouped", align_bytes=64)
+
+        def w_widen(g, h):
+            w_wide[g, h] = slot_planes("w_wide", PASS)
+            nc.scalar.copy(out=w_wide[g, h][:].rearrange("p j f -> p (j f)"), in_=w_raw[g, h][:].bitcast(FP8))
+
+        def w_group(g, h):
+            w_grouped[g, h] = grouped_tile("w_grouped", PASS)
+            dst = w_grouped[g, h][:].rearrange("p (t m j) -> p m t j", t=SLOTS, j=SLOTS)
+            src = w_wide[g, h][:].rearrange("p j (m t) -> p m t j", t=SLOTS)
+            for b in range(PASS // P):
+                block = slice(P // SLOTS * b, P // SLOTS * (b + 1))
+                column = PASS // P * h + b
+                nc.vector.tensor_scalar(
+                    out=dst[:, block], in0=src[:, block], scalar1=w_scale[:, g, column : column + 1], scalar2=None, op0=ALU.mult
+                )
+
         def w_quant(g, h):
-            w_mx[g, h] = mx_pair(keep, "w%d_%d" % (g, h), PASS)
-            codes, scales = w_mx[g, h]
-            nc.vector.quantize_mx(out=codes[:].bitcast(FP8X4), scales=scales[:], in_=w_grouped[g, h][:])
+            w_mx[g, h] = quantised("w%d_%d" % (g, h), w_grouped[g, h])
+
+        def hidden_sums(chunk, h, t):
+            per_bank = PASS // USERS[chunk]
+            first = USERS[chunk] * (t % per_bank)
+            if (chunk, h, t // per_bank) not in a_banks:
+                a_banks[chunk, h, t // per_bank] = bank()
+            return a_banks[chunk, h, t // per_bank][:, first : first + USERS[chunk]]
 
         def hidden_pass(chunk, h, t, g):
-            users = USERS[chunk][1]
-            per_bank = PASS // users
-            if g == 0 and t % per_bank == 0:
-                a_banks[chunk, h, t // per_bank] = bank()
-            first = users * (t % per_bank)
             w_codes, w_scales = w_mx[g, h]
             x_codes, x_scales = x_mx[chunk, g]
             nc.tensor.matmul_mx(
-                out=a_banks[chunk, h, t // per_bank][:, first : first + users],
+                out=hidden_sums(chunk, h, t),
                 lhsT=w_codes[:, P * t : P * (t + 1)].bitcast(FP8X4),
                 lhsT_scale=w_scales[:, P * t : P * (t + 1)],
                 rhs=x_codes[:].bitcast(FP8X4),
                 rhs_scale=x_scales[:],
                 start=(g == 0),
-                stop=(g == KG - 1),
+                stop=(g == K_PASSES - 1),
             )
 
-        def hidden(chunk, h, t):
-            for g in range(KG):
-                hidden_pass(chunk, h, t, g)
+        def hidden_early(h, g):
+            for t in (0, 2):
+                hidden_pass(NARROW, h, t, g)
+            for t in range(SLOTS):
+                hidden_pass(WIDE, h, t, g)
 
-        def h_relu(chunk, h, t):
-            users = USERS[chunk][1]
-            per_bank = PASS // users
-            if t == 0:
-                h_planes[chunk, h] = work.tile([P, 4, users], BF16, name="h_planes", tag="planes", bufs=5)
-            first = users * (t % per_bank)
-            nc.scalar.activation(
-                out=h_planes[chunk, h][:, t, :],
-                in_=a_banks[chunk, h, t // per_bank][:, first : first + users],
-                func=ACT.Relu,
-                scale=gain_col[:, 4 * h + t : 4 * h + t + 1],
-            )
+        def hidden_finish(h):
+            for t in (0, 2):
+                hidden_pass(NARROW, h, t, K_PASSES - 1)
+                for g in range(K_PASSES):
+                    hidden_pass(NARROW, h, t + 1, g)
+            for t in range(SLOTS):
+                hidden_pass(WIDE, h, t, K_PASSES - 1)
+
+        def h_relu(chunk, h):
+            h_planes[chunk, h] = slot_planes("h_planes", USERS[chunk])
+            for t in range(SLOTS):
+                nc.scalar.activation(
+                    out=h_planes[chunk, h][:, t, :],
+                    in_=hidden_sums(chunk, h, t),
+                    func=ACT.Relu,
+                    scale=gain_col[:, SLOTS * h + t : SLOTS * h + t + 1],
+                )
 
         def h_group(chunk, h):
-            h_grouped[chunk, h] = work.tile([P, 4 * USERS[chunk][1]], BF16, name="h_grouped", tag="grouped", align_bytes=64)
+            h_grouped[chunk, h] = grouped_tile("h_grouped", USERS[chunk])
             nc.vector.tensor_copy(
-                out=h_grouped[chunk, h][:].rearrange("p (c i t) -> p c t i", i=4, t=4),
+                out=h_grouped[chunk, h][:].rearrange("p (c i t) -> p c t i", i=4, t=SLOTS),
                 in_=h_planes[chunk, h][:].rearrange("p t (c i) -> p c t i", i=4),
             )
 
         def h_quant(chunk, h):
-            h_mx[chunk, h] = mx_pair(keep, "h%d_%d" % (chunk, h), USERS[chunk][1])
-            codes, scales = h_mx[chunk, h]
-            nc.vector.quantize_mx(out=codes[:].bitcast(FP8X4), scales=scales[:], in_=h_grouped[chunk, h][:])
+            h_mx[chunk, h] = quantised("h%d_%d" % (chunk, h), h_grouped[chunk, h])
 
         def wide_logits(c):
             z_banks[WIDE, c] = bank()
-            for h in range(FH):
+            for h in range(HALVES):
                 codes, scales = h_mx[WIDE, h]
                 nc.tensor.matmul_mx(
                     out=z_banks[WIDE, c][:],
@@ -239,32 +275,40 @@ def tile_click_value_planes_b4_kernel(
                     rhs=codes[:].bitcast(FP8X4),
                     rhs_scale=scales[:],
                     start=(h == 0),
-                    stop=(h == FH - 1),
+                    stop=(h == HALVES - 1),
                 )
 
         def wide_sigmoid(c):
-            probs[WIDE, c] = work.tile([P, PASS], F32, name="wide_prob", bufs=4)
+            probs[WIDE, c] = work.tile([P, USERS[WIDE]], F32, name="wide_prob", bufs=6)
             nc.scalar.activation(out=probs[WIDE, c][:], in_=z_banks[WIDE, c][:], func=ACT.Sigmoid, bias=bias_col[:, c : c + 1])
 
         def wide_turn(c):
-            turned[c] = bank()
-            for i in range(4):
-                nc.tensor.transpose(turned[c][:, P * i : P * (i + 1)], probs[WIDE, c][:, P * i : P * (i + 1)], ident[:])
+            prob_banks[c] = bank()
+            for i in range(USERS[WIDE] // P):
+                nc.tensor.transpose(prob_banks[c][:, P * i : P * (i + 1)], probs[WIDE, c][:, P * i : P * (i + 1)], ident[:])
 
         def wide_value(c):
-            n = c // 4
-            if c % 4 == 0:
-                y32[WIDE, n] = work.tile([P, 4, PASS], F32, name="y_wide", bufs=2)
+            n, part = divmod(c, PASS // P)
+            tiles = USERS[WIDE] // P
+            if part == 0:
+                y32[WIDE, n] = work.tile([P, tiles, PASS], F32, name="y_wide", bufs=2)
             nc.vector.tensor_tensor(
-                out=y32[WIDE, n][:, :, P * (c % 4) : P * (c % 4 + 1)],
-                in0=turned[c][:].rearrange("p (i m) -> p i m", i=4),
-                in1=bid_wide[:, P * c : P * (c + 1)].unsqueeze(1).to_broadcast([P, 4, P]),
+                out=y32[WIDE, n][:, :, P * part : P * (part + 1)],
+                in0=prob_banks[c][:].rearrange("p (i m) -> p i m", i=tiles),
+                in1=bid_spread[:, P * c : P * (c + 1)].unsqueeze(1).to_broadcast([P, tiles, P]),
                 op=ALU.mult,
+            )
+
+        def wide_store(step):
+            n, half = divmod(step, 2)
+            nc.sync.dma_start(
+                out=out_0[FIRST_USER[WIDE] : T, 2 * P * step : 2 * P * (step + 1)].rearrange("(i p) n -> p i n", p=P),
+                in_=y32[WIDE, n][:, :, 2 * P * half : 2 * P * (half + 1)],
             )
 
         def narrow_logits(n, i):
             z_banks[NARROW, n, i] = bank()
-            for h in range(FH):
+            for h in range(HALVES):
                 codes, scales = h_mx[NARROW, h]
                 nc.tensor.matmul_mx(
                     out=z_banks[NARROW, n, i][:],
@@ -273,47 +317,32 @@ def tile_click_value_planes_b4_kernel(
                     rhs=v_words[h][:, 2 * PASS * n : 2 * PASS * (n + 1)].bitcast(FP4X4),
                     rhs_scale=v_scales[:, h, PASS * n : PASS * (n + 1)],
                     start=(h == 0),
-                    stop=(h == FH - 1),
+                    stop=(h == HALVES - 1),
                 )
 
-        def narrow_bias(n, i):
+        def narrow_prob(n, i):
             logits[n, i] = work.tile([P, PASS], F32, name="narrow_logit", bufs=4)
-            nc.vector.tensor_tensor(
-                out=logits[n, i][:], in0=z_banks[NARROW, n, i][:], in1=bias_wide[:, PASS * n : PASS * (n + 1)], op=ALU.add
-            )
-
-        def narrow_sigmoid(n, i):
             probs[NARROW, n, i] = work.tile([P, PASS], F32, name="narrow_prob", bufs=4)
+            nc.vector.tensor_tensor(
+                out=logits[n, i][:], in0=z_banks[NARROW, n, i][:], in1=bias_spread[:, PASS * n : PASS * (n + 1)], op=ALU.add
+            )
             nc.scalar.activation(out=probs[NARROW, n, i][:], in_=logits[n, i][:], func=ACT.Sigmoid)
 
         def narrow_value(n, i):
             if i == 0:
-                y32[NARROW, n] = work.tile([P, 2, PASS], F32, name="y_narrow", bufs=2)
+                y32[NARROW, n] = work.tile([P, 2, PASS], F32, name="y_narrow")
             nc.vector.tensor_tensor(
-                out=y32[NARROW, n][:, i, :], in0=probs[NARROW, n, i][:], in1=bid_wide[:, PASS * n : PASS * (n + 1)], op=ALU.mult
+                out=y32[NARROW, n][:, i, :], in0=probs[NARROW, n, i][:], in1=bid_spread[:, PASS * n : PASS * (n + 1)], op=ALU.mult
             )
-
-        def wide_store(n, half):
-            items = slice(256 * half, 256 * (half + 1))
-            nc.sync.dma_start(
-                out=out_0[256:T, PASS * n : PASS * (n + 1)][:, items].rearrange("(i p) n -> p i n", p=P),
-                in_=y32[WIDE, n][:, :, items],
-            )
-
-        def pair_rows(n, pair):
-            if pair == 0:
-                return y32[NARROW, n][:]
-            return y32[WIDE, n][:, 2 * (pair - 1) : 2 * pair, :]
-
-        def y_store(n, pair):
-            nc.sync.dma_start(
-                out=out_0[256 * pair : 256 * (pair + 1), PASS * n : PASS * (n + 1)].rearrange("(i p) n -> p i n", p=P),
-                in_=pair_rows(n, pair),
-            )
+            if i == 1:
+                nc.sync.dma_start(
+                    out=out_0[0:PAIR, PASS * n : PASS * (n + 1)].rearrange("(i p) n -> p i n", p=P), in_=y32[NARROW, n][:]
+                )
 
         def y_round(n, pair, copy):
-            y16[n, pair] = work.tile([P, 2, 2, P, 2], BF16, name="y16", bufs=4)
-            copy(out=y16[n, pair][:], in_=pair_rows(n, pair).rearrange("p i (r u e) -> p i u r e", u=2, e=2))
+            rows = y32[NARROW, n][:] if pair == 0 else y32[WIDE, n][:, 2 * (pair - 1) : 2 * pair, :]
+            y16[n, pair] = work.tile([P, 2, 2, P, 2], BF16, name="y16", bufs=6)
+            copy(out=y16[n, pair][:], in_=rows.rearrange("p i (r u e) -> p i u r e", u=2, e=2))
 
         def y_turn(n, pair):
             y_banks[n, pair] = bank()
@@ -321,154 +350,153 @@ def tile_click_value_planes_b4_kernel(
             for ii in range(2):
                 for u in range(2):
                     nc.tensor.transpose(
-                        y_banks[n, pair][:, 256 * u + P * ii : 256 * u + P * (ii + 1)],
-                        words[:, 256 * ii + P * u : 256 * ii + P * (u + 1)],
+                        y_banks[n, pair][:, PAIR * u + P * ii : PAIR * u + P * (ii + 1)],
+                        words[:, 2 * P * ii + P * u : 2 * P * ii + P * (u + 1)],
                         ident[:],
                     )
 
-        def y_out(n, pair, copy):
-            y_grouped[n, pair] = work.tile([P, 1024], BF16, name="y_grouped", bufs=4, align_bytes=64)
-            copy(
-                out=y_grouped[n, pair][:].bitcast(F32).rearrange("p (r u) -> p r u", u=2),
-                in_=y_banks[n, pair][:].rearrange("p (u r) -> p r u", u=2),
+        def y_out(n, pair):
+            y_grouped[n, pair] = work.tile([P, SLOTS * PAIR], BF16, name="y_grouped", bufs=4, align_bytes=64)
+            nc.scalar.copy(
+                out=y_grouped[n, pair][:].bitcast(F32).rearrange("p (m u) -> p m u", u=2),
+                in_=y_banks[n, pair][:].rearrange("p (u m) -> p m u", u=2),
             )
 
         def y_quant(n, pair):
-            codes = work.tile([P, 256], U32, name="y_codes", bufs=4, align_bytes=64)
-            users = slice(256 * pair, 256 * (pair + 1))
-            scales = y_scales[4 * n : P, users]
-            nc.vector.quantize_mx(out=codes[:].bitcast(FP8X4), scales=scales, in_=y_grouped[n, pair][:])
-            nc.sync.dma_start(
-                out=out_1[n][:, users, :].rearrange("p m t -> p (m t)").bitcast(I32), in_=codes[:].bitcast(I32)
-            )
-
-        def store_scales():
-            for q in range(4):
-                nc.sync.dma_start(
-                    out=out_2[:, 4 * q : 4 * q + 4, :].bitcast(I32),
-                    in_=y_scales[32 * q : 32 * q + 16, :].bitcast(I32),
-                )
-
-        on_s, on_v = nc.scalar.copy, nc.vector.tensor_copy
-
-        def each_pass(step, what):
-            for g in range(KG):
-                step(what, g)
-
-        def each_slot(step, chunk, h):
-            for t in range(4):
-                step(chunk, h, t)
+            users = slice(PAIR * pair, PAIR * (pair + 1))
+            codes = work.tile([P, PAIR], U32, name="y_codes", bufs=6, align_bytes=64)
+            nc.vector.quantize_mx(out=codes[:].bitcast(FP8X4), scales=y_scales[4 * n : P, users], in_=y_grouped[n, pair][:])
+            nc.sync.dma_start(out=out_1[n][:, users, :].rearrange("p m t -> p (m t)").bitcast(I32), in_=codes[:].bitcast(I32))
 
         x_widen(0)
-        x_widen(1)
-        w_widen(0, 0, on_s)
-        each_pass(x_turn, 0)
-        x_widen(2)
-        x_widen(3)
+        w_widen(0, 0)
         pick_w_scales()
-        w_widen(1, 0, on_s)
-        each_pass(x_out, 0)
-        each_pass(x_turn, 1)
+        x_widen(1)
+        x_turn(0)
+        w_widen(1, 0)
+        x_widen(2)
         w_group(0, 0)
-        x_widen(4)
+        x_widen(3)
         w_quant(0, 0)
-        w_widen(2, 0, on_s)
-        each_pass(x_out, 1)
-        w_group(1, 0)
+        x_out(0)
+        x_turn(1)
+        x_widen(4)
         x_widen(5)
+        w_widen(2, 0)
+        w_group(1, 0)
+        x_turn(2)
+        x_out(1)
+        x_out(2)
+        x_quant(NARROW, 0)
         w_quant(1, 0)
-        each_pass(x_turn, 2)
-        each_pass(x_out, 2)
-        each_pass(x_quant, NARROW)
+        w_widen(0, 1)
         w_group(2, 0)
-        small_vectors()
-        w_widen(2, 1, on_v, (0, 1))
+        x_quant(WIDE, 0)
+        hidden_early(0, 0)
+        x_quant(NARROW, 1)
+        x_quant(WIDE, 1)
+        hidden_early(0, 1)
         w_quant(2, 0)
-        w_widen(0, 1, on_s)
-        each_slot(hidden, NARROW, 0)
-        each_pass(x_quant, WIDE)
-        w_widen(1, 1, on_s)
+        x_quant(NARROW, 2)
+        x_quant(WIDE, 2)
+        hidden_finish(0)
+        widen_vectors()
+        w_widen(1, 1)
         w_group(0, 1)
-        w_widen(2, 1, on_s, (2, 3))
-        each_slot(h_relu, NARROW, 0)
-        for t in range(4):
-            hidden(WIDE, 0, t)
-            h_relu(WIDE, 0, t)
-        w_quant(0, 1)
+        w_widen(2, 1)
         w_group(1, 1)
-        turn_bias()
+        w_quant(0, 1)
         w_quant(1, 1)
         w_group(2, 1)
-        for g in range(KG - 1):
-            for t in (0, 2):
-                hidden_pass(NARROW, 1, t, g)
-        for t in range(4):
-            for g in range(KG - 1):
-                hidden_pass(WIDE, 1, t, g)
+        h_relu(NARROW, 0)
+        h_relu(WIDE, 0)
+        turn_bias()
+        hidden_early(1, 0)
+        hidden_early(1, 1)
         h_group(NARROW, 0)
         w_quant(2, 1)
-        h_quant(NARROW, 0)
-        for t in (0, 2):
-            hidden_pass(NARROW, 1, t, KG - 1)
-            hidden(NARROW, 1, t + 1)
-        each_slot(h_relu, NARROW, 1)
-        for t in range(4):
-            hidden_pass(WIDE, 1, t, KG - 1)
-        each_slot(h_relu, WIDE, 1)
+        hidden_finish(1)
+        h_relu(NARROW, 1)
+        h_relu(WIDE, 1)
+
         h_group(WIDE, 0)
+        h_quant(NARROW, 0)
         h_group(NARROW, 1)
         h_quant(WIDE, 0)
         h_quant(NARROW, 1)
 
-        for n in range(2):
-            for i in range(2):
-                narrow_logits(n, i)
-        narrow_bias(0, 0)
-        narrow_sigmoid(0, 0)
+        early = [(n, i) for n in range(2) for i in range(2)]
+        for n, i in early:
+            narrow_logits(n, i)
+        narrow_prob(*early[0])
         h_group(WIDE, 1)
-        narrow_bias(0, 1)
+        narrow_prob(*early[1])
         h_quant(WIDE, 1)
-        narrow_sigmoid(0, 1)
-        for i in range(2):
-            narrow_bias(1, i)
-            narrow_sigmoid(1, i)
-        for n in range(2):
-            for i in range(2):
-                narrow_value(n, i)
-            y_store(n, 0)
+        for n, i in early[2:]:
+            narrow_prob(n, i)
+        for n, i in early:
+            narrow_value(n, i)
 
-        ON_S = [(0, 0), (1, 0), (2, 0), (3, 0), (0, 2), (3, 2)]
-        late_narrow = {1: (2, 0), 2: (2, 1), 4: (3, 0), 5: (3, 1)}
-        to_round = {0: [(0, 0)], 1: [(1, 0)], 2: [(0, 1)], 3: [(0, 2), (2, 0)], 4: [(1, 1)], 5: [(1, 2)], 6: [(2, 1), (3, 0)],
-                    7: [(2, 2)], 8: [(3, 1), (3, 2)]}
-        for s in range(11):
-            logits_now = [c for c in (2 * s, 2 * s + 1) if c < 16]
-            values_now = [c for c in (2 * s - 2, 2 * s - 1) if 0 <= c < 16]
-            for c in logits_now:
+        narrow_at = {3 * (n - 2) + 1 + i: (n, i) for n in range(2, GROUPS) for i in range(2)}
+        round_at = {step: [] for step in range(-TURN_LAG - 1, STEPS + 2)}
+        for n in range(GROUPS):
+            round_at[n if n < 2 else 3 * (n - 1)].append((n, 0))
+            round_at[2 * n + 2].append((n, 1))
+            round_at[2 * n + 3].append((n, 2))
+        for step in range(STEPS):
+            tiles_now = (2 * step, 2 * step + 1)
+            tiles_before = (2 * step - 2, 2 * step - 1) if step else ()
+            for c in tiles_now:
                 wide_logits(c)
-            if s in late_narrow:
-                narrow_logits(*late_narrow[s])
-            for c in values_now:
+            if step in narrow_at:
+                narrow_logits(*narrow_at[step])
+            for c in tiles_before:
                 wide_turn(c)
-            for unit in to_round.get(s - 1, []):
+            for unit in round_at[step - TURN_LAG]:
                 y_turn(*unit)
-            for c in logits_now:
+            for c in tiles_now:
                 wide_sigmoid(c)
-            for unit in to_round.get(s - 2, []):
+            for unit in round_at[step - TURN_LAG - 1]:
                 y_quant(*unit)
-            if s in late_narrow:
-                narrow_bias(*late_narrow[s])
-                narrow_sigmoid(*late_narrow[s])
-            for c in values_now:
+            if step in narrow_at:
+                narrow_prob(*narrow_at[step])
+            for c in tiles_before:
                 wide_value(c)
-            for unit in to_round.get(s - 1, []):
-                y_out(*unit, on_s)
-            if s - 1 in late_narrow:
-                narrow_value(*late_narrow[s - 1])
-            if 1 <= s <= 8:
-                wide_store((s - 1) // 2, (s - 1) % 2)
-            if s in (3, 6):
-                y_store(s // 3 + 1, 0)
-            for unit in to_round.get(s, []):
-                y_round(*unit, on_s if unit in ON_S else on_v)
-        store_scales()
+            if step:
+                wide_store(step - 1)
+            for unit in round_at[step - TURN_LAG]:
+                y_out(*unit)
+            if step - 1 in narrow_at:
+                narrow_value(*narrow_at[step - 1])
+            for n, pair in round_at[step]:
+                y_round(n, pair, on_scalar if pair == 2 or (n, pair) == (0, 0) else on_vector)
+
+        last_tiles = (ITEM_TILES - 2, ITEM_TILES - 1)
+        last_pairs = [(GROUPS - 1, 1), (GROUPS - 1, 2)]
+        for c in last_tiles:
+            wide_turn(c)
+        for unit in round_at[STEPS - 2]:
+            y_turn(*unit)
+        for unit in round_at[STEPS - 3]:
+            y_quant(*unit)
+        for c in last_tiles:
+            wide_value(c)
+        wide_store(STEPS - 1)
+        for unit in round_at[STEPS - 2]:
+            y_out(*unit)
+        for unit in round_at[STEPS - 1]:
+            y_turn(*unit)
+            y_out(*unit)
+        for n, pair in last_pairs:
+            y_round(n, pair, on_vector)
+        for unit in round_at[STEPS - 2]:
+            y_quant(*unit)
+        for unit in last_pairs:
+            y_turn(*unit)
+            y_out(*unit)
+        for unit in round_at[STEPS - 1] + last_pairs:
+            y_quant(*unit)
+        for q in range(P // QUAD):
+            nc.sync.dma_start(
+                out=out_2[:, 4 * q : 4 * q + 4, :].bitcast(I32), in_=y_scales[QUAD * q : QUAD * q + 4 * GROUPS, :].bitcast(I32)
+            )

@@ -192,9 +192,10 @@ def tile_click_value_planes_b4_kernel(
         def grouped_tile(name, width):
             return work.tile([P, SLOTS * width], BF16, name=name, tag="grouped", align_bytes=64)
 
-        def w_widen(g, h):
-            w_wide[g, h] = slot_planes("w_wide", PASS)
-            nc.scalar.copy(out=w_wide[g, h][:].rearrange("p j f -> p (j f)"), in_=w_raw[g, h][:].bitcast(FP8))
+        def w_widen(g, h, copy=on_scalar, part=slice(None)):
+            if (g, h) not in w_wide:
+                w_wide[g, h] = slot_planes("w_wide", PASS)
+            copy(out=w_wide[g, h][:].rearrange("p j f -> p (j f)")[:, part], in_=w_raw[g, h][:, part].bitcast(FP8))
 
         def w_group(g, h):
             w_grouped[g, h] = grouped_tile("w_grouped", PASS)
@@ -230,19 +231,16 @@ def tile_click_value_planes_b4_kernel(
                 stop=(g == K_PASSES - 1),
             )
 
-        def hidden_early(h, g):
-            for t in (0, 2):
-                hidden_pass(NARROW, h, t, g)
+        def hidden_wide(h, g):
             for t in range(SLOTS):
                 hidden_pass(WIDE, h, t, g)
 
-        def hidden_finish(h):
+        def hidden_narrow(h, g):
             for t in (0, 2):
-                hidden_pass(NARROW, h, t, K_PASSES - 1)
-                for g in range(K_PASSES):
-                    hidden_pass(NARROW, h, t + 1, g)
-            for t in range(SLOTS):
-                hidden_pass(WIDE, h, t, K_PASSES - 1)
+                hidden_pass(NARROW, h, t, g)
+                if g == K_PASSES - 1:
+                    for again in range(K_PASSES):
+                        hidden_pass(NARROW, h, t + 1, again)
 
         def h_relu(chunk, h):
             h_planes[chunk, h] = slot_planes("h_planes", USERS[chunk])
@@ -375,12 +373,12 @@ def tile_click_value_planes_b4_kernel(
         x_turn(0)
         w_widen(1, 0)
         x_widen(2)
-        w_group(0, 0)
         x_widen(3)
-        w_quant(0, 0)
+        w_group(0, 0)
         x_out(0)
         x_turn(1)
         x_widen(4)
+        w_quant(0, 0)
         x_widen(5)
         w_widen(2, 0)
         w_group(1, 0)
@@ -392,30 +390,37 @@ def tile_click_value_planes_b4_kernel(
         w_widen(0, 1)
         w_group(2, 0)
         x_quant(WIDE, 0)
-        hidden_early(0, 0)
+        hidden_narrow(0, 0)
+        hidden_wide(0, 0)
         x_quant(NARROW, 1)
         x_quant(WIDE, 1)
-        hidden_early(0, 1)
+        hidden_narrow(0, 1)
+        hidden_wide(0, 1)
         w_quant(2, 0)
         x_quant(NARROW, 2)
         x_quant(WIDE, 2)
-        hidden_finish(0)
+        hidden_narrow(0, 2)
+        hidden_wide(0, 2)
         widen_vectors()
         w_widen(1, 1)
         w_group(0, 1)
-        w_widen(2, 1)
-        w_group(1, 1)
+        w_widen(2, 1, on_vector, slice(0, 2 * PASS))
+        w_widen(2, 1, on_scalar, slice(2 * PASS, 4 * PASS))
         w_quant(0, 1)
-        w_quant(1, 1)
-        w_group(2, 1)
         h_relu(NARROW, 0)
         h_relu(WIDE, 0)
+        w_group(1, 1)
         turn_bias()
-        hidden_early(1, 0)
-        hidden_early(1, 1)
-        h_group(NARROW, 0)
+        hidden_narrow(1, 0)
+        hidden_wide(1, 0)
+        w_group(2, 1)
+        w_quant(1, 1)
+        hidden_narrow(1, 1)
         w_quant(2, 1)
-        hidden_finish(1)
+        hidden_narrow(1, 2)
+        hidden_wide(1, 1)
+        hidden_wide(1, 2)
+        h_group(NARROW, 0)
         h_relu(NARROW, 1)
         h_relu(WIDE, 1)
 
@@ -497,6 +502,6 @@ def tile_click_value_planes_b4_kernel(
         for unit in round_at[STEPS - 1] + last_pairs:
             y_quant(*unit)
         for q in range(P // QUAD):
-            nc.sync.dma_start(
+            nc.scalar.dma_start(
                 out=out_2[:, 4 * q : 4 * q + 4, :].bitcast(I32), in_=y_scales[QUAD * q : QUAD * q + 4 * GROUPS, :].bitcast(I32)
             )

@@ -199,8 +199,8 @@ def tile_click_value_planes_b4_kernel(
 
         def w_group(g, h):
             w_grouped[g, h] = grouped_tile("w_grouped", PASS)
-            dst = w_grouped[g, h][:].rearrange("p (t m j) -> p m t j", t=SLOTS, j=SLOTS)
-            src = w_wide[g, h][:].rearrange("p j (m t) -> p m t j", t=SLOTS)
+            dst = w_grouped[g, h][:].rearrange("p (t m j) -> p m j t", t=SLOTS, j=SLOTS)
+            src = w_wide[g, h][:].rearrange("p j (m t) -> p m j t", t=SLOTS)
             for b in range(PASS // P):
                 block = slice(P // SLOTS * b, P // SLOTS * (b + 1))
                 column = PASS // P * h + b

@@ -144,12 +144,17 @@ def tile_click_value_planes_b4_kernel(
         def chunk_of(pair):
             return NARROW if pair == 0 else WIDE
 
-        def x_widen(i):
+        def x_widen(i, scalar_engine=False):
             chunk = chunk_of(i // 2)
             row = i - FIRST_USER[chunk] // P
             x_wide[i] = work.tile([P, K], BF16, name="x_wide", bufs=4)
             for b in range(K // P):
                 block = slice(P * b, P * (b + 1))
+                if scalar_engine:
+                    nc.scalar.activation(
+                        out=x_wide[i][:, block], in_=x_raw[i][:, block].bitcast(FP8), func=ACT.Copy, scale=x_scale[chunk][:, row, b : b + 1]
+                    )
+                    continue
                 nc.vector.tensor_scalar(
                     out=x_wide[i][:, block],
                     in0=x_raw[i][:, block].bitcast(FP8),
@@ -373,39 +378,38 @@ def tile_click_value_planes_b4_kernel(
         x_turn(0)
         w_widen(1, 0)
         x_widen(2)
-        x_widen(3)
+        x_widen(3, True)
         w_group(0, 0)
         x_out(0)
         x_turn(1)
         x_widen(4)
         w_quant(0, 0)
-        x_widen(5)
         w_widen(2, 0)
+        x_widen(5, True)
         w_group(1, 0)
         x_turn(2)
         x_out(1)
-        x_out(2)
         x_quant(NARROW, 0)
         w_quant(1, 0)
+        x_out(2)
         w_widen(0, 1)
         w_group(2, 0)
+        x_quant(NARROW, 1)
+        x_quant(NARROW, 2)
+        w_quant(2, 0)
         x_quant(WIDE, 0)
         hidden_narrow(0, 0)
         hidden_wide(0, 0)
-        x_quant(NARROW, 1)
         x_quant(WIDE, 1)
         hidden_narrow(0, 1)
         hidden_wide(0, 1)
-        w_quant(2, 0)
-        x_quant(NARROW, 2)
         x_quant(WIDE, 2)
         hidden_narrow(0, 2)
         hidden_wide(0, 2)
         widen_vectors()
         w_widen(1, 1)
         w_group(0, 1)
-        w_widen(2, 1, on_vector, slice(0, 2 * PASS))
-        w_widen(2, 1, on_scalar, slice(2 * PASS, 4 * PASS))
+        w_widen(2, 1)
         w_quant(0, 1)
         h_relu(NARROW, 0)
         h_relu(WIDE, 0)

@@ -28,9 +28,15 @@ ITEM_TILES = N // P
 USER_TILES = T // P
 PAIR = 2 * P
 NARROW, WIDE = 0, 1
+VECTOR, SCALAR = 0, 1
 FIRST_USER = {NARROW: 0, WIDE: PAIR}
 USERS = {NARROW: PAIR, WIDE: 2 * PAIR}
 STEPS = ITEM_TILES // 2
+BANKS = 8
+HIDDEN_BANKS = {(NARROW, 0): (1, 2), (WIDE, 0): (3, 4, 5, 6), (NARROW, 1): (7, 0), (WIDE, 1): (1, 2, 3, 4)}
+BIAS_BANK = 7
+LOGIT_BANKS, NARROW_BANK, PROB_BANKS, PLANE_BANKS = (5, 6), 7, (0, 1), (2, 3, 4)
+EARLY_BANKS = (7, 0, 1, 2)
 TURN_LAG = 2
 
 
@@ -41,12 +47,18 @@ def tile_click_value_planes_b4_kernel(
     with ExitStack() as ctx:
         keep = ctx.enter_context(tc.tile_pool(name="keep", bufs=1))
         work = ctx.enter_context(tc.tile_pool(name="work", bufs=3))
-        psum = ctx.enter_context(tc.psum_pool(name="psum", bufs=8))
+        psum = ctx.enter_context(tc.psum_pool(name="psum", bufs=1))
         ctx.enter_context(tc.manual_schedule())
         on_scalar, on_vector = nc.scalar.copy, nc.vector.tensor_copy
 
-        def bank():
-            return psum.tile([P, PASS], F32, name="bank", tag="bank")
+        def bank(number):
+            return psum.tile([P, PASS], F32, name="bank%d" % number, tag="bank%d" % number)
+
+        taken = {ring: 0 for ring in (LOGIT_BANKS, PROB_BANKS, PLANE_BANKS)}
+
+        def next_bank(ring):
+            taken[ring] = taken[ring] + 1
+            return bank(ring[(taken[ring] - 1) % len(ring)])
 
         def quantised(name, grouped):
             width = grouped.shape[1] // SLOTS
@@ -96,16 +108,16 @@ def tile_click_value_planes_b4_kernel(
 
         load_x(0)
         load_x_scale(NARROW)
+        load_x(1)
         load_w(0, 0)
         nc.sync.dma_start(out=w_scale_all[:], in_=W_scale.rearrange("a b -> (a b)").partition_broadcast(P))
-        load_x(1)
-        load_x(2)
         load_x_scale(WIDE)
-        load_w(1, 0)
+        load_x(2)
         load_x(3)
-        load_w(2, 0)
+        load_w(1, 0)
         load_x(4)
         load_x(5)
+        load_w(2, 0)
         for g in range(K_PASSES):
             load_w(g, 1)
         nc.sync.dma_start(out=gain_bf[:], in_=gain.rearrange("(h p t) -> p h t", h=HALVES, t=SLOTS))
@@ -126,6 +138,8 @@ def tile_click_value_planes_b4_kernel(
         z_banks, logits, probs, prob_banks = {}, {}, {}, {}
         y32, y16, y_banks, y_grouped = {}, {}, {}, {}
 
+        bias_bank = []
+
         def pick_w_scales():
             rows = w_scale_all[:].rearrange("p (g q b) -> p g q b", q=P // QUAD, b=F // P)
             for q in range(P // QUAD):
@@ -137,35 +151,31 @@ def tile_click_value_planes_b4_kernel(
             nc.scalar.copy(out=bias_rows32[:], in_=bias_rows[:])
 
         def turn_bias():
-            turned = bank()
-            nc.tensor.transpose(turned[:, 0:P], bias_rows32[:], ident[:])
-            nc.scalar.copy(out=bias_col[:], in_=turned[:, 0:ITEM_TILES])
+            bias_bank.append(bank(BIAS_BANK))
+            nc.tensor.transpose(bias_bank[0][:, 0:P], bias_rows32[:], ident[:])
+
+        def bias_out():
+            nc.scalar.copy(out=bias_col[:], in_=bias_bank[0][:, 0:ITEM_TILES])
 
         def chunk_of(pair):
             return NARROW if pair == 0 else WIDE
 
-        def x_widen(i, scalar_engine=False):
+        def x_widen(i, first=0, last=K // P, on=VECTOR):
             chunk = chunk_of(i // 2)
             row = i - FIRST_USER[chunk] // P
-            x_wide[i] = work.tile([P, K], BF16, name="x_wide", bufs=4)
-            for b in range(K // P):
+            if i not in x_wide:
+                x_wide[i] = work.tile([P, K], BF16, name="x_wide", bufs=4)
+            for b in range(first, last):
                 block = slice(P * b, P * (b + 1))
-                if scalar_engine:
-                    nc.scalar.activation(
-                        out=x_wide[i][:, block], in_=x_raw[i][:, block].bitcast(FP8), func=ACT.Copy, scale=x_scale[chunk][:, row, b : b + 1]
-                    )
-                    continue
-                nc.vector.tensor_scalar(
-                    out=x_wide[i][:, block],
-                    in0=x_raw[i][:, block].bitcast(FP8),
-                    scalar1=x_scale[chunk][:, row, b : b + 1],
-                    scalar2=None,
-                    op0=ALU.mult,
-                )
+                source, scale = x_raw[i][:, block].bitcast(FP8), x_scale[chunk][:, row, b : b + 1]
+                if on == SCALAR:
+                    nc.scalar.activation(out=x_wide[i][:, block], in_=source, func=ACT.Copy, scale=scale)
+                else:
+                    nc.vector.tensor_scalar(out=x_wide[i][:, block], in0=source, scalar1=scale, scalar2=None, op0=ALU.mult)
 
         def x_turn(pair):
             for g in range(K_PASSES):
-                x_banks[pair, g] = bank()
+                x_banks[pair, g] = bank((K_PASSES * pair + g) % BANKS)
                 for ii in range(2):
                     words = x_wide[2 * pair + ii][:].bitcast(F32)
                     for u in range(2):
@@ -220,7 +230,7 @@ def tile_click_value_planes_b4_kernel(
             per_bank = PASS // USERS[chunk]
             first = USERS[chunk] * (t % per_bank)
             if (chunk, h, t // per_bank) not in a_banks:
-                a_banks[chunk, h, t // per_bank] = bank()
+                a_banks[chunk, h, t // per_bank] = bank(HIDDEN_BANKS[chunk, h][t // per_bank])
             return a_banks[chunk, h, t // per_bank][:, first : first + USERS[chunk]]
 
         def hidden_pass(chunk, h, t, g):
@@ -240,6 +250,10 @@ def tile_click_value_planes_b4_kernel(
             for t in range(SLOTS):
                 hidden_pass(WIDE, h, t, g)
 
+        def hidden_wide_slot(h, t):
+            for g in range(K_PASSES):
+                hidden_pass(WIDE, h, t, g)
+
         def hidden_narrow(h, g):
             for t in (0, 2):
                 hidden_pass(NARROW, h, t, g)
@@ -247,28 +261,30 @@ def tile_click_value_planes_b4_kernel(
                     for again in range(K_PASSES):
                         hidden_pass(NARROW, h, t + 1, again)
 
-        def h_relu(chunk, h):
-            h_planes[chunk, h] = slot_planes("h_planes", USERS[chunk])
-            for t in range(SLOTS):
-                nc.scalar.activation(
-                    out=h_planes[chunk, h][:, t, :],
-                    in_=hidden_sums(chunk, h, t),
-                    func=ACT.Relu,
-                    scale=gain_col[:, SLOTS * h + t : SLOTS * h + t + 1],
-                )
+        def h_relu(chunk, h, slots=range(SLOTS), on=SCALAR):
+            if (chunk, h) not in h_planes:
+                h_planes[chunk, h] = slot_planes("h_planes", USERS[chunk])
+            for t in slots:
+                plane, sums = h_planes[chunk, h][:, t, :], hidden_sums(chunk, h, t)
+                column = gain_col[:, SLOTS * h + t : SLOTS * h + t + 1]
+                if on == SCALAR:
+                    nc.scalar.activation(out=plane, in_=sums, func=ACT.Relu, scale=column)
+                else:
+                    nc.vector.tensor_scalar(out=plane, in0=sums, scalar1=0.0, scalar2=column, op0=ALU.max, op1=ALU.mult)
 
-        def h_group(chunk, h):
-            h_grouped[chunk, h] = grouped_tile("h_grouped", USERS[chunk])
-            nc.vector.tensor_copy(
-                out=h_grouped[chunk, h][:].rearrange("p (c i t) -> p c t i", i=4, t=SLOTS),
-                in_=h_planes[chunk, h][:].rearrange("p t (c i) -> p c t i", i=4),
+        def h_group(chunk, h, copy=on_vector, users=slice(None)):
+            if (chunk, h) not in h_grouped:
+                h_grouped[chunk, h] = grouped_tile("h_grouped", USERS[chunk])
+            copy(
+                out=h_grouped[chunk, h][:].rearrange("p (m t) -> p m t", t=SLOTS)[:, users].rearrange("p (c i) t -> p c t i", i=4),
+                in_=h_planes[chunk, h][:, :, users].rearrange("p t (c i) -> p c t i", i=4),
             )
 
         def h_quant(chunk, h):
             h_mx[chunk, h] = quantised("h%d_%d" % (chunk, h), h_grouped[chunk, h])
 
         def wide_logits(c):
-            z_banks[WIDE, c] = bank()
+            z_banks[WIDE, c] = next_bank(LOGIT_BANKS)
             for h in range(HALVES):
                 codes, scales = h_mx[WIDE, h]
                 nc.tensor.matmul_mx(
@@ -285,8 +301,8 @@ def tile_click_value_planes_b4_kernel(
             probs[WIDE, c] = work.tile([P, USERS[WIDE]], F32, name="wide_prob", bufs=6)
             nc.scalar.activation(out=probs[WIDE, c][:], in_=z_banks[WIDE, c][:], func=ACT.Sigmoid, bias=bias_col[:, c : c + 1])
 
-        def wide_turn(c):
-            prob_banks[c] = bank()
+        def wide_turn(c, number=None):
+            prob_banks[c] = next_bank(PROB_BANKS) if number is None else bank(number)
             for i in range(USERS[WIDE] // P):
                 nc.tensor.transpose(prob_banks[c][:, P * i : P * (i + 1)], probs[WIDE, c][:, P * i : P * (i + 1)], ident[:])
 
@@ -310,7 +326,7 @@ def tile_click_value_planes_b4_kernel(
             )
 
         def narrow_logits(n, i):
-            z_banks[NARROW, n, i] = bank()
+            z_banks[NARROW, n, i] = bank(EARLY_BANKS[2 * n + i] if n < 2 else NARROW_BANK)
             for h in range(HALVES):
                 codes, scales = h_mx[NARROW, h]
                 nc.tensor.matmul_mx(
@@ -323,12 +339,14 @@ def tile_click_value_planes_b4_kernel(
                     stop=(h == HALVES - 1),
                 )
 
-        def narrow_prob(n, i):
+        def narrow_bias(n, i):
             logits[n, i] = work.tile([P, PASS], F32, name="narrow_logit", bufs=4)
-            probs[NARROW, n, i] = work.tile([P, PASS], F32, name="narrow_prob", bufs=4)
             nc.vector.tensor_tensor(
                 out=logits[n, i][:], in0=z_banks[NARROW, n, i][:], in1=bias_spread[:, PASS * n : PASS * (n + 1)], op=ALU.add
             )
+
+        def narrow_sigmoid(n, i):
+            probs[NARROW, n, i] = work.tile([P, PASS], F32, name="narrow_prob", bufs=4)
             nc.scalar.activation(out=probs[NARROW, n, i][:], in_=logits[n, i][:], func=ACT.Sigmoid)
 
         def narrow_value(n, i):
@@ -342,13 +360,16 @@ def tile_click_value_planes_b4_kernel(
                     out=out_0[0:PAIR, PASS * n : PASS * (n + 1)].rearrange("(i p) n -> p i n", p=P), in_=y32[NARROW, n][:]
                 )
 
-        def y_round(n, pair, copy):
+        def y_round(n, pair, copy, first=0, last=P):
             rows = y32[NARROW, n][:] if pair == 0 else y32[WIDE, n][:, 2 * (pair - 1) : 2 * pair, :]
-            y16[n, pair] = work.tile([P, 2, 2, P, 2], BF16, name="y16", bufs=6)
-            copy(out=y16[n, pair][:], in_=rows.rearrange("p i (r u e) -> p i u r e", u=2, e=2))
+            if (n, pair) not in y16:
+                y16[n, pair] = work.tile([P, 2, 2, P, 2], BF16, name="y16", bufs=6)
+            copy(
+                out=y16[n, pair][:, :, :, first:last], in_=rows.rearrange("p i (r u e) -> p i u r e", u=2, e=2)[:, :, :, first:last]
+            )
 
         def y_turn(n, pair):
-            y_banks[n, pair] = bank()
+            y_banks[n, pair] = next_bank(PLANE_BANKS)
             words = y16[n, pair][:].rearrange("p i u r e -> p (i u r e)").bitcast(F32)
             for ii in range(2):
                 for u in range(2):
@@ -358,100 +379,111 @@ def tile_click_value_planes_b4_kernel(
                         ident[:],
                     )
 
-        def y_out(n, pair):
-            y_grouped[n, pair] = work.tile([P, SLOTS * PAIR], BF16, name="y_grouped", bufs=4, align_bytes=64)
-            nc.scalar.copy(
+        def y_out(n, pair, copy=on_scalar):
+            y_grouped[n, pair] = work.tile([P, SLOTS * PAIR], BF16, name="y_grouped", bufs=6, align_bytes=64)
+            copy(
                 out=y_grouped[n, pair][:].bitcast(F32).rearrange("p (m u) -> p m u", u=2),
                 in_=y_banks[n, pair][:].rearrange("p (u m) -> p m u", u=2),
             )
 
         def y_quant(n, pair):
             users = slice(PAIR * pair, PAIR * (pair + 1))
-            codes = work.tile([P, PAIR], U32, name="y_codes", bufs=6, align_bytes=64)
+            codes = work.tile([P, PAIR], U32, name="y_codes", bufs=8, align_bytes=64)
             nc.vector.quantize_mx(out=codes[:].bitcast(FP8X4), scales=y_scales[4 * n : P, users], in_=y_grouped[n, pair][:])
             nc.sync.dma_start(out=out_1[n][:, users, :].rearrange("p m t -> p (m t)").bitcast(I32), in_=codes[:].bitcast(I32))
 
         x_widen(0)
+        x_widen(1, 8, 12, SCALAR)
+        x_widen(1, 0, 8)
         w_widen(0, 0)
         pick_w_scales()
-        x_widen(1)
         x_turn(0)
-        w_widen(1, 0)
         x_widen(2)
-        x_widen(3, True)
+        x_widen(3, on=SCALAR)
         w_group(0, 0)
-        x_out(0)
+        w_widen(1, 0)
         x_turn(1)
         x_widen(4)
+        x_out(0)
         w_quant(0, 0)
-        w_widen(2, 0)
-        x_widen(5, True)
         w_group(1, 0)
+        w_widen(2, 0)
+        x_widen(5, 0, 9)
+        x_widen(5, 9, 12, SCALAR)
         x_turn(2)
-        x_out(1)
-        x_quant(NARROW, 0)
-        w_quant(1, 0)
-        x_out(2)
+        widen_vectors()
         w_widen(0, 1)
+        x_out(1)
+        w_quant(1, 0)
+        x_quant(NARROW, 0)
         w_group(2, 0)
         x_quant(NARROW, 1)
         x_quant(NARROW, 2)
+        x_out(2)
         w_quant(2, 0)
-        x_quant(WIDE, 0)
         hidden_narrow(0, 0)
-        hidden_wide(0, 0)
-        x_quant(WIDE, 1)
         hidden_narrow(0, 1)
-        hidden_wide(0, 1)
-        x_quant(WIDE, 2)
         hidden_narrow(0, 2)
-        hidden_wide(0, 2)
-        widen_vectors()
-        w_widen(1, 1)
-        w_group(0, 1)
-        w_widen(2, 1)
-        w_quant(0, 1)
-        h_relu(NARROW, 0)
-        h_relu(WIDE, 0)
-        w_group(1, 1)
         turn_bias()
-        hidden_narrow(1, 0)
-        hidden_wide(1, 0)
+        w_group(0, 1)
+        w_widen(1, 1)
+        x_quant(WIDE, 0)
+        w_quant(0, 1)
+        x_quant(WIDE, 1)
+        x_quant(WIDE, 2)
+        w_widen(2, 1)
+        bias_out()
+        hidden_wide(0, 0)
+        hidden_wide(0, 1)
+        hidden_wide(0, 2)
+        w_group(1, 1)
+        h_relu(NARROW, 0)
         w_group(2, 1)
         w_quant(1, 1)
+        h_relu(WIDE, 0)
+        hidden_narrow(1, 0)
+        hidden_pass(WIDE, 1, 0, 0)
+        hidden_pass(WIDE, 1, 1, 0)
+        hidden_pass(WIDE, 1, 2, 0)
         hidden_narrow(1, 1)
+        hidden_pass(WIDE, 1, 0, 1)
         w_quant(2, 1)
         hidden_narrow(1, 2)
-        hidden_wide(1, 1)
-        hidden_wide(1, 2)
+        hidden_pass(WIDE, 1, 0, 2)
+        hidden_pass(WIDE, 1, 1, 1)
+        hidden_pass(WIDE, 1, 1, 2)
+        hidden_pass(WIDE, 1, 2, 1)
+        hidden_pass(WIDE, 1, 2, 2)
+        hidden_wide_slot(1, 3)
         h_group(NARROW, 0)
         h_relu(NARROW, 1)
-        h_relu(WIDE, 1)
-
         h_group(WIDE, 0)
         h_quant(NARROW, 0)
         h_group(NARROW, 1)
+        h_relu(WIDE, 1)
         h_quant(WIDE, 0)
         h_quant(NARROW, 1)
-
-        early = [(n, i) for n in range(2) for i in range(2)]
-        for n, i in early:
-            narrow_logits(n, i)
-        narrow_prob(*early[0])
-        h_group(WIDE, 1)
-        narrow_prob(*early[1])
+        narrow_logits(0, 0)
+        narrow_logits(0, 1)
+        narrow_logits(1, 0)
+        narrow_logits(1, 1)
+        h_group(WIDE, 1, on_vector, slice(0, PAIR))
+        h_group(WIDE, 1, on_scalar, slice(PAIR, 2 * PAIR))
+        narrow_bias(0, 0)
+        narrow_bias(0, 1)
         h_quant(WIDE, 1)
-        for n, i in early[2:]:
-            narrow_prob(n, i)
-        for n, i in early:
-            narrow_value(n, i)
+        narrow_sigmoid(0, 0)
+        narrow_sigmoid(0, 1)
+        narrow_bias(1, 0)
+        narrow_bias(1, 1)
+        narrow_sigmoid(1, 0)
+        narrow_value(0, 0)
 
-        narrow_at = {3 * (n - 2) + 1 + i: (n, i) for n in range(2, GROUPS) for i in range(2)}
-        round_at = {step: [] for step in range(-TURN_LAG - 1, STEPS + 2)}
-        for n in range(GROUPS):
-            round_at[n if n < 2 else 3 * (n - 1)].append((n, 0))
-            round_at[2 * n + 2].append((n, 1))
-            round_at[2 * n + 3].append((n, 2))
+        narrow_at = {step: (2 + step // 2, step % 2) for step in range(4)}
+        value_at = {0: [(0, 1)], 1: [(1, 0), (1, 1)], 2: [(2, 0)], 3: [(2, 1)], 4: [(3, 0)], 5: [(3, 1)]}
+        vector_rounds = {3: [(0, 1)], 4: [(0, 2)], 5: [(1, 1)], 6: [(3, 0), (1, 2)], 7: [(2, 1)]}
+        scalar_rounds = {1: [(0, 0)], 2: [(1, 0)], 4: [(2, 0)]}
+        turn_at = {2: [(0, 0)], 3: [(1, 0)], 4: [(0, 1)], 5: [(0, 2)], 6: [(2, 0), (1, 1)], 7: [(1, 2), (3, 0)]}
         for step in range(STEPS):
             tiles_now = (2 * step, 2 * step + 1)
             tiles_before = (2 * step - 2, 2 * step - 1) if step else ()
@@ -459,52 +491,58 @@ def tile_click_value_planes_b4_kernel(
                 wide_logits(c)
             if step in narrow_at:
                 narrow_logits(*narrow_at[step])
-            for c in tiles_before:
-                wide_turn(c)
-            for unit in round_at[step - TURN_LAG]:
-                y_turn(*unit)
+            for unit in turn_at.get(step - 1, []):
+                y_out(*unit)
+            for unit in turn_at.get(step - 2, []):
+                y_quant(*unit)
             for c in tiles_now:
                 wide_sigmoid(c)
-            for unit in round_at[step - TURN_LAG - 1]:
-                y_quant(*unit)
+            if step == 0:
+                narrow_sigmoid(1, 1)
+            for unit in value_at.get(step, []):
+                narrow_value(*unit)
+            for unit in vector_rounds.get(step, []):
+                y_round(*unit, on_vector)
+            for unit in scalar_rounds.get(step, []):
+                y_round(*unit, on_scalar)
             if step in narrow_at:
-                narrow_prob(*narrow_at[step])
+                narrow_bias(*narrow_at[step])
+            for c in tiles_before:
+                wide_turn(c)
+            for unit in turn_at.get(step, []):
+                y_turn(*unit)
+            if step in narrow_at:
+                narrow_sigmoid(*narrow_at[step])
             for c in tiles_before:
                 wide_value(c)
             if step:
                 wide_store(step - 1)
-            for unit in round_at[step - TURN_LAG]:
-                y_out(*unit)
-            if step - 1 in narrow_at:
-                narrow_value(*narrow_at[step - 1])
-            for n, pair in round_at[step]:
-                y_round(n, pair, on_scalar if pair == 2 or (n, pair) == (0, 0) else on_vector)
-
-        last_tiles = (ITEM_TILES - 2, ITEM_TILES - 1)
-        last_pairs = [(GROUPS - 1, 1), (GROUPS - 1, 2)]
-        for c in last_tiles:
-            wide_turn(c)
-        for unit in round_at[STEPS - 2]:
-            y_turn(*unit)
-        for unit in round_at[STEPS - 3]:
-            y_quant(*unit)
-        for c in last_tiles:
-            wide_value(c)
-        wide_store(STEPS - 1)
-        for unit in round_at[STEPS - 2]:
-            y_out(*unit)
-        for unit in round_at[STEPS - 1]:
-            y_turn(*unit)
-            y_out(*unit)
-        for n, pair in last_pairs:
-            y_round(n, pair, on_vector)
-        for unit in round_at[STEPS - 2]:
-            y_quant(*unit)
-        for unit in last_pairs:
-            y_turn(*unit)
-            y_out(*unit)
-        for unit in round_at[STEPS - 1] + last_pairs:
-            y_quant(*unit)
+        wide_turn(14, 7)
+        wide_turn(15, 5)
+        y_round(2, 2, on_scalar)
+        y_turn(2, 1)
+        wide_value(14)
+        wide_value(15)
+        wide_store(7)
+        y_out(1, 2)
+        y_out(3, 0)
+        y_turn(2, 2)
+        y_quant(2, 0)
+        y_round(3, 1, on_vector)
+        y_round(3, 2, on_vector)
+        y_turn(3, 1)
+        y_out(2, 1)
+        y_out(2, 2)
+        y_turn(3, 2)
+        y_quant(1, 1)
+        y_quant(1, 2)
+        y_quant(3, 0)
+        y_out(3, 1)
+        y_quant(2, 1)
+        y_quant(2, 2)
+        y_out(3, 2)
+        y_quant(3, 1)
+        y_quant(3, 2)
         for q in range(P // QUAD):
             nc.scalar.dma_start(
                 out=out_2[:, 4 * q : 4 * q + 4, :].bitcast(I32), in_=y_scales[QUAD * q : QUAD * q + 4 * GROUPS, :].bitcast(I32)

@@ -35,7 +35,7 @@ STEPS = ITEM_TILES // 2
 BANKS = 8
 HIDDEN_BANKS = {(NARROW, 0): (1, 2), (WIDE, 0): (3, 4, 5, 6), (NARROW, 1): (7, 0), (WIDE, 1): (1, 2, 3, 4)}
 BIAS_BANK = 7
-LOGIT_BANKS, NARROW_BANK, PROB_BANKS, PLANE_BANKS = (5, 6), 7, (0, 1), (2, 3, 4)
+LOGIT_BANKS, PROB_BANKS, PLANE_BANKS = (5, 6, 7), (0, 1), (2, 3, 4)
 EARLY_BANKS = (7, 0, 1, 2)
 TURN_LAG = 2
 
@@ -90,12 +90,11 @@ def tile_click_value_planes_b4_kernel(
         nc.vector.memset(warm[:], 0.0)
         nc.vector.memset(bias_rows[:], 0.0)
         nc.vector.memset(v_scales[:].rearrange("p h n -> p (h n)").bitcast(I32), 0)
-        nc.scalar.activation(out=warm[:], in_=warm[:], func=ACT.Sigmoid)
         make_identity(nc, ident[:])
 
         def load_x_scale(chunk):
             users = slice(FIRST_USER[chunk], FIRST_USER[chunk] + USERS[chunk])
-            nc.sync.dma_start(out=x_scale[chunk][:, :, 0 : K // P], in_=X_scale[users, :].rearrange("(i p) c -> p i c", p=P))
+            nc.scalar.dma_start(out=x_scale[chunk][:, :, 0 : K // P], in_=X_scale[users, :].rearrange("(i p) c -> p i c", p=P))
 
         def load_x(i):
             nc.sync.dma_start(out=x_raw[i][:], in_=X_bytes[P * i : P * (i + 1), :])
@@ -108,10 +107,11 @@ def tile_click_value_planes_b4_kernel(
 
         load_x(0)
         load_x_scale(NARROW)
+        load_x_scale(WIDE)
+        nc.scalar.dma_start(out=w_scale_all[:], in_=W_scale.rearrange("a b -> (a b)").partition_broadcast(P))
+        nc.scalar.activation(out=warm[:], in_=warm[:], func=ACT.Sigmoid)
         load_x(1)
         load_w(0, 0)
-        nc.sync.dma_start(out=w_scale_all[:], in_=W_scale.rearrange("a b -> (a b)").partition_broadcast(P))
-        load_x_scale(WIDE)
         load_x(2)
         load_x(3)
         load_w(1, 0)
@@ -326,7 +326,7 @@ def tile_click_value_planes_b4_kernel(
             )
 
         def narrow_logits(n, i):
-            z_banks[NARROW, n, i] = bank(EARLY_BANKS[2 * n + i] if n < 2 else NARROW_BANK)
+            z_banks[NARROW, n, i] = bank(EARLY_BANKS[2 * n + i]) if n < 2 else next_bank(LOGIT_BANKS)
             for h in range(HALVES):
                 codes, scales = h_mx[NARROW, h]
                 nc.tensor.matmul_mx(
@@ -360,22 +360,24 @@ def tile_click_value_planes_b4_kernel(
                     out=out_0[0:PAIR, PASS * n : PASS * (n + 1)].rearrange("(i p) n -> p i n", p=P), in_=y32[NARROW, n][:]
                 )
 
-        def y_round(n, pair, copy, first=0, last=P):
-            rows = y32[NARROW, n][:] if pair == 0 else y32[WIDE, n][:, 2 * (pair - 1) : 2 * pair, :]
-            if (n, pair) not in y16:
-                y16[n, pair] = work.tile([P, 2, 2, P, 2], BF16, name="y16", bufs=6)
+        def y_round(chunk, n, copy, words=slice(0, P), tiles=slice(None)):
+            if (chunk, n) not in y16:
+                y16[chunk, n] = work.tile([P, USERS[chunk] // P, 2, P, 2], BF16, name="y16_%d" % chunk, bufs=3)
             copy(
-                out=y16[n, pair][:, :, :, first:last], in_=rows.rearrange("p i (r u e) -> p i u r e", u=2, e=2)[:, :, :, first:last]
+                out=y16[chunk, n][:, tiles, :, words],
+                in_=y32[chunk, n][:].rearrange("p i (r u e) -> p i u r e", u=2, e=2)[:, tiles, :, words],
             )
 
-        def y_turn(n, pair):
-            y_banks[n, pair] = next_bank(PLANE_BANKS)
-            words = y16[n, pair][:].rearrange("p i u r e -> p (i u r e)").bitcast(F32)
+        def y_turn(n, pair, number=None):
+            chunk = chunk_of(pair)
+            first_tile = 2 * pair - FIRST_USER[chunk] // P
+            y_banks[n, pair] = next_bank(PLANE_BANKS) if number is None else bank(number)
+            words = y16[chunk, n][:].rearrange("p i u r e -> p i (u r e)").bitcast(F32)
             for ii in range(2):
                 for u in range(2):
                     nc.tensor.transpose(
                         y_banks[n, pair][:, PAIR * u + P * ii : PAIR * u + P * (ii + 1)],
-                        words[:, 2 * P * ii + P * u : 2 * P * ii + P * (u + 1)],
+                        words[:, first_tile + ii, P * u : P * (u + 1)],
                         ident[:],
                     )
 
@@ -456,12 +458,13 @@ def tile_click_value_planes_b4_kernel(
         hidden_pass(WIDE, 1, 2, 2)
         hidden_wide_slot(1, 3)
         h_group(NARROW, 0)
-        h_relu(NARROW, 1)
-        h_group(WIDE, 0)
+        h_relu(NARROW, 1, (0, 1))
         h_quant(NARROW, 0)
-        h_group(NARROW, 1)
+        h_group(WIDE, 0)
+        h_relu(NARROW, 1, (2, 3), VECTOR)
         h_relu(WIDE, 1)
         h_quant(WIDE, 0)
+        h_group(NARROW, 1)
         h_quant(NARROW, 1)
         narrow_logits(0, 0)
         narrow_logits(0, 1)
@@ -470,8 +473,8 @@ def tile_click_value_planes_b4_kernel(
         h_group(WIDE, 1, on_vector, slice(0, PAIR))
         h_group(WIDE, 1, on_scalar, slice(PAIR, 2 * PAIR))
         narrow_bias(0, 0)
-        narrow_bias(0, 1)
         h_quant(WIDE, 1)
+        narrow_bias(0, 1)
         narrow_sigmoid(0, 0)
         narrow_sigmoid(0, 1)
         narrow_bias(1, 0)
@@ -479,67 +482,65 @@ def tile_click_value_planes_b4_kernel(
         narrow_sigmoid(1, 0)
         narrow_value(0, 0)
 
-        narrow_at = {step: (2 + step // 2, step % 2) for step in range(4)}
-        value_at = {0: [(0, 1)], 1: [(1, 0), (1, 1)], 2: [(2, 0)], 3: [(2, 1)], 4: [(3, 0)], 5: [(3, 1)]}
-        vector_rounds = {3: [(0, 1)], 4: [(0, 2)], 5: [(1, 1)], 6: [(3, 0), (1, 2)], 7: [(2, 1)]}
-        scalar_rounds = {1: [(0, 0)], 2: [(1, 0)], 4: [(2, 0)]}
-        turn_at = {2: [(0, 0)], 3: [(1, 0)], 4: [(0, 1)], 5: [(0, 2)], 6: [(2, 0), (1, 1)], 7: [(1, 2), (3, 0)]}
+        narrow_at = {1: (2, 0), 2: (2, 1), 4: (3, 0), 5: (3, 1)}
+        value_at = {0: [(0, 1)], 1: [(1, 0), (1, 1)], 2: [(2, 0)], 3: [(2, 1)], 5: [(3, 0)], 6: [(3, 1)]}
+        narrow_round = {0: (0, on_scalar), 2: (1, on_scalar), 4: (2, on_scalar), 7: (3, on_scalar)}
+        wide_on_scalar = ()
+        turn_at = {2: [(0, 0)], 3: [(0, 1), (1, 0)], 4: [(0, 2)], 5: [(1, 1), (2, 0)], 6: [(1, 2)]}
         for step in range(STEPS):
             tiles_now = (2 * step, 2 * step + 1)
             tiles_before = (2 * step - 2, 2 * step - 1) if step else ()
-            for c in tiles_now:
-                wide_logits(c)
             if step in narrow_at:
                 narrow_logits(*narrow_at[step])
+            for c in tiles_now:
+                wide_logits(c)
             for unit in turn_at.get(step - 1, []):
                 y_out(*unit)
             for unit in turn_at.get(step - 2, []):
                 y_quant(*unit)
+            if step >= 2:
+                y_round(WIDE, step // 2 - 1, on_scalar if step in wide_on_scalar else on_vector, slice(P // 2 * (step % 2), P // 2 * (step % 2 + 1)))
+            if step in narrow_at:
+                narrow_bias(*narrow_at[step])
             for c in tiles_now:
                 wide_sigmoid(c)
             if step == 0:
                 narrow_sigmoid(1, 1)
             for unit in value_at.get(step, []):
                 narrow_value(*unit)
-            for unit in vector_rounds.get(step, []):
-                y_round(*unit, on_vector)
-            for unit in scalar_rounds.get(step, []):
-                y_round(*unit, on_scalar)
             if step in narrow_at:
-                narrow_bias(*narrow_at[step])
+                narrow_sigmoid(*narrow_at[step])
+            if step in narrow_round:
+                y_round(NARROW, *narrow_round[step])
             for c in tiles_before:
                 wide_turn(c)
             for unit in turn_at.get(step, []):
                 y_turn(*unit)
-            if step in narrow_at:
-                narrow_sigmoid(*narrow_at[step])
             for c in tiles_before:
                 wide_value(c)
             if step:
                 wide_store(step - 1)
         wide_turn(14, 7)
-        wide_turn(15, 5)
-        y_round(2, 2, on_scalar)
         y_turn(2, 1)
+        wide_turn(15, 5)
+        y_turn(2, 2)
+        y_turn(3, 0)
+        y_round(WIDE, 3, on_scalar, slice(0, 64))
         wide_value(14)
         wide_value(15)
         wide_store(7)
-        y_out(1, 2)
-        y_out(3, 0)
-        y_turn(2, 2)
-        y_quant(2, 0)
-        y_round(3, 1, on_vector)
-        y_round(3, 2, on_vector)
-        y_turn(3, 1)
+        y_quant(1, 2)
         y_out(2, 1)
         y_out(2, 2)
-        y_turn(3, 2)
-        y_quant(1, 1)
-        y_quant(1, 2)
-        y_quant(3, 0)
-        y_out(3, 1)
+        y_round(WIDE, 3, on_vector, slice(64, 128), slice(0, 2))
+        y_round(WIDE, 3, on_vector, slice(64, 128), slice(2, 4))
+        y_out(3, 0, on_vector)
+        y_turn(3, 1, 0)
+        y_turn(3, 2, 1)
         y_quant(2, 1)
         y_quant(2, 2)
+        y_out(3, 1)
+        y_quant(3, 0)
         y_out(3, 2)
         y_quant(3, 1)
         y_quant(3, 2)

@@ -67,7 +67,7 @@ def tile_click_value_planes_b4_kernel(
             nc.vector.quantize_mx(out=codes[:].bitcast(FP8X4), scales=scales[:], in_=grouped[:])
             return codes, scales
 
-        x_scale = [keep.tile([P, USERS[c] // P, 16], F32, name="x_scale%d" % c) for c in (NARROW, WIDE)]
+        x_scale = [keep.tile([P, USERS[c] // P, K // P], F32, name="x_scale%d" % c) for c in (NARROW, WIDE)]
         x_raw = [keep.tile([P, K], U8, name="x_raw%d" % i) for i in range(USER_TILES)]
         w_raw = {
             (g, h): keep.tile([P, SLOTS * PASS], U8, name="w_raw%d_%d" % (g, h)) for g in range(K_PASSES) for h in range(HALVES)
@@ -94,10 +94,12 @@ def tile_click_value_planes_b4_kernel(
 
         def load_x_scale(chunk):
             users = slice(FIRST_USER[chunk], FIRST_USER[chunk] + USERS[chunk])
-            nc.scalar.dma_start(out=x_scale[chunk][:, :, 0 : K // P], in_=X_scale[users, :].rearrange("(i p) c -> p i c", p=P))
+            nc.sync.dma_start(out=x_scale[chunk][:], in_=X_scale[users, :].rearrange("(p i) c -> p i c", p=P))
 
         def load_x(i):
-            nc.sync.dma_start(out=x_raw[i][:], in_=X_bytes[P * i : P * (i + 1), :])
+            chunk = NARROW if i < 2 else WIDE
+            rows = X_bytes[FIRST_USER[chunk] : FIRST_USER[chunk] + USERS[chunk], :].rearrange("(p i) k -> p i k", p=P)
+            nc.sync.dma_start(out=x_raw[i][:], in_=rows[:, i - FIRST_USER[chunk] // P, :])
 
         def load_w(g, h):
             nc.sync.dma_start(
@@ -105,14 +107,14 @@ def tile_click_value_planes_b4_kernel(
                 in_=W_bytes[PASS * g : PASS * (g + 1), PASS * h : PASS * (h + 1)].rearrange("(p j) f -> p j f", j=SLOTS),
             )
 
+        nc.scalar.activation(out=warm[:], in_=warm[:], func=ACT.Sigmoid)
         load_x(0)
         load_x_scale(NARROW)
-        load_x_scale(WIDE)
-        nc.scalar.dma_start(out=w_scale_all[:], in_=W_scale.rearrange("a b -> (a b)").partition_broadcast(P))
-        nc.scalar.activation(out=warm[:], in_=warm[:], func=ACT.Sigmoid)
         load_x(1)
         load_w(0, 0)
+        load_x_scale(WIDE)
         load_x(2)
+        nc.sync.dma_start(out=w_scale_all[:], in_=W_scale.rearrange("a b -> (a b)").partition_broadcast(P))
         load_x(3)
         load_w(1, 0)
         load_x(4)
@@ -136,7 +138,7 @@ def tile_click_value_planes_b4_kernel(
         w_wide, w_grouped, w_mx = {}, {}, {}
         a_banks, h_planes, h_grouped, h_mx = {}, {}, {}, {}
         z_banks, logits, probs, prob_banks = {}, {}, {}, {}
-        y32, y16, y_banks, y_grouped = {}, {}, {}, {}
+        y_wide, y_narrow, y16, y_banks, y_grouped = {}, {}, {}, {}, {}
 
         bias_bank = []
 
@@ -187,15 +189,16 @@ def tile_click_value_planes_b4_kernel(
 
         def x_out(pair):
             chunk = chunk_of(pair)
-            first_word = 2 * (PAIR * pair - FIRST_USER[chunk])
+            first_tile = 2 * pair - FIRST_USER[chunk] // P
             for g in range(K_PASSES):
-                if first_word == 0:
+                if first_tile == 0:
                     x_grouped[chunk, g] = keep.tile(
                         [P, SLOTS * USERS[chunk]], BF16, name="x_grouped%d_%d" % (chunk, g), align_bytes=64
                     )
-                words = x_grouped[chunk, g][:].bitcast(F32)[:, first_word : first_word + 2 * PAIR]
+                words = x_grouped[chunk, g][:].bitcast(F32).rearrange("p (m i u) -> p m i u", m=P, u=2)
                 nc.scalar.copy(
-                    out=words.rearrange("p (m u) -> p m u", u=2), in_=x_banks[pair, g][:].rearrange("p (u m) -> p m u", u=2)
+                    out=words[:, :, first_tile : first_tile + 2, :],
+                    in_=x_banks[pair, g][:].rearrange("p (u i m) -> p m i u", u=2, i=2),
                 )
 
         def x_quant(chunk, g):
@@ -307,22 +310,21 @@ def tile_click_value_planes_b4_kernel(
                 nc.tensor.transpose(prob_banks[c][:, P * i : P * (i + 1)], probs[WIDE, c][:, P * i : P * (i + 1)], ident[:])
 
         def wide_value(c):
-            n, part = divmod(c, PASS // P)
+            step, part = divmod(c, 2)
             tiles = USERS[WIDE] // P
             if part == 0:
-                y32[WIDE, n] = work.tile([P, tiles, PASS], F32, name="y_wide", bufs=2)
+                y_wide[step] = work.tile([P, tiles, 2 * P], F32, name="y_wide", bufs=4)
             nc.vector.tensor_tensor(
-                out=y32[WIDE, n][:, :, P * part : P * (part + 1)],
+                out=y_wide[step][:, :, P * part : P * (part + 1)],
                 in0=prob_banks[c][:].rearrange("p (i m) -> p i m", i=tiles),
                 in1=bid_spread[:, P * c : P * (c + 1)].unsqueeze(1).to_broadcast([P, tiles, P]),
                 op=ALU.mult,
             )
 
         def wide_store(step):
-            n, half = divmod(step, 2)
             nc.sync.dma_start(
                 out=out_0[FIRST_USER[WIDE] : T, 2 * P * step : 2 * P * (step + 1)].rearrange("(i p) n -> p i n", p=P),
-                in_=y32[WIDE, n][:, :, 2 * P * half : 2 * P * (half + 1)],
+                in_=y_wide[step][:],
             )
 
         def narrow_logits(n, i):
@@ -351,22 +353,28 @@ def tile_click_value_planes_b4_kernel(
 
         def narrow_value(n, i):
             if i == 0:
-                y32[NARROW, n] = work.tile([P, 2, PASS], F32, name="y_narrow")
+                y_narrow[n] = work.tile([P, 2, PASS], F32, name="y_narrow")
             nc.vector.tensor_tensor(
-                out=y32[NARROW, n][:, i, :], in0=probs[NARROW, n, i][:], in1=bid_spread[:, PASS * n : PASS * (n + 1)], op=ALU.mult
+                out=y_narrow[n][:, i, :], in0=probs[NARROW, n, i][:], in1=bid_spread[:, PASS * n : PASS * (n + 1)], op=ALU.mult
             )
             if i == 1:
                 nc.sync.dma_start(
-                    out=out_0[0:PAIR, PASS * n : PASS * (n + 1)].rearrange("(i p) n -> p i n", p=P), in_=y32[NARROW, n][:]
+                    out=out_0[0:PAIR, PASS * n : PASS * (n + 1)].rearrange("(i p) n -> p i n", p=P), in_=y_narrow[n][:]
                 )
 
-        def y_round(chunk, n, copy, words=slice(0, P), tiles=slice(None)):
+        def y_round(chunk, n, rows, first, copy, tiles=slice(None)):
             if (chunk, n) not in y16:
                 y16[chunk, n] = work.tile([P, USERS[chunk] // P, 2, P, 2], BF16, name="y16_%d" % chunk, bufs=3)
             copy(
-                out=y16[chunk, n][:, tiles, :, words],
-                in_=y32[chunk, n][:].rearrange("p i (r u e) -> p i u r e", u=2, e=2)[:, tiles, :, words],
+                out=y16[chunk, n][:, tiles, :, first : first + rows.shape[2] // SLOTS],
+                in_=rows[:].rearrange("p i (r u e) -> p i u r e", u=2, e=2)[:, tiles],
             )
+
+        def wide_round(step, copy, tiles=slice(None)):
+            y_round(WIDE, step // 2, y_wide[step], P // 2 * (step % 2), copy, tiles)
+
+        def narrow_round(n, copy):
+            y_round(NARROW, n, y_narrow[n], 0, copy)
 
         def y_turn(n, pair, number=None):
             chunk = chunk_of(pair)
@@ -484,7 +492,7 @@ def tile_click_value_planes_b4_kernel(
 
         narrow_at = {1: (2, 0), 2: (2, 1), 4: (3, 0), 5: (3, 1)}
         value_at = {0: [(0, 1)], 1: [(1, 0), (1, 1)], 2: [(2, 0)], 3: [(2, 1)], 5: [(3, 0)], 6: [(3, 1)]}
-        narrow_round = {0: (0, on_scalar), 2: (1, on_scalar), 4: (2, on_scalar), 7: (3, on_scalar)}
+        narrow_round_at = {0: (0, on_scalar), 2: (1, on_scalar), 4: (2, on_scalar), 7: (3, on_scalar)}
         wide_on_scalar = ()
         turn_at = {2: [(0, 0)], 3: [(0, 1), (1, 0)], 4: [(0, 2)], 5: [(1, 1), (2, 0)], 6: [(1, 2)]}
         for step in range(STEPS):
@@ -499,7 +507,7 @@ def tile_click_value_planes_b4_kernel(
             for unit in turn_at.get(step - 2, []):
                 y_quant(*unit)
             if step >= 2:
-                y_round(WIDE, step // 2 - 1, on_scalar if step in wide_on_scalar else on_vector, slice(P // 2 * (step % 2), P // 2 * (step % 2 + 1)))
+                wide_round(step - 2, on_scalar if step in wide_on_scalar else on_vector)
             if step in narrow_at:
                 narrow_bias(*narrow_at[step])
             for c in tiles_now:
@@ -510,8 +518,8 @@ def tile_click_value_planes_b4_kernel(
                 narrow_value(*unit)
             if step in narrow_at:
                 narrow_sigmoid(*narrow_at[step])
-            if step in narrow_round:
-                y_round(NARROW, *narrow_round[step])
+            if step in narrow_round_at:
+                narrow_round(*narrow_round_at[step])
             for c in tiles_before:
                 wide_turn(c)
             for unit in turn_at.get(step, []):
@@ -525,15 +533,15 @@ def tile_click_value_planes_b4_kernel(
         wide_turn(15, 5)
         y_turn(2, 2)
         y_turn(3, 0)
-        y_round(WIDE, 3, on_scalar, slice(0, 64))
+        wide_round(6, on_scalar)
         wide_value(14)
         wide_value(15)
         wide_store(7)
         y_quant(1, 2)
         y_out(2, 1)
         y_out(2, 2)
-        y_round(WIDE, 3, on_vector, slice(64, 128), slice(0, 2))
-        y_round(WIDE, 3, on_vector, slice(64, 128), slice(2, 4))
+        wide_round(7, on_vector, slice(0, 2))
+        wide_round(7, on_vector, slice(2, 4))
         y_out(3, 0, on_vector)
         y_turn(3, 1, 0)
         y_turn(3, 2, 1)

@@ -466,13 +466,12 @@ def tile_click_value_planes_b4_kernel(
         hidden_pass(WIDE, 1, 2, 2)
         hidden_wide_slot(1, 3)
         h_group(NARROW, 0)
-        h_relu(NARROW, 1, (0, 1))
-        h_quant(NARROW, 0)
+        h_relu(NARROW, 1)
         h_group(WIDE, 0)
-        h_relu(NARROW, 1, (2, 3), VECTOR)
+        h_quant(NARROW, 0)
+        h_group(NARROW, 1)
         h_relu(WIDE, 1)
         h_quant(WIDE, 0)
-        h_group(NARROW, 1)
         h_quant(NARROW, 1)
         narrow_logits(0, 0)
         narrow_logits(0, 1)
@@ -481,8 +480,8 @@ def tile_click_value_planes_b4_kernel(
         h_group(WIDE, 1, on_vector, slice(0, PAIR))
         h_group(WIDE, 1, on_scalar, slice(PAIR, 2 * PAIR))
         narrow_bias(0, 0)
-        h_quant(WIDE, 1)
         narrow_bias(0, 1)
+        h_quant(WIDE, 1)
         narrow_sigmoid(0, 0)
         narrow_sigmoid(0, 1)
         narrow_bias(1, 0)

@@ -182,7 +182,7 @@ def tile_click_value_planes_b4_kernel(
                     words = x_wide[2 * pair + ii][:].bitcast(F32)
                     for u in range(2):
                         nc.tensor.transpose(
-                            x_banks[pair, g][:, PAIR * u + P * ii : PAIR * u + P * (ii + 1)],
+                            x_banks[pair, g][:, PAIR * u + ii : PAIR * (u + 1) : 2],
                             words[:, 2 * P * g + u : 2 * P * (g + 1) : 2],
                             ident[:],
                         )
@@ -198,7 +198,7 @@ def tile_click_value_planes_b4_kernel(
                 words = x_grouped[chunk, g][:].bitcast(F32).rearrange("p (m i u) -> p m i u", m=P, u=2)
                 nc.scalar.copy(
                     out=words[:, :, first_tile : first_tile + 2, :],
-                    in_=x_banks[pair, g][:].rearrange("p (u i m) -> p m i u", u=2, i=2),
+                    in_=x_banks[pair, g][:].rearrange("p (u m i) -> p m i u", u=2, i=2),
                 )
 
         def x_quant(chunk, g):

@@ -35,6 +35,7 @@ STEPS = ITEM_TILES // 2
 BANKS = 8
 HIDDEN_BANKS = {(NARROW, 0): (1, 2), (WIDE, 0): (3, 4, 5, 6), (NARROW, 1): (7, 0), (WIDE, 1): (1, 2, 3, 4)}
 BIAS_BANK = 7
+SCALE_BANK = 7
 LOGIT_BANKS, PROB_BANKS, PLANE_BANKS = (5, 6, 7), (0, 1), (2, 3, 4)
 EARLY_BANKS = (7, 0, 1, 2)
 TURN_LAG = 2
@@ -72,6 +73,7 @@ def tile_click_value_planes_b4_kernel(
         w_raw = {
             (g, h): keep.tile([P, SLOTS * PASS], U8, name="w_raw%d_%d" % (g, h)) for g in range(K_PASSES) for h in range(HALVES)
         }
+        w_scale_row = keep.tile([P, (K // P) * (F // P)], F32, name="w_scale_row")
         w_scale_all = keep.tile([P, (K // P) * (F // P)], F32, name="w_scale_all")
         w_scale = keep.tile([P, K_PASSES, F // P], F32, name="w_scale")
         gain_bf = keep.tile([P, HALVES, SLOTS], BF16, name="gain_bf")
@@ -87,6 +89,7 @@ def tile_click_value_planes_b4_kernel(
         warm = keep.tile([P, 1], F32, name="warm")
         y_scales = keep.tile([P, T], U8, name="y_scales", align_bytes=64)
 
+        nc.vector.memset(w_scale_row[:], 0.0)
         nc.vector.memset(warm[:], 0.0)
         nc.vector.memset(bias_rows[:], 0.0)
         nc.vector.memset(v_scales[:].rearrange("p h n -> p (h n)").bitcast(I32), 0)
@@ -112,9 +115,9 @@ def tile_click_value_planes_b4_kernel(
         load_x_scale(NARROW)
         load_x(1)
         load_w(0, 0)
+        nc.sync.dma_start(out=w_scale_row[0:1, :], in_=W_scale.rearrange("a b -> (a b)").unsqueeze(0))
         load_x_scale(WIDE)
         load_x(2)
-        nc.sync.dma_start(out=w_scale_all[:], in_=W_scale.rearrange("a b -> (a b)").partition_broadcast(P))
         load_x(3)
         load_w(1, 0)
         load_x(4)
@@ -131,8 +134,9 @@ def tile_click_value_planes_b4_kernel(
             )
         for h in range(HALVES):
             nc.sync.dma_start(out=v_words[h][:].bitcast(I32), in_=V_words[h].bitcast(I32))
-        nc.sync.dma_start(out=bias_spread[:], in_=item_bias.partition_broadcast(P))
-        nc.sync.dma_start(out=bid_spread[:], in_=bid.partition_broadcast(P))
+        for items in (slice(0, N // 2), slice(N // 2, N)):
+            nc.sync.dma_start(out=bias_spread[:, items], in_=item_bias[items].partition_broadcast(P))
+            nc.sync.dma_start(out=bid_spread[:, items], in_=bid[items].partition_broadcast(P))
 
         x_wide, x_banks, x_grouped, x_mx = {}, {}, {}, {}
         w_wide, w_grouped, w_mx = {}, {}, {}
@@ -141,6 +145,12 @@ def tile_click_value_planes_b4_kernel(
         y_wide, y_narrow, y16, y_banks, y_grouped = {}, {}, {}, {}, {}
 
         bias_bank = []
+
+        def spread_w_scales():
+            spread = bank(SCALE_BANK)
+            width = w_scale_row.shape[1]
+            nc.tensor.matmul(spread[:, 0:width], lhsT=ident[:, 0:1].to_broadcast([P, P]), rhs=w_scale_row[:], start=True, stop=True)
+            nc.scalar.copy(out=w_scale_all[:], in_=spread[:, 0:width])
 
         def pick_w_scales():
             rows = w_scale_all[:].rearrange("p (g q b) -> p g q b", q=P // QUAD, b=F // P)
@@ -406,6 +416,7 @@ def tile_click_value_planes_b4_kernel(
         x_widen(1, 8, 12, SCALAR)
         x_widen(1, 0, 8)
         w_widen(0, 0)
+        spread_w_scales()
         pick_w_scales()
         x_turn(0)
         x_widen(2)

@@ -34,7 +34,7 @@ USERS = {NARROW: PAIR, WIDE: 2 * PAIR}
 STEPS = ITEM_TILES // 2
 BANKS = 8
 HIDDEN_BANKS = {(NARROW, 0): (1, 2), (WIDE, 0): (3, 4, 5, 6), (NARROW, 1): (7, 0), (WIDE, 1): (1, 2, 3, 4)}
-BIAS_BANK = 7
+BIAS_BANK = 6
 SCALE_BANK = 7
 LOGIT_BANKS, PROB_BANKS, PLANE_BANKS = (5, 6, 7), (0, 1), (2, 3, 4)
 EARLY_BANKS = (7, 0, 1, 2)
@@ -73,8 +73,8 @@ def tile_click_value_planes_b4_kernel(
         w_raw = {
             (g, h): keep.tile([P, SLOTS * PASS], U8, name="w_raw%d_%d" % (g, h)) for g in range(K_PASSES) for h in range(HALVES)
         }
-        w_scale_row = keep.tile([P, (K // P) * (F // P)], F32, name="w_scale_row")
-        w_scale_all = keep.tile([P, (K // P) * (F // P)], F32, name="w_scale_all")
+        w_scale_rows = keep.tile([P, K_PASSES * (F // P)], F32, name="w_scale_rows")
+        quad_of = keep.tile([P, P], F32, name="quad_of")
         w_scale = keep.tile([P, K_PASSES, F // P], F32, name="w_scale")
         gain_bf = keep.tile([P, HALVES, SLOTS], BF16, name="gain_bf")
         gain_col = keep.tile([P, HALVES * SLOTS], F32, name="gain_col")
@@ -89,33 +89,45 @@ def tile_click_value_planes_b4_kernel(
         warm = keep.tile([P, 1], F32, name="warm")
         y_scales = keep.tile([P, T], U8, name="y_scales", align_bytes=64)
 
-        nc.vector.memset(w_scale_row[:], 0.0)
+        nc.vector.memset(w_scale_rows[:], 0.0)
         nc.vector.memset(warm[:], 0.0)
         nc.vector.memset(bias_rows[:], 0.0)
         nc.vector.memset(v_scales[:].rearrange("p h n -> p (h n)").bitcast(I32), 0)
         make_identity(nc, ident[:])
+        nc.vector.tensor_copy(
+            out=quad_of[:].rearrange("p (q r) -> p q r", r=QUAD),
+            in_=ident[:, 0 : P // QUAD].unsqueeze(2).to_broadcast([P, P // QUAD, QUAD]),
+        )
 
         def load_x_scale(chunk):
             users = slice(FIRST_USER[chunk], FIRST_USER[chunk] + USERS[chunk])
             nc.sync.dma_start(out=x_scale[chunk][:], in_=X_scale[users, :].rearrange("(p i) c -> p i c", p=P))
 
-        def load_x(i):
+        def load_x(i, columns=slice(0, K)):
             chunk = NARROW if i < 2 else WIDE
             rows = X_bytes[FIRST_USER[chunk] : FIRST_USER[chunk] + USERS[chunk], :].rearrange("(p i) k -> p i k", p=P)
-            nc.sync.dma_start(out=x_raw[i][:], in_=rows[:, i - FIRST_USER[chunk] // P, :])
+            nc.sync.dma_start(out=x_raw[i][:, columns], in_=rows[:, i - FIRST_USER[chunk] // P, columns])
 
-        def load_w(g, h):
+        def load_w_scales():
             nc.sync.dma_start(
-                out=w_raw[g, h][:].rearrange("p (j f) -> p j f", j=SLOTS),
-                in_=W_bytes[PASS * g : PASS * (g + 1), PASS * h : PASS * (h + 1)].rearrange("(p j) f -> p j f", j=SLOTS),
+                out=w_scale_rows[0 : P // QUAD, :].rearrange("q (g b) -> q g b", g=K_PASSES),
+                in_=W_scale.rearrange("(g q) b -> q g b", g=K_PASSES),
+            )
+
+        def load_w(g, h, rows=slice(0, SLOTS)):
+            nc.sync.dma_start(
+                out=w_raw[g, h][:].rearrange("p (j f) -> p j f", j=SLOTS)[:, rows],
+                in_=W_bytes[PASS * g : PASS * (g + 1), PASS * h : PASS * (h + 1)].rearrange("(p j) f -> p j f", j=SLOTS)[:, rows],
             )
 
         nc.scalar.activation(out=warm[:], in_=warm[:], func=ACT.Sigmoid)
-        load_x(0)
         load_x_scale(NARROW)
+        load_x(0, slice(0, PASS))
+        load_w(0, 0, slice(0, 2))
+        load_x(0, slice(PASS, K))
+        load_w(0, 0, slice(2, 4))
         load_x(1)
-        load_w(0, 0)
-        nc.sync.dma_start(out=w_scale_row[0:1, :], in_=W_scale.rearrange("a b -> (a b)").unsqueeze(0))
+        load_w_scales()
         load_x_scale(WIDE)
         load_x(2)
         load_x(3)
@@ -148,18 +160,14 @@ def tile_click_value_planes_b4_kernel(
 
         def spread_w_scales():
             spread = bank(SCALE_BANK)
-            width = w_scale_row.shape[1]
-            nc.tensor.matmul(spread[:, 0:width], lhsT=ident[:, 0:1].to_broadcast([P, P]), rhs=w_scale_row[:], start=True, stop=True)
-            nc.scalar.copy(out=w_scale_all[:], in_=spread[:, 0:width])
+            width = w_scale_rows.shape[1]
+            nc.tensor.matmul(spread[:, 0:width], lhsT=quad_of[:], rhs=w_scale_rows[:], start=True, stop=True)
+            nc.scalar.copy(out=w_scale[:].rearrange("p g b -> p (g b)"), in_=spread[:, 0:width])
 
-        def pick_w_scales():
-            rows = w_scale_all[:].rearrange("p (g q b) -> p g q b", q=P // QUAD, b=F // P)
-            for q in range(P // QUAD):
-                part = slice(QUAD * q, QUAD * (q + 1))
-                nc.scalar.copy(out=w_scale[part, :, :], in_=rows[part, :, q, :])
-
-        def widen_vectors():
+        def widen_gain():
             nc.scalar.copy(out=gain_col[:], in_=gain_bf[:].rearrange("p h t -> p (h t)"))
+
+        def widen_bias():
             nc.scalar.copy(out=bias_rows32[:], in_=bias_rows[:])
 
         def turn_bias():
@@ -413,13 +421,14 @@ def tile_click_value_planes_b4_kernel(
             nc.sync.dma_start(out=out_1[n][:, users, :].rearrange("p m t -> p (m t)").bitcast(I32), in_=codes[:].bitcast(I32))
 
         x_widen(0)
-        x_widen(1, 8, 12, SCALAR)
-        x_widen(1, 0, 8)
-        w_widen(0, 0)
+        w_widen(0, 0, on_scalar, slice(0, 2 * PASS))
+        w_widen(0, 0, on_scalar, slice(2 * PASS, 4 * PASS))
+        x_widen(1, 9, 12, SCALAR)
         spread_w_scales()
-        pick_w_scales()
+        x_widen(1, 0, 9)
         x_turn(0)
-        x_widen(2)
+        x_widen(2, 9, 12, SCALAR)
+        x_widen(2, 0, 9)
         x_widen(3, on=SCALAR)
         w_group(0, 0)
         w_widen(1, 0)
@@ -432,7 +441,6 @@ def tile_click_value_planes_b4_kernel(
         x_widen(5, 0, 9)
         x_widen(5, 9, 12, SCALAR)
         x_turn(2)
-        widen_vectors()
         w_widen(0, 1)
         x_out(1)
         w_quant(1, 0)
@@ -445,15 +453,14 @@ def tile_click_value_planes_b4_kernel(
         hidden_narrow(0, 0)
         hidden_narrow(0, 1)
         hidden_narrow(0, 2)
-        turn_bias()
         w_group(0, 1)
         w_widen(1, 1)
         x_quant(WIDE, 0)
         w_quant(0, 1)
         x_quant(WIDE, 1)
         x_quant(WIDE, 2)
+        widen_gain()
         w_widen(2, 1)
-        bias_out()
         hidden_wide(0, 0)
         hidden_wide(0, 1)
         hidden_wide(0, 2)
@@ -462,6 +469,7 @@ def tile_click_value_planes_b4_kernel(
         w_group(2, 1)
         w_quant(1, 1)
         h_relu(WIDE, 0)
+        widen_bias()
         hidden_narrow(1, 0)
         hidden_pass(WIDE, 1, 0, 0)
         hidden_pass(WIDE, 1, 1, 0)
@@ -476,13 +484,14 @@ def tile_click_value_planes_b4_kernel(
         hidden_pass(WIDE, 1, 2, 1)
         hidden_pass(WIDE, 1, 2, 2)
         hidden_wide_slot(1, 3)
+        turn_bias()
         h_group(NARROW, 0)
         h_relu(NARROW, 1)
-        h_group(WIDE, 0)
         h_quant(NARROW, 0)
+        h_group(WIDE, 0)
+        h_quant(WIDE, 0)
         h_group(NARROW, 1)
         h_relu(WIDE, 1)
-        h_quant(WIDE, 0)
         h_quant(NARROW, 1)
         narrow_logits(0, 0)
         narrow_logits(0, 1)
@@ -490,6 +499,7 @@ def tile_click_value_planes_b4_kernel(
         narrow_logits(1, 1)
         h_group(WIDE, 1, on_vector, slice(0, PAIR))
         h_group(WIDE, 1, on_scalar, slice(PAIR, 2 * PAIR))
+        bias_out()
         narrow_bias(0, 0)
         narrow_bias(0, 1)
         h_quant(WIDE, 1)

@@ -34,10 +34,10 @@ USERS = {NARROW: PAIR, WIDE: 2 * PAIR}
 STEPS = ITEM_TILES // 2
 BANKS = 8
 HIDDEN_BANKS = {(NARROW, 0): (1, 2), (WIDE, 0): (3, 4, 5, 6), (NARROW, 1): (7, 0), (WIDE, 1): (1, 2, 3, 4)}
-BIAS_BANK = 6
+BIAS_BANK = 4
 SCALE_BANK = 7
-LOGIT_BANKS, PROB_BANKS, PLANE_BANKS = (5, 6, 7), (0, 1), (2, 3, 4)
-EARLY_BANKS = (7, 0, 1, 2)
+LOGIT_BANKS, PROB_BANKS, PLANE_BANKS = (7, 0, 5), (6, 1), (2, 3, 4)
+NARROW_BANKS = (7, 0, 5, 6, 1, 2, 3, 4)
 TURN_LAG = 2
 
 
@@ -51,6 +51,9 @@ def tile_click_value_planes_b4_kernel(
         psum = ctx.enter_context(tc.psum_pool(name="psum", bufs=1))
         ctx.enter_context(tc.manual_schedule())
         on_scalar, on_vector = nc.scalar.copy, nc.vector.tensor_copy
+
+        def on_gpsimd(out, in_):
+            nc.gpsimd.tensor_scalar(out=out, in0=in_, scalar1=1.0, scalar2=0.0, op0=ALU.mult, op1=ALU.add)
 
         def bank(number):
             return psum.tile([P, PASS], F32, name="bank%d" % number, tag="bank%d" % number)
@@ -346,7 +349,7 @@ def tile_click_value_planes_b4_kernel(
             )
 
         def narrow_logits(n, i):
-            z_banks[NARROW, n, i] = bank(EARLY_BANKS[2 * n + i]) if n < 2 else next_bank(LOGIT_BANKS)
+            z_banks[NARROW, n, i] = bank(NARROW_BANKS[2 * n + i])
             for h in range(HALVES):
                 codes, scales = h_mx[NARROW, h]
                 nc.tensor.matmul_mx(
@@ -360,13 +363,13 @@ def tile_click_value_planes_b4_kernel(
                 )
 
         def narrow_bias(n, i):
-            logits[n, i] = work.tile([P, PASS], F32, name="narrow_logit", bufs=4)
+            logits[n, i] = work.tile([P, PASS], F32, name="narrow_logit", bufs=3)
             nc.vector.tensor_tensor(
                 out=logits[n, i][:], in0=z_banks[NARROW, n, i][:], in1=bias_spread[:, PASS * n : PASS * (n + 1)], op=ALU.add
             )
 
         def narrow_sigmoid(n, i):
-            probs[NARROW, n, i] = work.tile([P, PASS], F32, name="narrow_prob", bufs=4)
+            probs[NARROW, n, i] = work.tile([P, PASS], F32, name="narrow_prob", bufs=5)
             nc.scalar.activation(out=probs[NARROW, n, i][:], in_=logits[n, i][:], func=ACT.Sigmoid)
 
         def narrow_value(n, i):
@@ -392,7 +395,8 @@ def tile_click_value_planes_b4_kernel(
             y_round(WIDE, step // 2, y_wide[step], P // 2 * (step % 2), copy, tiles)
 
         def narrow_round(n, copy):
-            y_round(NARROW, n, y_narrow[n], 0, copy)
+            y16[NARROW, n] = work.tile([P, 2, 2, P, 2], BF16, name="y16_0", bufs=3)
+            copy(out=y16[NARROW, n][:], in_=y_narrow[n][:].rearrange("p i (r u e) -> p u i r e", u=2, e=2))
 
         def y_turn(n, pair, number=None):
             chunk = chunk_of(pair)
@@ -403,7 +407,7 @@ def tile_click_value_planes_b4_kernel(
                 for u in range(2):
                     nc.tensor.transpose(
                         y_banks[n, pair][:, PAIR * u + P * ii : PAIR * u + P * (ii + 1)],
-                        words[:, first_tile + ii, P * u : P * (u + 1)],
+                        words[:, first_tile + ii, P * u : P * (u + 1)] if pair else words[:, u, P * ii : P * (ii + 1)],
                         ident[:],
                     )
 
@@ -484,19 +488,21 @@ def tile_click_value_planes_b4_kernel(
         hidden_pass(WIDE, 1, 2, 1)
         hidden_pass(WIDE, 1, 2, 2)
         hidden_wide_slot(1, 3)
-        turn_bias()
         h_group(NARROW, 0)
         h_relu(NARROW, 1)
-        h_quant(NARROW, 0)
         h_group(WIDE, 0)
-        h_quant(WIDE, 0)
+        h_quant(NARROW, 0)
         h_group(NARROW, 1)
-        h_relu(WIDE, 1)
+        h_quant(WIDE, 0)
         h_quant(NARROW, 1)
+        h_relu(WIDE, 1, (0, 1, 2))
+        h_relu(WIDE, 1, (3,), VECTOR)
         narrow_logits(0, 0)
+        turn_bias()
         narrow_logits(0, 1)
         narrow_logits(1, 0)
         narrow_logits(1, 1)
+        narrow_logits(2, 0)
         h_group(WIDE, 1, on_vector, slice(0, PAIR))
         h_group(WIDE, 1, on_scalar, slice(PAIR, 2 * PAIR))
         bias_out()
@@ -506,38 +512,37 @@ def tile_click_value_planes_b4_kernel(
         narrow_sigmoid(0, 0)
         narrow_sigmoid(0, 1)
         narrow_bias(1, 0)
-        narrow_bias(1, 1)
         narrow_sigmoid(1, 0)
-        narrow_value(0, 0)
 
-        narrow_at = {1: (2, 0), 2: (2, 1), 4: (3, 0), 5: (3, 1)}
-        value_at = {0: [(0, 1)], 1: [(1, 0), (1, 1)], 2: [(2, 0)], 3: [(2, 1)], 5: [(3, 0)], 6: [(3, 1)]}
-        narrow_round_at = {0: (0, on_scalar), 2: (1, on_scalar), 4: (2, on_scalar), 7: (3, on_scalar)}
-        wide_on_scalar = ()
-        turn_at = {2: [(0, 0)], 3: [(0, 1), (1, 0)], 4: [(0, 2)], 5: [(1, 1), (2, 0)], 6: [(1, 2)]}
+        logits_at = {0: [(2, 1)], 2: [(3, 0), (3, 1)]}
+        bias_at = {0: [(1, 1), (2, 0)], 2: [(2, 1)], 3: [(3, 0)], 4: [(3, 1)]}
+        value_at = {0: [(0, 0)], 1: [(1, 0), (0, 1)], 2: [(2, 0), (1, 1)], 3: [(2, 1)], 5: [(3, 0)], 6: [(3, 1)]}
+        narrow_round_at = {1: (0, on_gpsimd), 2: (1, on_gpsimd), 3: (2, on_gpsimd), 6: (3, on_gpsimd)}
+        wide_on_scalar = (2, 4, 7)
+        turn_at = {3: [(0, 0)], 4: [(0, 1), (1, 0)], 5: [(0, 2)], 6: [(2, 0)], 7: [(1, 1)]}
         for step in range(STEPS):
             tiles_now = (2 * step, 2 * step + 1)
             tiles_before = (2 * step - 2, 2 * step - 1) if step else ()
-            if step in narrow_at:
-                narrow_logits(*narrow_at[step])
             for c in tiles_now:
                 wide_logits(c)
+            for unit in logits_at.get(step, []):
+                narrow_logits(*unit)
+            for unit in bias_at.get(step, []):
+                narrow_bias(*unit)
             for unit in turn_at.get(step - 1, []):
                 y_out(*unit)
             for unit in turn_at.get(step - 2, []):
                 y_quant(*unit)
-            if step >= 2:
-                wide_round(step - 2, on_scalar if step in wide_on_scalar else on_vector)
-            if step in narrow_at:
-                narrow_bias(*narrow_at[step])
+            if step >= 2 and step not in wide_on_scalar:
+                wide_round(step - 2, on_vector)
             for c in tiles_now:
                 wide_sigmoid(c)
-            if step == 0:
-                narrow_sigmoid(1, 1)
             for unit in value_at.get(step, []):
                 narrow_value(*unit)
-            if step in narrow_at:
-                narrow_sigmoid(*narrow_at[step])
+            for unit in bias_at.get(step, []):
+                narrow_sigmoid(*unit)
+            if step in wide_on_scalar:
+                wide_round(step - 2, on_scalar)
             if step in narrow_round_at:
                 narrow_round(*narrow_round_at[step])
             for c in tiles_before:
@@ -548,28 +553,33 @@ def tile_click_value_planes_b4_kernel(
                 wide_value(c)
             if step:
                 wide_store(step - 1)
-        wide_turn(14, 7)
-        y_turn(2, 1)
-        wide_turn(15, 5)
-        y_turn(2, 2)
+        y_turn(1, 2)
+        wide_turn(14, 5)
         y_turn(3, 0)
+        wide_turn(15, 7)
+        y_out(1, 1)
         wide_round(6, on_scalar)
+        y_quant(2, 0)
         wide_value(14)
         wide_value(15)
         wide_store(7)
-        y_quant(1, 2)
-        y_out(2, 1)
-        y_out(2, 2)
+        y_turn(2, 1)
+        y_turn(2, 2, 0)
+        y_quant(1, 1)
         wide_round(7, on_vector, slice(0, 2))
         wide_round(7, on_vector, slice(2, 4))
-        y_out(3, 0, on_vector)
-        y_turn(3, 1, 0)
+        y_out(1, 2, on_vector)
+        y_out(3, 0)
+        y_out(2, 1)
+        y_turn(3, 1, 6)
         y_turn(3, 2, 1)
-        y_quant(2, 1)
-        y_quant(2, 2)
-        y_out(3, 1)
+        y_out(2, 2, on_vector)
+        y_quant(1, 2)
         y_quant(3, 0)
+        y_out(3, 1)
+        y_quant(2, 1)
         y_out(3, 2)
+        y_quant(2, 2)
         y_quant(3, 1)
         y_quant(3, 2)
         for q in range(P // QUAD):

@@ -97,10 +97,6 @@ def tile_click_value_planes_b4_kernel(
         nc.vector.memset(bias_rows[:], 0.0)
         nc.vector.memset(v_scales[:].rearrange("p h n -> p (h n)").bitcast(I32), 0)
         make_identity(nc, ident[:])
-        nc.vector.tensor_copy(
-            out=quad_of[:].rearrange("p (q r) -> p q r", r=QUAD),
-            in_=ident[:, 0 : P // QUAD].unsqueeze(2).to_broadcast([P, P // QUAD, QUAD]),
-        )
 
         def load_x_scale(chunk):
             users = slice(FIRST_USER[chunk], FIRST_USER[chunk] + USERS[chunk])
@@ -411,6 +407,11 @@ def tile_click_value_planes_b4_kernel(
                         ident[:],
                     )
 
+        def keep_warm(number):
+            unread = bank(number)
+            for again in range(2):
+                nc.tensor.matmul(unread[:], lhsT=bid_spread[:, 0:P], rhs=bid_spread[:, 0:PASS], start=True, stop=True)
+
         def y_out(n, pair, copy=on_scalar):
             y_grouped[n, pair] = work.tile([P, SLOTS * PAIR], BF16, name="y_grouped", bufs=6, align_bytes=64)
             copy(
@@ -424,7 +425,12 @@ def tile_click_value_planes_b4_kernel(
             nc.vector.quantize_mx(out=codes[:].bitcast(FP8X4), scales=y_scales[4 * n : P, users], in_=y_grouped[n, pair][:])
             nc.sync.dma_start(out=out_1[n][:, users, :].rearrange("p m t -> p (m t)").bitcast(I32), in_=codes[:].bitcast(I32))
 
-        x_widen(0)
+        x_widen(0, 0, 4)
+        nc.vector.tensor_copy(
+            out=quad_of[:].rearrange("p (q r) -> p q r", r=QUAD),
+            in_=ident[:, 0 : P // QUAD].unsqueeze(2).to_broadcast([P, P // QUAD, QUAD]),
+        )
+        x_widen(0, 4, 12)
         w_widen(0, 0, on_scalar, slice(0, 2 * PASS))
         w_widen(0, 0, on_scalar, slice(2 * PASS, 4 * PASS))
         x_widen(1, 9, 12, SCALAR)
@@ -557,6 +563,7 @@ def tile_click_value_planes_b4_kernel(
         wide_turn(14, 5)
         y_turn(3, 0)
         wide_turn(15, 7)
+        keep_warm(0)
         y_out(1, 1)
         wide_round(6, on_scalar)
         y_quant(2, 0)
@@ -565,6 +572,7 @@ def tile_click_value_planes_b4_kernel(
         wide_store(7)
         y_turn(2, 1)
         y_turn(2, 2, 0)
+        keep_warm(5)
         y_quant(1, 1)
         wide_round(7, on_vector, slice(0, 2))
         wide_round(7, on_vector, slice(2, 4))
@@ -583,6 +591,7 @@ def tile_click_value_planes_b4_kernel(
         y_quant(3, 1)
         y_quant(3, 2)
         for q in range(P // QUAD):
-            nc.scalar.dma_start(
+            queue = nc.scalar if q % 2 else nc.sync
+            queue.dma_start(
                 out=out_2[:, 4 * q : 4 * q + 4, :].bitcast(I32), in_=y_scales[QUAD * q : QUAD * q + 4 * GROUPS, :].bitcast(I32)
             )

@@ -52,9 +52,6 @@ def tile_click_value_planes_b4_kernel(
         ctx.enter_context(tc.manual_schedule())
         on_scalar, on_vector = nc.scalar.copy, nc.vector.tensor_copy
 
-        def on_gpsimd(out, in_):
-            nc.gpsimd.tensor_scalar(out=out, in0=in_, scalar1=1.0, scalar2=0.0, op0=ALU.mult, op1=ALU.add)
-
         def bank(number):
             return psum.tile([P, PASS], F32, name="bank%d" % number, tag="bank%d" % number)
 
@@ -155,7 +152,13 @@ def tile_click_value_planes_b4_kernel(
         z_banks, logits, probs, prob_banks = {}, {}, {}, {}
         y_wide, y_narrow, y16, y_banks, y_grouped = {}, {}, {}, {}, {}
 
-        bias_bank = []
+        y_codes, bias_bank = {}, []
+
+        def make_quad_of():
+            nc.vector.tensor_copy(
+                out=quad_of[:].rearrange("p (q r) -> p q r", r=QUAD),
+                in_=ident[:, 0 : P // QUAD].unsqueeze(2).to_broadcast([P, P // QUAD, QUAD]),
+            )
 
         def spread_w_scales():
             spread = bank(SCALE_BANK)
@@ -359,7 +362,7 @@ def tile_click_value_planes_b4_kernel(
                 )
 
         def narrow_bias(n, i):
-            logits[n, i] = work.tile([P, PASS], F32, name="narrow_logit", bufs=3)
+            logits[n, i] = work.tile([P, PASS], F32, name="narrow_logit", bufs=4)
             nc.vector.tensor_tensor(
                 out=logits[n, i][:], in0=z_banks[NARROW, n, i][:], in1=bias_spread[:, PASS * n : PASS * (n + 1)], op=ALU.add
             )
@@ -369,30 +372,33 @@ def tile_click_value_planes_b4_kernel(
             nc.scalar.activation(out=probs[NARROW, n, i][:], in_=logits[n, i][:], func=ACT.Sigmoid)
 
         def narrow_value(n, i):
+            items = slice(PASS * n, PASS * (n + 1))
             if i == 0:
-                y_narrow[n] = work.tile([P, 2, PASS], F32, name="y_narrow")
-            nc.vector.tensor_tensor(
-                out=y_narrow[n][:, i, :], in0=probs[NARROW, n, i][:], in1=bid_spread[:, PASS * n : PASS * (n + 1)], op=ALU.mult
-            )
+                y_narrow[n] = work.tile([P, 2, PASS], F32, name="y_narrow", bufs=3)
+            nc.vector.tensor_tensor(out=y_narrow[n][:, i, :], in0=probs[NARROW, n, i][:], in1=bid_spread[:, items], op=ALU.mult)
             if i == 1:
-                nc.sync.dma_start(
-                    out=out_0[0:PAIR, PASS * n : PASS * (n + 1)].rearrange("(i p) n -> p i n", p=P), in_=y_narrow[n][:]
-                )
-
-        def y_round(chunk, n, rows, first, copy, tiles=slice(None)):
-            if (chunk, n) not in y16:
-                y16[chunk, n] = work.tile([P, USERS[chunk] // P, 2, P, 2], BF16, name="y16_%d" % chunk, bufs=3)
-            copy(
-                out=y16[chunk, n][:, tiles, :, first : first + rows.shape[2] // SLOTS],
-                in_=rows[:].rearrange("p i (r u e) -> p i u r e", u=2, e=2)[:, tiles],
-            )
+                nc.sync.dma_start(out=out_0[0:PAIR, items].rearrange("(i p) n -> p i n", p=P), in_=y_narrow[n][:])
+                narrow_round(n)
 
         def wide_round(step, copy, tiles=slice(None)):
-            y_round(WIDE, step // 2, y_wide[step], P // 2 * (step % 2), copy, tiles)
+            n, half = divmod(step, 2)
+            if (WIDE, n) not in y16:
+                y16[WIDE, n] = work.tile([P, USERS[WIDE] // P, 2, P, 2], BF16, name="y16_wide", bufs=2)
+            copy(
+                out=y16[WIDE, n][:, tiles, :, P // 2 * half : P // 2 * (half + 1)],
+                in_=y_wide[step][:, tiles].rearrange("p i (r u e) -> p i u r e", u=2, e=2),
+            )
 
-        def narrow_round(n, copy):
-            y16[NARROW, n] = work.tile([P, 2, 2, P, 2], BF16, name="y16_0", bufs=3)
-            copy(out=y16[NARROW, n][:], in_=y_narrow[n][:].rearrange("p i (r u e) -> p u i r e", u=2, e=2))
+        def narrow_round(n):
+            y16[NARROW, n] = work.tile([P, 2, 2, P, 2], BF16, name="y16_narrow", bufs=2)
+            nc.gpsimd.tensor_scalar(
+                out=y16[NARROW, n][:],
+                in0=y_narrow[n][:].rearrange("p i (r u e) -> p u i r e", u=2, e=2),
+                scalar1=1.0,
+                scalar2=0.0,
+                op0=ALU.mult,
+                op1=ALU.add,
+            )
 
         def y_turn(n, pair, number=None):
             chunk = chunk_of(pair)
@@ -407,29 +413,33 @@ def tile_click_value_planes_b4_kernel(
                         ident[:],
                     )
 
-        def keep_warm(number):
-            unread = bank(number)
-            for again in range(2):
-                nc.tensor.matmul(unread[:], lhsT=bid_spread[:, 0:P], rhs=bid_spread[:, 0:PASS], start=True, stop=True)
-
         def y_out(n, pair, copy=on_scalar):
-            y_grouped[n, pair] = work.tile([P, SLOTS * PAIR], BF16, name="y_grouped", bufs=6, align_bytes=64)
+            chunk = chunk_of(pair)
+            if (chunk, n) not in y_grouped:
+                y_grouped[chunk, n] = work.tile([P, SLOTS * USERS[chunk]], BF16, name="y_grouped%d" % chunk, bufs=3, align_bytes=64)
+            first_word = 2 * (PAIR * pair - FIRST_USER[chunk])
             copy(
-                out=y_grouped[n, pair][:].bitcast(F32).rearrange("p (m u) -> p m u", u=2),
+                out=y_grouped[chunk, n][:].bitcast(F32)[:, first_word : first_word + 2 * PAIR].rearrange("p (m u) -> p m u", u=2),
                 in_=y_banks[n, pair][:].rearrange("p (u m) -> p m u", u=2),
             )
 
-        def y_quant(n, pair):
-            users = slice(PAIR * pair, PAIR * (pair + 1))
-            codes = work.tile([P, PAIR], U32, name="y_codes", bufs=8, align_bytes=64)
-            nc.vector.quantize_mx(out=codes[:].bitcast(FP8X4), scales=y_scales[4 * n : P, users], in_=y_grouped[n, pair][:])
-            nc.sync.dma_start(out=out_1[n][:, users, :].rearrange("p m t -> p (m t)").bitcast(I32), in_=codes[:].bitcast(I32))
+        def y_quant(chunk, n, part=None):
+            if (chunk, n) not in y_codes:
+                y_codes[chunk, n] = work.tile([P, USERS[chunk]], U32, name="y_codes%d" % chunk, bufs=3, align_bytes=64)
+            first, last = (0, USERS[chunk]) if part is None else (PAIR * part, PAIR * (part + 1))
+            codes = y_codes[chunk, n]
+            nc.vector.quantize_mx(
+                out=codes[:, first:last].bitcast(FP8X4),
+                scales=y_scales[4 * n : P, FIRST_USER[chunk] + first : FIRST_USER[chunk] + last],
+                in_=y_grouped[chunk, n][:, SLOTS * first : SLOTS * last],
+            )
+            users = slice(FIRST_USER[chunk] + first, FIRST_USER[chunk] + last)
+            nc.sync.dma_start(
+                out=out_1[n][:, users, :].rearrange("p m t -> p (m t)").bitcast(I32), in_=codes[:, first:last].bitcast(I32)
+            )
 
         x_widen(0, 0, 4)
-        nc.vector.tensor_copy(
-            out=quad_of[:].rearrange("p (q r) -> p q r", r=QUAD),
-            in_=ident[:, 0 : P // QUAD].unsqueeze(2).to_broadcast([P, P // QUAD, QUAD]),
-        )
+        make_quad_of()
         x_widen(0, 4, 12)
         w_widen(0, 0, on_scalar, slice(0, 2 * PASS))
         w_widen(0, 0, on_scalar, slice(2 * PASS, 4 * PASS))
@@ -495,20 +505,21 @@ def tile_click_value_planes_b4_kernel(
         hidden_pass(WIDE, 1, 2, 2)
         hidden_wide_slot(1, 3)
         h_group(NARROW, 0)
-        h_relu(NARROW, 1)
+        h_relu(NARROW, 1, (0, 1))
         h_group(WIDE, 0)
+        h_relu(NARROW, 1, (2, 3), VECTOR)
         h_quant(NARROW, 0)
+        h_relu(WIDE, 1)
         h_group(NARROW, 1)
-        h_quant(WIDE, 0)
         h_quant(NARROW, 1)
-        h_relu(WIDE, 1, (0, 1, 2))
-        h_relu(WIDE, 1, (3,), VECTOR)
+        h_quant(WIDE, 0)
         narrow_logits(0, 0)
-        turn_bias()
         narrow_logits(0, 1)
+        turn_bias()
         narrow_logits(1, 0)
         narrow_logits(1, 1)
         narrow_logits(2, 0)
+        narrow_logits(2, 1)
         h_group(WIDE, 1, on_vector, slice(0, PAIR))
         h_group(WIDE, 1, on_scalar, slice(PAIR, 2 * PAIR))
         bias_out()
@@ -520,12 +531,13 @@ def tile_click_value_planes_b4_kernel(
         narrow_bias(1, 0)
         narrow_sigmoid(1, 0)
 
-        logits_at = {0: [(2, 1)], 2: [(3, 0), (3, 1)]}
+        logits_at = {2: [(3, 0)], 3: [(3, 1)]}
         bias_at = {0: [(1, 1), (2, 0)], 2: [(2, 1)], 3: [(3, 0)], 4: [(3, 1)]}
         value_at = {0: [(0, 0)], 1: [(1, 0), (0, 1)], 2: [(2, 0), (1, 1)], 3: [(2, 1)], 5: [(3, 0)], 6: [(3, 1)]}
-        narrow_round_at = {1: (0, on_gpsimd), 2: (1, on_gpsimd), 3: (2, on_gpsimd), 6: (3, on_gpsimd)}
         wide_on_scalar = (2, 4, 7)
+        out_on_vector = (7,)
         turn_at = {3: [(0, 0)], 4: [(0, 1), (1, 0)], 5: [(0, 2)], 6: [(2, 0)], 7: [(1, 1)]}
+        quant_at = {5: [(NARROW, 0)], 6: [(NARROW, 1)], 7: [(WIDE, 0)]}
         for step in range(STEPS):
             tiles_now = (2 * step, 2 * step + 1)
             tiles_before = (2 * step - 2, 2 * step - 1) if step else ()
@@ -536,8 +548,8 @@ def tile_click_value_planes_b4_kernel(
             for unit in bias_at.get(step, []):
                 narrow_bias(*unit)
             for unit in turn_at.get(step - 1, []):
-                y_out(*unit)
-            for unit in turn_at.get(step - 2, []):
+                y_out(*unit, on_vector if step in out_on_vector else on_scalar)
+            for unit in quant_at.get(step, []):
                 y_quant(*unit)
             if step >= 2 and step not in wide_on_scalar:
                 wide_round(step - 2, on_vector)
@@ -549,8 +561,6 @@ def tile_click_value_planes_b4_kernel(
                 narrow_sigmoid(*unit)
             if step in wide_on_scalar:
                 wide_round(step - 2, on_scalar)
-            if step in narrow_round_at:
-                narrow_round(*narrow_round_at[step])
             for c in tiles_before:
                 wide_turn(c)
             for unit in turn_at.get(step, []):
@@ -563,33 +573,29 @@ def tile_click_value_planes_b4_kernel(
         wide_turn(14, 5)
         y_turn(3, 0)
         wide_turn(15, 7)
-        keep_warm(0)
         y_out(1, 1)
         wide_round(6, on_scalar)
-        y_quant(2, 0)
+        y_quant(NARROW, 2)
         wide_value(14)
         wide_value(15)
         wide_store(7)
         y_turn(2, 1)
         y_turn(2, 2, 0)
-        keep_warm(5)
-        y_quant(1, 1)
+        y_out(1, 2, on_vector)
         wide_round(7, on_vector, slice(0, 2))
         wide_round(7, on_vector, slice(2, 4))
-        y_out(1, 2, on_vector)
-        y_out(3, 0)
         y_out(2, 1)
+        y_out(2, 2)
         y_turn(3, 1, 6)
         y_turn(3, 2, 1)
-        y_out(2, 2, on_vector)
-        y_quant(1, 2)
-        y_quant(3, 0)
+        y_quant(WIDE, 1)
+        y_out(3, 0, on_vector)
         y_out(3, 1)
-        y_quant(2, 1)
+        y_quant(WIDE, 2)
+        y_quant(NARROW, 3)
         y_out(3, 2)
-        y_quant(2, 2)
-        y_quant(3, 1)
-        y_quant(3, 2)
+        y_quant(WIDE, 3, 0)
+        y_quant(WIDE, 3, 1)
         for q in range(P // QUAD):
             queue = nc.scalar if q % 2 else nc.sync
             queue.dma_start(

@@ -424,18 +424,19 @@ def tile_click_value_planes_b4_kernel(
             )
 
         def y_quant(chunk, n, part=None):
-            if (chunk, n) not in y_codes:
-                y_codes[chunk, n] = work.tile([P, USERS[chunk]], U32, name="y_codes%d" % chunk, bufs=3, align_bytes=64)
+            if n not in y_codes:
+                y_codes[n] = work.tile([P, T], U32, name="y_codes", bufs=3, align_bytes=64)
             first, last = (0, USERS[chunk]) if part is None else (PAIR * part, PAIR * (part + 1))
-            codes = y_codes[chunk, n]
+            users = slice(FIRST_USER[chunk] + first, FIRST_USER[chunk] + last)
             nc.vector.quantize_mx(
-                out=codes[:, first:last].bitcast(FP8X4),
-                scales=y_scales[4 * n : P, FIRST_USER[chunk] + first : FIRST_USER[chunk] + last],
+                out=y_codes[n][:, users].bitcast(FP8X4),
+                scales=y_scales[4 * n : P, users],
                 in_=y_grouped[chunk, n][:, SLOTS * first : SLOTS * last],
             )
-            users = slice(FIRST_USER[chunk] + first, FIRST_USER[chunk] + last)
+
+        def codes_store(n, users=slice(0, T)):
             nc.sync.dma_start(
-                out=out_1[n][:, users, :].rearrange("p m t -> p (m t)").bitcast(I32), in_=codes[:, first:last].bitcast(I32)
+                out=out_1[n][:, users, :].rearrange("p m t -> p (m t)").bitcast(I32), in_=y_codes[n][:, users].bitcast(I32)
             )
 
         x_widen(0, 0, 4)
@@ -533,11 +534,12 @@ def tile_click_value_planes_b4_kernel(
 
         logits_at = {2: [(3, 0)], 3: [(3, 1)]}
         bias_at = {0: [(1, 1), (2, 0)], 2: [(2, 1)], 3: [(3, 0)], 4: [(3, 1)]}
-        value_at = {0: [(0, 0)], 1: [(1, 0), (0, 1)], 2: [(2, 0), (1, 1)], 3: [(2, 1)], 5: [(3, 0)], 6: [(3, 1)]}
+        value_at = {0: [(0, 0)], 1: [(1, 0), (0, 1)], 2: [(2, 0), (1, 1)], 3: [(2, 1)], 4: [(3, 0)], 5: [(3, 1)]}
         wide_on_scalar = (2, 4, 7)
-        out_on_vector = (7,)
-        turn_at = {3: [(0, 0)], 4: [(0, 1), (1, 0)], 5: [(0, 2)], 6: [(2, 0)], 7: [(1, 1)]}
-        quant_at = {5: [(NARROW, 0)], 6: [(NARROW, 1)], 7: [(WIDE, 0)]}
+        out_on_vector = ((1, 0), (1, 1))
+        turn_at = {3: [(0, 0)], 4: [(0, 1), (0, 2)], 5: [(1, 0)], 6: [(1, 1), (1, 2)]}
+        quant_at = {5: [(NARROW, 0)], 6: [(WIDE, 0)], 7: [(NARROW, 1)]}
+        codes_at = {6: [0]}
         for step in range(STEPS):
             tiles_now = (2 * step, 2 * step + 1)
             tiles_before = (2 * step - 2, 2 * step - 1) if step else ()
@@ -548,9 +550,11 @@ def tile_click_value_planes_b4_kernel(
             for unit in bias_at.get(step, []):
                 narrow_bias(*unit)
             for unit in turn_at.get(step - 1, []):
-                y_out(*unit, on_vector if step in out_on_vector else on_scalar)
+                y_out(*unit, on_vector if unit in out_on_vector else on_scalar)
             for unit in quant_at.get(step, []):
                 y_quant(*unit)
+            for n in codes_at.get(step, []):
+                codes_store(n)
             if step >= 2 and step not in wide_on_scalar:
                 wide_round(step - 2, on_vector)
             for c in tiles_now:
@@ -569,33 +573,36 @@ def tile_click_value_planes_b4_kernel(
                 wide_value(c)
             if step:
                 wide_store(step - 1)
-        y_turn(1, 2)
+        y_turn(2, 0)
         wide_turn(14, 5)
         y_turn(3, 0)
         wide_turn(15, 7)
-        y_out(1, 1)
+        y_out(2, 0)
         wide_round(6, on_scalar)
-        y_quant(NARROW, 2)
+        y_quant(WIDE, 1)
+        codes_store(1)
         wide_value(14)
         wide_value(15)
         wide_store(7)
         y_turn(2, 1)
         y_turn(2, 2, 0)
-        y_out(1, 2, on_vector)
+        y_quant(NARROW, 2)
         wide_round(7, on_vector, slice(0, 2))
         wide_round(7, on_vector, slice(2, 4))
         y_out(2, 1)
         y_out(2, 2)
         y_turn(3, 1, 6)
         y_turn(3, 2, 1)
-        y_quant(WIDE, 1)
         y_out(3, 0, on_vector)
         y_out(3, 1)
         y_quant(WIDE, 2)
+        codes_store(2)
         y_quant(NARROW, 3)
         y_out(3, 2)
         y_quant(WIDE, 3, 0)
+        codes_store(3, slice(0, 2 * PAIR))
         y_quant(WIDE, 3, 1)
+        codes_store(3, slice(2 * PAIR, T))
         for q in range(P // QUAD):
             queue = nc.scalar if q % 2 else nc.sync
             queue.dma_start(

@@ -186,7 +186,7 @@ def tile_click_value_planes_b4_kernel(
             chunk = chunk_of(i // 2)
             row = i - FIRST_USER[chunk] // P
             if i not in x_wide:
-                x_wide[i] = work.tile([P, K], BF16, name="x_wide", bufs=4)
+                x_wide[i] = work.tile([P, K], BF16, name="x_wide", tag="y_narrow", bufs=GROUPS)
             for b in range(first, last):
                 block = slice(P * b, P * (b + 1))
                 source, scale = x_raw[i][:, block].bitcast(FP8), x_scale[chunk][:, row, b : b + 1]
@@ -212,8 +212,8 @@ def tile_click_value_planes_b4_kernel(
             first_tile = 2 * pair - FIRST_USER[chunk] // P
             for g in range(K_PASSES):
                 if first_tile == 0:
-                    x_grouped[chunk, g] = keep.tile(
-                        [P, SLOTS * USERS[chunk]], BF16, name="x_grouped%d_%d" % (chunk, g), align_bytes=64
+                    x_grouped[chunk, g] = work.tile(
+                        [P, SLOTS * USERS[chunk]], BF16, name="x_grouped", tag="y_wide", bufs=STEPS, align_bytes=64
                     )
                 words = x_grouped[chunk, g][:].bitcast(F32).rearrange("p (m i u) -> p m i u", m=P, u=2)
                 nc.scalar.copy(
@@ -333,7 +333,7 @@ def tile_click_value_planes_b4_kernel(
             step, part = divmod(c, 2)
             tiles = USERS[WIDE] // P
             if part == 0:
-                y_wide[step] = work.tile([P, tiles, 2 * P], F32, name="y_wide", bufs=4)
+                y_wide[step] = work.tile([P, tiles, 2 * P], F32, name="y_wide", tag="y_wide", bufs=STEPS, align_bytes=64)
             nc.vector.tensor_tensor(
                 out=y_wide[step][:, :, P * part : P * (part + 1)],
                 in0=prob_banks[c][:].rearrange("p (i m) -> p i m", i=tiles),
@@ -374,7 +374,7 @@ def tile_click_value_planes_b4_kernel(
         def narrow_value(n, i):
             items = slice(PASS * n, PASS * (n + 1))
             if i == 0:
-                y_narrow[n] = work.tile([P, 2, PASS], F32, name="y_narrow", bufs=3)
+                y_narrow[n] = work.tile([P, 2, PASS], F32, name="y_narrow", tag="y_narrow", bufs=GROUPS)
             nc.vector.tensor_tensor(out=y_narrow[n][:, i, :], in0=probs[NARROW, n, i][:], in1=bid_spread[:, items], op=ALU.mult)
             if i == 1:
                 nc.sync.dma_start(out=out_0[0:PAIR, items].rearrange("(i p) n -> p i n", p=P), in_=y_narrow[n][:])
@@ -425,7 +425,7 @@ def tile_click_value_planes_b4_kernel(
 
         def y_quant(chunk, n, part=None):
             if n not in y_codes:
-                y_codes[n] = work.tile([P, T], U32, name="y_codes", bufs=3, align_bytes=64)
+                y_codes[n] = work.tile([P, T], U32, name="y_codes", bufs=GROUPS, align_bytes=64)
             first, last = (0, USERS[chunk]) if part is None else (PAIR * part, PAIR * (part + 1))
             users = slice(FIRST_USER[chunk] + first, FIRST_USER[chunk] + last)
             nc.vector.quantize_mx(

@@ -33,12 +33,6 @@ FIRST_USER = {NARROW: 0, WIDE: PAIR}
 USERS = {NARROW: PAIR, WIDE: 2 * PAIR}
 STEPS = ITEM_TILES // 2
 BANKS = 8
-HIDDEN_BANKS = {(NARROW, 0): (1, 2), (WIDE, 0): (3, 4, 5, 6), (NARROW, 1): (7, 0), (WIDE, 1): (1, 2, 3, 4)}
-BIAS_BANK = 4
-SCALE_BANK = 7
-LOGIT_BANKS, PROB_BANKS, PLANE_BANKS = (7, 0, 5), (6, 1), (2, 3, 4)
-NARROW_BANKS = (7, 0, 5, 6, 1, 2, 3, 4)
-TURN_LAG = 2
 
 
 def tile_click_value_planes_b4_kernel(
@@ -52,14 +46,16 @@ def tile_click_value_planes_b4_kernel(
         ctx.enter_context(tc.manual_schedule())
         on_scalar, on_vector = nc.scalar.copy, nc.vector.tensor_copy
 
-        def bank(number):
+        free_banks = list(range(BANKS))
+        bank_of = {}
+
+        def take_bank(key):
+            number = free_banks.pop(0)
+            bank_of[key] = number
             return psum.tile([P, PASS], F32, name="bank%d" % number, tag="bank%d" % number)
 
-        taken = {ring: 0 for ring in (LOGIT_BANKS, PROB_BANKS, PLANE_BANKS)}
-
-        def next_bank(ring):
-            taken[ring] = taken[ring] + 1
-            return bank(ring[(taken[ring] - 1) % len(ring)])
+        def give_back(key):
+            free_banks.append(bank_of[key])
 
         def quantised(name, grouped):
             width = grouped.shape[1] // SLOTS
@@ -150,7 +146,7 @@ def tile_click_value_planes_b4_kernel(
         w_wide, w_grouped, w_mx = {}, {}, {}
         a_banks, h_planes, h_grouped, h_mx = {}, {}, {}, {}
         z_banks, logits, probs, prob_banks = {}, {}, {}, {}
-        y_wide, y_narrow, y16, y_banks, y_grouped = {}, {}, {}, {}, {}
+        y_rows, y16, y_banks, y_grouped = {}, {}, {}, {}
 
         y_codes, bias_bank = {}, []
 
@@ -161,10 +157,11 @@ def tile_click_value_planes_b4_kernel(
             )
 
         def spread_w_scales():
-            spread = bank(SCALE_BANK)
+            spread = take_bank("scales")
             width = w_scale_rows.shape[1]
             nc.tensor.matmul(spread[:, 0:width], lhsT=quad_of[:], rhs=w_scale_rows[:], start=True, stop=True)
             nc.scalar.copy(out=w_scale[:].rearrange("p g b -> p (g b)"), in_=spread[:, 0:width])
+            give_back("scales")
 
         def widen_gain():
             nc.scalar.copy(out=gain_col[:], in_=gain_bf[:].rearrange("p h t -> p (h t)"))
@@ -173,11 +170,12 @@ def tile_click_value_planes_b4_kernel(
             nc.scalar.copy(out=bias_rows32[:], in_=bias_rows[:])
 
         def turn_bias():
-            bias_bank.append(bank(BIAS_BANK))
+            bias_bank.append(take_bank("bias"))
             nc.tensor.transpose(bias_bank[0][:, 0:P], bias_rows32[:], ident[:])
 
         def bias_out():
             nc.scalar.copy(out=bias_col[:], in_=bias_bank[0][:, 0:ITEM_TILES])
+            give_back("bias")
 
         def chunk_of(pair):
             return NARROW if pair == 0 else WIDE
@@ -186,7 +184,7 @@ def tile_click_value_planes_b4_kernel(
             chunk = chunk_of(i // 2)
             row = i - FIRST_USER[chunk] // P
             if i not in x_wide:
-                x_wide[i] = work.tile([P, K], BF16, name="x_wide", tag="y_narrow", bufs=GROUPS)
+                x_wide[i] = work.tile([P, K], BF16, name="x_wide", tag="rows", bufs=12, align_bytes=64)
             for b in range(first, last):
                 block = slice(P * b, P * (b + 1))
                 source, scale = x_raw[i][:, block].bitcast(FP8), x_scale[chunk][:, row, b : b + 1]
@@ -195,9 +193,9 @@ def tile_click_value_planes_b4_kernel(
                 else:
                     nc.vector.tensor_scalar(out=x_wide[i][:, block], in0=source, scalar1=scale, scalar2=None, op0=ALU.mult)
 
-        def x_turn(pair):
-            for g in range(K_PASSES):
-                x_banks[pair, g] = bank((K_PASSES * pair + g) % BANKS)
+        def x_turn(pair, passes=range(K_PASSES)):
+            for g in passes:
+                x_banks[pair, g] = take_bank(("x", pair, g))
                 for ii in range(2):
                     words = x_wide[2 * pair + ii][:].bitcast(F32)
                     for u in range(2):
@@ -207,19 +205,20 @@ def tile_click_value_planes_b4_kernel(
                             ident[:],
                         )
 
-        def x_out(pair):
+        def x_out(pair, passes=range(K_PASSES), copy=on_scalar):
             chunk = chunk_of(pair)
             first_tile = 2 * pair - FIRST_USER[chunk] // P
-            for g in range(K_PASSES):
-                if first_tile == 0:
+            for g in passes:
+                if (chunk, g) not in x_grouped:
                     x_grouped[chunk, g] = work.tile(
-                        [P, SLOTS * USERS[chunk]], BF16, name="x_grouped", tag="y_wide", bufs=STEPS, align_bytes=64
+                        [P, SLOTS * USERS[chunk]], BF16, name="x_grouped", tag="rows", bufs=12, align_bytes=64
                     )
                 words = x_grouped[chunk, g][:].bitcast(F32).rearrange("p (m i u) -> p m i u", m=P, u=2)
-                nc.scalar.copy(
+                copy(
                     out=words[:, :, first_tile : first_tile + 2, :],
                     in_=x_banks[pair, g][:].rearrange("p (u m i) -> p m i u", u=2, i=2),
                 )
+                give_back(("x", pair, g))
 
         def x_quant(chunk, g):
             x_mx[chunk, g] = quantised("x%d_%d" % (chunk, g), x_grouped[chunk, g])
@@ -253,7 +252,7 @@ def tile_click_value_planes_b4_kernel(
             per_bank = PASS // USERS[chunk]
             first = USERS[chunk] * (t % per_bank)
             if (chunk, h, t // per_bank) not in a_banks:
-                a_banks[chunk, h, t // per_bank] = bank(HIDDEN_BANKS[chunk, h][t // per_bank])
+                a_banks[chunk, h, t // per_bank] = take_bank(("a", chunk, h, t // per_bank))
             return a_banks[chunk, h, t // per_bank][:, first : first + USERS[chunk]]
 
         def hidden_pass(chunk, h, t, g):
@@ -294,6 +293,9 @@ def tile_click_value_planes_b4_kernel(
                     nc.scalar.activation(out=plane, in_=sums, func=ACT.Relu, scale=column)
                 else:
                     nc.vector.tensor_scalar(out=plane, in0=sums, scalar1=0.0, scalar2=column, op0=ALU.max, op1=ALU.mult)
+                per_bank = PASS // USERS[chunk]
+                if t % per_bank == per_bank - 1:
+                    give_back(("a", chunk, h, t // per_bank))
 
         def h_group(chunk, h, copy=on_vector, users=slice(None)):
             if (chunk, h) not in h_grouped:
@@ -307,7 +309,7 @@ def tile_click_value_planes_b4_kernel(
             h_mx[chunk, h] = quantised("h%d_%d" % (chunk, h), h_grouped[chunk, h])
 
         def wide_logits(c):
-            z_banks[WIDE, c] = next_bank(LOGIT_BANKS)
+            z_banks[WIDE, c] = take_bank(("z", c))
             for h in range(HALVES):
                 codes, scales = h_mx[WIDE, h]
                 nc.tensor.matmul_mx(
@@ -321,35 +323,36 @@ def tile_click_value_planes_b4_kernel(
                 )
 
         def wide_sigmoid(c):
-            probs[WIDE, c] = work.tile([P, USERS[WIDE]], F32, name="wide_prob", bufs=6)
+            probs[WIDE, c] = work.tile([P, USERS[WIDE]], F32, name="wide_prob", bufs=8)
             nc.scalar.activation(out=probs[WIDE, c][:], in_=z_banks[WIDE, c][:], func=ACT.Sigmoid, bias=bias_col[:, c : c + 1])
+            give_back(("z", c))
 
-        def wide_turn(c, number=None):
-            prob_banks[c] = next_bank(PROB_BANKS) if number is None else bank(number)
-            for i in range(USERS[WIDE] // P):
-                nc.tensor.transpose(prob_banks[c][:, P * i : P * (i + 1)], probs[WIDE, c][:, P * i : P * (i + 1)], ident[:])
+        def wide_turn(n, i):
+            prob_banks[n, i] = take_bank(("prob", n, i))
+            for j in range(SLOTS):
+                nc.tensor.transpose(
+                    prob_banks[n, i][:, P * j : P * (j + 1)], probs[WIDE, SLOTS * n + j][:, P * i : P * (i + 1)], ident[:]
+                )
 
-        def wide_value(c):
-            step, part = divmod(c, 2)
-            tiles = USERS[WIDE] // P
-            if part == 0:
-                y_wide[step] = work.tile([P, tiles, 2 * P], F32, name="y_wide", tag="y_wide", bufs=STEPS, align_bytes=64)
+        def value_tile(n, pair):
+            if (n, pair) not in y_rows:
+                y_rows[n, pair] = work.tile([P, 2, PASS], F32, name="y_rows", tag="rows", bufs=12, align_bytes=64)
+            return y_rows[n, pair]
+
+        def wide_value(n, i):
             nc.vector.tensor_tensor(
-                out=y_wide[step][:, :, P * part : P * (part + 1)],
-                in0=prob_banks[c][:].rearrange("p (i m) -> p i m", i=tiles),
-                in1=bid_spread[:, P * c : P * (c + 1)].unsqueeze(1).to_broadcast([P, tiles, P]),
-                op=ALU.mult,
+                out=value_tile(n, 1 + i // 2)[:, i % 2, :], in0=prob_banks[n, i][:], in1=bid_spread[:, PASS * n : PASS * (n + 1)], op=ALU.mult
             )
+            give_back(("prob", n, i))
 
-        def wide_store(step):
-            nc.sync.dma_start(
-                out=out_0[FIRST_USER[WIDE] : T, 2 * P * step : 2 * P * (step + 1)].rearrange("(i p) n -> p i n", p=P),
-                in_=y_wide[step][:],
-            )
+        def y_store(n, pair):
+            rows = out_0[PAIR * pair : PAIR * (pair + 1), PASS * n : PASS * (n + 1)].rearrange("(i p) n -> p i n", p=P)
+            nc.sync.dma_start(out=rows, in_=y_rows[n, pair][:])
 
-        def narrow_logits(n, i):
-            z_banks[NARROW, n, i] = bank(NARROW_BANKS[2 * n + i])
-            for h in range(HALVES):
+        def narrow_logits(n, i, halves=range(HALVES)):
+            for h in halves:
+                if h == 0:
+                    z_banks[NARROW, n, i] = take_bank(("z", n, i))
                 codes, scales = h_mx[NARROW, h]
                 nc.tensor.matmul_mx(
                     out=z_banks[NARROW, n, i][:],
@@ -366,62 +369,39 @@ def tile_click_value_planes_b4_kernel(
             nc.vector.tensor_tensor(
                 out=logits[n, i][:], in0=z_banks[NARROW, n, i][:], in1=bias_spread[:, PASS * n : PASS * (n + 1)], op=ALU.add
             )
+            give_back(("z", n, i))
 
         def narrow_sigmoid(n, i):
             probs[NARROW, n, i] = work.tile([P, PASS], F32, name="narrow_prob", bufs=5)
             nc.scalar.activation(out=probs[NARROW, n, i][:], in_=logits[n, i][:], func=ACT.Sigmoid)
 
         def narrow_value(n, i):
-            items = slice(PASS * n, PASS * (n + 1))
-            if i == 0:
-                y_narrow[n] = work.tile([P, 2, PASS], F32, name="y_narrow", tag="y_narrow", bufs=GROUPS)
-            nc.vector.tensor_tensor(out=y_narrow[n][:, i, :], in0=probs[NARROW, n, i][:], in1=bid_spread[:, items], op=ALU.mult)
-            if i == 1:
-                nc.sync.dma_start(out=out_0[0:PAIR, items].rearrange("(i p) n -> p i n", p=P), in_=y_narrow[n][:])
-                narrow_round(n)
+            nc.vector.tensor_tensor(out=value_tile(n, 0)[:, i, :], in0=probs[NARROW, n, i][:], in1=bid_spread[:, PASS * n : PASS * (n + 1)], op=ALU.mult)
 
-        def wide_round(step, copy, tiles=slice(None)):
-            n, half = divmod(step, 2)
-            if (WIDE, n) not in y16:
-                y16[WIDE, n] = work.tile([P, USERS[WIDE] // P, 2, P, 2], BF16, name="y16_wide", bufs=2)
-            copy(
-                out=y16[WIDE, n][:, tiles, :, P // 2 * half : P // 2 * (half + 1)],
-                in_=y_wide[step][:, tiles].rearrange("p i (r u e) -> p i u r e", u=2, e=2),
-            )
+        def on_gpsimd(out, in_):
+            nc.gpsimd.tensor_scalar(out=out, in0=in_, scalar1=1.0, scalar2=0.0, op0=ALU.mult, op1=ALU.add)
 
-        def narrow_round(n):
-            y16[NARROW, n] = work.tile([P, 2, 2, P, 2], BF16, name="y16_narrow", bufs=2)
-            nc.gpsimd.tensor_scalar(
-                out=y16[NARROW, n][:],
-                in0=y_narrow[n][:].rearrange("p i (r u e) -> p u i r e", u=2, e=2),
-                scalar1=1.0,
-                scalar2=0.0,
-                op0=ALU.mult,
-                op1=ALU.add,
-            )
+        def y_round(n, pair, copy):
+            y16[n, pair] = work.tile([P, 2, 2, P, 2], BF16, name="y16", bufs=8)
+            copy(out=y16[n, pair][:], in_=y_rows[n, pair][:].rearrange("p i (r u e) -> p u i r e", u=2, e=2))
 
-        def y_turn(n, pair, number=None):
-            chunk = chunk_of(pair)
-            first_tile = 2 * pair - FIRST_USER[chunk] // P
-            y_banks[n, pair] = next_bank(PLANE_BANKS) if number is None else bank(number)
-            words = y16[chunk, n][:].rearrange("p i u r e -> p i (u r e)").bitcast(F32)
+        def y_turn(n, pair):
+            y_banks[n, pair] = take_bank(("y", n, pair))
+            words = y16[n, pair][:].rearrange("p u i r e -> p u i (r e)").bitcast(F32)
             for ii in range(2):
                 for u in range(2):
-                    nc.tensor.transpose(
-                        y_banks[n, pair][:, PAIR * u + P * ii : PAIR * u + P * (ii + 1)],
-                        words[:, first_tile + ii, P * u : P * (u + 1)] if pair else words[:, u, P * ii : P * (ii + 1)],
-                        ident[:],
-                    )
+                    nc.tensor.transpose(y_banks[n, pair][:, PAIR * u + P * ii : PAIR * u + P * (ii + 1)], words[:, u, ii], ident[:])
 
         def y_out(n, pair, copy=on_scalar):
             chunk = chunk_of(pair)
             if (chunk, n) not in y_grouped:
-                y_grouped[chunk, n] = work.tile([P, SLOTS * USERS[chunk]], BF16, name="y_grouped%d" % chunk, bufs=3, align_bytes=64)
+                y_grouped[chunk, n] = work.tile([P, SLOTS * USERS[chunk]], BF16, name="y_grouped", tag=("y_grouped", "grouped")[chunk], bufs=3, align_bytes=64)
             first_word = 2 * (PAIR * pair - FIRST_USER[chunk])
             copy(
                 out=y_grouped[chunk, n][:].bitcast(F32)[:, first_word : first_word + 2 * PAIR].rearrange("p (m u) -> p m u", u=2),
                 in_=y_banks[n, pair][:].rearrange("p (u m) -> p m u", u=2),
             )
+            give_back(("y", n, pair))
 
         def y_quant(chunk, n, part=None):
             if n not in y_codes:
@@ -439,169 +419,300 @@ def tile_click_value_planes_b4_kernel(
                 out=out_1[n][:, users, :].rearrange("p m t -> p (m t)").bitcast(I32), in_=y_codes[n][:, users].bitcast(I32)
             )
 
-        x_widen(0, 0, 4)
-        make_quad_of()
-        x_widen(0, 4, 12)
+        x_widen(0, 0, 4, VECTOR)
         w_widen(0, 0, on_scalar, slice(0, 2 * PASS))
+        make_quad_of()
+        x_widen(0, 4, 8, VECTOR)
         w_widen(0, 0, on_scalar, slice(2 * PASS, 4 * PASS))
-        x_widen(1, 9, 12, SCALAR)
         spread_w_scales()
-        x_widen(1, 0, 9)
-        x_turn(0)
-        x_widen(2, 9, 12, SCALAR)
-        x_widen(2, 0, 9)
-        x_widen(3, on=SCALAR)
+        x_widen(0, 8, 12, VECTOR)
+        x_widen(1, 8, 12, SCALAR)
+        x_widen(1, 0, 4, VECTOR)
+        x_widen(2, 8, 12, SCALAR)
+        x_widen(1, 4, 8, VECTOR)
+        x_turn(0, (0,))
+        x_widen(2, 0, 4, VECTOR)
+        x_turn(0, (1,))
+        x_widen(3, 0, 4, SCALAR)
+        x_widen(2, 4, 8, VECTOR)
+        x_turn(0, (2,))
         w_group(0, 0)
+        x_widen(3, 4, 8, SCALAR)
+        x_turn(1, (0,))
+        x_widen(3, 8, 12, SCALAR)
+        x_turn(1, (1,))
+        x_widen(4, 0, 4, VECTOR)
         w_widen(1, 0)
-        x_turn(1)
-        x_widen(4)
-        x_out(0)
+        x_turn(1, (2,))
+        x_widen(4, 4, 8, VECTOR)
+        x_widen(4, 8, 12, VECTOR)
+        x_out(0, (0,), on_scalar)
         w_quant(0, 0)
+        x_out(0, (1,), on_scalar)
         w_group(1, 0)
+        x_out(0, (2,), on_scalar)
         w_widen(2, 0)
-        x_widen(5, 0, 9)
-        x_widen(5, 9, 12, SCALAR)
-        x_turn(2)
-        w_widen(0, 1)
-        x_out(1)
+        x_widen(5, 0, 4, VECTOR)
+        x_widen(5, 4, 8, VECTOR)
+        x_turn(2, (0,))
+        x_widen(5, 8, 12, SCALAR)
         w_quant(1, 0)
+        x_turn(2, (1,))
+        w_widen(0, 1)
         x_quant(NARROW, 0)
+        x_turn(2, (2,))
         w_group(2, 0)
+        hidden_pass(NARROW, 0, 0, 0)
+        hidden_pass(NARROW, 0, 2, 0)
+        x_out(1, (0,), on_scalar)
+        x_out(2, (0,), on_scalar)
         x_quant(NARROW, 1)
         x_quant(NARROW, 2)
-        x_out(2)
+        hidden_pass(NARROW, 0, 0, 1)
+        x_out(1, (1,), on_scalar)
+        hidden_pass(NARROW, 0, 2, 1)
         w_quant(2, 0)
-        hidden_narrow(0, 0)
-        hidden_narrow(0, 1)
-        hidden_narrow(0, 2)
+        x_out(2, (1,), on_scalar)
         w_group(0, 1)
-        w_widen(1, 1)
+        hidden_pass(NARROW, 0, 0, 2)
+        x_out(1, (2,), on_scalar)
+        for again in range(K_PASSES):
+            hidden_pass(NARROW, 0, 1, again)
+        hidden_pass(NARROW, 0, 2, 2)
+        widen_bias()
+        x_out(2, (2,), on_scalar)
         x_quant(WIDE, 0)
+        for again in range(K_PASSES):
+            hidden_pass(NARROW, 0, 3, again)
+        w_widen(1, 1)
+        turn_bias()
         w_quant(0, 1)
+        hidden_pass(WIDE, 0, 0, 0)
+        hidden_pass(WIDE, 0, 1, 0)
+        hidden_pass(WIDE, 0, 2, 0)
         x_quant(WIDE, 1)
-        x_quant(WIDE, 2)
+        bias_out()
+        hidden_pass(WIDE, 0, 3, 0)
         widen_gain()
         w_widen(2, 1)
-        hidden_wide(0, 0)
-        hidden_wide(0, 1)
-        hidden_wide(0, 2)
+        x_quant(WIDE, 2)
+        hidden_pass(WIDE, 0, 0, 1)
+        hidden_pass(WIDE, 0, 1, 1)
+        hidden_pass(WIDE, 0, 2, 1)
         w_group(1, 1)
-        h_relu(NARROW, 0)
+        hidden_pass(WIDE, 0, 3, 1)
+        h_relu(NARROW, 0, (0, 1), SCALAR)
+        hidden_pass(WIDE, 0, 0, 2)
+        hidden_pass(WIDE, 0, 1, 2)
+        h_relu(NARROW, 0, (2, 3), SCALAR)
+        hidden_pass(WIDE, 0, 2, 2)
+        hidden_pass(WIDE, 0, 3, 2)
         w_group(2, 1)
-        w_quant(1, 1)
-        h_relu(WIDE, 0)
-        widen_bias()
-        hidden_narrow(1, 0)
+        hidden_pass(NARROW, 1, 0, 0)
+        hidden_pass(NARROW, 1, 2, 0)
+        h_relu(WIDE, 0, (0,), SCALAR)
         hidden_pass(WIDE, 1, 0, 0)
         hidden_pass(WIDE, 1, 1, 0)
-        hidden_pass(WIDE, 1, 2, 0)
-        hidden_narrow(1, 1)
-        hidden_pass(WIDE, 1, 0, 1)
+        h_relu(WIDE, 0, (1,), SCALAR)
+        w_quant(1, 1)
+        h_relu(WIDE, 0, (2,), SCALAR)
         w_quant(2, 1)
-        hidden_narrow(1, 2)
+        hidden_pass(NARROW, 1, 0, 1)
+        h_relu(WIDE, 0, (3,), SCALAR)
+        hidden_pass(NARROW, 1, 2, 1)
+        hidden_pass(WIDE, 1, 0, 1)
+        h_group(NARROW, 0, on_vector)
+        hidden_pass(NARROW, 1, 0, 2)
+        for again in range(K_PASSES):
+            hidden_pass(NARROW, 1, 1, again)
+        h_quant(NARROW, 0)
+        hidden_pass(NARROW, 1, 2, 2)
+        h_group(WIDE, 0, on_vector, slice(0, PAIR))
+        h_relu(NARROW, 1, (0, 1), SCALAR)
+        for again in range(K_PASSES):
+            hidden_pass(NARROW, 1, 3, again)
         hidden_pass(WIDE, 1, 0, 2)
         hidden_pass(WIDE, 1, 1, 1)
-        hidden_pass(WIDE, 1, 1, 2)
-        hidden_pass(WIDE, 1, 2, 1)
-        hidden_pass(WIDE, 1, 2, 2)
-        hidden_wide_slot(1, 3)
-        h_group(NARROW, 0)
-        h_relu(NARROW, 1, (0, 1))
-        h_group(WIDE, 0)
         h_relu(NARROW, 1, (2, 3), VECTOR)
-        h_quant(NARROW, 0)
-        h_relu(WIDE, 1)
-        h_group(NARROW, 1)
-        h_quant(NARROW, 1)
+        h_relu(WIDE, 1, (0,), SCALAR)
+        hidden_pass(WIDE, 1, 1, 2)
+        h_group(WIDE, 0, on_vector, slice(PAIR, 2 * PAIR))
+        hidden_pass(WIDE, 1, 2, 0)
+        h_relu(WIDE, 1, (1,), SCALAR)
+        h_group(NARROW, 1, on_vector)
+        hidden_pass(WIDE, 1, 2, 1)
         h_quant(WIDE, 0)
-        narrow_logits(0, 0)
-        narrow_logits(0, 1)
-        turn_bias()
-        narrow_logits(1, 0)
-        narrow_logits(1, 1)
-        narrow_logits(2, 0)
-        narrow_logits(2, 1)
-        h_group(WIDE, 1, on_vector, slice(0, PAIR))
-        h_group(WIDE, 1, on_scalar, slice(PAIR, 2 * PAIR))
-        bias_out()
+        hidden_pass(WIDE, 1, 2, 2)
+        hidden_pass(WIDE, 1, 3, 0)
+        h_quant(NARROW, 1)
+        h_relu(WIDE, 1, (2,), SCALAR)
+        hidden_pass(WIDE, 1, 3, 1)
+        hidden_pass(WIDE, 1, 3, 2)
+        narrow_logits(0, 0, (0,))
+        narrow_logits(0, 1, (0,))
+        h_relu(WIDE, 1, (3,), SCALAR)
+        narrow_logits(1, 0, (0,))
+        narrow_logits(1, 1, (0,))
+        h_group(WIDE, 1, on_vector, slice(0, 3 * P))
+        h_group(WIDE, 1, on_scalar, slice(3 * P, 4 * P))
+        narrow_logits(0, 0, (1,))
+        narrow_logits(0, 1, (1,))
+        narrow_logits(1, 0, (1,))
+        narrow_logits(1, 1, (1,))
         narrow_bias(0, 0)
-        narrow_bias(0, 1)
+        narrow_logits(2, 0)
         h_quant(WIDE, 1)
         narrow_sigmoid(0, 0)
-        narrow_sigmoid(0, 1)
+        narrow_logits(2, 1)
+        narrow_bias(0, 1)
+        wide_logits(0)
         narrow_bias(1, 0)
+        wide_logits(1)
+        narrow_sigmoid(0, 1)
+        wide_logits(2)
+        narrow_bias(1, 1)
+        wide_sigmoid(0)
+        wide_logits(3)
+        narrow_value(0, 0)
+        wide_sigmoid(1)
+        narrow_logits(3, 0)
+        narrow_value(0, 1)
+        wide_sigmoid(2)
+        narrow_logits(3, 1)
+        narrow_bias(2, 0)
+        y_round(0, 0, on_gpsimd)
+        y_store(0, 0)
+        wide_sigmoid(3)
+        narrow_bias(2, 1)
         narrow_sigmoid(1, 0)
-
-        logits_at = {2: [(3, 0)], 3: [(3, 1)]}
-        bias_at = {0: [(1, 1), (2, 0)], 2: [(2, 1)], 3: [(3, 0)], 4: [(3, 1)]}
-        value_at = {0: [(0, 0)], 1: [(1, 0), (0, 1)], 2: [(2, 0), (1, 1)], 3: [(2, 1)], 4: [(3, 0)], 5: [(3, 1)]}
-        wide_on_scalar = (2, 4, 7)
-        out_on_vector = ((1, 0), (1, 1))
-        turn_at = {3: [(0, 0)], 4: [(0, 1), (0, 2)], 5: [(1, 0)], 6: [(1, 1), (1, 2)]}
-        quant_at = {5: [(NARROW, 0)], 6: [(WIDE, 0)], 7: [(NARROW, 1)]}
-        codes_at = {6: [0]}
-        for step in range(STEPS):
-            tiles_now = (2 * step, 2 * step + 1)
-            tiles_before = (2 * step - 2, 2 * step - 1) if step else ()
-            for c in tiles_now:
-                wide_logits(c)
-            for unit in logits_at.get(step, []):
-                narrow_logits(*unit)
-            for unit in bias_at.get(step, []):
-                narrow_bias(*unit)
-            for unit in turn_at.get(step - 1, []):
-                y_out(*unit, on_vector if unit in out_on_vector else on_scalar)
-            for unit in quant_at.get(step, []):
-                y_quant(*unit)
-            for n in codes_at.get(step, []):
-                codes_store(n)
-            if step >= 2 and step not in wide_on_scalar:
-                wide_round(step - 2, on_vector)
-            for c in tiles_now:
-                wide_sigmoid(c)
-            for unit in value_at.get(step, []):
-                narrow_value(*unit)
-            for unit in bias_at.get(step, []):
-                narrow_sigmoid(*unit)
-            if step in wide_on_scalar:
-                wide_round(step - 2, on_scalar)
-            for c in tiles_before:
-                wide_turn(c)
-            for unit in turn_at.get(step, []):
-                y_turn(*unit)
-            for c in tiles_before:
-                wide_value(c)
-            if step:
-                wide_store(step - 1)
+        wide_turn(0, 0)
+        wide_turn(0, 1)
+        narrow_sigmoid(1, 1)
+        wide_turn(0, 2)
+        wide_value(0, 0)
+        wide_turn(0, 3)
+        narrow_sigmoid(2, 0)
+        wide_value(0, 1)
+        wide_logits(4)
+        narrow_sigmoid(2, 1)
+        wide_logits(5)
+        wide_value(0, 2)
+        y_round(0, 1, on_gpsimd)
+        y_store(0, 1)
+        wide_sigmoid(4)
+        wide_logits(6)
+        wide_value(0, 3)
+        wide_logits(7)
+        wide_sigmoid(5)
+        narrow_bias(3, 0)
+        y_store(0, 2)
+        y_round(0, 2, on_gpsimd)
+        wide_logits(8)
+        wide_sigmoid(6)
+        narrow_bias(3, 1)
+        wide_logits(9)
+        wide_sigmoid(7)
+        narrow_value(1, 0)
+        narrow_value(1, 1)
+        narrow_sigmoid(3, 0)
+        wide_turn(1, 0)
+        wide_turn(1, 1)
+        narrow_sigmoid(3, 1)
+        y_round(1, 0, on_gpsimd)
+        y_store(1, 0)
+        wide_turn(1, 2)
+        wide_value(1, 0)
+        wide_turn(1, 3)
+        wide_sigmoid(8)
+        wide_value(1, 1)
+        y_turn(0, 0)
+        wide_logits(10)
+        wide_sigmoid(9)
+        wide_value(1, 2)
+        y_round(1, 1, on_gpsimd)
+        y_store(1, 1)
+        wide_logits(11)
+        wide_value(1, 3)
+        wide_sigmoid(10)
+        wide_logits(12)
+        y_out(0, 0, on_vector)
+        wide_sigmoid(11)
+        y_store(1, 2)
+        wide_logits(13)
+        narrow_value(2, 0)
+        y_round(1, 2, on_scalar)
+        wide_turn(2, 0)
+        wide_turn(2, 1)
+        narrow_value(2, 1)
+        wide_turn(2, 2)
+        wide_turn(2, 3)
+        wide_value(2, 0)
+        wide_sigmoid(12)
+        y_round(2, 0, on_gpsimd)
+        y_store(2, 0)
+        y_turn(0, 1)
+        wide_logits(14)
+        wide_value(2, 1)
+        wide_sigmoid(13)
+        wide_logits(15)
+        wide_value(2, 2)
+        y_store(2, 1)
+        y_round(2, 1, on_gpsimd)
+        wide_sigmoid(14)
+        y_turn(0, 2)
+        wide_value(2, 3)
+        y_turn(1, 0)
+        wide_sigmoid(15)
+        y_turn(1, 1)
+        y_out(0, 1, on_vector)
+        y_store(2, 2)
+        y_round(2, 2, on_scalar)
+        wide_turn(3, 0)
+        narrow_value(3, 0)
+        wide_turn(3, 1)
+        wide_turn(3, 2)
+        narrow_value(3, 1)
+        wide_turn(3, 3)
+        y_out(1, 0, on_scalar)
+        y_turn(1, 2)
+        wide_value(3, 0)
+        y_round(3, 0, on_gpsimd)
+        y_store(3, 0)
+        y_out(1, 1, on_scalar)
         y_turn(2, 0)
-        wide_turn(14, 5)
-        y_turn(3, 0)
-        wide_turn(15, 7)
-        y_out(2, 0)
-        wide_round(6, on_scalar)
-        y_quant(WIDE, 1)
-        codes_store(1)
-        wide_value(14)
-        wide_value(15)
-        wide_store(7)
+        wide_value(3, 1)
         y_turn(2, 1)
-        y_turn(2, 2, 0)
+        y_out(1, 2, on_scalar)
+        y_turn(2, 2)
+        wide_value(3, 2)
+        y_store(3, 1)
+        y_round(3, 1, on_gpsimd)
+        y_out(2, 0, on_scalar)
+        y_turn(3, 0)
+        wide_value(3, 3)
+        y_out(0, 2, on_vector)
+        y_round(3, 2, on_scalar)
+        y_store(3, 2)
+        y_turn(3, 1)
+        y_quant(NARROW, 0)
+        y_quant(WIDE, 0)
+        y_out(2, 1, on_scalar)
+        y_turn(3, 2)
+        y_quant(NARROW, 1)
+        codes_store(0)
+        y_out(2, 2, on_scalar)
+        y_quant(WIDE, 1)
+        y_out(3, 0, on_scalar)
         y_quant(NARROW, 2)
-        wide_round(7, on_vector, slice(0, 2))
-        wide_round(7, on_vector, slice(2, 4))
-        y_out(2, 1)
-        y_out(2, 2)
-        y_turn(3, 1, 6)
-        y_turn(3, 2, 1)
-        y_out(3, 0, on_vector)
-        y_out(3, 1)
+        codes_store(1)
         y_quant(WIDE, 2)
-        codes_store(2)
+        y_out(3, 1, on_scalar)
         y_quant(NARROW, 3)
-        y_out(3, 2)
+        codes_store(2)
+        y_out(3, 2, on_scalar)
         y_quant(WIDE, 3, 0)
-        codes_store(3, slice(0, 2 * PAIR))
         y_quant(WIDE, 3, 1)
+        codes_store(3, slice(0, 2 * PAIR))
         codes_store(3, slice(2 * PAIR, T))
         for q in range(P // QUAD):
             queue = nc.scalar if q % 2 else nc.sync

@@ -127,8 +127,9 @@ def tile_click_value_planes_b4_kernel(
         load_x(4)
         load_x(5)
         load_w(2, 0)
-        for g in range(K_PASSES):
-            load_w(g, 1)
+        load_w(0, 1)
+        load_w(1, 1)
+        load_w(2, 1)
         nc.sync.dma_start(out=gain_bf[:], in_=gain.rearrange("(h p t) -> p h t", h=HALVES, t=SLOTS))
         nc.sync.dma_start(out=bias_rows[0:ITEM_TILES, :], in_=item_bias.rearrange("(c p) -> c p", p=P))
         for q in range(P // QUAD):
@@ -142,13 +143,14 @@ def tile_click_value_planes_b4_kernel(
             nc.sync.dma_start(out=bias_spread[:, items], in_=item_bias[items].partition_broadcast(P))
             nc.sync.dma_start(out=bid_spread[:, items], in_=bid[items].partition_broadcast(P))
 
+        x_pairs, x_passes = {}, {}
         x_wide, x_banks, x_grouped, x_mx = {}, {}, {}, {}
         w_wide, w_grouped, w_mx = {}, {}, {}
         a_banks, h_planes, h_grouped, h_mx = {}, {}, {}, {}
         z_banks, logits, probs, prob_banks = {}, {}, {}, {}
         y_rows, y16, y_banks, y_grouped = {}, {}, {}, {}
 
-        y_codes, bias_bank = {}, []
+        y_codes, bias_bank, scale_bank = {}, [], []
 
         def make_quad_of():
             nc.vector.tensor_copy(
@@ -160,7 +162,10 @@ def tile_click_value_planes_b4_kernel(
             spread = take_bank("scales")
             width = w_scale_rows.shape[1]
             nc.tensor.matmul(spread[:, 0:width], lhsT=quad_of[:], rhs=w_scale_rows[:], start=True, stop=True)
-            nc.scalar.copy(out=w_scale[:].rearrange("p g b -> p (g b)"), in_=spread[:, 0:width])
+            scale_bank.append(spread[:, 0:width])
+
+        def w_scales_out():
+            nc.scalar.copy(out=w_scale[:].rearrange("p g b -> p (g b)"), in_=scale_bank[0])
             give_back("scales")
 
         def widen_gain():
@@ -183,8 +188,9 @@ def tile_click_value_planes_b4_kernel(
         def x_widen(i, first=0, last=K // P, on=VECTOR):
             chunk = chunk_of(i // 2)
             row = i - FIRST_USER[chunk] // P
-            if i not in x_wide:
-                x_wide[i] = work.tile([P, K], BF16, name="x_wide", tag="rows", bufs=12, align_bytes=64)
+            if i // 2 not in x_pairs:
+                x_pairs[i // 2] = work.tile([P, 2 * K], BF16, name="x_wide", tag="rows", bufs=6, align_bytes=64)
+            x_wide[i] = x_pairs[i // 2][:, K * (i % 2) : K * (i % 2 + 1)]
             for b in range(first, last):
                 block = slice(P * b, P * (b + 1))
                 source, scale = x_raw[i][:, block].bitcast(FP8), x_scale[chunk][:, row, b : b + 1]
@@ -197,7 +203,7 @@ def tile_click_value_planes_b4_kernel(
             for g in passes:
                 x_banks[pair, g] = take_bank(("x", pair, g))
                 for ii in range(2):
-                    words = x_wide[2 * pair + ii][:].bitcast(F32)
+                    words = x_wide[2 * pair + ii].bitcast(F32)
                     for u in range(2):
                         nc.tensor.transpose(
                             x_banks[pair, g][:, PAIR * u + ii : PAIR * (u + 1) : 2],
@@ -209,11 +215,10 @@ def tile_click_value_planes_b4_kernel(
             chunk = chunk_of(pair)
             first_tile = 2 * pair - FIRST_USER[chunk] // P
             for g in passes:
-                if (chunk, g) not in x_grouped:
-                    x_grouped[chunk, g] = work.tile(
-                        [P, SLOTS * USERS[chunk]], BF16, name="x_grouped", tag="rows", bufs=12, align_bytes=64
-                    )
-                words = x_grouped[chunk, g][:].bitcast(F32).rearrange("p (m i u) -> p m i u", m=P, u=2)
+                if g not in x_passes:
+                    x_passes[g] = work.tile([P, SLOTS * T], BF16, name="x_grouped", tag="rows", bufs=6, align_bytes=64)
+                x_grouped[chunk, g] = x_passes[g][:, SLOTS * FIRST_USER[chunk] : SLOTS * (FIRST_USER[chunk] + USERS[chunk])]
+                words = x_grouped[chunk, g].bitcast(F32).rearrange("p (m i u) -> p m i u", m=P, u=2)
                 copy(
                     out=words[:, :, first_tile : first_tile + 2, :],
                     in_=x_banks[pair, g][:].rearrange("p (u m i) -> p m i u", u=2, i=2),
@@ -224,10 +229,10 @@ def tile_click_value_planes_b4_kernel(
             x_mx[chunk, g] = quantised("x%d_%d" % (chunk, g), x_grouped[chunk, g])
 
         def slot_planes(name, width):
-            return work.tile([P, SLOTS, width], BF16, name=name, tag="planes", bufs=5)
+            return work.tile([P, SLOTS, width], BF16, name=name, tag="planes", bufs=6)
 
         def grouped_tile(name, width):
-            return work.tile([P, SLOTS * width], BF16, name=name, tag="grouped", align_bytes=64)
+            return work.tile([P, SLOTS * width], BF16, name=name, tag="grouped", bufs=GROUPS, align_bytes=64)
 
         def w_widen(g, h, copy=on_scalar, part=slice(None)):
             if (g, h) not in w_wide:
@@ -323,7 +328,7 @@ def tile_click_value_planes_b4_kernel(
                 )
 
         def wide_sigmoid(c):
-            probs[WIDE, c] = work.tile([P, USERS[WIDE]], F32, name="wide_prob", bufs=8)
+            probs[WIDE, c] = work.tile([P, USERS[WIDE]], F32, name="wide_prob", bufs=12)
             nc.scalar.activation(out=probs[WIDE, c][:], in_=z_banks[WIDE, c][:], func=ACT.Sigmoid, bias=bias_col[:, c : c + 1])
             give_back(("z", c))
 
@@ -334,20 +339,30 @@ def tile_click_value_planes_b4_kernel(
                     prob_banks[n, i][:, P * j : P * (j + 1)], probs[WIDE, SLOTS * n + j][:, P * i : P * (i + 1)], ident[:]
                 )
 
-        def value_tile(n, pair):
-            if (n, pair) not in y_rows:
-                y_rows[n, pair] = work.tile([P, 2, PASS], F32, name="y_rows", tag="rows", bufs=12, align_bytes=64)
-            return y_rows[n, pair]
+        def bundle(n, pair):
+            return ((NARROW, n // 2), n % 2, 2) if pair == 0 else ((WIDE, n), 2 * (pair - 1), 1)
+
+        def value_rows(n, i):
+            key, first, step = bundle(n, i // 2)
+            if key not in y_rows:
+                y_rows[key] = work.tile([P, SLOTS * PASS], F32, name="y_rows", tag="rows", bufs=6, align_bytes=64)
+            slot = first + step * (i % 2)
+            return y_rows[key][:, PASS * slot : PASS * (slot + 1)]
 
         def wide_value(n, i):
             nc.vector.tensor_tensor(
-                out=value_tile(n, 1 + i // 2)[:, i % 2, :], in0=prob_banks[n, i][:], in1=bid_spread[:, PASS * n : PASS * (n + 1)], op=ALU.mult
+                out=value_rows(n, 2 + i), in0=prob_banks[n, i][:], in1=bid_spread[:, PASS * n : PASS * (n + 1)], op=ALU.mult
             )
             give_back(("prob", n, i))
 
-        def y_store(n, pair):
-            rows = out_0[PAIR * pair : PAIR * (pair + 1), PASS * n : PASS * (n + 1)].rearrange("(i p) n -> p i n", p=P)
-            nc.sync.dma_start(out=rows, in_=y_rows[n, pair][:])
+        def y_store(n, pair, groups=1):
+            key, first, step = bundle(n, pair)
+            rows = out_0[PAIR * pair : PAIR * (pair + 1), PASS * n : PASS * (n + groups)].rearrange("(i p) n -> p i n", p=P)
+            if pair == 0:
+                source = y_rows[key][:].rearrange("p (i n) -> p i n", i=2)[:, :, PASS * first : PASS * (first + groups)]
+            else:
+                source = y_rows[key][:, PASS * first : PASS * (first + 2)].rearrange("p (i n) -> p i n", i=2)
+            nc.sync.dma_start(out=rows, in_=source)
 
         def narrow_logits(n, i, halves=range(HALVES)):
             for h in halves:
@@ -376,26 +391,33 @@ def tile_click_value_planes_b4_kernel(
             nc.scalar.activation(out=probs[NARROW, n, i][:], in_=logits[n, i][:], func=ACT.Sigmoid)
 
         def narrow_value(n, i):
-            nc.vector.tensor_tensor(out=value_tile(n, 0)[:, i, :], in0=probs[NARROW, n, i][:], in1=bid_spread[:, PASS * n : PASS * (n + 1)], op=ALU.mult)
+            nc.vector.tensor_tensor(out=value_rows(n, i), in0=probs[NARROW, n, i][:], in1=bid_spread[:, PASS * n : PASS * (n + 1)], op=ALU.mult)
 
         def on_gpsimd(out, in_):
             nc.gpsimd.tensor_scalar(out=out, in0=in_, scalar1=1.0, scalar2=0.0, op0=ALU.mult, op1=ALU.add)
 
-        def y_round(n, pair, copy):
-            y16[n, pair] = work.tile([P, 2, 2, P, 2], BF16, name="y16", bufs=8)
-            copy(out=y16[n, pair][:], in_=y_rows[n, pair][:].rearrange("p i (r u e) -> p u i r e", u=2, e=2))
+        def y_round(key, copy, first=0, last=SLOTS):
+            if key not in y16:
+                y16[key] = work.tile([P, 2, SLOTS, P, 2], BF16, name="y16", tag="planes", bufs=6)
+            copy(
+                out=y16[key][:, :, first:last],
+                in_=y_rows[key][:, PASS * first : PASS * last].rearrange("p (i r u e) -> p u i r e", r=P, u=2, e=2),
+            )
 
         def y_turn(n, pair):
+            key, first, step = bundle(n, pair)
             y_banks[n, pair] = take_bank(("y", n, pair))
-            words = y16[n, pair][:].rearrange("p u i r e -> p u i (r e)").bitcast(F32)
+            words = y16[key][:].rearrange("p u i r e -> p u i (r e)").bitcast(F32)
             for ii in range(2):
                 for u in range(2):
-                    nc.tensor.transpose(y_banks[n, pair][:, PAIR * u + P * ii : PAIR * u + P * (ii + 1)], words[:, u, ii], ident[:])
+                    nc.tensor.transpose(
+                        y_banks[n, pair][:, PAIR * u + P * ii : PAIR * u + P * (ii + 1)], words[:, u, first + step * ii], ident[:]
+                    )
 
         def y_out(n, pair, copy=on_scalar):
             chunk = chunk_of(pair)
             if (chunk, n) not in y_grouped:
-                y_grouped[chunk, n] = work.tile([P, SLOTS * USERS[chunk]], BF16, name="y_grouped", tag=("y_grouped", "grouped")[chunk], bufs=3, align_bytes=64)
+                y_grouped[chunk, n] = work.tile([P, SLOTS * USERS[chunk]], BF16, name="y_grouped", tag=("y_grouped", "grouped")[chunk], bufs=GROUPS, align_bytes=64)
             first_word = 2 * (PAIR * pair - FIRST_USER[chunk])
             copy(
                 out=y_grouped[chunk, n][:].bitcast(F32)[:, first_word : first_word + 2 * PAIR].rearrange("p (m u) -> p m u", u=2),
@@ -428,9 +450,10 @@ def tile_click_value_planes_b4_kernel(
         x_widen(0, 8, 12, VECTOR)
         x_widen(1, 8, 12, SCALAR)
         x_widen(1, 0, 4, VECTOR)
-        x_widen(2, 8, 12, SCALAR)
+        w_scales_out()
         x_widen(1, 4, 8, VECTOR)
         x_turn(0, (0,))
+        x_widen(2, 8, 12, SCALAR)
         x_widen(2, 0, 4, VECTOR)
         x_turn(0, (1,))
         x_widen(3, 0, 4, SCALAR)
@@ -458,8 +481,8 @@ def tile_click_value_planes_b4_kernel(
         x_widen(5, 8, 12, SCALAR)
         w_quant(1, 0)
         x_turn(2, (1,))
-        w_widen(0, 1)
         x_quant(NARROW, 0)
+        w_widen(0, 1)
         x_turn(2, (2,))
         w_group(2, 0)
         hidden_pass(NARROW, 0, 0, 0)
@@ -469,8 +492,8 @@ def tile_click_value_planes_b4_kernel(
         x_quant(NARROW, 1)
         x_quant(NARROW, 2)
         hidden_pass(NARROW, 0, 0, 1)
-        x_out(1, (1,), on_scalar)
         hidden_pass(NARROW, 0, 2, 1)
+        x_out(1, (1,), on_scalar)
         w_quant(2, 0)
         x_out(2, (1,), on_scalar)
         w_group(0, 1)
@@ -484,15 +507,15 @@ def tile_click_value_planes_b4_kernel(
         x_quant(WIDE, 0)
         for again in range(K_PASSES):
             hidden_pass(NARROW, 0, 3, again)
-        w_widen(1, 1)
         turn_bias()
+        w_widen(1, 1)
         w_quant(0, 1)
         hidden_pass(WIDE, 0, 0, 0)
         hidden_pass(WIDE, 0, 1, 0)
         hidden_pass(WIDE, 0, 2, 0)
         x_quant(WIDE, 1)
-        bias_out()
         hidden_pass(WIDE, 0, 3, 0)
+        bias_out()
         widen_gain()
         w_widen(2, 1)
         x_quant(WIDE, 2)
@@ -504,215 +527,211 @@ def tile_click_value_planes_b4_kernel(
         h_relu(NARROW, 0, (0, 1), SCALAR)
         hidden_pass(WIDE, 0, 0, 2)
         hidden_pass(WIDE, 0, 1, 2)
-        h_relu(NARROW, 0, (2, 3), SCALAR)
         hidden_pass(WIDE, 0, 2, 2)
+        h_relu(NARROW, 0, (2, 3), SCALAR)
         hidden_pass(WIDE, 0, 3, 2)
         w_group(2, 1)
         hidden_pass(NARROW, 1, 0, 0)
         hidden_pass(NARROW, 1, 2, 0)
-        h_relu(WIDE, 0, (0,), SCALAR)
         hidden_pass(WIDE, 1, 0, 0)
+        h_relu(WIDE, 0, (0,), SCALAR)
         hidden_pass(WIDE, 1, 1, 0)
         h_relu(WIDE, 0, (1,), SCALAR)
         w_quant(1, 1)
         h_relu(WIDE, 0, (2,), SCALAR)
         w_quant(2, 1)
         hidden_pass(NARROW, 1, 0, 1)
-        h_relu(WIDE, 0, (3,), SCALAR)
         hidden_pass(NARROW, 1, 2, 1)
+        h_relu(WIDE, 0, (3,), SCALAR)
         hidden_pass(WIDE, 1, 0, 1)
+        hidden_pass(WIDE, 1, 1, 1)
         h_group(NARROW, 0, on_vector)
         hidden_pass(NARROW, 1, 0, 2)
+        h_quant(NARROW, 0)
         for again in range(K_PASSES):
             hidden_pass(NARROW, 1, 1, again)
-        h_quant(NARROW, 0)
-        hidden_pass(NARROW, 1, 2, 2)
         h_group(WIDE, 0, on_vector, slice(0, PAIR))
+        hidden_pass(NARROW, 1, 2, 2)
         h_relu(NARROW, 1, (0, 1), SCALAR)
         for again in range(K_PASSES):
             hidden_pass(NARROW, 1, 3, again)
         hidden_pass(WIDE, 1, 0, 2)
-        hidden_pass(WIDE, 1, 1, 1)
-        h_relu(NARROW, 1, (2, 3), VECTOR)
-        h_relu(WIDE, 1, (0,), SCALAR)
         hidden_pass(WIDE, 1, 1, 2)
-        h_group(WIDE, 0, on_vector, slice(PAIR, 2 * PAIR))
+        h_relu(NARROW, 1, (2, 3), VECTOR)
         hidden_pass(WIDE, 1, 2, 0)
+        h_relu(WIDE, 1, (0,), SCALAR)
+        h_group(WIDE, 0, on_vector, slice(PAIR, 2 * PAIR))
+        hidden_pass(WIDE, 1, 2, 1)
         h_relu(WIDE, 1, (1,), SCALAR)
         h_group(NARROW, 1, on_vector)
-        hidden_pass(WIDE, 1, 2, 1)
-        h_quant(WIDE, 0)
         hidden_pass(WIDE, 1, 2, 2)
         hidden_pass(WIDE, 1, 3, 0)
-        h_quant(NARROW, 1)
+        h_quant(WIDE, 0)
         h_relu(WIDE, 1, (2,), SCALAR)
         hidden_pass(WIDE, 1, 3, 1)
+        h_quant(NARROW, 1)
         hidden_pass(WIDE, 1, 3, 2)
         narrow_logits(0, 0, (0,))
         narrow_logits(0, 1, (0,))
         h_relu(WIDE, 1, (3,), SCALAR)
         narrow_logits(1, 0, (0,))
         narrow_logits(1, 1, (0,))
-        h_group(WIDE, 1, on_vector, slice(0, 3 * P))
-        h_group(WIDE, 1, on_scalar, slice(3 * P, 4 * P))
+        h_group(WIDE, 1, on_vector, slice(0, PAIR))
+        h_group(WIDE, 1, on_scalar, slice(PAIR, 2 * PAIR))
         narrow_logits(0, 0, (1,))
         narrow_logits(0, 1, (1,))
         narrow_logits(1, 0, (1,))
-        narrow_logits(1, 1, (1,))
         narrow_bias(0, 0)
+        narrow_logits(1, 1, (1,))
         narrow_logits(2, 0)
         h_quant(WIDE, 1)
         narrow_sigmoid(0, 0)
-        narrow_logits(2, 1)
         narrow_bias(0, 1)
         wide_logits(0)
         narrow_bias(1, 0)
         wide_logits(1)
-        narrow_sigmoid(0, 1)
-        wide_logits(2)
-        narrow_bias(1, 1)
         wide_sigmoid(0)
-        wide_logits(3)
-        narrow_value(0, 0)
-        wide_sigmoid(1)
+        narrow_logits(2, 1)
+        narrow_bias(1, 1)
+        narrow_sigmoid(0, 1)
         narrow_logits(3, 0)
-        narrow_value(0, 1)
-        wide_sigmoid(2)
+        narrow_value(0, 0)
+        narrow_sigmoid(1, 0)
         narrow_logits(3, 1)
-        narrow_bias(2, 0)
-        y_round(0, 0, on_gpsimd)
+        narrow_value(0, 1)
+        wide_logits(2)
+        narrow_sigmoid(1, 1)
+        narrow_value(1, 0)
         y_store(0, 0)
+        wide_logits(3)
+        wide_sigmoid(1)
+        narrow_value(1, 1)
+        wide_logits(4)
+        wide_sigmoid(2)
+        narrow_bias(2, 0)
+        y_round((NARROW, 0), on_gpsimd)
+        y_store(1, 0)
+        wide_logits(5)
         wide_sigmoid(3)
         narrow_bias(2, 1)
-        narrow_sigmoid(1, 0)
-        wide_turn(0, 0)
-        wide_turn(0, 1)
-        narrow_sigmoid(1, 1)
-        wide_turn(0, 2)
-        wide_value(0, 0)
-        wide_turn(0, 3)
-        narrow_sigmoid(2, 0)
-        wide_value(0, 1)
-        wide_logits(4)
-        narrow_sigmoid(2, 1)
-        wide_logits(5)
-        wide_value(0, 2)
-        y_round(0, 1, on_gpsimd)
-        y_store(0, 1)
-        wide_sigmoid(4)
         wide_logits(6)
-        wide_value(0, 3)
-        wide_logits(7)
-        wide_sigmoid(5)
+        wide_sigmoid(4)
         narrow_bias(3, 0)
-        y_store(0, 2)
-        y_round(0, 2, on_gpsimd)
-        wide_logits(8)
-        wide_sigmoid(6)
+        wide_turn(0, 0)
+        wide_logits(7)
+        narrow_sigmoid(2, 0)
         narrow_bias(3, 1)
+        wide_logits(8)
+        narrow_sigmoid(2, 1)
+        wide_value(0, 0)
         wide_logits(9)
-        wide_sigmoid(7)
-        narrow_value(1, 0)
-        narrow_value(1, 1)
-        narrow_sigmoid(3, 0)
-        wide_turn(1, 0)
-        wide_turn(1, 1)
-        narrow_sigmoid(3, 1)
-        y_round(1, 0, on_gpsimd)
-        y_store(1, 0)
-        wide_turn(1, 2)
-        wide_value(1, 0)
-        wide_turn(1, 3)
-        wide_sigmoid(8)
-        wide_value(1, 1)
-        y_turn(0, 0)
-        wide_logits(10)
-        wide_sigmoid(9)
-        wide_value(1, 2)
-        y_round(1, 1, on_gpsimd)
-        y_store(1, 1)
-        wide_logits(11)
-        wide_value(1, 3)
-        wide_sigmoid(10)
-        wide_logits(12)
-        y_out(0, 0, on_vector)
-        wide_sigmoid(11)
-        y_store(1, 2)
-        wide_logits(13)
+        wide_sigmoid(5)
         narrow_value(2, 0)
-        y_round(1, 2, on_scalar)
-        wide_turn(2, 0)
-        wide_turn(2, 1)
+        wide_logits(10)
+        narrow_sigmoid(3, 0)
         narrow_value(2, 1)
-        wide_turn(2, 2)
-        wide_turn(2, 3)
-        wide_value(2, 0)
-        wide_sigmoid(12)
-        y_round(2, 0, on_gpsimd)
+        wide_logits(11)
+        narrow_sigmoid(3, 1)
+        narrow_value(3, 0)
         y_store(2, 0)
-        y_turn(0, 1)
-        wide_logits(14)
-        wide_value(2, 1)
+        wide_turn(0, 1)
+        wide_turn(0, 2)
+        wide_sigmoid(6)
+        narrow_value(3, 1)
+        wide_sigmoid(7)
+        wide_value(0, 1)
+        wide_turn(0, 3)
+        y_round((NARROW, 1), on_gpsimd)
+        y_store(3, 0)
+        wide_sigmoid(8)
+        wide_value(0, 2)
+        y_turn(0, 0)
+        y_store(0, 1)
+        wide_turn(1, 0)
+        wide_value(0, 3)
+        wide_sigmoid(9)
+        wide_turn(1, 1)
+        wide_logits(12)
+        wide_value(1, 0)
+        wide_sigmoid(10)
+        y_store(0, 2)
+        wide_logits(13)
+        wide_value(1, 1)
+        wide_sigmoid(11)
+        y_round((WIDE, 0), on_gpsimd)
+        wide_turn(1, 2)
+        wide_turn(1, 3)
+        y_store(1, 1)
+        wide_sigmoid(12)
+        wide_turn(2, 0)
+        wide_value(1, 2)
+        wide_turn(2, 1)
         wide_sigmoid(13)
+        wide_value(1, 3)
+        wide_logits(14)
+        y_out(0, 0, on_scalar)
         wide_logits(15)
+        wide_value(2, 0)
+        y_store(1, 2)
+        wide_sigmoid(14)
+        wide_turn(2, 2)
+        wide_value(2, 1)
+        y_round((WIDE, 1), on_gpsimd)
+        wide_turn(2, 3)
+        wide_sigmoid(15)
+        y_turn(1, 0)
         wide_value(2, 2)
         y_store(2, 1)
-        y_round(2, 1, on_gpsimd)
-        wide_sigmoid(14)
-        y_turn(0, 2)
-        wide_value(2, 3)
-        y_turn(1, 0)
-        wide_sigmoid(15)
-        y_turn(1, 1)
-        y_out(0, 1, on_vector)
-        y_store(2, 2)
-        y_round(2, 2, on_scalar)
+        y_turn(0, 1)
         wide_turn(3, 0)
-        narrow_value(3, 0)
-        wide_turn(3, 1)
-        wide_turn(3, 2)
-        narrow_value(3, 1)
-        wide_turn(3, 3)
+        wide_value(2, 3)
         y_out(1, 0, on_scalar)
-        y_turn(1, 2)
+        y_turn(0, 2)
+        y_out(0, 1, on_scalar)
+        wide_turn(3, 1)
         wide_value(3, 0)
-        y_round(3, 0, on_gpsimd)
-        y_store(3, 0)
-        y_out(1, 1, on_scalar)
-        y_turn(2, 0)
+        y_store(2, 2)
+        wide_turn(3, 2)
+        y_out(0, 2, on_scalar)
+        wide_turn(3, 3)
         wide_value(3, 1)
-        y_turn(2, 1)
-        y_out(1, 2, on_scalar)
-        y_turn(2, 2)
+        y_round((WIDE, 2), on_gpsimd, 0, 2)
+        y_turn(1, 1)
+        y_round((WIDE, 2), on_scalar, 2, 4)
         wide_value(3, 2)
         y_store(3, 1)
-        y_round(3, 1, on_gpsimd)
-        y_out(2, 0, on_scalar)
-        y_turn(3, 0)
+        y_turn(1, 2)
+        y_turn(2, 0)
         wide_value(3, 3)
-        y_out(0, 2, on_vector)
-        y_round(3, 2, on_scalar)
+        y_out(1, 1, on_scalar)
+        y_out(1, 2, on_vector)
         y_store(3, 2)
-        y_turn(3, 1)
+        y_turn(2, 1)
+        y_round((WIDE, 3), on_scalar, 0, 2)
+        y_turn(2, 2)
         y_quant(NARROW, 0)
+        y_turn(3, 0)
+        y_round((WIDE, 3), on_vector, 2, 4)
         y_quant(WIDE, 0)
-        y_out(2, 1, on_scalar)
+        y_out(2, 0, on_scalar)
+        y_turn(3, 1)
         y_turn(3, 2)
         y_quant(NARROW, 1)
+        y_out(2, 1, on_scalar)
         codes_store(0)
-        y_out(2, 2, on_scalar)
         y_quant(WIDE, 1)
-        y_out(3, 0, on_scalar)
+        y_out(2, 2, on_scalar)
         y_quant(NARROW, 2)
         codes_store(1)
+        y_out(3, 0, on_scalar)
         y_quant(WIDE, 2)
         y_out(3, 1, on_scalar)
         y_quant(NARROW, 3)
         codes_store(2)
         y_out(3, 2, on_scalar)
         y_quant(WIDE, 3, 0)
-        y_quant(WIDE, 3, 1)
         codes_store(3, slice(0, 2 * PAIR))
+        y_quant(WIDE, 3, 1)
         codes_store(3, slice(2 * PAIR, T))
         for q in range(P // QUAD):
             queue = nc.scalar if q % 2 else nc.sync

@@ -441,284 +441,284 @@ def tile_click_value_planes_b4_kernel(
                 out=out_1[n][:, users, :].rearrange("p m t -> p (m t)").bitcast(I32), in_=y_codes[n][:, users].bitcast(I32)
             )
 
-        x_widen(0, 0, 4, VECTOR)
+        x_widen(0, 4, 8, VECTOR)
+        x_widen(0, 0, 4, SCALAR)
+        x_widen(0, 8, 12, VECTOR)
         w_widen(0, 0, on_scalar, slice(0, 2 * PASS))
         make_quad_of()
-        x_widen(0, 4, 8, VECTOR)
-        w_widen(0, 0, on_scalar, slice(2 * PASS, 4 * PASS))
-        spread_w_scales()
-        x_widen(0, 8, 12, VECTOR)
-        x_widen(1, 8, 12, SCALAR)
         x_widen(1, 0, 4, VECTOR)
-        w_scales_out()
+        spread_w_scales()
+        w_widen(0, 0, on_scalar, slice(2 * PASS, 4 * PASS))
         x_widen(1, 4, 8, VECTOR)
         x_turn(0, (0,))
-        x_widen(2, 8, 12, SCALAR)
+        x_widen(1, 8, 12, SCALAR)
         x_widen(2, 0, 4, VECTOR)
         x_turn(0, (1,))
+        w_scales_out()
         x_widen(3, 0, 4, SCALAR)
-        x_widen(2, 4, 8, VECTOR)
-        x_turn(0, (2,))
         w_group(0, 0)
-        x_widen(3, 4, 8, SCALAR)
+        x_widen(2, 8, 12, SCALAR)
         x_turn(1, (0,))
-        x_widen(3, 8, 12, SCALAR)
-        x_turn(1, (1,))
-        x_widen(4, 0, 4, VECTOR)
         w_widen(1, 0)
-        x_turn(1, (2,))
-        x_widen(4, 4, 8, VECTOR)
-        x_widen(4, 8, 12, VECTOR)
-        x_out(0, (0,), on_scalar)
-        w_quant(0, 0)
+        x_widen(2, 4, 8, VECTOR)
+        x_widen(3, 4, 8, VECTOR)
+        x_widen(4, 0, 4, VECTOR)
         x_out(0, (1,), on_scalar)
-        w_group(1, 0)
-        x_out(0, (2,), on_scalar)
-        w_widen(2, 0)
+        x_widen(4, 4, 8, VECTOR)
+        x_out(0, (0,), on_scalar)
         x_widen(5, 0, 4, VECTOR)
         x_widen(5, 4, 8, VECTOR)
+        w_widen(2, 0)
         x_turn(2, (0,))
-        x_widen(5, 8, 12, SCALAR)
-        w_quant(1, 0)
-        x_turn(2, (1,))
+        w_quant(0, 0)
+        x_turn(1, (1,))
         x_quant(NARROW, 0)
-        w_widen(0, 1)
-        x_turn(2, (2,))
-        w_group(2, 0)
+        x_turn(2, (1,))
+        x_out(2, (0,), on_scalar)
+        w_group(1, 0)
+        x_turn(0, (2,))
+        x_out(1, (0,), on_scalar)
         hidden_pass(NARROW, 0, 0, 0)
         hidden_pass(NARROW, 0, 2, 0)
-        x_out(1, (0,), on_scalar)
-        x_out(2, (0,), on_scalar)
+        x_widen(3, 8, 12, SCALAR)
+        x_widen(4, 8, 12, VECTOR)
+        x_widen(5, 8, 12, SCALAR)
+        x_turn(1, (2,))
         x_quant(NARROW, 1)
-        x_quant(NARROW, 2)
-        hidden_pass(NARROW, 0, 0, 1)
-        hidden_pass(NARROW, 0, 2, 1)
-        x_out(1, (1,), on_scalar)
-        w_quant(2, 0)
+        w_group(2, 0)
         x_out(2, (1,), on_scalar)
-        w_group(0, 1)
-        hidden_pass(NARROW, 0, 0, 2)
-        x_out(1, (2,), on_scalar)
-        for again in range(K_PASSES):
-            hidden_pass(NARROW, 0, 1, again)
-        hidden_pass(NARROW, 0, 2, 2)
-        widen_bias()
-        x_out(2, (2,), on_scalar)
+        x_turn(2, (2,))
+        x_out(1, (1,), on_scalar)
+        w_widen(0, 1)
         x_quant(WIDE, 0)
-        for again in range(K_PASSES):
-            hidden_pass(NARROW, 0, 3, again)
-        turn_bias()
-        w_widen(1, 1)
-        w_quant(0, 1)
+        w_quant(1, 0)
         hidden_pass(WIDE, 0, 0, 0)
         hidden_pass(WIDE, 0, 1, 0)
-        hidden_pass(WIDE, 0, 2, 0)
+        x_out(0, (2,), on_scalar)
         x_quant(WIDE, 1)
+        hidden_pass(WIDE, 0, 2, 0)
+        widen_bias()
         hidden_pass(WIDE, 0, 3, 0)
-        bias_out()
-        widen_gain()
-        w_widen(2, 1)
-        x_quant(WIDE, 2)
+        x_out(2, (2,), on_scalar)
+        w_quant(2, 0)
+        x_out(1, (2,), on_scalar)
+        x_quant(NARROW, 2)
+        turn_bias()
+        hidden_pass(NARROW, 0, 0, 1)
+        hidden_pass(NARROW, 0, 2, 1)
+        w_group(0, 1)
         hidden_pass(WIDE, 0, 0, 1)
+        w_widen(1, 1)
         hidden_pass(WIDE, 0, 1, 1)
         hidden_pass(WIDE, 0, 2, 1)
-        w_group(1, 1)
         hidden_pass(WIDE, 0, 3, 1)
+        hidden_pass(NARROW, 0, 0, 2)
+        widen_gain()
+        x_quant(WIDE, 2)
+        w_widen(2, 1)
+        for again in range(K_PASSES):
+            hidden_pass(NARROW, 0, 1, again)
+        w_group(1, 1)
+        hidden_pass(NARROW, 0, 2, 2)
+        for again in range(K_PASSES):
+            hidden_pass(NARROW, 0, 3, again)
         h_relu(NARROW, 0, (0, 1), SCALAR)
         hidden_pass(WIDE, 0, 0, 2)
         hidden_pass(WIDE, 0, 1, 2)
-        hidden_pass(WIDE, 0, 2, 2)
         h_relu(NARROW, 0, (2, 3), SCALAR)
+        w_quant(0, 1)
+        hidden_pass(WIDE, 0, 2, 2)
         hidden_pass(WIDE, 0, 3, 2)
-        w_group(2, 1)
-        hidden_pass(NARROW, 1, 0, 0)
-        hidden_pass(NARROW, 1, 2, 0)
-        hidden_pass(WIDE, 1, 0, 0)
-        h_relu(WIDE, 0, (0,), SCALAR)
-        hidden_pass(WIDE, 1, 1, 0)
         h_relu(WIDE, 0, (1,), SCALAR)
         w_quant(1, 1)
-        h_relu(WIDE, 0, (2,), SCALAR)
-        w_quant(2, 1)
+        hidden_pass(NARROW, 1, 0, 0)
+        hidden_pass(NARROW, 1, 2, 0)
+        h_relu(WIDE, 0, (0,), SCALAR)
+        w_group(2, 1)
         hidden_pass(NARROW, 1, 0, 1)
         hidden_pass(NARROW, 1, 2, 1)
+        hidden_pass(WIDE, 1, 0, 0)
         h_relu(WIDE, 0, (3,), SCALAR)
         hidden_pass(WIDE, 1, 0, 1)
+        h_relu(WIDE, 0, (2,), SCALAR)
+        hidden_pass(WIDE, 1, 1, 0)
+        w_quant(2, 1)
+        bias_out()
         hidden_pass(WIDE, 1, 1, 1)
         h_group(NARROW, 0, on_vector)
+        hidden_pass(WIDE, 1, 2, 0)
+        h_group(WIDE, 0, on_vector, slice(0, PAIR))
+        hidden_pass(WIDE, 1, 2, 1)
+        hidden_pass(WIDE, 1, 3, 0)
         hidden_pass(NARROW, 1, 0, 2)
         h_quant(NARROW, 0)
+        h_group(WIDE, 0, on_vector, slice(PAIR, 2 * PAIR))
         for again in range(K_PASSES):
             hidden_pass(NARROW, 1, 1, again)
-        h_group(WIDE, 0, on_vector, slice(0, PAIR))
         hidden_pass(NARROW, 1, 2, 2)
         h_relu(NARROW, 1, (0, 1), SCALAR)
         for again in range(K_PASSES):
             hidden_pass(NARROW, 1, 3, again)
         hidden_pass(WIDE, 1, 0, 2)
         hidden_pass(WIDE, 1, 1, 2)
-        h_relu(NARROW, 1, (2, 3), VECTOR)
-        hidden_pass(WIDE, 1, 2, 0)
-        h_relu(WIDE, 1, (0,), SCALAR)
-        h_group(WIDE, 0, on_vector, slice(PAIR, 2 * PAIR))
-        hidden_pass(WIDE, 1, 2, 1)
-        h_relu(WIDE, 1, (1,), SCALAR)
-        h_group(NARROW, 1, on_vector)
+        h_relu(NARROW, 1, (2, 3), SCALAR)
         hidden_pass(WIDE, 1, 2, 2)
-        hidden_pass(WIDE, 1, 3, 0)
-        h_quant(WIDE, 0)
-        h_relu(WIDE, 1, (2,), SCALAR)
         hidden_pass(WIDE, 1, 3, 1)
-        h_quant(NARROW, 1)
+        h_relu(WIDE, 1, (0,), SCALAR)
+        h_group(NARROW, 1, on_vector)
         hidden_pass(WIDE, 1, 3, 2)
+        h_relu(WIDE, 1, (2,), SCALAR)
         narrow_logits(0, 0, (0,))
+        h_quant(NARROW, 1)
         narrow_logits(0, 1, (0,))
-        h_relu(WIDE, 1, (3,), SCALAR)
+        h_quant(WIDE, 0)
         narrow_logits(1, 0, (0,))
-        narrow_logits(1, 1, (0,))
-        h_group(WIDE, 1, on_vector, slice(0, PAIR))
-        h_group(WIDE, 1, on_scalar, slice(PAIR, 2 * PAIR))
+        h_relu(WIDE, 1, (1,), SCALAR)
         narrow_logits(0, 0, (1,))
         narrow_logits(0, 1, (1,))
+        h_relu(WIDE, 1, (3,), SCALAR)
         narrow_logits(1, 0, (1,))
         narrow_bias(0, 0)
+        narrow_logits(1, 1, (0,))
+        h_group(WIDE, 1, on_scalar, slice(PAIR, 2 * PAIR))
+        narrow_bias(0, 1)
         narrow_logits(1, 1, (1,))
         narrow_logits(2, 0)
-        h_quant(WIDE, 1)
+        h_group(WIDE, 1, on_vector, slice(0, PAIR))
         narrow_sigmoid(0, 0)
-        narrow_bias(0, 1)
-        wide_logits(0)
-        narrow_bias(1, 0)
-        wide_logits(1)
-        wide_sigmoid(0)
         narrow_logits(2, 1)
-        narrow_bias(1, 1)
-        narrow_sigmoid(0, 1)
+        narrow_bias(1, 0)
         narrow_logits(3, 0)
-        narrow_value(0, 0)
-        narrow_sigmoid(1, 0)
+        narrow_sigmoid(0, 1)
+        h_quant(WIDE, 1)
         narrow_logits(3, 1)
+        narrow_sigmoid(1, 0)
+        narrow_bias(1, 1)
+        wide_logits(0)
         narrow_value(0, 1)
-        wide_logits(2)
         narrow_sigmoid(1, 1)
-        narrow_value(1, 0)
-        y_store(0, 0)
-        wide_logits(3)
-        wide_sigmoid(1)
+        wide_logits(1)
+        narrow_value(0, 0)
+        wide_sigmoid(0)
+        wide_logits(2)
         narrow_value(1, 1)
-        wide_logits(4)
+        y_store(0, 0)
+        wide_sigmoid(1)
+        wide_logits(3)
+        narrow_value(1, 0)
         wide_sigmoid(2)
-        narrow_bias(2, 0)
+        wide_logits(4)
+        narrow_bias(2, 1)
         y_round((NARROW, 0), on_gpsimd)
         y_store(1, 0)
         wide_logits(5)
         wide_sigmoid(3)
-        narrow_bias(2, 1)
+        narrow_bias(2, 0)
         wide_logits(6)
-        wide_sigmoid(4)
-        narrow_bias(3, 0)
-        wide_turn(0, 0)
-        wide_logits(7)
-        narrow_sigmoid(2, 0)
-        narrow_bias(3, 1)
-        wide_logits(8)
         narrow_sigmoid(2, 1)
+        narrow_bias(3, 1)
+        wide_turn(0, 0)
+        narrow_sigmoid(2, 0)
+        wide_turn(0, 1)
+        narrow_bias(3, 0)
+        wide_turn(0, 2)
+        wide_sigmoid(4)
+        wide_turn(0, 3)
         wide_value(0, 0)
+        narrow_sigmoid(3, 1)
+        wide_logits(7)
+        narrow_value(2, 1)
+        wide_logits(8)
+        narrow_sigmoid(3, 0)
+        narrow_value(2, 0)
         wide_logits(9)
         wide_sigmoid(5)
-        narrow_value(2, 0)
-        wide_logits(10)
-        narrow_sigmoid(3, 0)
-        narrow_value(2, 1)
-        wide_logits(11)
-        narrow_sigmoid(3, 1)
-        narrow_value(3, 0)
-        y_store(2, 0)
-        wide_turn(0, 1)
-        wide_turn(0, 2)
-        wide_sigmoid(6)
         narrow_value(3, 1)
+        y_store(2, 0)
+        wide_sigmoid(6)
+        wide_logits(10)
+        narrow_value(3, 0)
         wide_sigmoid(7)
+        wide_logits(11)
         wide_value(0, 1)
-        wide_turn(0, 3)
         y_round((NARROW, 1), on_gpsimd)
         y_store(3, 0)
         wide_sigmoid(8)
-        wide_value(0, 2)
-        y_turn(0, 0)
-        y_store(0, 1)
         wide_turn(1, 0)
-        wide_value(0, 3)
-        wide_sigmoid(9)
+        wide_value(0, 2)
+        y_store(0, 1)
         wide_turn(1, 1)
-        wide_logits(12)
-        wide_value(1, 0)
+        wide_sigmoid(9)
+        wide_turn(1, 2)
+        wide_value(0, 3)
+        wide_turn(1, 3)
         wide_sigmoid(10)
+        wide_value(1, 0)
+        wide_logits(12)
         y_store(0, 2)
+        wide_sigmoid(11)
         wide_logits(13)
         wide_value(1, 1)
-        wide_sigmoid(11)
         y_round((WIDE, 0), on_gpsimd)
-        wide_turn(1, 2)
-        wide_turn(1, 3)
-        y_store(1, 1)
         wide_sigmoid(12)
-        wide_turn(2, 0)
+        wide_logits(14)
         wide_value(1, 2)
-        wide_turn(2, 1)
+        y_store(1, 1)
+        wide_turn(2, 0)
         wide_sigmoid(13)
         wide_value(1, 3)
-        wide_logits(14)
-        y_out(0, 0, on_scalar)
-        wide_logits(15)
-        wide_value(2, 0)
-        y_store(1, 2)
+        wide_turn(2, 1)
         wide_sigmoid(14)
+        wide_value(2, 0)
         wide_turn(2, 2)
+        y_store(1, 2)
+        wide_logits(15)
         wide_value(2, 1)
+        y_turn(0, 0)
         y_round((WIDE, 1), on_gpsimd)
-        wide_turn(2, 3)
-        wide_sigmoid(15)
-        y_turn(1, 0)
         wide_value(2, 2)
+        wide_sigmoid(15)
+        wide_turn(2, 3)
         y_store(2, 1)
-        y_turn(0, 1)
-        wide_turn(3, 0)
+        y_turn(1, 0)
+        y_out(0, 0, on_scalar)
         wide_value(2, 3)
-        y_out(1, 0, on_scalar)
-        y_turn(0, 2)
-        y_out(0, 1, on_scalar)
+        wide_turn(3, 0)
         wide_turn(3, 1)
-        wide_value(3, 0)
+        y_out(1, 0, on_scalar)
         y_store(2, 2)
+        wide_value(3, 0)
+        y_turn(0, 1)
         wide_turn(3, 2)
-        y_out(0, 2, on_scalar)
-        wide_turn(3, 3)
-        wide_value(3, 1)
-        y_round((WIDE, 2), on_gpsimd, 0, 2)
-        y_turn(1, 1)
         y_round((WIDE, 2), on_scalar, 2, 4)
+        wide_value(3, 1)
+        wide_turn(3, 3)
+        y_round((WIDE, 2), on_gpsimd, 0, 2)
+        y_turn(0, 2)
         wide_value(3, 2)
         y_store(3, 1)
-        y_turn(1, 2)
         y_turn(2, 0)
+        y_out(0, 1, on_scalar)
+        y_turn(1, 1)
         wide_value(3, 3)
-        y_out(1, 1, on_scalar)
-        y_out(1, 2, on_vector)
+        y_turn(1, 2)
+        y_out(0, 2, on_scalar)
+        y_out(2, 0, on_vector)
         y_store(3, 2)
         y_turn(2, 1)
         y_round((WIDE, 3), on_scalar, 0, 2)
         y_turn(2, 2)
-        y_quant(NARROW, 0)
-        y_turn(3, 0)
         y_round((WIDE, 3), on_vector, 2, 4)
+        y_turn(3, 0)
+        y_quant(NARROW, 0)
+        y_out(1, 1, on_scalar)
         y_quant(WIDE, 0)
-        y_out(2, 0, on_scalar)
         y_turn(3, 1)
         y_turn(3, 2)
+        y_out(1, 2, on_scalar)
         y_quant(NARROW, 1)
-        y_out(2, 1, on_scalar)
         codes_store(0)
+        y_out(2, 1, on_scalar)
         y_quant(WIDE, 1)
         y_out(2, 2, on_scalar)
         y_quant(NARROW, 2)

@@ -441,13 +441,13 @@ def tile_click_value_planes_b4_kernel(
                 out=out_1[n][:, users, :].rearrange("p m t -> p (m t)").bitcast(I32), in_=y_codes[n][:, users].bitcast(I32)
             )
 
-        x_widen(0, 4, 8, VECTOR)
+        make_quad_of()
         x_widen(0, 0, 4, SCALAR)
+        x_widen(0, 4, 8, VECTOR)
+        spread_w_scales()
         x_widen(0, 8, 12, VECTOR)
         w_widen(0, 0, on_scalar, slice(0, 2 * PASS))
-        make_quad_of()
         x_widen(1, 0, 4, VECTOR)
-        spread_w_scales()
         w_widen(0, 0, on_scalar, slice(2 * PASS, 4 * PASS))
         x_widen(1, 4, 8, VECTOR)
         x_turn(0, (0,))
@@ -459,22 +459,22 @@ def tile_click_value_planes_b4_kernel(
         w_group(0, 0)
         x_widen(2, 8, 12, SCALAR)
         x_turn(1, (0,))
-        w_widen(1, 0)
         x_widen(2, 4, 8, VECTOR)
+        w_widen(1, 0)
         x_widen(3, 4, 8, VECTOR)
         x_widen(4, 0, 4, VECTOR)
         x_out(0, (1,), on_scalar)
         x_widen(4, 4, 8, VECTOR)
         x_out(0, (0,), on_scalar)
         x_widen(5, 0, 4, VECTOR)
-        x_widen(5, 4, 8, VECTOR)
         w_widen(2, 0)
+        x_widen(5, 4, 8, VECTOR)
         x_turn(2, (0,))
         w_quant(0, 0)
         x_turn(1, (1,))
-        x_quant(NARROW, 0)
-        x_turn(2, (1,))
         x_out(2, (0,), on_scalar)
+        x_turn(2, (1,))
+        x_quant(NARROW, 0)
         w_group(1, 0)
         x_turn(0, (2,))
         x_out(1, (0,), on_scalar)
@@ -495,14 +495,14 @@ def tile_click_value_planes_b4_kernel(
         hidden_pass(WIDE, 0, 0, 0)
         hidden_pass(WIDE, 0, 1, 0)
         x_out(0, (2,), on_scalar)
-        x_quant(WIDE, 1)
         hidden_pass(WIDE, 0, 2, 0)
+        x_quant(WIDE, 1)
         widen_bias()
         hidden_pass(WIDE, 0, 3, 0)
-        x_out(2, (2,), on_scalar)
         w_quant(2, 0)
-        x_out(1, (2,), on_scalar)
+        x_out(2, (2,), on_scalar)
         x_quant(NARROW, 2)
+        x_out(1, (2,), on_scalar)
         turn_bias()
         hidden_pass(NARROW, 0, 0, 1)
         hidden_pass(NARROW, 0, 2, 1)
@@ -518,211 +518,211 @@ def tile_click_value_planes_b4_kernel(
         w_widen(2, 1)
         for again in range(K_PASSES):
             hidden_pass(NARROW, 0, 1, again)
-        w_group(1, 1)
         hidden_pass(NARROW, 0, 2, 2)
+        w_group(1, 1)
         for again in range(K_PASSES):
             hidden_pass(NARROW, 0, 3, again)
         h_relu(NARROW, 0, (0, 1), SCALAR)
         hidden_pass(WIDE, 0, 0, 2)
         hidden_pass(WIDE, 0, 1, 2)
         h_relu(NARROW, 0, (2, 3), SCALAR)
-        w_quant(0, 1)
         hidden_pass(WIDE, 0, 2, 2)
+        w_quant(0, 1)
         hidden_pass(WIDE, 0, 3, 2)
-        h_relu(WIDE, 0, (1,), SCALAR)
         w_quant(1, 1)
+        h_relu(WIDE, 0, (1,), SCALAR)
         hidden_pass(NARROW, 1, 0, 0)
         hidden_pass(NARROW, 1, 2, 0)
-        h_relu(WIDE, 0, (0,), SCALAR)
         w_group(2, 1)
+        h_relu(WIDE, 0, (0,), SCALAR)
         hidden_pass(NARROW, 1, 0, 1)
         hidden_pass(NARROW, 1, 2, 1)
         hidden_pass(WIDE, 1, 0, 0)
         h_relu(WIDE, 0, (3,), SCALAR)
         hidden_pass(WIDE, 1, 0, 1)
-        h_relu(WIDE, 0, (2,), SCALAR)
         hidden_pass(WIDE, 1, 1, 0)
+        h_relu(WIDE, 0, (2,), SCALAR)
         w_quant(2, 1)
-        bias_out()
         hidden_pass(WIDE, 1, 1, 1)
-        h_group(NARROW, 0, on_vector)
+        bias_out()
         hidden_pass(WIDE, 1, 2, 0)
-        h_group(WIDE, 0, on_vector, slice(0, PAIR))
+        h_group(WIDE, 0, on_scalar, slice(0, PAIR))
+        h_group(NARROW, 0, on_vector)
         hidden_pass(WIDE, 1, 2, 1)
-        hidden_pass(WIDE, 1, 3, 0)
+        h_group(WIDE, 0, on_vector, slice(PAIR, 2 * PAIR))
         hidden_pass(NARROW, 1, 0, 2)
         h_quant(NARROW, 0)
-        h_group(WIDE, 0, on_vector, slice(PAIR, 2 * PAIR))
         for again in range(K_PASSES):
             hidden_pass(NARROW, 1, 1, again)
         hidden_pass(NARROW, 1, 2, 2)
-        h_relu(NARROW, 1, (0, 1), SCALAR)
+        h_relu(NARROW, 1, (0, 1), VECTOR)
         for again in range(K_PASSES):
             hidden_pass(NARROW, 1, 3, again)
         hidden_pass(WIDE, 1, 0, 2)
         hidden_pass(WIDE, 1, 1, 2)
         h_relu(NARROW, 1, (2, 3), SCALAR)
         hidden_pass(WIDE, 1, 2, 2)
-        hidden_pass(WIDE, 1, 3, 1)
+        hidden_pass(WIDE, 1, 3, 0)
         h_relu(WIDE, 1, (0,), SCALAR)
         h_group(NARROW, 1, on_vector)
-        hidden_pass(WIDE, 1, 3, 2)
+        hidden_pass(WIDE, 1, 3, 1)
         h_relu(WIDE, 1, (2,), SCALAR)
-        narrow_logits(0, 0, (0,))
         h_quant(NARROW, 1)
-        narrow_logits(0, 1, (0,))
+        hidden_pass(WIDE, 1, 3, 2)
         h_quant(WIDE, 0)
-        narrow_logits(1, 0, (0,))
+        narrow_logits(0, 0, (0,))
         h_relu(WIDE, 1, (1,), SCALAR)
+        narrow_logits(0, 1, (0,))
+        narrow_logits(1, 0, (0,))
+        h_relu(WIDE, 1, (3,), SCALAR)
         narrow_logits(0, 0, (1,))
         narrow_logits(0, 1, (1,))
-        h_relu(WIDE, 1, (3,), SCALAR)
         narrow_logits(1, 0, (1,))
         narrow_bias(0, 0)
-        narrow_logits(1, 1, (0,))
         h_group(WIDE, 1, on_scalar, slice(PAIR, 2 * PAIR))
+        narrow_logits(1, 1, (0,))
         narrow_bias(0, 1)
         narrow_logits(1, 1, (1,))
         narrow_logits(2, 0)
-        h_group(WIDE, 1, on_vector, slice(0, PAIR))
         narrow_sigmoid(0, 0)
+        h_group(WIDE, 1, on_vector, slice(0, PAIR))
         narrow_logits(2, 1)
+        narrow_sigmoid(0, 1)
         narrow_bias(1, 0)
         narrow_logits(3, 0)
-        narrow_sigmoid(0, 1)
         h_quant(WIDE, 1)
-        narrow_logits(3, 1)
         narrow_sigmoid(1, 0)
+        narrow_logits(3, 1)
         narrow_bias(1, 1)
         wide_logits(0)
         narrow_value(0, 1)
         narrow_sigmoid(1, 1)
         wide_logits(1)
         narrow_value(0, 0)
-        wide_sigmoid(0)
         wide_logits(2)
+        wide_sigmoid(0)
         narrow_value(1, 1)
+        wide_logits(3)
         y_store(0, 0)
         wide_sigmoid(1)
-        wide_logits(3)
+        wide_logits(4)
         narrow_value(1, 0)
         wide_sigmoid(2)
-        wide_logits(4)
+        wide_logits(5)
         narrow_bias(2, 1)
         y_round((NARROW, 0), on_gpsimd)
         y_store(1, 0)
-        wide_logits(5)
         wide_sigmoid(3)
-        narrow_bias(2, 0)
         wide_logits(6)
-        narrow_sigmoid(2, 1)
-        narrow_bias(3, 1)
-        wide_turn(0, 0)
-        narrow_sigmoid(2, 0)
-        wide_turn(0, 1)
-        narrow_bias(3, 0)
-        wide_turn(0, 2)
+        narrow_bias(2, 0)
         wide_sigmoid(4)
-        wide_turn(0, 3)
-        wide_value(0, 0)
-        narrow_sigmoid(3, 1)
-        wide_logits(7)
-        narrow_value(2, 1)
-        wide_logits(8)
-        narrow_sigmoid(3, 0)
-        narrow_value(2, 0)
-        wide_logits(9)
+        wide_turn(0, 0)
+        narrow_bias(3, 1)
+        wide_turn(0, 1)
         wide_sigmoid(5)
-        narrow_value(3, 1)
-        y_store(2, 0)
+        wide_turn(0, 2)
+        narrow_bias(3, 0)
+        wide_turn(0, 3)
         wide_sigmoid(6)
-        wide_logits(10)
-        narrow_value(3, 0)
-        wide_sigmoid(7)
-        wide_logits(11)
+        wide_logits(7)
+        wide_value(0, 0)
+        narrow_sigmoid(2, 1)
+        wide_logits(8)
         wide_value(0, 1)
-        y_round((NARROW, 1), on_gpsimd)
-        y_store(3, 0)
-        wide_sigmoid(8)
-        wide_turn(1, 0)
+        narrow_sigmoid(2, 0)
+        wide_logits(9)
         wide_value(0, 2)
         y_store(0, 1)
-        wide_turn(1, 1)
-        wide_sigmoid(9)
-        wide_turn(1, 2)
+        wide_logits(10)
+        wide_sigmoid(7)
         wide_value(0, 3)
-        wide_turn(1, 3)
-        wide_sigmoid(10)
-        wide_value(1, 0)
-        wide_logits(12)
+        wide_logits(11)
+        narrow_sigmoid(3, 1)
+        narrow_value(2, 1)
         y_store(0, 2)
-        wide_sigmoid(11)
+        wide_logits(12)
+        narrow_sigmoid(3, 0)
+        narrow_value(2, 0)
         wide_logits(13)
-        wide_value(1, 1)
-        y_round((WIDE, 0), on_gpsimd)
-        wide_sigmoid(12)
+        wide_sigmoid(8)
+        narrow_value(3, 1)
+        y_store(2, 0)
         wide_logits(14)
+        wide_sigmoid(9)
+        y_round((WIDE, 0), on_vector)
+        wide_logits(15)
+        wide_sigmoid(10)
+        wide_turn(1, 0)
+        wide_turn(1, 1)
+        narrow_value(3, 0)
+        wide_sigmoid(11)
+        y_turn(0, 0)
+        wide_value(1, 0)
+        y_round((NARROW, 1), on_gpsimd)
+        y_store(3, 0)
+        wide_sigmoid(12)
+        wide_turn(1, 2)
+        wide_value(1, 1)
+        wide_turn(1, 3)
+        wide_sigmoid(13)
+        y_turn(1, 0)
         wide_value(1, 2)
         y_store(1, 1)
         wide_turn(2, 0)
-        wide_sigmoid(13)
+        wide_sigmoid(14)
+        y_turn(0, 1)
         wide_value(1, 3)
         wide_turn(2, 1)
-        wide_sigmoid(14)
-        wide_value(2, 0)
-        wide_turn(2, 2)
-        y_store(1, 2)
-        wide_logits(15)
-        wide_value(2, 1)
-        y_turn(0, 0)
-        y_round((WIDE, 1), on_gpsimd)
-        wide_value(2, 2)
         wide_sigmoid(15)
-        wide_turn(2, 3)
-        y_store(2, 1)
-        y_turn(1, 0)
+        wide_turn(2, 2)
+        wide_value(2, 0)
+        y_store(1, 2)
         y_out(0, 0, on_scalar)
-        wide_value(2, 3)
-        wide_turn(3, 0)
-        wide_turn(3, 1)
-        y_out(1, 0, on_scalar)
-        y_store(2, 2)
-        wide_value(3, 0)
-        y_turn(0, 1)
-        wide_turn(3, 2)
-        y_round((WIDE, 2), on_scalar, 2, 4)
-        wide_value(3, 1)
-        wide_turn(3, 3)
-        y_round((WIDE, 2), on_gpsimd, 0, 2)
         y_turn(0, 2)
+        y_round((WIDE, 1), on_gpsimd)
+        wide_value(2, 1)
+        wide_turn(2, 3)
+        y_out(1, 0, on_scalar)
+        y_turn(2, 0)
+        wide_value(2, 2)
+        wide_turn(3, 0)
+        y_store(2, 1)
+        y_out(0, 1, on_scalar)
+        wide_turn(3, 1)
+        wide_value(2, 3)
+        wide_turn(3, 2)
+        y_out(0, 2, on_scalar)
+        wide_value(3, 0)
+        y_store(2, 2)
+        y_out(2, 0, on_scalar)
+        wide_value(3, 1)
+        y_round((WIDE, 2), on_gpsimd, 0, 2)
+        y_turn(1, 1)
+        y_round((WIDE, 2), on_scalar, 2, 4)
+        wide_turn(3, 3)
         wide_value(3, 2)
         y_store(3, 1)
-        y_turn(2, 0)
-        y_out(0, 1, on_scalar)
-        y_turn(1, 1)
-        wide_value(3, 3)
         y_turn(1, 2)
-        y_out(0, 2, on_scalar)
-        y_out(2, 0, on_vector)
-        y_store(3, 2)
+        wide_value(3, 3)
+        y_out(1, 1, on_scalar)
         y_turn(2, 1)
-        y_round((WIDE, 3), on_scalar, 0, 2)
+        y_quant(NARROW, 0)
+        y_store(3, 2)
         y_turn(2, 2)
+        y_out(1, 2, on_scalar)
         y_round((WIDE, 3), on_vector, 2, 4)
         y_turn(3, 0)
-        y_quant(NARROW, 0)
-        y_out(1, 1, on_scalar)
+        y_round((WIDE, 3), on_scalar, 0, 2)
         y_quant(WIDE, 0)
-        y_turn(3, 1)
-        y_turn(3, 2)
-        y_out(1, 2, on_scalar)
         y_quant(NARROW, 1)
         codes_store(0)
-        y_out(2, 1, on_scalar)
         y_quant(WIDE, 1)
-        y_out(2, 2, on_scalar)
+        y_out(2, 1, on_scalar)
+        y_turn(3, 1)
+        y_turn(3, 2)
         y_quant(NARROW, 2)
         codes_store(1)
+        y_out(2, 2, on_scalar)
         y_out(3, 0, on_scalar)
         y_quant(WIDE, 2)
         y_out(3, 1, on_scalar)

@@ -82,6 +82,7 @@ def tile_click_value_planes_b4_kernel(
         bias_spread = keep.tile([P, N], BF16, name="bias_spread")
         bid_spread = keep.tile([P, N], BF16, name="bid_spread")
         ident = keep.tile([P, P], F32, name="ident")
+        all_codes = keep.tile([P, GROUPS * T], U32, name="y_codes", align_bytes=64)
         warm = keep.tile([P, 1], F32, name="warm")
         y_scales = keep.tile([P, T], U8, name="y_scales", align_bytes=64)
 
@@ -426,8 +427,7 @@ def tile_click_value_planes_b4_kernel(
             give_back(("y", n, pair))
 
         def y_quant(chunk, n, part=None):
-            if n not in y_codes:
-                y_codes[n] = work.tile([P, T], U32, name="y_codes", bufs=GROUPS, align_bytes=64)
+            y_codes[n] = all_codes[:, T * n : T * (n + 1)]
             first, last = (0, USERS[chunk]) if part is None else (PAIR * part, PAIR * (part + 1))
             users = slice(FIRST_USER[chunk] + first, FIRST_USER[chunk] + last)
             nc.vector.quantize_mx(
@@ -459,8 +459,8 @@ def tile_click_value_planes_b4_kernel(
         w_group(0, 0)
         x_widen(2, 8, 12, SCALAR)
         x_turn(1, (0,))
-        x_widen(2, 4, 8, VECTOR)
         w_widen(1, 0)
+        x_widen(2, 4, 8, VECTOR)
         x_widen(3, 4, 8, VECTOR)
         x_widen(4, 0, 4, VECTOR)
         x_out(0, (1,), on_scalar)
@@ -473,51 +473,51 @@ def tile_click_value_planes_b4_kernel(
         w_quant(0, 0)
         x_turn(1, (1,))
         x_out(2, (0,), on_scalar)
-        x_turn(2, (1,))
         x_quant(NARROW, 0)
+        x_turn(2, (1,))
         w_group(1, 0)
-        x_turn(0, (2,))
         x_out(1, (0,), on_scalar)
+        x_turn(0, (2,))
         hidden_pass(NARROW, 0, 0, 0)
-        hidden_pass(NARROW, 0, 2, 0)
         x_widen(3, 8, 12, SCALAR)
-        x_widen(4, 8, 12, VECTOR)
+        hidden_pass(NARROW, 0, 2, 0)
         x_widen(5, 8, 12, SCALAR)
+        x_widen(4, 8, 12, VECTOR)
         x_turn(1, (2,))
         x_quant(NARROW, 1)
-        w_group(2, 0)
         x_out(2, (1,), on_scalar)
         x_turn(2, (2,))
+        w_group(2, 0)
         x_out(1, (1,), on_scalar)
         w_widen(0, 1)
         x_quant(WIDE, 0)
         w_quant(1, 0)
         hidden_pass(WIDE, 0, 0, 0)
-        hidden_pass(WIDE, 0, 1, 0)
         x_out(0, (2,), on_scalar)
+        hidden_pass(WIDE, 0, 1, 0)
         hidden_pass(WIDE, 0, 2, 0)
         x_quant(WIDE, 1)
         widen_bias()
         hidden_pass(WIDE, 0, 3, 0)
-        w_quant(2, 0)
         x_out(2, (2,), on_scalar)
-        x_quant(NARROW, 2)
+        w_quant(2, 0)
         x_out(1, (2,), on_scalar)
         turn_bias()
         hidden_pass(NARROW, 0, 0, 1)
         hidden_pass(NARROW, 0, 2, 1)
-        w_group(0, 1)
+        x_quant(NARROW, 2)
         hidden_pass(WIDE, 0, 0, 1)
         w_widen(1, 1)
+        w_group(0, 1)
         hidden_pass(WIDE, 0, 1, 1)
         hidden_pass(WIDE, 0, 2, 1)
         hidden_pass(WIDE, 0, 3, 1)
         hidden_pass(NARROW, 0, 0, 2)
         widen_gain()
-        x_quant(WIDE, 2)
         w_widen(2, 1)
         for again in range(K_PASSES):
             hidden_pass(NARROW, 0, 1, again)
+        x_quant(WIDE, 2)
         hidden_pass(NARROW, 0, 2, 2)
         w_group(1, 1)
         for again in range(K_PASSES):
@@ -527,31 +527,30 @@ def tile_click_value_planes_b4_kernel(
         hidden_pass(WIDE, 0, 1, 2)
         h_relu(NARROW, 0, (2, 3), SCALAR)
         hidden_pass(WIDE, 0, 2, 2)
-        w_quant(0, 1)
         hidden_pass(WIDE, 0, 3, 2)
-        w_quant(1, 1)
+        w_quant(0, 1)
         h_relu(WIDE, 0, (1,), SCALAR)
+        w_quant(1, 1)
         hidden_pass(NARROW, 1, 0, 0)
+        h_relu(WIDE, 0, (0,), SCALAR)
         hidden_pass(NARROW, 1, 2, 0)
         w_group(2, 1)
-        h_relu(WIDE, 0, (0,), SCALAR)
         hidden_pass(NARROW, 1, 0, 1)
+        h_relu(WIDE, 0, (3,), SCALAR)
         hidden_pass(NARROW, 1, 2, 1)
         hidden_pass(WIDE, 1, 0, 0)
-        h_relu(WIDE, 0, (3,), SCALAR)
+        h_relu(WIDE, 0, (2,), SCALAR)
         hidden_pass(WIDE, 1, 0, 1)
         hidden_pass(WIDE, 1, 1, 0)
-        h_relu(WIDE, 0, (2,), SCALAR)
-        w_quant(2, 1)
-        hidden_pass(WIDE, 1, 1, 1)
         bias_out()
-        hidden_pass(WIDE, 1, 2, 0)
+        w_quant(2, 1)
         h_group(WIDE, 0, on_scalar, slice(0, PAIR))
+        hidden_pass(WIDE, 1, 1, 1)
+        hidden_pass(WIDE, 1, 2, 0)
         h_group(NARROW, 0, on_vector)
         hidden_pass(WIDE, 1, 2, 1)
-        h_group(WIDE, 0, on_vector, slice(PAIR, 2 * PAIR))
-        hidden_pass(NARROW, 1, 0, 2)
         h_quant(NARROW, 0)
+        hidden_pass(NARROW, 1, 0, 2)
         for again in range(K_PASSES):
             hidden_pass(NARROW, 1, 1, again)
         hidden_pass(NARROW, 1, 2, 2)
@@ -559,6 +558,7 @@ def tile_click_value_planes_b4_kernel(
         for again in range(K_PASSES):
             hidden_pass(NARROW, 1, 3, again)
         hidden_pass(WIDE, 1, 0, 2)
+        h_group(WIDE, 0, on_vector, slice(PAIR, 2 * PAIR))
         hidden_pass(WIDE, 1, 1, 2)
         h_relu(NARROW, 1, (2, 3), SCALAR)
         hidden_pass(WIDE, 1, 2, 2)
@@ -570,160 +570,160 @@ def tile_click_value_planes_b4_kernel(
         h_quant(NARROW, 1)
         hidden_pass(WIDE, 1, 3, 2)
         h_quant(WIDE, 0)
-        narrow_logits(0, 0, (0,))
         h_relu(WIDE, 1, (1,), SCALAR)
+        narrow_logits(0, 0, (0,))
         narrow_logits(0, 1, (0,))
         narrow_logits(1, 0, (0,))
         h_relu(WIDE, 1, (3,), SCALAR)
         narrow_logits(0, 0, (1,))
         narrow_logits(0, 1, (1,))
+        h_group(WIDE, 1, on_scalar, slice(PAIR, 2 * PAIR))
         narrow_logits(1, 0, (1,))
         narrow_bias(0, 0)
-        h_group(WIDE, 1, on_scalar, slice(PAIR, 2 * PAIR))
         narrow_logits(1, 1, (0,))
-        narrow_bias(0, 1)
-        narrow_logits(1, 1, (1,))
-        narrow_logits(2, 0)
-        narrow_sigmoid(0, 0)
         h_group(WIDE, 1, on_vector, slice(0, PAIR))
+        narrow_logits(1, 1, (1,))
+        narrow_sigmoid(0, 0)
+        narrow_logits(2, 0)
+        narrow_bias(0, 1)
         narrow_logits(2, 1)
-        narrow_sigmoid(0, 1)
-        narrow_bias(1, 0)
-        narrow_logits(3, 0)
         h_quant(WIDE, 1)
-        narrow_sigmoid(1, 0)
+        narrow_sigmoid(0, 1)
+        narrow_logits(3, 0)
+        narrow_bias(1, 0)
         narrow_logits(3, 1)
         narrow_bias(1, 1)
+        narrow_sigmoid(1, 0)
         wide_logits(0)
-        narrow_value(0, 1)
+        narrow_value(0, 0)
         narrow_sigmoid(1, 1)
         wide_logits(1)
-        narrow_value(0, 0)
-        wide_logits(2)
+        narrow_value(0, 1)
         wide_sigmoid(0)
-        narrow_value(1, 1)
-        wide_logits(3)
+        wide_logits(2)
+        narrow_bias(2, 0)
         y_store(0, 0)
         wide_sigmoid(1)
-        wide_logits(4)
+        wide_logits(3)
         narrow_value(1, 0)
+        wide_logits(4)
         wide_sigmoid(2)
+        narrow_value(1, 1)
         wide_logits(5)
+        wide_sigmoid(3)
+        wide_logits(6)
         narrow_bias(2, 1)
         y_round((NARROW, 0), on_gpsimd)
         y_store(1, 0)
-        wide_sigmoid(3)
-        wide_logits(6)
-        narrow_bias(2, 0)
         wide_sigmoid(4)
         wide_turn(0, 0)
-        narrow_bias(3, 1)
-        wide_turn(0, 1)
-        wide_sigmoid(5)
-        wide_turn(0, 2)
         narrow_bias(3, 0)
-        wide_turn(0, 3)
-        wide_sigmoid(6)
-        wide_logits(7)
+        wide_sigmoid(5)
+        wide_turn(0, 1)
         wide_value(0, 0)
-        narrow_sigmoid(2, 1)
-        wide_logits(8)
+        wide_turn(0, 2)
+        wide_sigmoid(6)
+        wide_turn(0, 3)
         wide_value(0, 1)
+        wide_logits(7)
         narrow_sigmoid(2, 0)
+        narrow_bias(3, 1)
+        wide_logits(8)
+        y_store(0, 1)
+        narrow_sigmoid(2, 1)
+        y_round((WIDE, 0), on_gpsimd, 0, 2)
         wide_logits(9)
         wide_value(0, 2)
-        y_store(0, 1)
-        wide_logits(10)
         wide_sigmoid(7)
+        wide_logits(10)
         wide_value(0, 3)
-        wide_logits(11)
-        narrow_sigmoid(3, 1)
-        narrow_value(2, 1)
-        y_store(0, 2)
-        wide_logits(12)
         narrow_sigmoid(3, 0)
+        wide_logits(11)
         narrow_value(2, 0)
-        wide_logits(13)
+        y_store(0, 2)
+        narrow_sigmoid(3, 1)
+        wide_logits(12)
+        narrow_value(2, 1)
         wide_sigmoid(8)
-        narrow_value(3, 1)
-        y_store(2, 0)
-        wide_logits(14)
-        wide_sigmoid(9)
-        y_round((WIDE, 0), on_vector)
-        wide_logits(15)
-        wide_sigmoid(10)
         wide_turn(1, 0)
-        wide_turn(1, 1)
         narrow_value(3, 0)
-        wide_sigmoid(11)
-        y_turn(0, 0)
+        y_store(2, 0)
+        wide_turn(1, 1)
+        wide_sigmoid(9)
+        wide_turn(1, 2)
+        narrow_value(3, 1)
+        wide_turn(1, 3)
+        wide_sigmoid(10)
+        wide_logits(13)
         wide_value(1, 0)
         y_round((NARROW, 1), on_gpsimd)
         y_store(3, 0)
-        wide_sigmoid(12)
-        wide_turn(1, 2)
+        wide_sigmoid(11)
+        wide_logits(14)
         wide_value(1, 1)
-        wide_turn(1, 3)
-        wide_sigmoid(13)
-        y_turn(1, 0)
+        wide_sigmoid(12)
+        wide_logits(15)
         wide_value(1, 2)
         y_store(1, 1)
+        wide_sigmoid(13)
         wide_turn(2, 0)
-        wide_sigmoid(14)
-        y_turn(0, 1)
         wide_value(1, 3)
         wide_turn(2, 1)
-        wide_sigmoid(15)
-        wide_turn(2, 2)
+        wide_sigmoid(14)
+        y_turn(0, 0)
         wide_value(2, 0)
         y_store(1, 2)
+        y_round((WIDE, 1), on_gpsimd)
+        wide_turn(2, 2)
+        wide_sigmoid(15)
+        wide_value(2, 1)
+        y_turn(1, 0)
+        wide_turn(2, 3)
+        y_round((WIDE, 0), on_scalar, 2, 4)
+        wide_value(2, 2)
+        y_store(2, 1)
+        wide_turn(3, 0)
+        y_turn(0, 1)
+        wide_value(2, 3)
+        wide_turn(3, 1)
         y_out(0, 0, on_scalar)
         y_turn(0, 2)
-        y_round((WIDE, 1), on_gpsimd)
-        wide_value(2, 1)
-        wide_turn(2, 3)
-        y_out(1, 0, on_scalar)
-        y_turn(2, 0)
-        wide_value(2, 2)
-        wide_turn(3, 0)
-        y_store(2, 1)
-        y_out(0, 1, on_scalar)
-        wide_turn(3, 1)
-        wide_value(2, 3)
-        wide_turn(3, 2)
-        y_out(0, 2, on_scalar)
         wide_value(3, 0)
         y_store(2, 2)
-        y_out(2, 0, on_scalar)
+        wide_turn(3, 2)
+        y_out(1, 0, on_scalar)
+        y_round((WIDE, 2), on_gpsimd)
+        y_turn(2, 0)
         wide_value(3, 1)
-        y_round((WIDE, 2), on_gpsimd, 0, 2)
-        y_turn(1, 1)
-        y_round((WIDE, 2), on_scalar, 2, 4)
+        y_out(0, 1, on_scalar)
         wide_turn(3, 3)
         wide_value(3, 2)
+        y_turn(1, 1)
         y_store(3, 1)
+        y_out(0, 2, on_scalar)
         y_turn(1, 2)
         wide_value(3, 3)
-        y_out(1, 1, on_scalar)
-        y_turn(2, 1)
-        y_quant(NARROW, 0)
+        y_out(2, 0, on_scalar)
+        y_out(1, 1, on_vector)
         y_store(3, 2)
+        y_round((WIDE, 3), on_scalar, 0, 2)
+        y_quant(NARROW, 0)
+        y_turn(2, 1)
+        y_round((WIDE, 3), on_vector, 2, 4)
         y_turn(2, 2)
         y_out(1, 2, on_scalar)
-        y_round((WIDE, 3), on_vector, 2, 4)
         y_turn(3, 0)
-        y_round((WIDE, 3), on_scalar, 0, 2)
         y_quant(WIDE, 0)
+        y_turn(3, 1)
+        y_out(2, 1, on_scalar)
+        y_turn(3, 2)
         y_quant(NARROW, 1)
         codes_store(0)
         y_quant(WIDE, 1)
-        y_out(2, 1, on_scalar)
-        y_turn(3, 1)
-        y_turn(3, 2)
-        y_quant(NARROW, 2)
-        codes_store(1)
         y_out(2, 2, on_scalar)
+        y_quant(NARROW, 2)
         y_out(3, 0, on_scalar)
+        codes_store(1)
         y_quant(WIDE, 2)
         y_out(3, 1, on_scalar)
         y_quant(NARROW, 3)

@@ -77,7 +77,7 @@ def tile_click_value_planes_b4_kernel(
         v_words = [keep.tile([P, 2 * N], U8, name="v_words%d" % h, align_bytes=64) for h in range(HALVES)]
         v_scales = keep.tile([P, HALVES, N], U8, name="v_scales", align_bytes=64)
         bias_rows = keep.tile([P, P], BF16, name="bias_rows")
-        bias_rows32 = keep.tile([P, P], F32, name="bias_rows32")
+        picks = keep.tile([P, ITEM_TILES], BF16, name="picks")
         bias_col = keep.tile([P, ITEM_TILES], F32, name="bias_col")
         bias_spread = keep.tile([P, N], BF16, name="bias_spread")
         bid_spread = keep.tile([P, N], BF16, name="bid_spread")
@@ -173,11 +173,11 @@ def tile_click_value_planes_b4_kernel(
             nc.scalar.copy(out=gain_col[:], in_=gain_bf[:].rearrange("p h t -> p (h t)"))
 
         def widen_bias():
-            nc.scalar.copy(out=bias_rows32[:], in_=bias_rows[:])
+            nc.scalar.copy(out=picks[:], in_=ident[:, 0:ITEM_TILES])
 
         def turn_bias():
             bias_bank.append(take_bank("bias"))
-            nc.tensor.transpose(bias_bank[0][:, 0:P], bias_rows32[:], ident[:])
+            nc.tensor.matmul(bias_bank[0][:, 0:ITEM_TILES], lhsT=bias_rows[:], rhs=picks[:], start=True, stop=True)
 
         def bias_out():
             nc.scalar.copy(out=bias_col[:], in_=bias_bank[0][:, 0:ITEM_TILES])
@@ -397,6 +397,11 @@ def tile_click_value_planes_b4_kernel(
         def on_gpsimd(out, in_):
             nc.gpsimd.tensor_scalar(out=out, in0=in_, scalar1=1.0, scalar2=0.0, op0=ALU.mult, op1=ALU.add)
 
+        def tile_store(b, i):
+            nc.sync.dma_start(
+                out=out_0[P * i : P * (i + 1), 2 * PASS * b : 2 * PASS * (b + 1)], in_=y_rows[NARROW, b][:, 2 * PASS * i : 2 * PASS * (i + 1)]
+            )
+
         def y_round(key, copy, first=0, last=SLOTS):
             if key not in y16:
                 y16[key] = work.tile([P, 2, SLOTS, P, 2], BF16, name="y16", tag="planes", bufs=6)
@@ -442,6 +447,7 @@ def tile_click_value_planes_b4_kernel(
             )
 
         make_quad_of()
+        widen_bias()
         x_widen(0, 0, 4, SCALAR)
         x_widen(0, 4, 8, VECTOR)
         spread_w_scales()
@@ -497,19 +503,18 @@ def tile_click_value_planes_b4_kernel(
         hidden_pass(WIDE, 0, 1, 0)
         hidden_pass(WIDE, 0, 2, 0)
         x_quant(WIDE, 1)
-        widen_bias()
-        hidden_pass(WIDE, 0, 3, 0)
         x_out(2, (2,), on_scalar)
+        hidden_pass(WIDE, 0, 3, 0)
         w_quant(2, 0)
         x_out(1, (2,), on_scalar)
         turn_bias()
         hidden_pass(NARROW, 0, 0, 1)
         hidden_pass(NARROW, 0, 2, 1)
-        x_quant(NARROW, 2)
         hidden_pass(WIDE, 0, 0, 1)
+        x_quant(NARROW, 2)
         w_widen(1, 1)
-        w_group(0, 1)
         hidden_pass(WIDE, 0, 1, 1)
+        w_group(0, 1)
         hidden_pass(WIDE, 0, 2, 1)
         hidden_pass(WIDE, 0, 3, 1)
         hidden_pass(NARROW, 0, 0, 2)
@@ -519,32 +524,32 @@ def tile_click_value_planes_b4_kernel(
             hidden_pass(NARROW, 0, 1, again)
         x_quant(WIDE, 2)
         hidden_pass(NARROW, 0, 2, 2)
-        w_group(1, 1)
         for again in range(K_PASSES):
             hidden_pass(NARROW, 0, 3, again)
         h_relu(NARROW, 0, (0, 1), SCALAR)
+        w_group(1, 1)
         hidden_pass(WIDE, 0, 0, 2)
         hidden_pass(WIDE, 0, 1, 2)
         h_relu(NARROW, 0, (2, 3), SCALAR)
         hidden_pass(WIDE, 0, 2, 2)
         hidden_pass(WIDE, 0, 3, 2)
-        w_quant(0, 1)
         h_relu(WIDE, 0, (1,), SCALAR)
+        w_quant(0, 1)
+        h_relu(WIDE, 0, (0,), SCALAR)
         w_quant(1, 1)
         hidden_pass(NARROW, 1, 0, 0)
-        h_relu(WIDE, 0, (0,), SCALAR)
         hidden_pass(NARROW, 1, 2, 0)
+        h_relu(WIDE, 0, (3,), SCALAR)
         w_group(2, 1)
         hidden_pass(NARROW, 1, 0, 1)
-        h_relu(WIDE, 0, (3,), SCALAR)
         hidden_pass(NARROW, 1, 2, 1)
         hidden_pass(WIDE, 1, 0, 0)
         h_relu(WIDE, 0, (2,), SCALAR)
         hidden_pass(WIDE, 1, 0, 1)
-        hidden_pass(WIDE, 1, 1, 0)
         bias_out()
-        w_quant(2, 1)
+        hidden_pass(WIDE, 1, 1, 0)
         h_group(WIDE, 0, on_scalar, slice(0, PAIR))
+        w_quant(2, 1)
         hidden_pass(WIDE, 1, 1, 1)
         hidden_pass(WIDE, 1, 2, 0)
         h_group(NARROW, 0, on_vector)
@@ -572,52 +577,52 @@ def tile_click_value_planes_b4_kernel(
         h_quant(WIDE, 0)
         h_relu(WIDE, 1, (1,), SCALAR)
         narrow_logits(0, 0, (0,))
-        narrow_logits(0, 1, (0,))
         narrow_logits(1, 0, (0,))
+        narrow_logits(0, 1, (0,))
         h_relu(WIDE, 1, (3,), SCALAR)
         narrow_logits(0, 0, (1,))
-        narrow_logits(0, 1, (1,))
-        h_group(WIDE, 1, on_scalar, slice(PAIR, 2 * PAIR))
         narrow_logits(1, 0, (1,))
+        h_group(WIDE, 1, on_scalar, slice(PAIR, 2 * PAIR))
+        narrow_logits(0, 1, (1,))
         narrow_bias(0, 0)
         narrow_logits(1, 1, (0,))
         h_group(WIDE, 1, on_vector, slice(0, PAIR))
         narrow_logits(1, 1, (1,))
         narrow_sigmoid(0, 0)
         narrow_logits(2, 0)
-        narrow_bias(0, 1)
-        narrow_logits(2, 1)
-        h_quant(WIDE, 1)
-        narrow_sigmoid(0, 1)
-        narrow_logits(3, 0)
         narrow_bias(1, 0)
+        narrow_logits(3, 0)
+        h_quant(WIDE, 1)
+        narrow_sigmoid(1, 0)
+        narrow_logits(2, 1)
+        narrow_bias(0, 1)
         narrow_logits(3, 1)
         narrow_bias(1, 1)
-        narrow_sigmoid(1, 0)
+        narrow_sigmoid(0, 1)
         wide_logits(0)
         narrow_value(0, 0)
         narrow_sigmoid(1, 1)
         wide_logits(1)
-        narrow_value(0, 1)
+        narrow_value(1, 0)
         wide_sigmoid(0)
         wide_logits(2)
         narrow_bias(2, 0)
-        y_store(0, 0)
+        tile_store(0, 0)
         wide_sigmoid(1)
         wide_logits(3)
-        narrow_value(1, 0)
+        narrow_value(0, 1)
         wide_logits(4)
         wide_sigmoid(2)
         narrow_value(1, 1)
         wide_logits(5)
         wide_sigmoid(3)
         wide_logits(6)
-        narrow_bias(2, 1)
+        narrow_bias(3, 0)
         y_round((NARROW, 0), on_gpsimd)
-        y_store(1, 0)
+        tile_store(0, 1)
         wide_sigmoid(4)
         wide_turn(0, 0)
-        narrow_bias(3, 0)
+        narrow_bias(2, 1)
         wide_sigmoid(5)
         wide_turn(0, 1)
         wide_value(0, 0)
@@ -630,24 +635,24 @@ def tile_click_value_planes_b4_kernel(
         narrow_bias(3, 1)
         wide_logits(8)
         y_store(0, 1)
-        narrow_sigmoid(2, 1)
+        narrow_sigmoid(3, 0)
         y_round((WIDE, 0), on_gpsimd, 0, 2)
         wide_logits(9)
         wide_value(0, 2)
         wide_sigmoid(7)
         wide_logits(10)
         wide_value(0, 3)
-        narrow_sigmoid(3, 0)
+        narrow_sigmoid(2, 1)
         wide_logits(11)
         narrow_value(2, 0)
         y_store(0, 2)
         narrow_sigmoid(3, 1)
         wide_logits(12)
-        narrow_value(2, 1)
+        narrow_value(3, 0)
         wide_sigmoid(8)
         wide_turn(1, 0)
-        narrow_value(3, 0)
-        y_store(2, 0)
+        narrow_value(2, 1)
+        tile_store(1, 0)
         wide_turn(1, 1)
         wide_sigmoid(9)
         wide_turn(1, 2)
@@ -657,7 +662,7 @@ def tile_click_value_planes_b4_kernel(
         wide_logits(13)
         wide_value(1, 0)
         y_round((NARROW, 1), on_gpsimd)
-        y_store(3, 0)
+        tile_store(1, 1)
         wide_sigmoid(11)
         wide_logits(14)
         wide_value(1, 1)
@@ -729,10 +734,8 @@ def tile_click_value_planes_b4_kernel(
         y_quant(NARROW, 3)
         codes_store(2)
         y_out(3, 2, on_scalar)
-        y_quant(WIDE, 3, 0)
-        codes_store(3, slice(0, 2 * PAIR))
-        y_quant(WIDE, 3, 1)
-        codes_store(3, slice(2 * PAIR, T))
+        y_quant(WIDE, 3)
+        codes_store(3)
         for q in range(P // QUAD):
             queue = nc.scalar if q % 2 else nc.sync
             queue.dma_start(

@@ -86,11 +86,12 @@ def tile_click_value_planes_b4_kernel(
         warm = keep.tile([P, 1], F32, name="warm")
         y_scales = keep.tile([P, T], U8, name="y_scales", align_bytes=64)
 
+        nc.vector.memset(ident[:], 0.0)
         nc.vector.memset(w_scale_rows[:], 0.0)
         nc.vector.memset(warm[:], 0.0)
         nc.vector.memset(bias_rows[:], 0.0)
         nc.vector.memset(v_scales[:].rearrange("p h n -> p (h n)").bitcast(I32), 0)
-        make_identity(nc, ident[:])
+        make_identity(nc, ident[:], nomemset=True)
 
         def load_x_scale(chunk):
             users = slice(FIRST_USER[chunk], FIRST_USER[chunk] + USERS[chunk])
@@ -446,14 +447,13 @@ def tile_click_value_planes_b4_kernel(
                 out=out_1[n][:, users, :].rearrange("p m t -> p (m t)").bitcast(I32), in_=y_codes[n][:, users].bitcast(I32)
             )
 
-        make_quad_of()
-        widen_bias()
-        x_widen(0, 0, 4, SCALAR)
         x_widen(0, 4, 8, VECTOR)
-        spread_w_scales()
+        x_widen(0, 0, 4, SCALAR)
         x_widen(0, 8, 12, VECTOR)
         w_widen(0, 0, on_scalar, slice(0, 2 * PASS))
+        make_quad_of()
         x_widen(1, 0, 4, VECTOR)
+        spread_w_scales()
         w_widen(0, 0, on_scalar, slice(2 * PASS, 4 * PASS))
         x_widen(1, 4, 8, VECTOR)
         x_turn(0, (0,))
@@ -461,12 +461,13 @@ def tile_click_value_planes_b4_kernel(
         x_widen(2, 0, 4, VECTOR)
         x_turn(0, (1,))
         w_scales_out()
-        x_widen(3, 0, 4, SCALAR)
+        widen_bias()
         w_group(0, 0)
+        x_widen(3, 0, 4, SCALAR)
         x_widen(2, 8, 12, SCALAR)
         x_turn(1, (0,))
-        w_widen(1, 0)
         x_widen(2, 4, 8, VECTOR)
+        w_widen(1, 0)
         x_widen(3, 4, 8, VECTOR)
         x_widen(4, 0, 4, VECTOR)
         x_out(0, (1,), on_scalar)
@@ -479,8 +480,8 @@ def tile_click_value_planes_b4_kernel(
         w_quant(0, 0)
         x_turn(1, (1,))
         x_out(2, (0,), on_scalar)
-        x_quant(NARROW, 0)
         x_turn(2, (1,))
+        x_quant(NARROW, 0)
         w_group(1, 0)
         x_out(1, (0,), on_scalar)
         x_turn(0, (2,))
@@ -488,8 +489,8 @@ def tile_click_value_planes_b4_kernel(
         x_widen(3, 8, 12, SCALAR)
         hidden_pass(NARROW, 0, 2, 0)
         x_widen(5, 8, 12, SCALAR)
-        x_widen(4, 8, 12, VECTOR)
         x_turn(1, (2,))
+        x_widen(4, 8, 12, VECTOR)
         x_quant(NARROW, 1)
         x_out(2, (1,), on_scalar)
         x_turn(2, (2,))
@@ -497,33 +498,33 @@ def tile_click_value_planes_b4_kernel(
         x_out(1, (1,), on_scalar)
         w_widen(0, 1)
         x_quant(WIDE, 0)
+        x_out(0, (2,), on_scalar)
         w_quant(1, 0)
         hidden_pass(WIDE, 0, 0, 0)
-        x_out(0, (2,), on_scalar)
         hidden_pass(WIDE, 0, 1, 0)
         hidden_pass(WIDE, 0, 2, 0)
-        x_quant(WIDE, 1)
         x_out(2, (2,), on_scalar)
+        x_quant(WIDE, 1)
         hidden_pass(WIDE, 0, 3, 0)
-        w_quant(2, 0)
         x_out(1, (2,), on_scalar)
+        w_quant(2, 0)
         turn_bias()
         hidden_pass(NARROW, 0, 0, 1)
         hidden_pass(NARROW, 0, 2, 1)
         hidden_pass(WIDE, 0, 0, 1)
-        x_quant(NARROW, 2)
         w_widen(1, 1)
+        x_quant(NARROW, 2)
         hidden_pass(WIDE, 0, 1, 1)
-        w_group(0, 1)
         hidden_pass(WIDE, 0, 2, 1)
+        w_group(0, 1)
         hidden_pass(WIDE, 0, 3, 1)
         hidden_pass(NARROW, 0, 0, 2)
         widen_gain()
         w_widen(2, 1)
         for again in range(K_PASSES):
             hidden_pass(NARROW, 0, 1, again)
-        x_quant(WIDE, 2)
         hidden_pass(NARROW, 0, 2, 2)
+        x_quant(WIDE, 2)
         for again in range(K_PASSES):
             hidden_pass(NARROW, 0, 3, again)
         h_relu(NARROW, 0, (0, 1), SCALAR)
@@ -546,8 +547,8 @@ def tile_click_value_planes_b4_kernel(
         hidden_pass(WIDE, 1, 0, 0)
         h_relu(WIDE, 0, (2,), SCALAR)
         hidden_pass(WIDE, 1, 0, 1)
-        bias_out()
         hidden_pass(WIDE, 1, 1, 0)
+        bias_out()
         h_group(WIDE, 0, on_scalar, slice(0, PAIR))
         w_quant(2, 1)
         hidden_pass(WIDE, 1, 1, 1)
@@ -575,21 +576,21 @@ def tile_click_value_planes_b4_kernel(
         h_quant(NARROW, 1)
         hidden_pass(WIDE, 1, 3, 2)
         h_quant(WIDE, 0)
-        h_relu(WIDE, 1, (1,), SCALAR)
         narrow_logits(0, 0, (0,))
+        h_relu(WIDE, 1, (1,), SCALAR)
         narrow_logits(1, 0, (0,))
         narrow_logits(0, 1, (0,))
         h_relu(WIDE, 1, (3,), SCALAR)
         narrow_logits(0, 0, (1,))
         narrow_logits(1, 0, (1,))
-        h_group(WIDE, 1, on_scalar, slice(PAIR, 2 * PAIR))
         narrow_logits(0, 1, (1,))
         narrow_bias(0, 0)
+        h_group(WIDE, 1, on_scalar, slice(PAIR, 2 * PAIR))
         narrow_logits(1, 1, (0,))
         h_group(WIDE, 1, on_vector, slice(0, PAIR))
         narrow_logits(1, 1, (1,))
-        narrow_sigmoid(0, 0)
         narrow_logits(2, 0)
+        narrow_sigmoid(0, 0)
         narrow_bias(1, 0)
         narrow_logits(3, 0)
         h_quant(WIDE, 1)
@@ -601,20 +602,20 @@ def tile_click_value_planes_b4_kernel(
         narrow_sigmoid(0, 1)
         wide_logits(0)
         narrow_value(0, 0)
-        narrow_sigmoid(1, 1)
         wide_logits(1)
+        narrow_sigmoid(1, 1)
+        wide_logits(2)
         narrow_value(1, 0)
         wide_sigmoid(0)
-        wide_logits(2)
+        wide_logits(3)
         narrow_bias(2, 0)
         tile_store(0, 0)
         wide_sigmoid(1)
-        wide_logits(3)
-        narrow_value(0, 1)
         wide_logits(4)
+        narrow_value(0, 1)
         wide_sigmoid(2)
-        narrow_value(1, 1)
         wide_logits(5)
+        narrow_value(1, 1)
         wide_sigmoid(3)
         wide_logits(6)
         narrow_bias(3, 0)
@@ -622,42 +623,42 @@ def tile_click_value_planes_b4_kernel(
         tile_store(0, 1)
         wide_sigmoid(4)
         wide_turn(0, 0)
+        wide_turn(0, 1)
         narrow_bias(2, 1)
         wide_sigmoid(5)
-        wide_turn(0, 1)
-        wide_value(0, 0)
         wide_turn(0, 2)
-        wide_sigmoid(6)
         wide_turn(0, 3)
-        wide_value(0, 1)
+        wide_value(0, 0)
+        wide_sigmoid(6)
         wide_logits(7)
+        wide_value(0, 1)
+        wide_logits(8)
         narrow_sigmoid(2, 0)
         narrow_bias(3, 1)
-        wide_logits(8)
         y_store(0, 1)
+        wide_logits(9)
         narrow_sigmoid(3, 0)
         y_round((WIDE, 0), on_gpsimd, 0, 2)
-        wide_logits(9)
         wide_value(0, 2)
-        wide_sigmoid(7)
         wide_logits(10)
+        wide_sigmoid(7)
+        wide_logits(11)
         wide_value(0, 3)
         narrow_sigmoid(2, 1)
-        wide_logits(11)
+        wide_logits(12)
         narrow_value(2, 0)
         y_store(0, 2)
         narrow_sigmoid(3, 1)
-        wide_logits(12)
-        narrow_value(3, 0)
-        wide_sigmoid(8)
         wide_turn(1, 0)
+        narrow_value(3, 0)
+        wide_turn(1, 1)
+        wide_sigmoid(8)
+        wide_turn(1, 2)
         narrow_value(2, 1)
         tile_store(1, 0)
-        wide_turn(1, 1)
         wide_sigmoid(9)
-        wide_turn(1, 2)
-        narrow_value(3, 1)
         wide_turn(1, 3)
+        narrow_value(3, 1)
         wide_sigmoid(10)
         wide_logits(13)
         wide_value(1, 0)
@@ -666,47 +667,47 @@ def tile_click_value_planes_b4_kernel(
         wide_sigmoid(11)
         wide_logits(14)
         wide_value(1, 1)
-        wide_sigmoid(12)
         wide_logits(15)
+        wide_sigmoid(12)
         wide_value(1, 2)
         y_store(1, 1)
-        wide_sigmoid(13)
         wide_turn(2, 0)
-        wide_value(1, 3)
+        wide_sigmoid(13)
         wide_turn(2, 1)
-        wide_sigmoid(14)
+        wide_value(1, 3)
         y_turn(0, 0)
+        wide_sigmoid(14)
+        wide_turn(2, 2)
         wide_value(2, 0)
         y_store(1, 2)
         y_round((WIDE, 1), on_gpsimd)
-        wide_turn(2, 2)
-        wide_sigmoid(15)
-        wide_value(2, 1)
         y_turn(1, 0)
+        wide_sigmoid(15)
         wide_turn(2, 3)
+        wide_value(2, 1)
         y_round((WIDE, 0), on_scalar, 2, 4)
+        wide_turn(3, 0)
         wide_value(2, 2)
         y_store(2, 1)
-        wide_turn(3, 0)
         y_turn(0, 1)
-        wide_value(2, 3)
         wide_turn(3, 1)
+        wide_value(2, 3)
         y_out(0, 0, on_scalar)
         y_turn(0, 2)
         wide_value(3, 0)
-        y_store(2, 2)
         wide_turn(3, 2)
+        y_store(2, 2)
         y_out(1, 0, on_scalar)
-        y_round((WIDE, 2), on_gpsimd)
         y_turn(2, 0)
+        y_round((WIDE, 2), on_gpsimd)
         wide_value(3, 1)
-        y_out(0, 1, on_scalar)
         wide_turn(3, 3)
-        wide_value(3, 2)
+        y_out(0, 1, on_scalar)
         y_turn(1, 1)
+        wide_value(3, 2)
         y_store(3, 1)
-        y_out(0, 2, on_scalar)
         y_turn(1, 2)
+        y_out(0, 2, on_scalar)
         wide_value(3, 3)
         y_out(2, 0, on_scalar)
         y_out(1, 1, on_vector)
@@ -716,12 +717,12 @@ def tile_click_value_planes_b4_kernel(
         y_turn(2, 1)
         y_round((WIDE, 3), on_vector, 2, 4)
         y_turn(2, 2)
-        y_out(1, 2, on_scalar)
         y_turn(3, 0)
+        y_out(1, 2, on_scalar)
         y_quant(WIDE, 0)
         y_turn(3, 1)
-        y_out(2, 1, on_scalar)
         y_turn(3, 2)
+        y_out(2, 1, on_scalar)
         y_quant(NARROW, 1)
         codes_store(0)
         y_quant(WIDE, 1)

@@ -31,7 +31,7 @@ NARROW, WIDE = 0, 1
 VECTOR, SCALAR = 0, 1
 FIRST_USER = {NARROW: 0, WIDE: PAIR}
 USERS = {NARROW: PAIR, WIDE: 2 * PAIR}
-STEPS = ITEM_TILES // 2
+WIDE_TILES = USERS[WIDE] // P
 BANKS = 8
 
 
@@ -82,7 +82,7 @@ def tile_click_value_planes_b4_kernel(
         bias_spread = keep.tile([P, N], BF16, name="bias_spread")
         bid_spread = keep.tile([P, N], BF16, name="bid_spread")
         ident = keep.tile([P, P], F32, name="ident")
-        all_codes = keep.tile([P, GROUPS * T], U32, name="y_codes", align_bytes=64)
+        y_codes = keep.tile([P, GROUPS * T], U32, name="y_codes", align_bytes=64)
         warm = keep.tile([P, 1], F32, name="warm")
         y_scales = keep.tile([P, T], U8, name="y_scales", align_bytes=64)
 
@@ -151,8 +151,7 @@ def tile_click_value_planes_b4_kernel(
         a_banks, h_planes, h_grouped, h_mx = {}, {}, {}, {}
         z_banks, logits, probs, prob_banks = {}, {}, {}, {}
         y_rows, y16, y_banks, y_grouped = {}, {}, {}, {}
-
-        y_codes, bias_bank, scale_bank = {}, [], []
+        bias_bank, scale_bank = [], []
 
         def make_quad_of():
             nc.vector.tensor_copy(
@@ -173,7 +172,7 @@ def tile_click_value_planes_b4_kernel(
         def widen_gain():
             nc.scalar.copy(out=gain_col[:], in_=gain_bf[:].rearrange("p h t -> p (h t)"))
 
-        def widen_bias():
+        def make_picks():
             nc.scalar.copy(out=picks[:], in_=ident[:, 0:ITEM_TILES])
 
         def turn_bias():
@@ -187,13 +186,13 @@ def tile_click_value_planes_b4_kernel(
         def chunk_of(pair):
             return NARROW if pair == 0 else WIDE
 
-        def x_widen(i, first=0, last=K // P, on=VECTOR):
+        def x_widen(i, g, on=VECTOR):
             chunk = chunk_of(i // 2)
             row = i - FIRST_USER[chunk] // P
             if i // 2 not in x_pairs:
                 x_pairs[i // 2] = work.tile([P, 2 * K], BF16, name="x_wide", tag="rows", bufs=6, align_bytes=64)
             x_wide[i] = x_pairs[i // 2][:, K * (i % 2) : K * (i % 2 + 1)]
-            for b in range(first, last):
+            for b in range(SLOTS * g, SLOTS * (g + 1)):
                 block = slice(P * b, P * (b + 1))
                 source, scale = x_raw[i][:, block].bitcast(FP8), x_scale[chunk][:, row, b : b + 1]
                 if on == SCALAR:
@@ -201,31 +200,29 @@ def tile_click_value_planes_b4_kernel(
                 else:
                     nc.vector.tensor_scalar(out=x_wide[i][:, block], in0=source, scalar1=scale, scalar2=None, op0=ALU.mult)
 
-        def x_turn(pair, passes=range(K_PASSES)):
-            for g in passes:
-                x_banks[pair, g] = take_bank(("x", pair, g))
-                for ii in range(2):
-                    words = x_wide[2 * pair + ii].bitcast(F32)
-                    for u in range(2):
-                        nc.tensor.transpose(
-                            x_banks[pair, g][:, PAIR * u + ii : PAIR * (u + 1) : 2],
-                            words[:, 2 * P * g + u : 2 * P * (g + 1) : 2],
-                            ident[:],
-                        )
+        def x_turn(pair, g):
+            x_banks[pair, g] = take_bank(("x", pair, g))
+            for ii in range(2):
+                words = x_wide[2 * pair + ii].bitcast(F32)
+                for u in range(2):
+                    nc.tensor.transpose(
+                        x_banks[pair, g][:, PAIR * u + ii : PAIR * (u + 1) : 2],
+                        words[:, 2 * P * g + u : 2 * P * (g + 1) : 2],
+                        ident[:],
+                    )
 
-        def x_out(pair, passes=range(K_PASSES), copy=on_scalar):
+        def x_out(pair, g):
             chunk = chunk_of(pair)
             first_tile = 2 * pair - FIRST_USER[chunk] // P
-            for g in passes:
-                if g not in x_passes:
-                    x_passes[g] = work.tile([P, SLOTS * T], BF16, name="x_grouped", tag="rows", bufs=6, align_bytes=64)
-                x_grouped[chunk, g] = x_passes[g][:, SLOTS * FIRST_USER[chunk] : SLOTS * (FIRST_USER[chunk] + USERS[chunk])]
-                words = x_grouped[chunk, g].bitcast(F32).rearrange("p (m i u) -> p m i u", m=P, u=2)
-                copy(
-                    out=words[:, :, first_tile : first_tile + 2, :],
-                    in_=x_banks[pair, g][:].rearrange("p (u m i) -> p m i u", u=2, i=2),
-                )
-                give_back(("x", pair, g))
+            if g not in x_passes:
+                x_passes[g] = work.tile([P, SLOTS * T], BF16, name="x_grouped", tag="rows", bufs=6, align_bytes=64)
+            x_grouped[chunk, g] = x_passes[g][:, SLOTS * FIRST_USER[chunk] : SLOTS * (FIRST_USER[chunk] + USERS[chunk])]
+            words = x_grouped[chunk, g].bitcast(F32).rearrange("p (m i u) -> p m i u", m=P, u=2)
+            nc.scalar.copy(
+                out=words[:, :, first_tile : first_tile + 2, :],
+                in_=x_banks[pair, g][:].rearrange("p (u m i) -> p m i u", u=2, i=2),
+            )
+            give_back(("x", pair, g))
 
         def x_quant(chunk, g):
             x_mx[chunk, g] = quantised("x%d_%d" % (chunk, g), x_grouped[chunk, g])
@@ -236,10 +233,10 @@ def tile_click_value_planes_b4_kernel(
         def grouped_tile(name, width):
             return work.tile([P, SLOTS * width], BF16, name=name, tag="grouped", bufs=GROUPS, align_bytes=64)
 
-        def w_widen(g, h, copy=on_scalar, part=slice(None)):
+        def w_widen(g, h, part=slice(None)):
             if (g, h) not in w_wide:
                 w_wide[g, h] = slot_planes("w_wide", PASS)
-            copy(out=w_wide[g, h][:].rearrange("p j f -> p (j f)")[:, part], in_=w_raw[g, h][:, part].bitcast(FP8))
+            nc.scalar.copy(out=w_wide[g, h][:].rearrange("p j f -> p (j f)")[:, part], in_=w_raw[g, h][:, part].bitcast(FP8))
 
         def w_group(g, h):
             w_grouped[g, h] = grouped_tile("w_grouped", PASS)
@@ -277,10 +274,6 @@ def tile_click_value_planes_b4_kernel(
 
         def hidden_wide(h, g):
             for t in range(SLOTS):
-                hidden_pass(WIDE, h, t, g)
-
-        def hidden_wide_slot(h, t):
-            for g in range(K_PASSES):
                 hidden_pass(WIDE, h, t, g)
 
         def hidden_narrow(h, g):
@@ -344,27 +337,25 @@ def tile_click_value_planes_b4_kernel(
         def bundle(n, pair):
             return ((NARROW, n // 2), n % 2, 2) if pair == 0 else ((WIDE, n), 2 * (pair - 1), 1)
 
-        def value_rows(n, i):
+        def value_row(n, i):
             key, first, step = bundle(n, i // 2)
             if key not in y_rows:
                 y_rows[key] = work.tile([P, SLOTS * PASS], F32, name="y_rows", tag="rows", bufs=6, align_bytes=64)
-            slot = first + step * (i % 2)
-            return y_rows[key][:, PASS * slot : PASS * (slot + 1)]
+            row = first + step * (i % 2)
+            return y_rows[key][:, PASS * row : PASS * (row + 1)]
 
         def wide_value(n, i):
             nc.vector.tensor_tensor(
-                out=value_rows(n, 2 + i), in0=prob_banks[n, i][:], in1=bid_spread[:, PASS * n : PASS * (n + 1)], op=ALU.mult
+                out=value_row(n, 2 + i), in0=prob_banks[n, i][:], in1=bid_spread[:, PASS * n : PASS * (n + 1)], op=ALU.mult
             )
             give_back(("prob", n, i))
 
-        def y_store(n, pair, groups=1):
-            key, first, step = bundle(n, pair)
-            rows = out_0[PAIR * pair : PAIR * (pair + 1), PASS * n : PASS * (n + groups)].rearrange("(i p) n -> p i n", p=P)
-            if pair == 0:
-                source = y_rows[key][:].rearrange("p (i n) -> p i n", i=2)[:, :, PASS * first : PASS * (first + groups)]
-            else:
-                source = y_rows[key][:, PASS * first : PASS * (first + 2)].rearrange("p (i n) -> p i n", i=2)
-            nc.sync.dma_start(out=rows, in_=source)
+        def wide_store(n, pair):
+            first = bundle(n, pair)[1]
+            nc.sync.dma_start(
+                out=out_0[PAIR * pair : PAIR * (pair + 1), PASS * n : PASS * (n + 1)].rearrange("(i p) n -> p i n", p=P),
+                in_=y_rows[WIDE, n][:, PASS * first : PASS * (first + 2)].rearrange("p (i n) -> p i n", i=2),
+            )
 
         def narrow_logits(n, i, halves=range(HALVES)):
             for h in halves:
@@ -393,15 +384,19 @@ def tile_click_value_planes_b4_kernel(
             nc.scalar.activation(out=probs[NARROW, n, i][:], in_=logits[n, i][:], func=ACT.Sigmoid)
 
         def narrow_value(n, i):
-            nc.vector.tensor_tensor(out=value_rows(n, i), in0=probs[NARROW, n, i][:], in1=bid_spread[:, PASS * n : PASS * (n + 1)], op=ALU.mult)
+            nc.vector.tensor_tensor(
+                out=value_row(n, i), in0=probs[NARROW, n, i][:], in1=bid_spread[:, PASS * n : PASS * (n + 1)], op=ALU.mult
+            )
+
+        def narrow_store(half, i):
+            width = 2 * PASS
+            nc.sync.dma_start(
+                out=out_0[P * i : P * (i + 1), width * half : width * (half + 1)],
+                in_=y_rows[NARROW, half][:, width * i : width * (i + 1)],
+            )
 
         def on_gpsimd(out, in_):
             nc.gpsimd.tensor_scalar(out=out, in0=in_, scalar1=1.0, scalar2=0.0, op0=ALU.mult, op1=ALU.add)
-
-        def tile_store(b, i):
-            nc.sync.dma_start(
-                out=out_0[P * i : P * (i + 1), 2 * PASS * b : 2 * PASS * (b + 1)], in_=y_rows[NARROW, b][:, 2 * PASS * i : 2 * PASS * (i + 1)]
-            )
 
         def y_round(key, copy, first=0, last=SLOTS):
             if key not in y16:
@@ -424,7 +419,10 @@ def tile_click_value_planes_b4_kernel(
         def y_out(n, pair, copy=on_scalar):
             chunk = chunk_of(pair)
             if (chunk, n) not in y_grouped:
-                y_grouped[chunk, n] = work.tile([P, SLOTS * USERS[chunk]], BF16, name="y_grouped", tag=("y_grouped", "grouped")[chunk], bufs=GROUPS, align_bytes=64)
+                tag = "grouped" if chunk == WIDE else "y_grouped"
+                y_grouped[chunk, n] = work.tile(
+                    [P, SLOTS * USERS[chunk]], BF16, name="y_grouped", tag=tag, bufs=GROUPS, align_bytes=64
+                )
             first_word = 2 * (PAIR * pair - FIRST_USER[chunk])
             copy(
                 out=y_grouped[chunk, n][:].bitcast(F32)[:, first_word : first_word + 2 * PAIR].rearrange("p (m u) -> p m u", u=2),
@@ -432,311 +430,230 @@ def tile_click_value_planes_b4_kernel(
             )
             give_back(("y", n, pair))
 
-        def y_quant(chunk, n, part=None):
-            y_codes[n] = all_codes[:, T * n : T * (n + 1)]
-            first, last = (0, USERS[chunk]) if part is None else (PAIR * part, PAIR * (part + 1))
-            users = slice(FIRST_USER[chunk] + first, FIRST_USER[chunk] + last)
+        def y_quant(chunk, n):
+            first, last = FIRST_USER[chunk], FIRST_USER[chunk] + USERS[chunk]
             nc.vector.quantize_mx(
-                out=y_codes[n][:, users].bitcast(FP8X4),
-                scales=y_scales[4 * n : P, users],
-                in_=y_grouped[chunk, n][:, SLOTS * first : SLOTS * last],
+                out=y_codes[:, T * n + first : T * n + last].bitcast(FP8X4),
+                scales=y_scales[4 * n : P, first:last],
+                in_=y_grouped[chunk, n][:],
             )
 
-        def codes_store(n, users=slice(0, T)):
+        def codes_store(n):
             nc.sync.dma_start(
-                out=out_1[n][:, users, :].rearrange("p m t -> p (m t)").bitcast(I32), in_=y_codes[n][:, users].bitcast(I32)
+                out=out_1[n].rearrange("p m t -> p (m t)").bitcast(I32), in_=y_codes[:, T * n : T * (n + 1)].bitcast(I32)
             )
 
-        x_widen(0, 4, 8, VECTOR)
-        x_widen(0, 0, 4, SCALAR)
-        x_widen(0, 8, 12, VECTOR)
-        w_widen(0, 0, on_scalar, slice(0, 2 * PASS))
+        x_widen(0, 0, SCALAR)
+        x_widen(0, 1)
+        x_widen(0, 2)
+        w_widen(0, 0, slice(0, 2 * PASS))
+        w_widen(0, 0, slice(2 * PASS, 4 * PASS))
         make_quad_of()
-        x_widen(1, 0, 4, VECTOR)
         spread_w_scales()
-        w_widen(0, 0, on_scalar, slice(2 * PASS, 4 * PASS))
-        x_widen(1, 4, 8, VECTOR)
-        x_turn(0, (0,))
-        x_widen(1, 8, 12, SCALAR)
-        x_widen(2, 0, 4, VECTOR)
-        x_turn(0, (1,))
+        x_widen(1, 0)
+        x_widen(1, 1)
+        x_widen(1, 2, SCALAR)
+        x_turn(0, 0)
+        x_turn(0, 1)
         w_scales_out()
-        widen_bias()
+        make_picks()
+        x_widen(2, 0)
         w_group(0, 0)
-        x_widen(3, 0, 4, SCALAR)
-        x_widen(2, 8, 12, SCALAR)
-        x_turn(1, (0,))
-        x_widen(2, 4, 8, VECTOR)
+        x_widen(3, 0, SCALAR)
+        x_widen(2, 2, SCALAR)
+        x_turn(1, 0)
         w_widen(1, 0)
-        x_widen(3, 4, 8, VECTOR)
-        x_widen(4, 0, 4, VECTOR)
-        x_out(0, (1,), on_scalar)
-        x_widen(4, 4, 8, VECTOR)
-        x_out(0, (0,), on_scalar)
-        x_widen(5, 0, 4, VECTOR)
+        for i in range(2, 4):
+            x_widen(i, 1)
+        for i in range(4, 6):
+            x_widen(i, 0)
+            x_widen(i, 1)
+        x_out(0, 0)
+        x_out(0, 1)
         w_widen(2, 0)
-        x_widen(5, 4, 8, VECTOR)
-        x_turn(2, (0,))
+        x_turn(2, 0)
+        x_turn(1, 1)
+        x_turn(2, 1)
+        x_turn(0, 2)
         w_quant(0, 0)
-        x_turn(1, (1,))
-        x_out(2, (0,), on_scalar)
-        x_turn(2, (1,))
         x_quant(NARROW, 0)
         w_group(1, 0)
-        x_out(1, (0,), on_scalar)
-        x_turn(0, (2,))
-        hidden_pass(NARROW, 0, 0, 0)
-        x_widen(3, 8, 12, SCALAR)
-        hidden_pass(NARROW, 0, 2, 0)
-        x_widen(5, 8, 12, SCALAR)
-        x_turn(1, (2,))
-        x_widen(4, 8, 12, VECTOR)
+        x_out(1, 0)
+        x_out(2, 0)
+        hidden_narrow(0, 0)
+        x_widen(3, 2, SCALAR)
+        x_widen(5, 2, SCALAR)
+        x_widen(4, 2)
         x_quant(NARROW, 1)
-        x_out(2, (1,), on_scalar)
-        x_turn(2, (2,))
         w_group(2, 0)
-        x_out(1, (1,), on_scalar)
+        x_out(1, 1)
+        x_out(2, 1)
+        x_turn(1, 2)
+        x_turn(2, 2)
         w_widen(0, 1)
         x_quant(WIDE, 0)
-        x_out(0, (2,), on_scalar)
         w_quant(1, 0)
-        hidden_pass(WIDE, 0, 0, 0)
-        hidden_pass(WIDE, 0, 1, 0)
-        hidden_pass(WIDE, 0, 2, 0)
-        x_out(2, (2,), on_scalar)
+        for pair in range(3):
+            x_out(pair, 2)
+        hidden_wide(0, 0)
         x_quant(WIDE, 1)
-        hidden_pass(WIDE, 0, 3, 0)
-        x_out(1, (2,), on_scalar)
         w_quant(2, 0)
-        turn_bias()
-        hidden_pass(NARROW, 0, 0, 1)
-        hidden_pass(NARROW, 0, 2, 1)
-        hidden_pass(WIDE, 0, 0, 1)
-        w_widen(1, 1)
         x_quant(NARROW, 2)
-        hidden_pass(WIDE, 0, 1, 1)
-        hidden_pass(WIDE, 0, 2, 1)
+        turn_bias()
+        hidden_narrow(0, 1)
+        hidden_wide(0, 1)
+        hidden_narrow(0, 2)
+
+        w_widen(1, 1)
         w_group(0, 1)
-        hidden_pass(WIDE, 0, 3, 1)
-        hidden_pass(NARROW, 0, 0, 2)
+        x_quant(WIDE, 2)
+        hidden_wide(0, 2)
         widen_gain()
         w_widen(2, 1)
-        for again in range(K_PASSES):
-            hidden_pass(NARROW, 0, 1, again)
-        hidden_pass(NARROW, 0, 2, 2)
-        x_quant(WIDE, 2)
-        for again in range(K_PASSES):
-            hidden_pass(NARROW, 0, 3, again)
-        h_relu(NARROW, 0, (0, 1), SCALAR)
         w_group(1, 1)
-        hidden_pass(WIDE, 0, 0, 2)
-        hidden_pass(WIDE, 0, 1, 2)
-        h_relu(NARROW, 0, (2, 3), SCALAR)
-        hidden_pass(WIDE, 0, 2, 2)
-        hidden_pass(WIDE, 0, 3, 2)
-        h_relu(WIDE, 0, (1,), SCALAR)
+        h_relu(NARROW, 0)
         w_quant(0, 1)
-        h_relu(WIDE, 0, (0,), SCALAR)
         w_quant(1, 1)
-        hidden_pass(NARROW, 1, 0, 0)
-        hidden_pass(NARROW, 1, 2, 0)
-        h_relu(WIDE, 0, (3,), SCALAR)
         w_group(2, 1)
-        hidden_pass(NARROW, 1, 0, 1)
-        hidden_pass(NARROW, 1, 2, 1)
-        hidden_pass(WIDE, 1, 0, 0)
-        h_relu(WIDE, 0, (2,), SCALAR)
-        hidden_pass(WIDE, 1, 0, 1)
-        hidden_pass(WIDE, 1, 1, 0)
+        h_relu(WIDE, 0)
         bias_out()
-        h_group(WIDE, 0, on_scalar, slice(0, PAIR))
+        hidden_narrow(1, 0)
+        hidden_narrow(1, 1)
+        for t in range(SLOTS - 1):
+            hidden_pass(WIDE, 1, t, 0)
+            hidden_pass(WIDE, 1, t, 1)
         w_quant(2, 1)
-        hidden_pass(WIDE, 1, 1, 1)
-        hidden_pass(WIDE, 1, 2, 0)
-        h_group(NARROW, 0, on_vector)
-        hidden_pass(WIDE, 1, 2, 1)
+        hidden_narrow(1, 2)
+        for t in range(SLOTS - 1):
+            hidden_pass(WIDE, 1, t, 2)
+        for g in range(K_PASSES):
+            hidden_pass(WIDE, 1, SLOTS - 1, g)
+
+        h_group(NARROW, 0)
         h_quant(NARROW, 0)
-        hidden_pass(NARROW, 1, 0, 2)
-        for again in range(K_PASSES):
-            hidden_pass(NARROW, 1, 1, again)
-        hidden_pass(NARROW, 1, 2, 2)
+        h_group(WIDE, 0, on_scalar, slice(0, PAIR))
         h_relu(NARROW, 1, (0, 1), VECTOR)
-        for again in range(K_PASSES):
-            hidden_pass(NARROW, 1, 3, again)
-        hidden_pass(WIDE, 1, 0, 2)
+        h_relu(NARROW, 1, (2, 3))
         h_group(WIDE, 0, on_vector, slice(PAIR, 2 * PAIR))
-        hidden_pass(WIDE, 1, 1, 2)
-        h_relu(NARROW, 1, (2, 3), SCALAR)
-        hidden_pass(WIDE, 1, 2, 2)
-        hidden_pass(WIDE, 1, 3, 0)
-        h_relu(WIDE, 1, (0,), SCALAR)
-        h_group(NARROW, 1, on_vector)
-        hidden_pass(WIDE, 1, 3, 1)
-        h_relu(WIDE, 1, (2,), SCALAR)
+        h_group(NARROW, 1)
         h_quant(NARROW, 1)
-        hidden_pass(WIDE, 1, 3, 2)
         h_quant(WIDE, 0)
-        narrow_logits(0, 0, (0,))
-        h_relu(WIDE, 1, (1,), SCALAR)
-        narrow_logits(1, 0, (0,))
-        narrow_logits(0, 1, (0,))
-        h_relu(WIDE, 1, (3,), SCALAR)
-        narrow_logits(0, 0, (1,))
-        narrow_logits(1, 0, (1,))
-        narrow_logits(0, 1, (1,))
+        h_relu(WIDE, 1)
+        opened = ((0, 0), (1, 0), (0, 1))
+        for h in range(HALVES):
+            for n, i in opened:
+                narrow_logits(n, i, (h,))
+        narrow_logits(1, 1)
+        for i in range(2):
+            narrow_logits(2, i)
+            narrow_logits(3, i)
         narrow_bias(0, 0)
-        h_group(WIDE, 1, on_scalar, slice(PAIR, 2 * PAIR))
-        narrow_logits(1, 1, (0,))
         h_group(WIDE, 1, on_vector, slice(0, PAIR))
-        narrow_logits(1, 1, (1,))
-        narrow_logits(2, 0)
-        narrow_sigmoid(0, 0)
+        h_group(WIDE, 1, on_scalar, slice(PAIR, 2 * PAIR))
         narrow_bias(1, 0)
-        narrow_logits(3, 0)
         h_quant(WIDE, 1)
-        narrow_sigmoid(1, 0)
-        narrow_logits(2, 1)
         narrow_bias(0, 1)
-        narrow_logits(3, 1)
         narrow_bias(1, 1)
-        narrow_sigmoid(0, 1)
-        wide_logits(0)
+        for i in range(2):
+            narrow_sigmoid(0, i)
+            narrow_sigmoid(1, i)
+
+        for c in range(SLOTS):
+            wide_logits(c)
         narrow_value(0, 0)
-        wide_logits(1)
-        narrow_sigmoid(1, 1)
-        wide_logits(2)
         narrow_value(1, 0)
+        narrow_store(0, 0)
         wide_sigmoid(0)
-        wide_logits(3)
-        narrow_bias(2, 0)
-        tile_store(0, 0)
-        wide_sigmoid(1)
         wide_logits(4)
-        narrow_value(0, 1)
-        wide_sigmoid(2)
+        wide_sigmoid(1)
         wide_logits(5)
-        narrow_value(1, 1)
-        wide_sigmoid(3)
+        narrow_bias(2, 0)
         wide_logits(6)
-        narrow_bias(3, 0)
+        wide_sigmoid(2)
+        narrow_value(0, 1)
+        narrow_value(1, 1)
         y_round((NARROW, 0), on_gpsimd)
-        tile_store(0, 1)
+        narrow_store(0, 1)
+        wide_sigmoid(3)
+        narrow_bias(3, 0)
         wide_sigmoid(4)
-        wide_turn(0, 0)
-        wide_turn(0, 1)
         narrow_bias(2, 1)
         wide_sigmoid(5)
-        wide_turn(0, 2)
-        wide_turn(0, 3)
-        wide_value(0, 0)
+        for i in range(WIDE_TILES):
+            wide_turn(0, i)
         wide_sigmoid(6)
-        wide_logits(7)
+        wide_value(0, 0)
         wide_value(0, 1)
-        wide_logits(8)
-        narrow_sigmoid(2, 0)
-        narrow_bias(3, 1)
-        y_store(0, 1)
-        wide_logits(9)
-        narrow_sigmoid(3, 0)
+        wide_store(0, 1)
         y_round((WIDE, 0), on_gpsimd, 0, 2)
+        narrow_bias(3, 1)
         wide_value(0, 2)
-        wide_logits(10)
-        wide_sigmoid(7)
-        wide_logits(11)
         wide_value(0, 3)
-        narrow_sigmoid(2, 1)
-        wide_logits(12)
-        narrow_value(2, 0)
-        y_store(0, 2)
-        narrow_sigmoid(3, 1)
-        wide_turn(1, 0)
-        narrow_value(3, 0)
-        wide_turn(1, 1)
-        wide_sigmoid(8)
-        wide_turn(1, 2)
-        narrow_value(2, 1)
-        tile_store(1, 0)
-        wide_sigmoid(9)
-        wide_turn(1, 3)
-        narrow_value(3, 1)
-        wide_sigmoid(10)
-        wide_logits(13)
-        wide_value(1, 0)
+        wide_store(0, 2)
+        for c in range(7, 13):
+            wide_logits(c)
+        for i in range(2):
+            narrow_sigmoid(2, i)
+            narrow_sigmoid(3, i)
+            if i == 0:
+                wide_sigmoid(7)
+            narrow_value(2, i)
+            narrow_value(3, i)
+            narrow_store(1, i)
         y_round((NARROW, 1), on_gpsimd)
-        tile_store(1, 1)
-        wide_sigmoid(11)
-        wide_logits(14)
-        wide_value(1, 1)
-        wide_logits(15)
-        wide_sigmoid(12)
-        wide_value(1, 2)
-        y_store(1, 1)
-        wide_turn(2, 0)
-        wide_sigmoid(13)
-        wide_turn(2, 1)
-        wide_value(1, 3)
-        y_turn(0, 0)
-        wide_sigmoid(14)
-        wide_turn(2, 2)
-        wide_value(2, 0)
-        y_store(1, 2)
-        y_round((WIDE, 1), on_gpsimd)
-        y_turn(1, 0)
-        wide_sigmoid(15)
-        wide_turn(2, 3)
-        wide_value(2, 1)
-        y_round((WIDE, 0), on_scalar, 2, 4)
-        wide_turn(3, 0)
-        wide_value(2, 2)
-        y_store(2, 1)
-        y_turn(0, 1)
-        wide_turn(3, 1)
-        wide_value(2, 3)
-        y_out(0, 0, on_scalar)
-        y_turn(0, 2)
-        wide_value(3, 0)
-        wide_turn(3, 2)
-        y_store(2, 2)
-        y_out(1, 0, on_scalar)
-        y_turn(2, 0)
-        y_round((WIDE, 2), on_gpsimd)
-        wide_value(3, 1)
-        wide_turn(3, 3)
-        y_out(0, 1, on_scalar)
+        wide_sigmoid(8)
+        for i in range(WIDE_TILES):
+            wide_turn(1, i)
+            if i == 2:
+                wide_sigmoid(9)
+        for c in range(13, ITEM_TILES):
+            wide_sigmoid(c - 3)
+            wide_logits(c)
+
+        planes_between = {(2, 1): (0, 0), (2, 2): (1, 0), (3, 0): (0, 1), (3, 1): (0, 2), (3, 2): (2, 0)}
+        for n in range(1, GROUPS):
+            for i in range(WIDE_TILES):
+                if n == 1 and i > 0:
+                    wide_sigmoid(12 + i)
+                if n == 3 and i == 0:
+                    y_round((WIDE, 0), on_scalar, 2, 4)
+                    y_out(0, 0)
+                    y_out(1, 0)
+                if n > 1:
+                    wide_turn(n, i)
+                    if (n, i) in planes_between:
+                        y_turn(*planes_between[n, i])
+                wide_value(n, i)
+                if i % 2:
+                    wide_store(n, 1 + i // 2)
+            if n < GROUPS - 1:
+                y_round((WIDE, n), on_gpsimd)
+        y_out(0, 1)
+        y_out(0, 2)
+        y_out(2, 0)
+
         y_turn(1, 1)
-        wide_value(3, 2)
-        y_store(3, 1)
         y_turn(1, 2)
-        y_out(0, 2, on_scalar)
-        wide_value(3, 3)
-        y_out(2, 0, on_scalar)
-        y_out(1, 1, on_vector)
-        y_store(3, 2)
         y_round((WIDE, 3), on_scalar, 0, 2)
+        y_out(1, 1, on_vector)
         y_quant(NARROW, 0)
-        y_turn(2, 1)
         y_round((WIDE, 3), on_vector, 2, 4)
+        y_turn(2, 1)
         y_turn(2, 2)
-        y_turn(3, 0)
-        y_out(1, 2, on_scalar)
-        y_quant(WIDE, 0)
-        y_turn(3, 1)
-        y_turn(3, 2)
-        y_out(2, 1, on_scalar)
-        y_quant(NARROW, 1)
-        codes_store(0)
-        y_quant(WIDE, 1)
-        y_out(2, 2, on_scalar)
-        y_quant(NARROW, 2)
-        y_out(3, 0, on_scalar)
-        codes_store(1)
-        y_quant(WIDE, 2)
-        y_out(3, 1, on_scalar)
-        y_quant(NARROW, 3)
-        codes_store(2)
-        y_out(3, 2, on_scalar)
-        y_quant(WIDE, 3)
-        codes_store(3)
+        for pair in range(3):
+            y_turn(3, pair)
+        y_out(1, 2)
+        for n in range(GROUPS):
+            if n > 0:
+                y_quant(NARROW, n)
+            y_quant(WIDE, n)
+            codes_store(n)
+            if n == 0:
+                y_out(2, 1)
+                y_out(2, 2)
+            if n == 1:
+                for pair in range(3):
+                    y_out(3, pair)
         for q in range(P // QUAD):
             queue = nc.scalar if q % 2 else nc.sync
             queue.dma_start(

@@ -33,6 +33,7 @@ FIRST_USER = {NARROW: 0, WIDE: PAIR}
 USERS = {NARROW: PAIR, WIDE: 2 * PAIR}
 WIDE_TILES = USERS[WIDE] // P
 BANKS = 8
+PROB_BUFS = {NARROW: 8, WIDE: 12}
 
 
 def tile_click_value_planes_b4_kernel(
@@ -252,68 +253,106 @@ def tile_click_value_planes_b4_kernel(
         def w_quant(g, h):
             w_mx[g, h] = quantised("w%d_%d" % (g, h), w_grouped[g, h])
 
-        def hidden_sums(chunk, h, t):
-            per_bank = PASS // USERS[chunk]
-            first = USERS[chunk] * (t % per_bank)
-            if (chunk, h, t // per_bank) not in a_banks:
-                a_banks[chunk, h, t // per_bank] = take_bank(("a", chunk, h, t // per_bank))
-            return a_banks[chunk, h, t // per_bank][:, first : first + USERS[chunk]]
+        def w_operand(g, h, t):
+            codes, scales = w_mx[g, h]
+            return codes[:, P * t : P * (t + 1)].bitcast(FP8X4), scales[:, P * t : P * (t + 1)]
 
-        def hidden_pass(chunk, h, t, g):
-            w_codes, w_scales = w_mx[g, h]
+        def slot_sums(chunk, h, t):
+            per_bank = PASS // USERS[chunk]
+            key = ("slot", chunk, h, t // per_bank)
+            if key not in a_banks:
+                a_banks[key] = take_bank(key)
+            first = USERS[chunk] * (t % per_bank)
+            return a_banks[key][:, first : first + USERS[chunk]]
+
+        def slot_pass(chunk, h, t, g):
+            per_bank = PASS // USERS[chunk]
+            w_codes, w_scales = w_operand(g, h, t)
             x_codes, x_scales = x_mx[chunk, g]
             nc.tensor.matmul_mx(
-                out=hidden_sums(chunk, h, t),
-                lhsT=w_codes[:, P * t : P * (t + 1)].bitcast(FP8X4),
-                lhsT_scale=w_scales[:, P * t : P * (t + 1)],
+                out=slot_sums(chunk, h, t),
+                lhsT=w_codes,
+                lhsT_scale=w_scales,
                 rhs=x_codes[:].bitcast(FP8X4),
                 rhs_scale=x_scales[:],
-                start=(g == 0),
-                stop=(g == K_PASSES - 1),
+                start=(g == 0 and t % per_bank == 0),
+                stop=(g == K_PASSES - 1 and t % per_bank == per_bank - 1),
             )
 
-        def hidden_wide(h, g):
+        def tile_pass(i, h, g):
+            chunk = chunk_of(i // 2)
+            users = slice(P * i - FIRST_USER[chunk], P * (i + 1) - FIRST_USER[chunk])
+            if g == 0:
+                a_banks[i, h] = take_bank(("a", i, h))
+            x_codes, x_scales = x_mx[chunk, g]
             for t in range(SLOTS):
-                hidden_pass(WIDE, h, t, g)
+                w_codes, w_scales = w_operand(g, h, t)
+                nc.tensor.matmul_mx(
+                    out=a_banks[i, h][:, P * t : P * (t + 1)],
+                    lhsT=w_codes,
+                    lhsT_scale=w_scales,
+                    rhs=x_codes[:, users].bitcast(FP8X4),
+                    rhs_scale=x_scales[:, users],
+                    start=(g == 0 and t == 0),
+                    stop=(g == K_PASSES - 1 and t == SLOTS - 1),
+                )
 
-        def hidden_narrow(h, g):
-            for t in (0, 2):
-                hidden_pass(NARROW, h, t, g)
-                if g == K_PASSES - 1:
-                    for again in range(K_PASSES):
-                        hidden_pass(NARROW, h, t + 1, again)
-
-        def h_relu(chunk, h, slots=range(SLOTS), on=SCALAR):
-            if (chunk, h) not in h_planes:
-                h_planes[chunk, h] = slot_planes("h_planes", USERS[chunk])
-            for t in slots:
-                plane, sums = h_planes[chunk, h][:, t, :], hidden_sums(chunk, h, t)
-                column = gain_col[:, SLOTS * h + t : SLOTS * h + t + 1]
-                if on == SCALAR:
-                    nc.scalar.activation(out=plane, in_=sums, func=ACT.Relu, scale=column)
-                else:
-                    nc.vector.tensor_scalar(out=plane, in0=sums, scalar1=0.0, scalar2=column, op0=ALU.max, op1=ALU.mult)
-                per_bank = PASS // USERS[chunk]
-                if t % per_bank == per_bank - 1:
-                    give_back(("a", chunk, h, t // per_bank))
-
-        def h_group(chunk, h, copy=on_vector, users=slice(None)):
+        def h_tile(chunk, h):
             if (chunk, h) not in h_grouped:
                 h_grouped[chunk, h] = grouped_tile("h_grouped", USERS[chunk])
+            return h_grouped[chunk, h]
+
+        def h_fused(i, h):
+            chunk = chunk_of(i // 2)
+            first = SLOTS * (P * i - FIRST_USER[chunk])
+            nc.vector.scalar_tensor_tensor(
+                out=h_tile(chunk, h)[:, first : first + PASS].rearrange("p (m t) -> p m t", t=SLOTS),
+                in0=a_banks[i, h][:].rearrange("p (t m) -> p m t", t=SLOTS),
+                scalar=0.0,
+                in1=gain_col[:, SLOTS * h : SLOTS * (h + 1)].unsqueeze(1).to_broadcast([P, P, SLOTS]),
+                op0=ALU.max,
+                op1=ALU.mult,
+            )
+            give_back(("a", i, h))
+
+        def h_relu(chunk, h, t):
+            if (chunk, h) not in h_planes:
+                h_planes[chunk, h] = slot_planes("h_planes", USERS[chunk])
+            column = gain_col[:, SLOTS * h + t : SLOTS * h + t + 1]
+            nc.scalar.activation(out=h_planes[chunk, h][:, t, :], in_=slot_sums(chunk, h, t), func=ACT.Relu, scale=column)
+            per_bank = PASS // USERS[chunk]
+            if t % per_bank == per_bank - 1:
+                give_back(("slot", chunk, h, t // per_bank))
+
+        def h_group(chunk, h, copy, users=slice(None)):
             copy(
-                out=h_grouped[chunk, h][:].rearrange("p (m t) -> p m t", t=SLOTS)[:, users].rearrange("p (c i) t -> p c t i", i=4),
+                out=h_tile(chunk, h)[:].rearrange("p (m t) -> p m t", t=SLOTS)[:, users].rearrange("p (c i) t -> p c t i", i=4),
                 in_=h_planes[chunk, h][:, :, users].rearrange("p t (c i) -> p c t i", i=4),
             )
 
-        def h_quant(chunk, h):
-            h_mx[chunk, h] = quantised("h%d_%d" % (chunk, h), h_grouped[chunk, h])
+        def h_quant(chunk, h, users=slice(None)):
+            if (chunk, h) not in h_mx:
+                h_mx[chunk, h] = (
+                    keep.tile([P, USERS[chunk]], U32, name="h_codes%d_%d" % (chunk, h), align_bytes=64),
+                    keep.tile([P, USERS[chunk]], U8, name="h_scales%d_%d" % (chunk, h), align_bytes=64),
+                )
+            codes, scales = h_mx[chunk, h]
+            grouped = h_grouped[chunk, h][:].rearrange("p (m t) -> p m t", t=SLOTS)[:, users].rearrange("p m t -> p (m t)")
+            nc.vector.quantize_mx(out=codes[:, users].bitcast(FP8X4), scales=scales[:, users], in_=grouped)
 
-        def wide_logits(c):
-            z_banks[WIDE, c] = take_bank(("z", c))
-            for h in range(HALVES):
-                codes, scales = h_mx[WIDE, h]
+        def item_sums(chunk, c):
+            per_bank = PASS // USERS[chunk]
+            key = ("z", chunk, c // per_bank)
+            if key not in z_banks:
+                z_banks[key] = take_bank(key)
+            first = USERS[chunk] * (c % per_bank)
+            return z_banks[key][:, first : first + USERS[chunk]]
+
+        def item_logits(chunk, c, halves=range(HALVES)):
+            for h in halves:
+                codes, scales = h_mx[chunk, h]
                 nc.tensor.matmul_mx(
-                    out=z_banks[WIDE, c][:],
+                    out=item_sums(chunk, c),
                     lhsT=v_words[h][:, 2 * P * c : 2 * P * (c + 1)].bitcast(FP4X4),
                     lhsT_scale=v_scales[:, h, P * c : P * (c + 1)],
                     rhs=codes[:].bitcast(FP8X4),
@@ -322,16 +361,20 @@ def tile_click_value_planes_b4_kernel(
                     stop=(h == HALVES - 1),
                 )
 
-        def wide_sigmoid(c):
-            probs[WIDE, c] = work.tile([P, USERS[WIDE]], F32, name="wide_prob", bufs=12)
-            nc.scalar.activation(out=probs[WIDE, c][:], in_=z_banks[WIDE, c][:], func=ACT.Sigmoid, bias=bias_col[:, c : c + 1])
-            give_back(("z", c))
+        def item_sigmoid(chunk, c):
+            probs[chunk, c] = work.tile([P, USERS[chunk]], F32, name="prob%d" % chunk, bufs=PROB_BUFS[chunk])
+            nc.scalar.activation(out=probs[chunk, c][:], in_=item_sums(chunk, c), func=ACT.Sigmoid, bias=bias_col[:, c : c + 1])
+            per_bank = PASS // USERS[chunk]
+            if c % per_bank == per_bank - 1:
+                give_back(("z", chunk, c // per_bank))
 
-        def wide_turn(n, i):
+        def prob_turn(n, i):
+            chunk = chunk_of(i // 2)
+            first = P * i - FIRST_USER[chunk]
             prob_banks[n, i] = take_bank(("prob", n, i))
             for j in range(SLOTS):
                 nc.tensor.transpose(
-                    prob_banks[n, i][:, P * j : P * (j + 1)], probs[WIDE, SLOTS * n + j][:, P * i : P * (i + 1)], ident[:]
+                    prob_banks[n, i][:, P * j : P * (j + 1)], probs[chunk, SLOTS * n + j][:, first : first + P], ident[:]
                 )
 
         def bundle(n, pair):
@@ -344,9 +387,9 @@ def tile_click_value_planes_b4_kernel(
             row = first + step * (i % 2)
             return y_rows[key][:, PASS * row : PASS * (row + 1)]
 
-        def wide_value(n, i):
+        def turned_value(n, i):
             nc.vector.tensor_tensor(
-                out=value_row(n, 2 + i), in0=prob_banks[n, i][:], in1=bid_spread[:, PASS * n : PASS * (n + 1)], op=ALU.mult
+                out=value_row(n, i), in0=prob_banks[n, i][:], in1=bid_spread[:, PASS * n : PASS * (n + 1)], op=ALU.mult
             )
             give_back(("prob", n, i))
 
@@ -357,13 +400,13 @@ def tile_click_value_planes_b4_kernel(
                 in_=y_rows[WIDE, n][:, PASS * first : PASS * (first + 2)].rearrange("p (i n) -> p i n", i=2),
             )
 
-        def narrow_logits(n, i, halves=range(HALVES)):
+        def user_logits(n, i, halves=range(HALVES)):
             for h in halves:
                 if h == 0:
-                    z_banks[NARROW, n, i] = take_bank(("z", n, i))
+                    z_banks[n, i] = take_bank(("z", n, i))
                 codes, scales = h_mx[NARROW, h]
                 nc.tensor.matmul_mx(
-                    out=z_banks[NARROW, n, i][:],
+                    out=z_banks[n, i][:],
                     lhsT=codes[:, P * i : P * (i + 1)].bitcast(FP8X4),
                     lhsT_scale=scales[:, P * i : P * (i + 1)],
                     rhs=v_words[h][:, 2 * PASS * n : 2 * PASS * (n + 1)].bitcast(FP4X4),
@@ -372,20 +415,20 @@ def tile_click_value_planes_b4_kernel(
                     stop=(h == HALVES - 1),
                 )
 
-        def narrow_bias(n, i):
-            logits[n, i] = work.tile([P, PASS], F32, name="narrow_logit", bufs=4)
+        def user_bias(n, i):
+            logits[n, i] = work.tile([P, PASS], F32, name="user_logit", bufs=4)
             nc.vector.tensor_tensor(
-                out=logits[n, i][:], in0=z_banks[NARROW, n, i][:], in1=bias_spread[:, PASS * n : PASS * (n + 1)], op=ALU.add
+                out=logits[n, i][:], in0=z_banks[n, i][:], in1=bias_spread[:, PASS * n : PASS * (n + 1)], op=ALU.add
             )
             give_back(("z", n, i))
 
-        def narrow_sigmoid(n, i):
-            probs[NARROW, n, i] = work.tile([P, PASS], F32, name="narrow_prob", bufs=5)
-            nc.scalar.activation(out=probs[NARROW, n, i][:], in_=logits[n, i][:], func=ACT.Sigmoid)
+        def user_sigmoid(n, i):
+            probs["user", n, i] = work.tile([P, PASS], F32, name="user_prob", bufs=4)
+            nc.scalar.activation(out=probs["user", n, i][:], in_=logits[n, i][:], func=ACT.Sigmoid)
 
-        def narrow_value(n, i):
+        def user_value(n, i):
             nc.vector.tensor_tensor(
-                out=value_row(n, i), in0=probs[NARROW, n, i][:], in1=bid_spread[:, PASS * n : PASS * (n + 1)], op=ALU.mult
+                out=value_row(n, i), in0=probs["user", n, i][:], in1=bid_spread[:, PASS * n : PASS * (n + 1)], op=ALU.mult
             )
 
         def narrow_store(half, i):
@@ -480,7 +523,8 @@ def tile_click_value_planes_b4_kernel(
         w_group(1, 0)
         x_out(1, 0)
         x_out(2, 0)
-        hidden_narrow(0, 0)
+        for t in range(SLOTS):
+            slot_pass(NARROW, 0, t, 0)
         x_widen(3, 2, SCALAR)
         x_widen(5, 2, SCALAR)
         x_widen(4, 2)
@@ -495,165 +539,159 @@ def tile_click_value_planes_b4_kernel(
         w_quant(1, 0)
         for pair in range(3):
             x_out(pair, 2)
-        hidden_wide(0, 0)
+        for t in range(SLOTS):
+            slot_pass(WIDE, 0, t, 0)
         x_quant(WIDE, 1)
         w_quant(2, 0)
         x_quant(NARROW, 2)
         turn_bias()
-        hidden_narrow(0, 1)
-        hidden_wide(0, 1)
-        hidden_narrow(0, 2)
+        for chunk, g in ((NARROW, 1), (WIDE, 1), (NARROW, 2)):
+            for t in range(SLOTS):
+                slot_pass(chunk, 0, t, g)
 
         w_widen(1, 1)
         w_group(0, 1)
         x_quant(WIDE, 2)
-        hidden_wide(0, 2)
+        for t in range(SLOTS):
+            slot_pass(WIDE, 0, t, 2)
         widen_gain()
+        bias_out()
         w_widen(2, 1)
         w_group(1, 1)
-        h_relu(NARROW, 0)
+        for t in range(SLOTS):
+            h_relu(NARROW, 0, t)
         w_quant(0, 1)
         w_quant(1, 1)
         w_group(2, 1)
-        h_relu(WIDE, 0)
-        bias_out()
-        hidden_narrow(1, 0)
-        hidden_narrow(1, 1)
-        for t in range(SLOTS - 1):
-            hidden_pass(WIDE, 1, t, 0)
-            hidden_pass(WIDE, 1, t, 1)
+        for t in range(SLOTS):
+            h_relu(WIDE, 0, t)
+        for g in range(2):
+            tile_pass(0, 1, g)
+            tile_pass(1, 1, g)
+        for t in range(SLOTS):
+            slot_pass(WIDE, 1, t, 0)
+            slot_pass(WIDE, 1, t, 1)
+        h_group(NARROW, 0, on_vector, slice(0, P))
         w_quant(2, 1)
-        hidden_narrow(1, 2)
-        for t in range(SLOTS - 1):
-            hidden_pass(WIDE, 1, t, 2)
-        for g in range(K_PASSES):
-            hidden_pass(WIDE, 1, SLOTS - 1, g)
+        tile_pass(0, 1, 2)
+        tile_pass(1, 1, 2)
+        for t in range(SLOTS):
+            slot_pass(WIDE, 1, t, 2)
 
-        h_group(NARROW, 0)
-        h_quant(NARROW, 0)
-        h_group(WIDE, 0, on_scalar, slice(0, PAIR))
-        h_relu(NARROW, 1, (0, 1), VECTOR)
-        h_relu(NARROW, 1, (2, 3))
-        h_group(WIDE, 0, on_vector, slice(PAIR, 2 * PAIR))
-        h_group(NARROW, 1)
-        h_quant(NARROW, 1)
+        h_group(NARROW, 0, on_vector, slice(P, PAIR))
+        h_group(WIDE, 0, on_scalar)
+        h_quant(NARROW, 0, slice(0, P))
+        h_quant(NARROW, 0, slice(P, PAIR))
+        h_fused(0, 1)
+        h_fused(1, 1)
+        h_quant(NARROW, 1, slice(0, P))
         h_quant(WIDE, 0)
-        h_relu(WIDE, 1)
-        opened = ((0, 0), (1, 0), (0, 1))
+        h_quant(NARROW, 1, slice(P, PAIR))
+        for t in range(SLOTS):
+            h_relu(WIDE, 1, t)
         for h in range(HALVES):
-            for n, i in opened:
-                narrow_logits(n, i, (h,))
-        narrow_logits(1, 1)
+            user_logits(0, 0, (h,))
+            user_logits(1, 0, (h,))
+        user_logits(0, 1)
+        user_logits(1, 1)
+        user_bias(0, 0)
+        user_bias(1, 0)
         for i in range(2):
-            narrow_logits(2, i)
-            narrow_logits(3, i)
-        narrow_bias(0, 0)
+            user_logits(2, i)
+            user_logits(3, i)
         h_group(WIDE, 1, on_vector, slice(0, PAIR))
         h_group(WIDE, 1, on_scalar, slice(PAIR, 2 * PAIR))
-        narrow_bias(1, 0)
+        user_bias(0, 1)
         h_quant(WIDE, 1)
-        narrow_bias(0, 1)
-        narrow_bias(1, 1)
+        user_bias(1, 1)
         for i in range(2):
-            narrow_sigmoid(0, i)
-            narrow_sigmoid(1, i)
-
+            user_sigmoid(0, i)
+            user_sigmoid(1, i)
         for c in range(SLOTS):
-            wide_logits(c)
-        narrow_value(0, 0)
-        narrow_value(1, 0)
-        narrow_store(0, 0)
-        wide_sigmoid(0)
-        wide_logits(4)
-        wide_sigmoid(1)
-        wide_logits(5)
-        narrow_bias(2, 0)
-        wide_logits(6)
-        wide_sigmoid(2)
-        narrow_value(0, 1)
-        narrow_value(1, 1)
-        y_round((NARROW, 0), on_gpsimd)
-        narrow_store(0, 1)
-        wide_sigmoid(3)
-        narrow_bias(3, 0)
-        wide_sigmoid(4)
-        narrow_bias(2, 1)
-        wide_sigmoid(5)
-        for i in range(WIDE_TILES):
-            wide_turn(0, i)
-        wide_sigmoid(6)
-        wide_value(0, 0)
-        wide_value(0, 1)
-        wide_store(0, 1)
-        y_round((WIDE, 0), on_gpsimd, 0, 2)
-        narrow_bias(3, 1)
-        wide_value(0, 2)
-        wide_value(0, 3)
-        wide_store(0, 2)
-        for c in range(7, 13):
-            wide_logits(c)
+            item_logits(WIDE, c)
         for i in range(2):
-            narrow_sigmoid(2, i)
-            narrow_sigmoid(3, i)
-            if i == 0:
-                wide_sigmoid(7)
-            narrow_value(2, i)
-            narrow_value(3, i)
+            user_value(0, i)
+            user_value(1, i)
+            narrow_store(0, i)
+        y_round((NARROW, 0), on_gpsimd)
+        for c in range(3):
+            item_sigmoid(WIDE, c)
+            item_logits(WIDE, 4 + c)
+        for i in range(2):
+            user_bias(2, i)
+            user_bias(3, i)
+        for c in range(3, 7):
+            item_sigmoid(WIDE, c)
+        for i in range(2, 6):
+            prob_turn(0, i)
+        user_sigmoid(2, 0)
+        user_sigmoid(3, 0)
+        for i in range(2, 6):
+            turned_value(0, i)
+            if i % 2:
+                wide_store(0, i // 2)
+            if i == 3:
+                y_round((WIDE, 0), on_gpsimd, 0, 2)
+        for c in range(7, 13):
+            item_logits(WIDE, c)
+            if c == 7:
+                user_sigmoid(2, 1)
+                user_sigmoid(3, 1)
+            if c < 11:
+                item_sigmoid(WIDE, c)
+        for i in range(2):
+            user_value(2, i)
+            user_value(3, i)
             narrow_store(1, i)
         y_round((NARROW, 1), on_gpsimd)
-        wide_sigmoid(8)
-        for i in range(WIDE_TILES):
-            wide_turn(1, i)
-            if i == 2:
-                wide_sigmoid(9)
-        for c in range(13, ITEM_TILES):
-            wide_sigmoid(c - 3)
-            wide_logits(c)
-
-        planes_between = {(2, 1): (0, 0), (2, 2): (1, 0), (3, 0): (0, 1), (3, 1): (0, 2), (3, 2): (2, 0)}
-        for n in range(1, GROUPS):
-            for i in range(WIDE_TILES):
-                if n == 1 and i > 0:
-                    wide_sigmoid(12 + i)
-                if n == 3 and i == 0:
-                    y_round((WIDE, 0), on_scalar, 2, 4)
-                    y_out(0, 0)
-                    y_out(1, 0)
-                if n > 1:
-                    wide_turn(n, i)
-                    if (n, i) in planes_between:
-                        y_turn(*planes_between[n, i])
-                wide_value(n, i)
+        for i in range(2, 6):
+            prob_turn(1, i)
+        y_turn(0, 0)
+        y_turn(1, 0)
+        item_sigmoid(WIDE, 11)
+        item_sigmoid(WIDE, 12)
+        y_out(0, 0)
+        for i in range(2, 6):
+            turned_value(1, i)
+            if i % 2:
+                wide_store(1, i // 2)
+        y_round((WIDE, 1), on_gpsimd)
+        for c in range(13, 16):
+            item_logits(WIDE, c)
+            item_sigmoid(WIDE, c)
+        y_out(1, 0)
+        y_round((WIDE, 0), on_scalar, 2, 4)
+        planes_between = {(2, 5): (0, 1), (3, 2): (2, 0), (3, 3): (0, 2), (3, 4): (3, 0)}
+        for n in range(2, 4):
+            for i in range(2, 6):
+                prob_turn(n, i)
+                if (n, i) in planes_between:
+                    y_turn(*planes_between[n, i])
+                    y_out(*planes_between[n, i])
+                turned_value(n, i)
                 if i % 2:
-                    wide_store(n, 1 + i // 2)
-            if n < GROUPS - 1:
-                y_round((WIDE, n), on_gpsimd)
-        y_out(0, 1)
-        y_out(0, 2)
-        y_out(2, 0)
-
+                    wide_store(n, i // 2)
+            if n == 2:
+                y_round((WIDE, 2), on_gpsimd)
         y_turn(1, 1)
         y_turn(1, 2)
+        y_out(1, 1)
         y_round((WIDE, 3), on_scalar, 0, 2)
-        y_out(1, 1, on_vector)
+        y_out(1, 2, on_vector)
         y_quant(NARROW, 0)
         y_round((WIDE, 3), on_vector, 2, 4)
         y_turn(2, 1)
         y_turn(2, 2)
-        for pair in range(3):
-            y_turn(3, pair)
-        y_out(1, 2)
+        y_turn(3, 1)
+        y_turn(3, 2)
+        for n in range(2, 4):
+            y_out(n, 1)
+            y_out(n, 2)
         for n in range(GROUPS):
             if n > 0:
                 y_quant(NARROW, n)
             y_quant(WIDE, n)
             codes_store(n)
-            if n == 0:
-                y_out(2, 1)
-                y_out(2, 2)
-            if n == 1:
-                for pair in range(3):
-                    y_out(3, pair)
         for q in range(P // QUAD):
             queue = nc.scalar if q % 2 else nc.sync
             queue.dma_start(

@@ -33,7 +33,7 @@ FIRST_USER = {NARROW: 0, WIDE: PAIR}
 USERS = {NARROW: PAIR, WIDE: 2 * PAIR}
 WIDE_TILES = USERS[WIDE] // P
 BANKS = 8
-PROB_BUFS = {NARROW: 8, WIDE: 12}
+PROB_BUFS = {NARROW: 4, WIDE: 12}
 
 
 def tile_click_value_planes_b4_kernel(
@@ -315,11 +315,15 @@ def tile_click_value_planes_b4_kernel(
             )
             give_back(("a", i, h))
 
-        def h_relu(chunk, h, t):
+        def h_relu(chunk, h, t, on=SCALAR):
             if (chunk, h) not in h_planes:
                 h_planes[chunk, h] = slot_planes("h_planes", USERS[chunk])
             column = gain_col[:, SLOTS * h + t : SLOTS * h + t + 1]
-            nc.scalar.activation(out=h_planes[chunk, h][:, t, :], in_=slot_sums(chunk, h, t), func=ACT.Relu, scale=column)
+            plane, sums = h_planes[chunk, h][:, t, :], slot_sums(chunk, h, t)
+            if on == SCALAR:
+                nc.scalar.activation(out=plane, in_=sums, func=ACT.Relu, scale=column)
+            else:
+                nc.vector.tensor_scalar(out=plane, in0=sums, scalar1=0.0, scalar2=column, op0=ALU.max, op1=ALU.mult)
             per_bank = PASS // USERS[chunk]
             if t % per_bank == per_bank - 1:
                 give_back(("slot", chunk, h, t // per_bank))
@@ -349,6 +353,7 @@ def tile_click_value_planes_b4_kernel(
             return z_banks[key][:, first : first + USERS[chunk]]
 
         def item_logits(chunk, c, halves=range(HALVES)):
+            per_bank = PASS // USERS[chunk]
             for h in halves:
                 codes, scales = h_mx[chunk, h]
                 nc.tensor.matmul_mx(
@@ -357,8 +362,8 @@ def tile_click_value_planes_b4_kernel(
                     lhsT_scale=v_scales[:, h, P * c : P * (c + 1)],
                     rhs=codes[:].bitcast(FP8X4),
                     rhs_scale=scales[:],
-                    start=(h == 0),
-                    stop=(h == HALVES - 1),
+                    start=(h == 0 and c % per_bank == 0),
+                    stop=(h == HALVES - 1 and c % per_bank == per_bank - 1),
                 )
 
         def item_sigmoid(chunk, c):
@@ -416,19 +421,30 @@ def tile_click_value_planes_b4_kernel(
                 )
 
         def user_bias(n, i):
-            logits[n, i] = work.tile([P, PASS], F32, name="user_logit", bufs=4)
+            if (n // 2, i) not in logits:
+                logits[n // 2, i] = work.tile([P, 2 * PASS], F32, name="user_logit", bufs=3)
             nc.vector.tensor_tensor(
-                out=logits[n, i][:], in0=z_banks[n, i][:], in1=bias_spread[:, PASS * n : PASS * (n + 1)], op=ALU.add
+                out=logits[n // 2, i][:, PASS * (n % 2) : PASS * (n % 2 + 1)],
+                in0=z_banks[n, i][:],
+                in1=bias_spread[:, PASS * n : PASS * (n + 1)],
+                op=ALU.add,
             )
             give_back(("z", n, i))
 
-        def user_sigmoid(n, i):
-            probs["user", n, i] = work.tile([P, PASS], F32, name="user_prob", bufs=4)
-            nc.scalar.activation(out=probs["user", n, i][:], in_=logits[n, i][:], func=ACT.Sigmoid)
+        def user_sigmoid(i, n, groups=1):
+            if ("user", n // 2, i) not in probs:
+                probs["user", n // 2, i] = work.tile([P, 2 * PASS], F32, name="user_prob", bufs=3)
+            columns = slice(PASS * (n % 2), PASS * (n % 2 + groups))
+            nc.scalar.activation(out=probs["user", n // 2, i][:, columns], in_=logits[n // 2, i][:, columns], func=ACT.Sigmoid)
 
-        def user_value(n, i):
+        def user_value(i, n, groups=1):
+            value_row(n, i)
+            first = PASS * (2 * i + n % 2)
             nc.vector.tensor_tensor(
-                out=value_row(n, i), in0=probs["user", n, i][:], in1=bid_spread[:, PASS * n : PASS * (n + 1)], op=ALU.mult
+                out=y_rows[NARROW, n // 2][:, first : first + PASS * groups],
+                in0=probs["user", n // 2, i][:, PASS * (n % 2) : PASS * (n % 2 + groups)],
+                in1=bid_spread[:, PASS * n : PASS * (n + groups)],
+                op=ALU.mult,
             )
 
         def narrow_store(half, i):
@@ -557,18 +573,23 @@ def tile_click_value_planes_b4_kernel(
         widen_gain()
         bias_out()
         w_widen(2, 1)
+        w_quant(0, 1)
         w_group(1, 1)
         for t in range(SLOTS):
             h_relu(NARROW, 0, t)
-        w_quant(0, 1)
+        tile_pass(0, 1, 0)
+        tile_pass(1, 1, 0)
+        for t in range(2):
+            slot_pass(WIDE, 1, t, 0)
         w_quant(1, 1)
         w_group(2, 1)
         for t in range(SLOTS):
             h_relu(WIDE, 0, t)
-        for g in range(2):
-            tile_pass(0, 1, g)
-            tile_pass(1, 1, g)
-        for t in range(SLOTS):
+        tile_pass(0, 1, 1)
+        tile_pass(1, 1, 1)
+        for t in range(2):
+            slot_pass(WIDE, 1, t, 1)
+        for t in range(2, 4):
             slot_pass(WIDE, 1, t, 0)
             slot_pass(WIDE, 1, t, 1)
         h_group(NARROW, 0, on_vector, slice(0, P))
@@ -579,9 +600,10 @@ def tile_click_value_planes_b4_kernel(
             slot_pass(WIDE, 1, t, 2)
 
         h_group(NARROW, 0, on_vector, slice(P, PAIR))
-        h_group(WIDE, 0, on_scalar)
+        h_group(WIDE, 0, on_scalar, slice(P, 4 * P))
         h_quant(NARROW, 0, slice(0, P))
         h_quant(NARROW, 0, slice(P, PAIR))
+        h_group(WIDE, 0, on_vector, slice(0, P))
         h_fused(0, 1)
         h_fused(1, 1)
         h_quant(NARROW, 1, slice(0, P))
@@ -604,50 +626,46 @@ def tile_click_value_planes_b4_kernel(
         user_bias(0, 1)
         h_quant(WIDE, 1)
         user_bias(1, 1)
-        for i in range(2):
-            user_sigmoid(0, i)
-            user_sigmoid(1, i)
+        user_sigmoid(0, 0, 2)
+        user_sigmoid(1, 0)
+        user_sigmoid(1, 1)
         for c in range(SLOTS):
             item_logits(WIDE, c)
         for i in range(2):
-            user_value(0, i)
-            user_value(1, i)
+            user_value(i, 0, 2)
             narrow_store(0, i)
         y_round((NARROW, 0), on_gpsimd)
         for c in range(3):
             item_sigmoid(WIDE, c)
             item_logits(WIDE, 4 + c)
-        for i in range(2):
-            user_bias(2, i)
-            user_bias(3, i)
+        user_bias(2, 0)
+        user_bias(3, 0)
+        user_bias(2, 1)
         for c in range(3, 7):
             item_sigmoid(WIDE, c)
         for i in range(2, 6):
             prob_turn(0, i)
-        user_sigmoid(2, 0)
-        user_sigmoid(3, 0)
+        user_sigmoid(0, 2, 2)
         for i in range(2, 6):
             turned_value(0, i)
             if i % 2:
                 wide_store(0, i // 2)
             if i == 3:
                 y_round((WIDE, 0), on_gpsimd, 0, 2)
+                user_bias(3, 1)
         for c in range(7, 13):
             item_logits(WIDE, c)
             if c == 7:
-                user_sigmoid(2, 1)
-                user_sigmoid(3, 1)
+                user_sigmoid(1, 2, 2)
             if c < 11:
                 item_sigmoid(WIDE, c)
         for i in range(2):
-            user_value(2, i)
-            user_value(3, i)
+            user_value(i, 2, 2)
             narrow_store(1, i)
         y_round((NARROW, 1), on_gpsimd)
         for i in range(2, 6):
             prob_turn(1, i)
         y_turn(0, 0)
-        y_turn(1, 0)
         item_sigmoid(WIDE, 11)
         item_sigmoid(WIDE, 12)
         y_out(0, 0)
@@ -659,9 +677,8 @@ def tile_click_value_planes_b4_kernel(
         for c in range(13, 16):
             item_logits(WIDE, c)
             item_sigmoid(WIDE, c)
-        y_out(1, 0)
         y_round((WIDE, 0), on_scalar, 2, 4)
-        planes_between = {(2, 5): (0, 1), (3, 2): (2, 0), (3, 3): (0, 2), (3, 4): (3, 0)}
+        planes_between = {(2, 3): (1, 0), (2, 5): (0, 1), (3, 2): (2, 0), (3, 3): (0, 2), (3, 4): (3, 0)}
         for n in range(2, 4):
             for i in range(2, 6):
                 prob_turn(n, i)
@@ -679,6 +696,8 @@ def tile_click_value_planes_b4_kernel(
         y_round((WIDE, 3), on_scalar, 0, 2)
         y_out(1, 2, on_vector)
         y_quant(NARROW, 0)
+        y_quant(WIDE, 0)
+        codes_store(0)
         y_round((WIDE, 3), on_vector, 2, 4)
         y_turn(2, 1)
         y_turn(2, 2)
@@ -687,9 +706,8 @@ def tile_click_value_planes_b4_kernel(
         for n in range(2, 4):
             y_out(n, 1)
             y_out(n, 2)
-        for n in range(GROUPS):
-            if n > 0:
-                y_quant(NARROW, n)
+        for n in range(1, GROUPS):
+            y_quant(NARROW, n)
             y_quant(WIDE, n)
             codes_store(n)
         for q in range(P // QUAD):

@@ -555,15 +555,20 @@ def tile_click_value_planes_b4_kernel(
         w_quant(1, 0)
         for pair in range(3):
             x_out(pair, 2)
-        for t in range(SLOTS):
+        for t in range(SLOTS - 1):
             slot_pass(WIDE, 0, t, 0)
         x_quant(WIDE, 1)
         w_quant(2, 0)
         x_quant(NARROW, 2)
+        for t in range(SLOTS):
+            slot_pass(NARROW, 0, t, 1)
+        for t in range(SLOTS - 1):
+            slot_pass(WIDE, 0, t, 1)
+        for g in range(2):
+            slot_pass(WIDE, 0, SLOTS - 1, g)
+        for t in range(SLOTS):
+            slot_pass(NARROW, 0, t, 2)
         turn_bias()
-        for chunk, g in ((NARROW, 1), (WIDE, 1), (NARROW, 2)):
-            for t in range(SLOTS):
-                slot_pass(chunk, 0, t, g)
 
         w_widen(1, 1)
         w_group(0, 1)
@@ -571,8 +576,8 @@ def tile_click_value_planes_b4_kernel(
         for t in range(SLOTS):
             slot_pass(WIDE, 0, t, 2)
         widen_gain()
-        bias_out()
         w_widen(2, 1)
+        bias_out()
         w_quant(0, 1)
         w_group(1, 1)
         for t in range(SLOTS):
@@ -601,9 +606,8 @@ def tile_click_value_planes_b4_kernel(
 
         h_group(NARROW, 0, on_vector, slice(P, PAIR))
         h_group(WIDE, 0, on_scalar, slice(P, 4 * P))
-        h_quant(NARROW, 0, slice(0, P))
-        h_quant(NARROW, 0, slice(P, PAIR))
         h_group(WIDE, 0, on_vector, slice(0, P))
+        h_quant(NARROW, 0)
         h_fused(0, 1)
         h_fused(1, 1)
         h_quant(NARROW, 1, slice(0, P))

@@ -31,9 +31,7 @@ NARROW, WIDE = 0, 1
 VECTOR, SCALAR = 0, 1
 FIRST_USER = {NARROW: 0, WIDE: PAIR}
 USERS = {NARROW: PAIR, WIDE: 2 * PAIR}
-WIDE_TILES = USERS[WIDE] // P
 BANKS = 8
-PROB_BUFS = {NARROW: 4, WIDE: 12}
 
 
 def tile_click_value_planes_b4_kernel(
@@ -71,7 +69,7 @@ def tile_click_value_planes_b4_kernel(
             (g, h): keep.tile([P, SLOTS * PASS], U8, name="w_raw%d_%d" % (g, h)) for g in range(K_PASSES) for h in range(HALVES)
         }
         w_scale_rows = keep.tile([P, K_PASSES * (F // P)], F32, name="w_scale_rows")
-        quad_of = keep.tile([P, P], F32, name="quad_of")
+        same_quad = keep.tile([P, P], F32, name="same_quad")
         w_scale = keep.tile([P, K_PASSES, F // P], F32, name="w_scale")
         gain_bf = keep.tile([P, HALVES, SLOTS], BF16, name="gain_bf")
         gain_col = keep.tile([P, HALVES * SLOTS], F32, name="gain_col")
@@ -93,6 +91,9 @@ def tile_click_value_planes_b4_kernel(
         nc.vector.memset(bias_rows[:], 0.0)
         nc.vector.memset(v_scales[:].rearrange("p h n -> p (h n)").bitcast(I32), 0)
         make_identity(nc, ident[:], nomemset=True)
+        nc.vector.memset(same_quad[:], 0.0)
+        for q in range(P // QUAD):
+            nc.vector.memset(same_quad[QUAD * q : QUAD * (q + 1), QUAD * q : QUAD * (q + 1)], 1.0)
 
         def load_x_scale(chunk):
             users = slice(FIRST_USER[chunk], FIRST_USER[chunk] + USERS[chunk])
@@ -105,7 +106,7 @@ def tile_click_value_planes_b4_kernel(
 
         def load_w_scales():
             nc.sync.dma_start(
-                out=w_scale_rows[0 : P // QUAD, :].rearrange("q (g b) -> q g b", g=K_PASSES),
+                out=w_scale_rows[0:P:QUAD, :].rearrange("q (g b) -> q g b", g=K_PASSES),
                 in_=W_scale.rearrange("(g q) b -> q g b", g=K_PASSES),
             )
 
@@ -154,16 +155,10 @@ def tile_click_value_planes_b4_kernel(
         y_rows, y16, y_banks, y_grouped = {}, {}, {}, {}
         bias_bank, scale_bank = [], []
 
-        def make_quad_of():
-            nc.vector.tensor_copy(
-                out=quad_of[:].rearrange("p (q r) -> p q r", r=QUAD),
-                in_=ident[:, 0 : P // QUAD].unsqueeze(2).to_broadcast([P, P // QUAD, QUAD]),
-            )
-
         def spread_w_scales():
             spread = take_bank("scales")
             width = w_scale_rows.shape[1]
-            nc.tensor.matmul(spread[:, 0:width], lhsT=quad_of[:], rhs=w_scale_rows[:], start=True, stop=True)
+            nc.tensor.matmul(spread[:, 0:width], lhsT=same_quad[:], rhs=w_scale_rows[:], start=True, stop=True)
             scale_bank.append(spread[:, 0:width])
 
         def w_scales_out():
@@ -279,16 +274,15 @@ def tile_click_value_planes_b4_kernel(
                 stop=(g == K_PASSES - 1 and t % per_bank == per_bank - 1),
             )
 
-        def tile_pass(i, h, g):
-            chunk = chunk_of(i // 2)
-            users = slice(P * i - FIRST_USER[chunk], P * (i + 1) - FIRST_USER[chunk])
+        def tile_pass(i, g):
+            users = slice(P * i, P * (i + 1))
             if g == 0:
-                a_banks[i, h] = take_bank(("a", i, h))
-            x_codes, x_scales = x_mx[chunk, g]
+                a_banks[i] = take_bank(("tile", i))
+            x_codes, x_scales = x_mx[NARROW, g]
             for t in range(SLOTS):
-                w_codes, w_scales = w_operand(g, h, t)
+                w_codes, w_scales = w_operand(g, 1, t)
                 nc.tensor.matmul_mx(
-                    out=a_banks[i, h][:, P * t : P * (t + 1)],
+                    out=a_banks[i][:, P * t : P * (t + 1)],
                     lhsT=w_codes,
                     lhsT_scale=w_scales,
                     rhs=x_codes[:, users].bitcast(FP8X4),
@@ -302,28 +296,22 @@ def tile_click_value_planes_b4_kernel(
                 h_grouped[chunk, h] = grouped_tile("h_grouped", USERS[chunk])
             return h_grouped[chunk, h]
 
-        def h_fused(i, h):
-            chunk = chunk_of(i // 2)
-            first = SLOTS * (P * i - FIRST_USER[chunk])
+        def h_fused(i):
             nc.vector.scalar_tensor_tensor(
-                out=h_tile(chunk, h)[:, first : first + PASS].rearrange("p (m t) -> p m t", t=SLOTS),
-                in0=a_banks[i, h][:].rearrange("p (t m) -> p m t", t=SLOTS),
+                out=h_tile(NARROW, 1)[:, PASS * i : PASS * (i + 1)].rearrange("p (m t) -> p m t", t=SLOTS),
+                in0=a_banks[i][:].rearrange("p (t m) -> p m t", t=SLOTS),
                 scalar=0.0,
-                in1=gain_col[:, SLOTS * h : SLOTS * (h + 1)].unsqueeze(1).to_broadcast([P, P, SLOTS]),
+                in1=gain_col[:, SLOTS : 2 * SLOTS].unsqueeze(1).to_broadcast([P, P, SLOTS]),
                 op0=ALU.max,
                 op1=ALU.mult,
             )
-            give_back(("a", i, h))
+            give_back(("tile", i))
 
-        def h_relu(chunk, h, t, on=SCALAR):
+        def h_relu(chunk, h, t):
             if (chunk, h) not in h_planes:
                 h_planes[chunk, h] = slot_planes("h_planes", USERS[chunk])
             column = gain_col[:, SLOTS * h + t : SLOTS * h + t + 1]
-            plane, sums = h_planes[chunk, h][:, t, :], slot_sums(chunk, h, t)
-            if on == SCALAR:
-                nc.scalar.activation(out=plane, in_=sums, func=ACT.Relu, scale=column)
-            else:
-                nc.vector.tensor_scalar(out=plane, in0=sums, scalar1=0.0, scalar2=column, op0=ALU.max, op1=ALU.mult)
+            nc.scalar.activation(out=h_planes[chunk, h][:, t, :], in_=slot_sums(chunk, h, t), func=ACT.Relu, scale=column)
             per_bank = PASS // USERS[chunk]
             if t % per_bank == per_bank - 1:
                 give_back(("slot", chunk, h, t // per_bank))
@@ -344,43 +332,30 @@ def tile_click_value_planes_b4_kernel(
             grouped = h_grouped[chunk, h][:].rearrange("p (m t) -> p m t", t=SLOTS)[:, users].rearrange("p m t -> p (m t)")
             nc.vector.quantize_mx(out=codes[:, users].bitcast(FP8X4), scales=scales[:, users], in_=grouped)
 
-        def item_sums(chunk, c):
-            per_bank = PASS // USERS[chunk]
-            key = ("z", chunk, c // per_bank)
-            if key not in z_banks:
-                z_banks[key] = take_bank(key)
-            first = USERS[chunk] * (c % per_bank)
-            return z_banks[key][:, first : first + USERS[chunk]]
-
-        def item_logits(chunk, c, halves=range(HALVES)):
-            per_bank = PASS // USERS[chunk]
-            for h in halves:
-                codes, scales = h_mx[chunk, h]
+        def item_logits(c):
+            z_banks[c] = take_bank(("item", c))
+            for h in range(HALVES):
+                codes, scales = h_mx[WIDE, h]
                 nc.tensor.matmul_mx(
-                    out=item_sums(chunk, c),
+                    out=z_banks[c][:],
                     lhsT=v_words[h][:, 2 * P * c : 2 * P * (c + 1)].bitcast(FP4X4),
                     lhsT_scale=v_scales[:, h, P * c : P * (c + 1)],
                     rhs=codes[:].bitcast(FP8X4),
                     rhs_scale=scales[:],
-                    start=(h == 0 and c % per_bank == 0),
-                    stop=(h == HALVES - 1 and c % per_bank == per_bank - 1),
+                    start=(h == 0),
+                    stop=(h == HALVES - 1),
                 )
 
-        def item_sigmoid(chunk, c):
-            probs[chunk, c] = work.tile([P, USERS[chunk]], F32, name="prob%d" % chunk, bufs=PROB_BUFS[chunk])
-            nc.scalar.activation(out=probs[chunk, c][:], in_=item_sums(chunk, c), func=ACT.Sigmoid, bias=bias_col[:, c : c + 1])
-            per_bank = PASS // USERS[chunk]
-            if c % per_bank == per_bank - 1:
-                give_back(("z", chunk, c // per_bank))
+        def item_sigmoid(c):
+            probs[c] = work.tile([P, USERS[WIDE]], F32, name="item_prob", bufs=12)
+            nc.scalar.activation(out=probs[c][:], in_=z_banks[c][:], func=ACT.Sigmoid, bias=bias_col[:, c : c + 1])
+            give_back(("item", c))
 
         def prob_turn(n, i):
-            chunk = chunk_of(i // 2)
-            first = P * i - FIRST_USER[chunk]
+            first = P * i - FIRST_USER[WIDE]
             prob_banks[n, i] = take_bank(("prob", n, i))
             for j in range(SLOTS):
-                nc.tensor.transpose(
-                    prob_banks[n, i][:, P * j : P * (j + 1)], probs[chunk, SLOTS * n + j][:, first : first + P], ident[:]
-                )
+                nc.tensor.transpose(prob_banks[n, i][:, P * j : P * (j + 1)], probs[SLOTS * n + j][:, first : first + P], ident[:])
 
         def bundle(n, pair):
             return ((NARROW, n // 2), n % 2, 2) if pair == 0 else ((WIDE, n), 2 * (pair - 1), 1)
@@ -507,7 +482,6 @@ def tile_click_value_planes_b4_kernel(
         x_widen(0, 2)
         w_widen(0, 0, slice(0, 2 * PASS))
         w_widen(0, 0, slice(2 * PASS, 4 * PASS))
-        make_quad_of()
         spread_w_scales()
         x_widen(1, 0)
         x_widen(1, 1)
@@ -582,16 +556,16 @@ def tile_click_value_planes_b4_kernel(
         w_group(1, 1)
         for t in range(SLOTS):
             h_relu(NARROW, 0, t)
-        tile_pass(0, 1, 0)
-        tile_pass(1, 1, 0)
+        tile_pass(0, 0)
+        tile_pass(1, 0)
         for t in range(2):
             slot_pass(WIDE, 1, t, 0)
         w_quant(1, 1)
         w_group(2, 1)
         for t in range(SLOTS):
             h_relu(WIDE, 0, t)
-        tile_pass(0, 1, 1)
-        tile_pass(1, 1, 1)
+        tile_pass(0, 1)
+        tile_pass(1, 1)
         for t in range(2):
             slot_pass(WIDE, 1, t, 1)
         for t in range(2, 4):
@@ -599,8 +573,8 @@ def tile_click_value_planes_b4_kernel(
             slot_pass(WIDE, 1, t, 1)
         h_group(NARROW, 0, on_vector, slice(0, P))
         w_quant(2, 1)
-        tile_pass(0, 1, 2)
-        tile_pass(1, 1, 2)
+        tile_pass(0, 2)
+        tile_pass(1, 2)
         for t in range(SLOTS):
             slot_pass(WIDE, 1, t, 2)
 
@@ -608,8 +582,8 @@ def tile_click_value_planes_b4_kernel(
         h_group(WIDE, 0, on_scalar, slice(P, 4 * P))
         h_group(WIDE, 0, on_vector, slice(0, P))
         h_quant(NARROW, 0)
-        h_fused(0, 1)
-        h_fused(1, 1)
+        h_fused(0)
+        h_fused(1)
         h_quant(NARROW, 1, slice(0, P))
         h_quant(WIDE, 0)
         h_quant(NARROW, 1, slice(P, PAIR))
@@ -633,20 +607,21 @@ def tile_click_value_planes_b4_kernel(
         user_sigmoid(0, 0, 2)
         user_sigmoid(1, 0)
         user_sigmoid(1, 1)
+
         for c in range(SLOTS):
-            item_logits(WIDE, c)
+            item_logits(c)
         for i in range(2):
             user_value(i, 0, 2)
             narrow_store(0, i)
         y_round((NARROW, 0), on_gpsimd)
         for c in range(3):
-            item_sigmoid(WIDE, c)
-            item_logits(WIDE, 4 + c)
+            item_sigmoid(c)
+            item_logits(4 + c)
         user_bias(2, 0)
         user_bias(3, 0)
         user_bias(2, 1)
         for c in range(3, 7):
-            item_sigmoid(WIDE, c)
+            item_sigmoid(c)
         for i in range(2, 6):
             prob_turn(0, i)
         user_sigmoid(0, 2, 2)
@@ -658,31 +633,30 @@ def tile_click_value_planes_b4_kernel(
                 y_round((WIDE, 0), on_gpsimd, 0, 2)
                 user_bias(3, 1)
         for c in range(7, 13):
-            item_logits(WIDE, c)
+            item_logits(c)
             if c == 7:
                 user_sigmoid(1, 2, 2)
             if c < 11:
-                item_sigmoid(WIDE, c)
+                item_sigmoid(c)
         for i in range(2):
             user_value(i, 2, 2)
             narrow_store(1, i)
         y_round((NARROW, 1), on_gpsimd)
         for i in range(2, 6):
             prob_turn(1, i)
-        y_turn(0, 0)
-        item_sigmoid(WIDE, 11)
-        item_sigmoid(WIDE, 12)
-        y_out(0, 0)
+        item_sigmoid(11)
+        item_sigmoid(12)
+        y_round((WIDE, 0), on_scalar, 2, 4)
         for i in range(2, 6):
             turned_value(1, i)
             if i % 2:
                 wide_store(1, i // 2)
         y_round((WIDE, 1), on_gpsimd)
         for c in range(13, 16):
-            item_logits(WIDE, c)
-            item_sigmoid(WIDE, c)
-        y_round((WIDE, 0), on_scalar, 2, 4)
-        planes_between = {(2, 3): (1, 0), (2, 5): (0, 1), (3, 2): (2, 0), (3, 3): (0, 2), (3, 4): (3, 0)}
+            item_logits(c)
+            item_sigmoid(c)
+
+        planes_between = {(2, 3): (0, 0), (2, 4): (1, 0), (2, 5): (0, 1), (3, 2): (2, 0), (3, 3): (0, 2), (3, 4): (3, 0)}
         for n in range(2, 4):
             for i in range(2, 6):
                 prob_turn(n, i)
@@ -694,6 +668,7 @@ def tile_click_value_planes_b4_kernel(
                     wide_store(n, i // 2)
             if n == 2:
                 y_round((WIDE, 2), on_gpsimd)
+
         y_turn(1, 1)
         y_turn(1, 2)
         y_out(1, 1)

@@ -450,7 +450,7 @@ def tile_click_value_planes_b4_kernel(
                         y_banks[n, pair][:, PAIR * u + P * ii : PAIR * u + P * (ii + 1)], words[:, u, first + step * ii], ident[:]
                     )
 
-        def y_out(n, pair, copy=on_scalar):
+        def y_out(n, pair):
             chunk = chunk_of(pair)
             if (chunk, n) not in y_grouped:
                 tag = "grouped" if chunk == WIDE else "y_grouped"
@@ -458,18 +458,19 @@ def tile_click_value_planes_b4_kernel(
                     [P, SLOTS * USERS[chunk]], BF16, name="y_grouped", tag=tag, bufs=GROUPS, align_bytes=64
                 )
             first_word = 2 * (PAIR * pair - FIRST_USER[chunk])
-            copy(
+            nc.scalar.copy(
                 out=y_grouped[chunk, n][:].bitcast(F32)[:, first_word : first_word + 2 * PAIR].rearrange("p (m u) -> p m u", u=2),
                 in_=y_banks[n, pair][:].rearrange("p (u m) -> p m u", u=2),
             )
             give_back(("y", n, pair))
 
-        def y_quant(chunk, n):
-            first, last = FIRST_USER[chunk], FIRST_USER[chunk] + USERS[chunk]
+        def y_quant(chunk, n, first=0, count=None):
+            count = count or USERS[chunk]
+            user = FIRST_USER[chunk] + first
             nc.vector.quantize_mx(
-                out=y_codes[:, T * n + first : T * n + last].bitcast(FP8X4),
-                scales=y_scales[4 * n : P, first:last],
-                in_=y_grouped[chunk, n][:],
+                out=y_codes[:, T * n + user : T * n + user + count].bitcast(FP8X4),
+                scales=y_scales[4 * n : P, user : user + count],
+                in_=y_grouped[chunk, n][:, SLOTS * first : SLOTS * (first + count)],
             )
 
         def codes_store(n):
@@ -656,7 +657,8 @@ def tile_click_value_planes_b4_kernel(
             item_logits(c)
             item_sigmoid(c)
 
-        planes_between = {(2, 3): (0, 0), (2, 4): (1, 0), (2, 5): (0, 1), (3, 2): (2, 0), (3, 3): (0, 2), (3, 4): (3, 0)}
+        planes_between = {(2, 3): (0, 0), (2, 4): (1, 0), (2, 5): (0, 1), (3, 2): (0, 2), (3, 4): (1, 1)}
+        rounds_behind = {(2, 4): (on_gpsimd, 0, 3), (2, 5): (on_scalar, 3, 4), (3, 2): (on_scalar, 0, 1)}
         for n in range(2, 4):
             for i in range(2, 6):
                 prob_turn(n, i)
@@ -666,29 +668,24 @@ def tile_click_value_planes_b4_kernel(
                 turned_value(n, i)
                 if i % 2:
                     wide_store(n, i // 2)
-            if n == 2:
-                y_round((WIDE, 2), on_gpsimd)
+                if (n, i) in rounds_behind:
+                    y_round((WIDE, n), *rounds_behind[n, i])
 
-        y_turn(1, 1)
-        y_turn(1, 2)
-        y_out(1, 1)
-        y_round((WIDE, 3), on_scalar, 0, 2)
-        y_out(1, 2, on_vector)
         y_quant(NARROW, 0)
+        y_round((WIDE, 3), on_vector, 1, 4)
+        for n, pair in [(1, 2)] + [(n, pair) for n in range(2, 4) for pair in range(3)]:
+            y_turn(n, pair)
+            y_out(n, pair)
         y_quant(WIDE, 0)
         codes_store(0)
-        y_round((WIDE, 3), on_vector, 2, 4)
-        y_turn(2, 1)
-        y_turn(2, 2)
-        y_turn(3, 1)
-        y_turn(3, 2)
-        for n in range(2, 4):
-            y_out(n, 1)
-            y_out(n, 2)
-        for n in range(1, GROUPS):
+        for n in range(1, GROUPS - 1):
             y_quant(NARROW, n)
             y_quant(WIDE, n)
             codes_store(n)
+        y_quant(NARROW, GROUPS - 1)
+        for first in (0, PAIR):
+            y_quant(WIDE, GROUPS - 1, first, PAIR)
+        codes_store(GROUPS - 1)
         for q in range(P // QUAD):
             queue = nc.scalar if q % 2 else nc.sync
             queue.dma_start(

@@ -32,6 +32,9 @@ VECTOR, SCALAR = 0, 1
 FIRST_USER = {NARROW: 0, WIDE: PAIR}
 USERS = {NARROW: PAIR, WIDE: 2 * PAIR}
 BANKS = 8
+ROW_TILES = 6
+PLANE_TILES = 6
+PROB_TILES = 12
 
 
 def tile_click_value_planes_b4_kernel(
@@ -186,7 +189,7 @@ def tile_click_value_planes_b4_kernel(
             chunk = chunk_of(i // 2)
             row = i - FIRST_USER[chunk] // P
             if i // 2 not in x_pairs:
-                x_pairs[i // 2] = work.tile([P, 2 * K], BF16, name="x_wide", tag="rows", bufs=6, align_bytes=64)
+                x_pairs[i // 2] = work.tile([P, 2 * K], BF16, name="x_wide", tag="rows", bufs=ROW_TILES, align_bytes=64)
             x_wide[i] = x_pairs[i // 2][:, K * (i % 2) : K * (i % 2 + 1)]
             for b in range(SLOTS * g, SLOTS * (g + 1)):
                 block = slice(P * b, P * (b + 1))
@@ -211,7 +214,7 @@ def tile_click_value_planes_b4_kernel(
             chunk = chunk_of(pair)
             first_tile = 2 * pair - FIRST_USER[chunk] // P
             if g not in x_passes:
-                x_passes[g] = work.tile([P, SLOTS * T], BF16, name="x_grouped", tag="rows", bufs=6, align_bytes=64)
+                x_passes[g] = work.tile([P, SLOTS * T], BF16, name="x_grouped", tag="rows", bufs=ROW_TILES, align_bytes=64)
             x_grouped[chunk, g] = x_passes[g][:, SLOTS * FIRST_USER[chunk] : SLOTS * (FIRST_USER[chunk] + USERS[chunk])]
             words = x_grouped[chunk, g].bitcast(F32).rearrange("p (m i u) -> p m i u", m=P, u=2)
             nc.scalar.copy(
@@ -224,7 +227,7 @@ def tile_click_value_planes_b4_kernel(
             x_mx[chunk, g] = quantised("x%d_%d" % (chunk, g), x_grouped[chunk, g])
 
         def slot_planes(name, width):
-            return work.tile([P, SLOTS, width], BF16, name=name, tag="planes", bufs=6)
+            return work.tile([P, SLOTS, width], BF16, name=name, tag="planes", bufs=PLANE_TILES)
 
         def grouped_tile(name, width):
             return work.tile([P, SLOTS * width], BF16, name=name, tag="grouped", bufs=GROUPS, align_bytes=64)
@@ -347,7 +350,7 @@ def tile_click_value_planes_b4_kernel(
                 )
 
         def item_sigmoid(c):
-            probs[c] = work.tile([P, USERS[WIDE]], F32, name="item_prob", bufs=12)
+            probs[c] = work.tile([P, USERS[WIDE]], F32, name="item_prob", bufs=PROB_TILES)
             nc.scalar.activation(out=probs[c][:], in_=z_banks[c][:], func=ACT.Sigmoid, bias=bias_col[:, c : c + 1])
             give_back(("item", c))
 
@@ -363,7 +366,7 @@ def tile_click_value_planes_b4_kernel(
         def value_row(n, i):
             key, first, step = bundle(n, i // 2)
             if key not in y_rows:
-                y_rows[key] = work.tile([P, SLOTS * PASS], F32, name="y_rows", tag="rows", bufs=6, align_bytes=64)
+                y_rows[key] = work.tile([P, SLOTS * PASS], F32, name="y_rows", tag="rows", bufs=ROW_TILES, align_bytes=64)
             row = first + step * (i % 2)
             return y_rows[key][:, PASS * row : PASS * (row + 1)]
 
@@ -397,7 +400,7 @@ def tile_click_value_planes_b4_kernel(
 
         def user_bias(n, i):
             if (n // 2, i) not in logits:
-                logits[n // 2, i] = work.tile([P, 2 * PASS], F32, name="user_logit", bufs=3)
+                logits[n // 2, i] = work.tile([P, 2 * PASS], F32, name="user_logit")
             nc.vector.tensor_tensor(
                 out=logits[n // 2, i][:, PASS * (n % 2) : PASS * (n % 2 + 1)],
                 in0=z_banks[n, i][:],
@@ -408,7 +411,7 @@ def tile_click_value_planes_b4_kernel(
 
         def user_sigmoid(i, n, groups=1):
             if ("user", n // 2, i) not in probs:
-                probs["user", n // 2, i] = work.tile([P, 2 * PASS], F32, name="user_prob", bufs=3)
+                probs["user", n // 2, i] = work.tile([P, 2 * PASS], F32, name="user_prob")
             columns = slice(PASS * (n % 2), PASS * (n % 2 + groups))
             nc.scalar.activation(out=probs["user", n // 2, i][:, columns], in_=logits[n // 2, i][:, columns], func=ACT.Sigmoid)
 
@@ -434,7 +437,7 @@ def tile_click_value_planes_b4_kernel(
 
         def y_round(key, copy, first=0, last=SLOTS):
             if key not in y16:
-                y16[key] = work.tile([P, 2, SLOTS, P, 2], BF16, name="y16", tag="planes", bufs=6)
+                y16[key] = work.tile([P, 2, SLOTS, P, 2], BF16, name="y16", tag="planes", bufs=PLANE_TILES)
             copy(
                 out=y16[key][:, :, first:last],
                 in_=y_rows[key][:, PASS * first : PASS * last].rearrange("p (i r u e) -> p u i r e", r=P, u=2, e=2),
@@ -464,13 +467,12 @@ def tile_click_value_planes_b4_kernel(
             )
             give_back(("y", n, pair))
 
-        def y_quant(chunk, n, first=0, count=None):
-            count = count or USERS[chunk]
-            user = FIRST_USER[chunk] + first
+        def y_quant(chunk, n):
+            first, last = FIRST_USER[chunk], FIRST_USER[chunk] + USERS[chunk]
             nc.vector.quantize_mx(
-                out=y_codes[:, T * n + user : T * n + user + count].bitcast(FP8X4),
-                scales=y_scales[4 * n : P, user : user + count],
-                in_=y_grouped[chunk, n][:, SLOTS * first : SLOTS * (first + count)],
+                out=y_codes[:, T * n + first : T * n + last].bitcast(FP8X4),
+                scales=y_scales[4 * n : P, first:last],
+                in_=y_grouped[chunk, n][:],
             )
 
         def codes_store(n):
@@ -658,7 +660,7 @@ def tile_click_value_planes_b4_kernel(
             item_sigmoid(c)
 
         planes_between = {(2, 3): (0, 0), (2, 4): (1, 0), (2, 5): (0, 1), (3, 2): (0, 2), (3, 4): (1, 1)}
-        rounds_behind = {(2, 4): (on_gpsimd, 0, 3), (2, 5): (on_scalar, 3, 4), (3, 2): (on_scalar, 0, 1)}
+        rounds_behind = {(2, 4): (on_gpsimd, 0, 3), (2, 5): (on_scalar, 3, 4)}
         for n in range(2, 4):
             for i in range(2, 6):
                 prob_turn(n, i)
@@ -672,20 +674,16 @@ def tile_click_value_planes_b4_kernel(
                     y_round((WIDE, n), *rounds_behind[n, i])
 
         y_quant(NARROW, 0)
-        y_round((WIDE, 3), on_vector, 1, 4)
+        y_round((WIDE, 3), on_vector)
         for n, pair in [(1, 2)] + [(n, pair) for n in range(2, 4) for pair in range(3)]:
             y_turn(n, pair)
             y_out(n, pair)
         y_quant(WIDE, 0)
         codes_store(0)
-        for n in range(1, GROUPS - 1):
+        for n in range(1, GROUPS):
             y_quant(NARROW, n)
             y_quant(WIDE, n)
             codes_store(n)
-        y_quant(NARROW, GROUPS - 1)
-        for first in (0, PAIR):
-            y_quant(WIDE, GROUPS - 1, first, PAIR)
-        codes_store(GROUPS - 1)
         for q in range(P // QUAD):
             queue = nc.scalar if q % 2 else nc.sync
             queue.dma_start(

from contextlib import ExitStack

import concourse.mybir as mybir
from concourse.masks import make_identity

T, K, F, N = 768, 1536, 1024, 2048
FLOPS = 2 * T * K * F + 2 * T * F * N

F32 = mybir.dt.float32
BF16 = mybir.dt.bfloat16
I32 = mybir.dt.int32
U32 = mybir.dt.uint32
U8 = mybir.dt.uint8
FP8 = mybir.dt.float8_e4m3fn
FP8X4 = mybir.dt.float8_e4m3fn_x4
FP4X4 = mybir.dt.float4_e2m1fn_x4
ALU = mybir.AluOpType
ACT = mybir.ActivationFunctionType

P = 128
SLOTS = 4
PASS = P * SLOTS
QUAD = 32
K_PASSES = K // PASS
HALVES = F // PASS
GROUPS = N // PASS
ITEM_TILES = N // P
USER_TILES = T // P
PAIR = 2 * P
NARROW, WIDE = 0, 1
VECTOR, SCALAR = 0, 1
FIRST_USER = {NARROW: 0, WIDE: PAIR}
USERS = {NARROW: PAIR, WIDE: 2 * PAIR}
BANKS = 8
ROW_TILES = 6
PLANE_TILES = 6
PROB_TILES = 12


def tile_click_value_planes_b4_kernel(
    tc, X_bytes, X_scale, W_bytes, W_scale, gain, V_words, V_scales, item_bias, bid, out_0, out_1, out_2
):
    nc = tc.nc
    with ExitStack() as ctx:
        keep = ctx.enter_context(tc.tile_pool(name="keep", bufs=1))
        work = ctx.enter_context(tc.tile_pool(name="work", bufs=3))
        psum = ctx.enter_context(tc.psum_pool(name="psum", bufs=1))
        ctx.enter_context(tc.manual_schedule())
        on_scalar, on_vector = nc.scalar.copy, nc.vector.tensor_copy

        free_banks = list(range(BANKS))
        bank_of = {}

        def take_bank(key):
            number = free_banks.pop(0)
            bank_of[key] = number
            return psum.tile([P, PASS], F32, name="bank%d" % number, tag="bank%d" % number)

        def give_back(key):
            free_banks.append(bank_of[key])

        def quantised(name, grouped):
            width = grouped.shape[1] // SLOTS
            codes = keep.tile([P, width], U32, name=name + "_codes", align_bytes=64)
            scales = keep.tile([P, width], U8, name=name + "_scales", align_bytes=64)
            nc.vector.quantize_mx(out=codes[:].bitcast(FP8X4), scales=scales[:], in_=grouped[:])
            return codes, scales

        x_scale = [keep.tile([P, USERS[c] // P, K // P], F32, name="x_scale%d" % c) for c in (NARROW, WIDE)]
        x_raw = [keep.tile([P, K], U8, name="x_raw%d" % i) for i in range(USER_TILES)]
        w_raw = {
            (g, h): keep.tile([P, SLOTS * PASS], U8, name="w_raw%d_%d" % (g, h)) for g in range(K_PASSES) for h in range(HALVES)
        }
        w_scale_rows = keep.tile([P, K_PASSES * (F // P)], F32, name="w_scale_rows")
        same_quad = keep.tile([P, P], F32, name="same_quad")
        w_scale = keep.tile([P, K_PASSES, F // P], F32, name="w_scale")
        gain_bf = keep.tile([P, HALVES, SLOTS], BF16, name="gain_bf")
        gain_col = keep.tile([P, HALVES * SLOTS], F32, name="gain_col")
        v_words = [keep.tile([P, 2 * N], U8, name="v_words%d" % h, align_bytes=64) for h in range(HALVES)]
        v_scales = keep.tile([P, HALVES, N], U8, name="v_scales", align_bytes=64)
        bias_rows = keep.tile([P, P], BF16, name="bias_rows")
        picks = keep.tile([P, ITEM_TILES], BF16, name="picks")
        bias_col = keep.tile([P, ITEM_TILES], F32, name="bias_col")
        bias_spread = keep.tile([P, N], BF16, name="bias_spread")
        bid_spread = keep.tile([P, N], BF16, name="bid_spread")
        ident = keep.tile([P, P], F32, name="ident")
        y_codes = keep.tile([P, GROUPS * T], U32, name="y_codes", align_bytes=64)
        warm = keep.tile([P, 1], F32, name="warm")
        y_scales = keep.tile([P, T], U8, name="y_scales", align_bytes=64)

        nc.vector.memset(ident[:], 0.0)
        nc.vector.memset(w_scale_rows[:], 0.0)
        nc.vector.memset(warm[:], 0.0)
        nc.vector.memset(bias_rows[:], 0.0)
        nc.vector.memset(v_scales[:].rearrange("p h n -> p (h n)").bitcast(I32), 0)
        make_identity(nc, ident[:], nomemset=True)
        nc.vector.memset(same_quad[:], 0.0)
        for q in range(P // QUAD):
            nc.vector.memset(same_quad[QUAD * q : QUAD * (q + 1), QUAD * q : QUAD * (q + 1)], 1.0)

        def load_x_scale(chunk):
            users = slice(FIRST_USER[chunk], FIRST_USER[chunk] + USERS[chunk])
            nc.sync.dma_start(out=x_scale[chunk][:], in_=X_scale[users, :].rearrange("(p i) c -> p i c", p=P))

        def load_x(i, columns=slice(0, K)):
            chunk = NARROW if i < 2 else WIDE
            rows = X_bytes[FIRST_USER[chunk] : FIRST_USER[chunk] + USERS[chunk], :].rearrange("(p i) k -> p i k", p=P)
            nc.sync.dma_start(out=x_raw[i][:, columns], in_=rows[:, i - FIRST_USER[chunk] // P, columns])

        def load_w_scales():
            nc.sync.dma_start(
                out=w_scale_rows[0:P:QUAD, :].rearrange("q (g b) -> q g b", g=K_PASSES),
                in_=W_scale.rearrange("(g q) b -> q g b", g=K_PASSES),
            )

        def load_w(g, h, rows=slice(0, SLOTS)):
            nc.sync.dma_start(
                out=w_raw[g, h][:].rearrange("p (j f) -> p j f", j=SLOTS)[:, rows],
                in_=W_bytes[PASS * g : PASS * (g + 1), PASS * h : PASS * (h + 1)].rearrange("(p j) f -> p j f", j=SLOTS)[:, rows],
            )

        nc.scalar.activation(out=warm[:], in_=warm[:], func=ACT.Sigmoid)
        load_x_scale(NARROW)
        load_x(0, slice(0, PASS))
        load_w(0, 0, slice(0, 2))
        load_x(0, slice(PASS, K))
        load_w(0, 0, slice(2, 4))
        load_x(1)
        load_w_scales()
        load_x_scale(WIDE)
        load_x(2)
        load_x(3)
        load_w(1, 0)
        load_x(4)
        load_x(5)
        load_w(2, 0)
        load_w(0, 1)
        load_w(1, 1)
        load_w(2, 1)
        nc.sync.dma_start(out=gain_bf[:], in_=gain.rearrange("(h p t) -> p h t", h=HALVES, t=SLOTS))
        nc.sync.dma_start(out=bias_rows[0:ITEM_TILES, :], in_=item_bias.rearrange("(c p) -> c p", p=P))
        for q in range(P // QUAD):
            nc.sync.dma_start(
                out=v_scales[QUAD * q : QUAD * q + 4, :, :].bitcast(I32),
                in_=V_scales[:, 4 * q : 4 * q + 4, :].rearrange("h r n -> r h n").bitcast(I32),
            )
        for h in range(HALVES):
            nc.sync.dma_start(out=v_words[h][:].bitcast(I32), in_=V_words[h].bitcast(I32))
        for items in (slice(0, N // 2), slice(N // 2, N)):
            nc.sync.dma_start(out=bias_spread[:, items], in_=item_bias[items].partition_broadcast(P))
            nc.sync.dma_start(out=bid_spread[:, items], in_=bid[items].partition_broadcast(P))

        x_pairs, x_passes = {}, {}
        x_wide, x_banks, x_grouped, x_mx = {}, {}, {}, {}
        w_wide, w_grouped, w_mx = {}, {}, {}
        a_banks, h_planes, h_grouped, h_mx = {}, {}, {}, {}
        z_banks, logits, probs, prob_banks = {}, {}, {}, {}
        y_rows, y16, y_banks, y_grouped = {}, {}, {}, {}
        bias_bank, scale_bank = [], []

        def spread_w_scales():
            spread = take_bank("scales")
            width = w_scale_rows.shape[1]
            nc.tensor.matmul(spread[:, 0:width], lhsT=same_quad[:], rhs=w_scale_rows[:], start=True, stop=True)
            scale_bank.append(spread[:, 0:width])

        def w_scales_out():
            nc.scalar.copy(out=w_scale[:].rearrange("p g b -> p (g b)"), in_=scale_bank[0])
            give_back("scales")

        def widen_gain():
            nc.scalar.copy(out=gain_col[:], in_=gain_bf[:].rearrange("p h t -> p (h t)"))

        def make_picks():
            nc.scalar.copy(out=picks[:], in_=ident[:, 0:ITEM_TILES])

        def turn_bias():
            bias_bank.append(take_bank("bias"))
            nc.tensor.matmul(bias_bank[0][:, 0:ITEM_TILES], lhsT=bias_rows[:], rhs=picks[:], start=True, stop=True)

        def bias_out():
            nc.scalar.copy(out=bias_col[:], in_=bias_bank[0][:, 0:ITEM_TILES])
            give_back("bias")

        def chunk_of(pair):
            return NARROW if pair == 0 else WIDE

        def x_widen(i, g, on=VECTOR):
            chunk = chunk_of(i // 2)
            row = i - FIRST_USER[chunk] // P
            if i // 2 not in x_pairs:
                x_pairs[i // 2] = work.tile([P, 2 * K], BF16, name="x_wide", tag="rows", bufs=ROW_TILES, align_bytes=64)
            x_wide[i] = x_pairs[i // 2][:, K * (i % 2) : K * (i % 2 + 1)]
            for b in range(SLOTS * g, SLOTS * (g + 1)):
                block = slice(P * b, P * (b + 1))
                source, scale = x_raw[i][:, block].bitcast(FP8), x_scale[chunk][:, row, b : b + 1]
                if on == SCALAR:
                    nc.scalar.activation(out=x_wide[i][:, block], in_=source, func=ACT.Copy, scale=scale)
                else:
                    nc.vector.tensor_scalar(out=x_wide[i][:, block], in0=source, scalar1=scale, scalar2=None, op0=ALU.mult)

        def x_turn(pair, g):
            x_banks[pair, g] = take_bank(("x", pair, g))
            for ii in range(2):
                words = x_wide[2 * pair + ii].bitcast(F32)
                for u in range(2):
                    nc.tensor.transpose(
                        x_banks[pair, g][:, PAIR * u + ii : PAIR * (u + 1) : 2],
                        words[:, 2 * P * g + u : 2 * P * (g + 1) : 2],
                        ident[:],
                    )

        def x_out(pair, g):
            chunk = chunk_of(pair)
            first_tile = 2 * pair - FIRST_USER[chunk] // P
            if g not in x_passes:
                x_passes[g] = work.tile([P, SLOTS * T], BF16, name="x_grouped", tag="rows", bufs=ROW_TILES, align_bytes=64)
            x_grouped[chunk, g] = x_passes[g][:, SLOTS * FIRST_USER[chunk] : SLOTS * (FIRST_USER[chunk] + USERS[chunk])]
            words = x_grouped[chunk, g].bitcast(F32).rearrange("p (m i u) -> p m i u", m=P, u=2)
            nc.scalar.copy(
                out=words[:, :, first_tile : first_tile + 2, :],
                in_=x_banks[pair, g][:].rearrange("p (u m i) -> p m i u", u=2, i=2),
            )
            give_back(("x", pair, g))

        def x_quant(chunk, g):
            x_mx[chunk, g] = quantised("x%d_%d" % (chunk, g), x_grouped[chunk, g])

        def slot_planes(name, width):
            return work.tile([P, SLOTS, width], BF16, name=name, tag="planes", bufs=PLANE_TILES)

        def grouped_tile(name, width):
            return work.tile([P, SLOTS * width], BF16, name=name, tag="grouped", bufs=GROUPS, align_bytes=64)

        def w_widen(g, h, part=slice(None)):
            if (g, h) not in w_wide:
                w_wide[g, h] = slot_planes("w_wide", PASS)
            nc.scalar.copy(out=w_wide[g, h][:].rearrange("p j f -> p (j f)")[:, part], in_=w_raw[g, h][:, part].bitcast(FP8))

        def w_group(g, h):
            w_grouped[g, h] = grouped_tile("w_grouped", PASS)
            dst = w_grouped[g, h][:].rearrange("p (t m j) -> p m j t", t=SLOTS, j=SLOTS)
            src = w_wide[g, h][:].rearrange("p j (m t) -> p m j t", t=SLOTS)
            for b in range(PASS // P):
                block = slice(P // SLOTS * b, P // SLOTS * (b + 1))
                column = PASS // P * h + b
                nc.vector.tensor_scalar(
                    out=dst[:, block], in0=src[:, block], scalar1=w_scale[:, g, column : column + 1], scalar2=None, op0=ALU.mult
                )

        def w_quant(g, h):
            w_mx[g, h] = quantised("w%d_%d" % (g, h), w_grouped[g, h])

        def w_operand(g, h, t):
            codes, scales = w_mx[g, h]
            return codes[:, P * t : P * (t + 1)].bitcast(FP8X4), scales[:, P * t : P * (t + 1)]

        def slot_sums(chunk, h, t):
            per_bank = PASS // USERS[chunk]
            key = ("slot", chunk, h, t // per_bank)
            if key not in a_banks:
                a_banks[key] = take_bank(key)
            first = USERS[chunk] * (t % per_bank)
            return a_banks[key][:, first : first + USERS[chunk]]

        def slot_pass(chunk, h, t, g):
            per_bank = PASS // USERS[chunk]
            w_codes, w_scales = w_operand(g, h, t)
            x_codes, x_scales = x_mx[chunk, g]
            nc.tensor.matmul_mx(
                out=slot_sums(chunk, h, t),
                lhsT=w_codes,
                lhsT_scale=w_scales,
                rhs=x_codes[:].bitcast(FP8X4),
                rhs_scale=x_scales[:],
                start=(g == 0 and t % per_bank == 0),
                stop=(g == K_PASSES - 1 and t % per_bank == per_bank - 1),
            )

        def tile_pass(i, g):
            users = slice(P * i, P * (i + 1))
            if g == 0:
                a_banks[i] = take_bank(("tile", i))
            x_codes, x_scales = x_mx[NARROW, g]
            for t in range(SLOTS):
                w_codes, w_scales = w_operand(g, 1, t)
                nc.tensor.matmul_mx(
                    out=a_banks[i][:, P * t : P * (t + 1)],
                    lhsT=w_codes,
                    lhsT_scale=w_scales,
                    rhs=x_codes[:, users].bitcast(FP8X4),
                    rhs_scale=x_scales[:, users],
                    start=(g == 0 and t == 0),
                    stop=(g == K_PASSES - 1 and t == SLOTS - 1),
                )

        def h_tile(chunk, h):
            if (chunk, h) not in h_grouped:
                h_grouped[chunk, h] = grouped_tile("h_grouped", USERS[chunk])
            return h_grouped[chunk, h]

        def h_fused(i):
            nc.vector.scalar_tensor_tensor(
                out=h_tile(NARROW, 1)[:, PASS * i : PASS * (i + 1)].rearrange("p (m t) -> p m t", t=SLOTS),
                in0=a_banks[i][:].rearrange("p (t m) -> p m t", t=SLOTS),
                scalar=0.0,
                in1=gain_col[:, SLOTS : 2 * SLOTS].unsqueeze(1).to_broadcast([P, P, SLOTS]),
                op0=ALU.max,
                op1=ALU.mult,
            )
            give_back(("tile", i))

        def h_relu(chunk, h, t):
            if (chunk, h) not in h_planes:
                h_planes[chunk, h] = slot_planes("h_planes", USERS[chunk])
            column = gain_col[:, SLOTS * h + t : SLOTS * h + t + 1]
            nc.scalar.activation(out=h_planes[chunk, h][:, t, :], in_=slot_sums(chunk, h, t), func=ACT.Relu, scale=column)
            per_bank = PASS // USERS[chunk]
            if t % per_bank == per_bank - 1:
                give_back(("slot", chunk, h, t // per_bank))

        def h_group(chunk, h, copy, users=slice(None)):
            copy(
                out=h_tile(chunk, h)[:].rearrange("p (m t) -> p m t", t=SLOTS)[:, users].rearrange("p (c i) t -> p c t i", i=4),
                in_=h_planes[chunk, h][:, :, users].rearrange("p t (c i) -> p c t i", i=4),
            )

        def h_quant(chunk, h, users=slice(None)):
            if (chunk, h) not in h_mx:
                h_mx[chunk, h] = (
                    keep.tile([P, USERS[chunk]], U32, name="h_codes%d_%d" % (chunk, h), align_bytes=64),
                    keep.tile([P, USERS[chunk]], U8, name="h_scales%d_%d" % (chunk, h), align_bytes=64),
                )
            codes, scales = h_mx[chunk, h]
            grouped = h_grouped[chunk, h][:].rearrange("p (m t) -> p m t", t=SLOTS)[:, users].rearrange("p m t -> p (m t)")
            nc.vector.quantize_mx(out=codes[:, users].bitcast(FP8X4), scales=scales[:, users], in_=grouped)

        def item_logits(c):
            z_banks[c] = take_bank(("item", c))
            for h in range(HALVES):
                codes, scales = h_mx[WIDE, h]
                nc.tensor.matmul_mx(
                    out=z_banks[c][:],
                    lhsT=v_words[h][:, 2 * P * c : 2 * P * (c + 1)].bitcast(FP4X4),
                    lhsT_scale=v_scales[:, h, P * c : P * (c + 1)],
                    rhs=codes[:].bitcast(FP8X4),
                    rhs_scale=scales[:],
                    start=(h == 0),
                    stop=(h == HALVES - 1),
                )

        def item_sigmoid(c):
            probs[c] = work.tile([P, USERS[WIDE]], F32, name="item_prob", bufs=PROB_TILES)
            nc.scalar.activation(out=probs[c][:], in_=z_banks[c][:], func=ACT.Sigmoid, bias=bias_col[:, c : c + 1])
            give_back(("item", c))

        def prob_turn(n, i):
            first = P * i - FIRST_USER[WIDE]
            prob_banks[n, i] = take_bank(("prob", n, i))
            for j in range(SLOTS):
                nc.tensor.transpose(prob_banks[n, i][:, P * j : P * (j + 1)], probs[SLOTS * n + j][:, first : first + P], ident[:])

        def bundle(n, pair):
            return ((NARROW, n // 2), n % 2, 2) if pair == 0 else ((WIDE, n), 2 * (pair - 1), 1)

        def value_row(n, i):
            key, first, step = bundle(n, i // 2)
            if key not in y_rows:
                y_rows[key] = work.tile([P, SLOTS * PASS], F32, name="y_rows", tag="rows", bufs=ROW_TILES, align_bytes=64)
            row = first + step * (i % 2)
            return y_rows[key][:, PASS * row : PASS * (row + 1)]

        def turned_value(n, i):
            nc.vector.tensor_tensor(
                out=value_row(n, i), in0=prob_banks[n, i][:], in1=bid_spread[:, PASS * n : PASS * (n + 1)], op=ALU.mult
            )
            give_back(("prob", n, i))

        def wide_store(n, pair):
            first = bundle(n, pair)[1]
            nc.sync.dma_start(
                out=out_0[PAIR * pair : PAIR * (pair + 1), PASS * n : PASS * (n + 1)].rearrange("(i p) n -> p i n", p=P),
                in_=y_rows[WIDE, n][:, PASS * first : PASS * (first + 2)].rearrange("p (i n) -> p i n", i=2),
            )

        def user_logits(n, i, halves=range(HALVES)):
            for h in halves:
                if h == 0:
                    z_banks[n, i] = take_bank(("z", n, i))
                codes, scales = h_mx[NARROW, h]
                nc.tensor.matmul_mx(
                    out=z_banks[n, i][:],
                    lhsT=codes[:, P * i : P * (i + 1)].bitcast(FP8X4),
                    lhsT_scale=scales[:, P * i : P * (i + 1)],
                    rhs=v_words[h][:, 2 * PASS * n : 2 * PASS * (n + 1)].bitcast(FP4X4),
                    rhs_scale=v_scales[:, h, PASS * n : PASS * (n + 1)],
                    start=(h == 0),
                    stop=(h == HALVES - 1),
                )

        def user_bias(n, i):
            if (n // 2, i) not in logits:
                logits[n // 2, i] = work.tile([P, 2 * PASS], F32, name="user_logit")
            nc.vector.tensor_tensor(
                out=logits[n // 2, i][:, PASS * (n % 2) : PASS * (n % 2 + 1)],
                in0=z_banks[n, i][:],
                in1=bias_spread[:, PASS * n : PASS * (n + 1)],
                op=ALU.add,
            )
            give_back(("z", n, i))

        def user_sigmoid(i, n, groups=1):
            if ("user", n // 2, i) not in probs:
                probs["user", n // 2, i] = work.tile([P, 2 * PASS], F32, name="user_prob")
            columns = slice(PASS * (n % 2), PASS * (n % 2 + groups))
            nc.scalar.activation(out=probs["user", n // 2, i][:, columns], in_=logits[n // 2, i][:, columns], func=ACT.Sigmoid)

        def user_value(i, n, groups=1):
            value_row(n, i)
            first = PASS * (2 * i + n % 2)
            nc.vector.tensor_tensor(
                out=y_rows[NARROW, n // 2][:, first : first + PASS * groups],
                in0=probs["user", n // 2, i][:, PASS * (n % 2) : PASS * (n % 2 + groups)],
                in1=bid_spread[:, PASS * n : PASS * (n + groups)],
                op=ALU.mult,
            )

        def narrow_store(half, i):
            width = 2 * PASS
            nc.sync.dma_start(
                out=out_0[P * i : P * (i + 1), width * half : width * (half + 1)],
                in_=y_rows[NARROW, half][:, width * i : width * (i + 1)],
            )

        def on_gpsimd(out, in_):
            nc.gpsimd.tensor_scalar(out=out, in0=in_, scalar1=1.0, scalar2=0.0, op0=ALU.mult, op1=ALU.add)

        def y_round(key, copy, first=0, last=SLOTS):
            if key not in y16:
                y16[key] = work.tile([P, 2, SLOTS, P, 2], BF16, name="y16", tag="planes", bufs=PLANE_TILES)
            copy(
                out=y16[key][:, :, first:last],
                in_=y_rows[key][:, PASS * first : PASS * last].rearrange("p (i r u e) -> p u i r e", r=P, u=2, e=2),
            )

        def y_turn(n, pair):
            key, first, step = bundle(n, pair)
            y_banks[n, pair] = take_bank(("y", n, pair))
            words = y16[key][:].rearrange("p u i r e -> p u i (r e)").bitcast(F32)
            for ii in range(2):
                for u in range(2):
                    nc.tensor.transpose(
                        y_banks[n, pair][:, PAIR * u + P * ii : PAIR * u + P * (ii + 1)], words[:, u, first + step * ii], ident[:]
                    )

        def y_out(n, pair):
            chunk = chunk_of(pair)
            if (chunk, n) not in y_grouped:
                tag = "grouped" if chunk == WIDE else "y_grouped"
                y_grouped[chunk, n] = work.tile(
                    [P, SLOTS * USERS[chunk]], BF16, name="y_grouped", tag=tag, bufs=GROUPS, align_bytes=64
                )
            first_word = 2 * (PAIR * pair - FIRST_USER[chunk])
            nc.scalar.copy(
                out=y_grouped[chunk, n][:].bitcast(F32)[:, first_word : first_word + 2 * PAIR].rearrange("p (m u) -> p m u", u=2),
                in_=y_banks[n, pair][:].rearrange("p (u m) -> p m u", u=2),
            )
            give_back(("y", n, pair))

        def y_quant(chunk, n):
            first, last = FIRST_USER[chunk], FIRST_USER[chunk] + USERS[chunk]
            nc.vector.quantize_mx(
                out=y_codes[:, T * n + first : T * n + last].bitcast(FP8X4),
                scales=y_scales[4 * n : P, first:last],
                in_=y_grouped[chunk, n][:],
            )

        def codes_store(n):
            nc.sync.dma_start(
                out=out_1[n].rearrange("p m t -> p (m t)").bitcast(I32), in_=y_codes[:, T * n : T * (n + 1)].bitcast(I32)
            )

        x_widen(0, 0, SCALAR)
        x_widen(0, 1)
        x_widen(0, 2)
        w_widen(0, 0, slice(0, 2 * PASS))
        w_widen(0, 0, slice(2 * PASS, 4 * PASS))
        spread_w_scales()
        x_widen(1, 0)
        x_widen(1, 1)
        x_widen(1, 2, SCALAR)
        x_turn(0, 0)
        x_turn(0, 1)
        w_scales_out()
        make_picks()
        x_widen(2, 0)
        w_group(0, 0)
        x_widen(3, 0, SCALAR)
        x_widen(2, 2, SCALAR)
        x_turn(1, 0)
        w_widen(1, 0)
        for i in range(2, 4):
            x_widen(i, 1)
        for i in range(4, 6):
            x_widen(i, 0)
            x_widen(i, 1)
        x_out(0, 0)
        x_out(0, 1)
        w_widen(2, 0)
        x_turn(2, 0)
        x_turn(1, 1)
        x_turn(2, 1)
        x_turn(0, 2)
        w_quant(0, 0)
        x_quant(NARROW, 0)
        w_group(1, 0)
        x_out(1, 0)
        x_out(2, 0)
        for t in range(SLOTS):
            slot_pass(NARROW, 0, t, 0)
        x_widen(3, 2, SCALAR)
        x_widen(5, 2, SCALAR)
        x_widen(4, 2)
        x_quant(NARROW, 1)
        w_group(2, 0)
        x_out(1, 1)
        x_out(2, 1)
        x_turn(1, 2)
        x_turn(2, 2)
        w_widen(0, 1)
        x_quant(WIDE, 0)
        w_quant(1, 0)
        for pair in range(3):
            x_out(pair, 2)
        for t in range(SLOTS - 1):
            slot_pass(WIDE, 0, t, 0)
        x_quant(WIDE, 1)
        w_quant(2, 0)
        x_quant(NARROW, 2)
        for t in range(SLOTS):
            slot_pass(NARROW, 0, t, 1)
        for t in range(SLOTS - 1):
            slot_pass(WIDE, 0, t, 1)
        for g in range(2):
            slot_pass(WIDE, 0, SLOTS - 1, g)
        for t in range(SLOTS):
            slot_pass(NARROW, 0, t, 2)
        turn_bias()

        w_widen(1, 1)
        w_group(0, 1)
        x_quant(WIDE, 2)
        for t in range(SLOTS):
            slot_pass(WIDE, 0, t, 2)
        widen_gain()
        w_widen(2, 1)
        bias_out()
        w_quant(0, 1)
        w_group(1, 1)
        for t in range(SLOTS):
            h_relu(NARROW, 0, t)
        tile_pass(0, 0)
        tile_pass(1, 0)
        for t in range(2):
            slot_pass(WIDE, 1, t, 0)
        w_quant(1, 1)
        w_group(2, 1)
        for t in range(SLOTS):
            h_relu(WIDE, 0, t)
        tile_pass(0, 1)
        tile_pass(1, 1)
        for t in range(2):
            slot_pass(WIDE, 1, t, 1)
        for t in range(2, 4):
            slot_pass(WIDE, 1, t, 0)
            slot_pass(WIDE, 1, t, 1)
        h_group(NARROW, 0, on_vector, slice(0, P))
        w_quant(2, 1)
        tile_pass(0, 2)
        tile_pass(1, 2)
        for t in range(SLOTS):
            slot_pass(WIDE, 1, t, 2)

        h_group(NARROW, 0, on_vector, slice(P, PAIR))
        h_group(WIDE, 0, on_scalar, slice(P, 4 * P))
        h_group(WIDE, 0, on_vector, slice(0, P))
        h_quant(NARROW, 0)
        h_fused(0)
        h_fused(1)
        h_quant(NARROW, 1, slice(0, P))
        h_quant(WIDE, 0)
        h_quant(NARROW, 1, slice(P, PAIR))
        for t in range(SLOTS):
            h_relu(WIDE, 1, t)
        for h in range(HALVES):
            user_logits(0, 0, (h,))
            user_logits(1, 0, (h,))
        user_logits(0, 1)
        user_logits(1, 1)
        user_bias(0, 0)
        user_bias(1, 0)
        for i in range(2):
            user_logits(2, i)
            user_logits(3, i)
        h_group(WIDE, 1, on_vector, slice(0, PAIR))
        h_group(WIDE, 1, on_scalar, slice(PAIR, 2 * PAIR))
        user_bias(0, 1)
        h_quant(WIDE, 1)
        user_bias(1, 1)
        user_sigmoid(0, 0, 2)
        user_sigmoid(1, 0)
        user_sigmoid(1, 1)

        for c in range(SLOTS):
            item_logits(c)
        for i in range(2):
            user_value(i, 0, 2)
            narrow_store(0, i)
        y_round((NARROW, 0), on_gpsimd)
        for c in range(3):
            item_sigmoid(c)
            item_logits(4 + c)
        user_bias(2, 0)
        user_bias(3, 0)
        user_bias(2, 1)
        for c in range(3, 7):
            item_sigmoid(c)
        for i in range(2, 6):
            prob_turn(0, i)
        user_sigmoid(0, 2, 2)
        for i in range(2, 6):
            turned_value(0, i)
            if i % 2:
                wide_store(0, i // 2)
            if i == 3:
                y_round((WIDE, 0), on_gpsimd, 0, 2)
                user_bias(3, 1)
        for c in range(7, 13):
            item_logits(c)
            if c == 7:
                user_sigmoid(1, 2, 2)
            if c < 11:
                item_sigmoid(c)
        for i in range(2):
            user_value(i, 2, 2)
            narrow_store(1, i)
        y_round((NARROW, 1), on_gpsimd)
        for i in range(2, 6):
            prob_turn(1, i)
        item_sigmoid(11)
        item_sigmoid(12)
        y_round((WIDE, 0), on_scalar, 2, 4)
        for i in range(2, 6):
            turned_value(1, i)
            if i % 2:
                wide_store(1, i // 2)
        y_round((WIDE, 1), on_gpsimd)
        for c in range(13, 16):
            item_logits(c)
            item_sigmoid(c)

        planes_between = {(2, 3): (0, 0), (2, 4): (1, 0), (2, 5): (0, 1), (3, 2): (0, 2), (3, 4): (1, 1)}
        rounds_behind = {(2, 4): (on_gpsimd, 0, 3), (2, 5): (on_scalar, 3, 4)}
        for n in range(2, 4):
            for i in range(2, 6):
                prob_turn(n, i)
                if (n, i) in planes_between:
                    y_turn(*planes_between[n, i])
                    y_out(*planes_between[n, i])
                turned_value(n, i)
                if i % 2:
                    wide_store(n, i // 2)
                if (n, i) in rounds_behind:
                    y_round((WIDE, n), *rounds_behind[n, i])

        y_quant(NARROW, 0)
        y_round((WIDE, 3), on_vector)
        for n, pair in [(1, 2)] + [(n, pair) for n in range(2, 4) for pair in range(3)]:
            y_turn(n, pair)
            y_out(n, pair)
        y_quant(WIDE, 0)
        codes_store(0)
        for n in range(1, GROUPS):
            y_quant(NARROW, n)
            y_quant(WIDE, n)
            codes_store(n)
        for q in range(P // QUAD):
            queue = nc.scalar if q % 2 else nc.sync
            queue.dma_start(
                out=out_2[:, 4 * q : 4 * q + 4, :].bitcast(I32), in_=y_scales[QUAD * q : QUAD * q + 4 * GROUPS, :].bitcast(I32)
            )
